import numpy as np, ml_dtypes
CORES = [16,17,18,19,32,33,34,35]
N = 8
BF = ml_dtypes.bfloat16
def gentries(a):
    return np.ascontiguousarray(a.reshape(8, 16, -1).transpose(0, 2, 1)).reshape(8, -1)
def gtable(e):
    e = np.asarray(e); return np.ascontiguousarray(e.reshape(8, -1, 16).transpose(0, 2, 1)).reshape(128, -1).astype(np.int32)
P, M, B, R, VI, HO, NEED = 3072, 4096, 128, 32, 3, 3, 10
F, C, TM = B // 2, M // (B // 2), R // 2
HALF = (16 - NEED) // 2
def stock(rng):
    mem = np.stack([rng.permutation(M) for g in range(8)]); fo = np.zeros((8, M), np.int64)
    np.put_along_axis(fo, mem, np.tile(np.repeat(np.arange(F), C), (8, 1)), 1)
    ml = rng.choice(np.array([1, 1, 2, 2, 3, 3, 4, 5, 6, TM]), (8, F))
    st = rng.integers(1, F, (8, F, TM)); st[:, :, 0] = np.arange(F)
    return mem.reshape(8, F, C), fo, ml, np.add.accumulate(st, axis=2) % F
def runs(rng, st, fam, same):
    mem, fo, ml, mot = st; sh = fam.shape + (R,); gi = np.arange(8)[:, None]; gj = np.arange(8)[:, None, None]; s = np.arange(R)
    n = ml[gi, fam]; ln = np.minimum(n + rng.integers(0, n + 2), R)
    key = rng.random(sh); key[..., 0] = -1.0; key = np.where(s < ln[..., None], key, 2.0)
    k = np.add.accumulate((np.argsort(np.argsort(key, axis=-1), axis=-1) < n[..., None]).astype(np.int64), axis=-1) - 1
    k = np.minimum(k, TM - 1); fs = mot[gi, fam]; nm = mem[gj, fs, rng.integers(0, C, fs.shape)]
    t = np.take_along_axis(nm, k, -1); alike = mem[gj, np.take_along_axis(fs, k, -1), rng.integers(0, C, sh)]
    hit = (s == ln[..., None] - 1) | (rng.random(sh) < 0.06)
    return ln, np.where(hit, np.where(rng.random(sh) < same, t, alike), rng.integers(0, M, sh)), t
def voices(rng, st, base, alts, mode):
    x = base[:, np.arange(8)[:, None], st[1]]; pool = np.argsort(rng.random((256, 16)), axis=-1)
    m = pool[rng.integers(0, 256, (N, 8, M))] < rng.choice(np.array(alts), (N, 8, M))[..., None]
    if mode == "flip": y = -x
    elif mode == "near": y = np.where(x == 15, 14, x + 1)
    else: y = (x + 15 + rng.integers(1, 31, x.shape)) % 31 - 15
    return np.where(m, y, x)
def parts(rng, same=0.3, lo=F, mode="any", alts=(0, 1, HALF, HALF, HALF + 1), base=None, skew=1):
    st = stock(rng); fo = st[1]; gi = np.arange(8)[:, None]; s = np.arange(R)
    if base is None: base = rng.integers(-15, 16, (N, 8, F, 16))
    d = {"fo": fo, "x": voices(rng, st, base, alts, mode)}
    cf = np.argsort(rng.random((N, 8, B)), axis=-1) // 2; own = np.argsort(cf, axis=-1, kind="stable").reshape(N, 8, F, 2)
    ln, u, t = runs(rng, st, cf, same); d["cf"] = cf
    d["bl"] = np.where(rng.random(ln.shape) < 0.15, np.maximum(ln - 1, 1), ln); d["bu"] = u; d["bt"] = t
    bk = own[np.arange(N)[:, None, None], gi, fo[None], rng.integers(0, 2, (N, 8, M))]; v = rng.random(bk.shape)
    d["bk"] = np.where(v < 0.1, -1, np.where(v < 0.16, rng.integers(0, B, bk.shape), bk))
    ln, u, t = runs(rng, st, (lo * rng.random((N, 8, P // 2)) ** skew).astype(np.int64), same); m = s < ln[..., None]
    d["pu"] = np.stack([np.stack([np.resize(u[q, g][m[q, g]], P) for g in range(8)]) for q in range(N)])
    d["pt"] = np.stack([np.stack([np.resize(t[q, g][m[q, g]], P) for g in range(8)]) for q in range(N)])
    d["pn"] = np.where(rng.random((N, 8)) < 0.3, P, rng.integers(3 * P // 4, P + 1, (N, 8)))
    d["th"] = rng.integers(550, 850, (N, 8))
    return d
def pack(d):
    i = lambda a, *sh: np.ascontiguousarray(np.reshape(a, (N, 8) + sh)).astype(np.int32)
    return {"tones": np.ascontiguousarray(d["x"].transpose(0, 1, 3, 2)).reshape(N, 128, M).astype(np.float32).astype(BF),
            "pu": np.stack([gtable(a) for a in d["pu"]]), "pt": np.stack([gtable(a) for a in d["pt"]]), "pn": i(d["pn"], 1),
            "bu": i(d["bu"], B * R), "bt": i(d["bt"], B * R), "bl": i(d["bl"], B), "bk": i(d["bk"], M), "th": i(d["th"], 1)}
def signs(rng, *sh):
    return 15 * (2 * rng.integers(0, 2, sh) - 1)
def setup_inputs(rng):
    return pack(parts(rng))
def setup_inputs_spread(rng):
    b = rng.integers(-15, 16, (N, 8, F, 16)); b = np.sign(b) * (np.abs(b) >> rng.choice(np.array([0, 0, 0, 1, 2, 3]), (N, 8, F, 1)))
    d = parts(rng, same=0.5, base=b, skew=3)
    w = (2 * rng.integers(0, 2, (N, 8)) - 1) * np.minimum(np.exp2(12 * rng.random((N, 8))).astype(np.int64), 3600)
    d["th"] = np.where(rng.random((N, 8)) < 0.4, w, rng.integers(150, 900, (N, 8)))
    d["pn"] = np.where(rng.random((N, 8)) < 0.3, np.minimum(np.exp2(12 * rng.random((N, 8))).astype(np.int64), P), rng.integers(1, P + 1, (N, 8)))
    d["bk"] = np.where(rng.random((N, 8, M)) < 0.25, rng.integers(-1, B, (N, 8, M)), d["bk"])
    return pack(d)
def poles(rng, sh):
    mt = rng.integers(0, 3, sh + (1,)); mu = rng.integers(0, 3, sh + (1,)); a = rng.integers(0, 2, sh + (R,))
    t = np.where(mt == 0, a, np.where(mt == 1, a[..., :1], np.arange(R) % 2)); u = np.where(mu == 0, rng.integers(0, 2, sh + (R,)), np.where(mu == 1, t, 1 - t))
    return u * (M - 1), t * (M - 1)
def setup_inputs_ends(rng):
    lo = F // 4; d = parts(rng, same=0.8, lo=lo, mode="flip", base=signs(rng, N, 8, F, 16)); x = d["x"]
    v = signs(rng, N, 8, 16); x[:, :, 0] = v; x[:, :, M - 1] = -v
    m = rng.random((N, 8, P // R, 1)) < 0.75; u, t = poles(rng, (N, 8, P // R))
    d["pu"] = np.where(m, u, d["pu"].reshape(u.shape)).reshape(N, 8, P); d["pt"] = np.where(m, t, d["pt"].reshape(u.shape)).reshape(N, 8, P)
    dead = d["cf"] >= lo; u, t = poles(rng, (N, 8, B)); one = np.where(rng.random((N, 8, B)) < 0.5, 1, R)
    dead[..., 0] = True; dead[..., B - 1] = True
    d["bl"] = np.where(dead, one, d["bl"]); d["bu"] = np.where(dead[..., None], u, d["bu"]); d["bt"] = np.where(dead[..., None], t, d["bt"])
    d["bk"] = np.where(d["fo"][None] < lo, d["bk"], np.where(rng.random((N, 8, M)) < 0.5, -1, B - 1)); d["bk"][..., 0] = 0; d["bk"][..., M - 1] = B - 1
    d["bt"][:, :, 0] = 0; d["bt"][:, :, B - 1] = M - 1; turn = np.where(np.arange(R) % 2 == 0, M - 1, 0)
    for q in range(N):
        d["th"][q, rng.permutation(7)] = np.array([3600, 3600, -3600, -3600, -3600, 3151, 3150]); d["th"][q, 7] = 3600
        d["pn"][q, rng.permutation(7)] = np.array([1, 1, P, P, P, P - 1 - int(rng.integers(0, R)), P // 2 + int(rng.integers(0, R))]); d["pn"][q, 7] = P
        d["pt"][q, 7, P - R:] = turn; d["pu"][q, 7, P - R:] = M - 1 - turn; d["pu"][q, 7, P - 1] = turn[R - 1]
        for g in range(8):
            if d["th"][q, g] == 3600: d["bt"][q, g, B - 1] = turn; d["bl"][q, g, B - 1] = R
    return pack(d)
def setup_inputs_corners(rng):
    d = parts(rng); x = d["x"]; sh = int(rng.integers(0, 8)); s = np.arange(R)
    for g in range(8):
        kind = (g + sh) % 8; nm = rng.permutation(M); e, z, rest = nm[:12], nm[12], nm[13:]; lx = rng.integers(2, R + 1, 12); grow = int(np.sum(lx - 1))
        if kind == 7:
            d["bk"][::2, g] = -1; d["pn"][:, g] = P; continue
        for q in range(N):
            x[q, g, nm[:13]] = signs(rng, 13, 16); d["th"][q, g] = 3600; cs = rng.permutation(B)[:12]
            d["bk"][q, g] = -1; d["bk"][q, g, e] = cs; ln = lx
            a = rest[rng.integers(0, len(rest), P)]; b = rest[rng.integers(0, len(rest), P)]; at = R * (1 + rng.permutation(P // (2 * R) - 1)[:12])
            if kind == 4: at[0] = P - R
            ix = at[:, None] + s
            n = P; bt = np.repeat(e[:, None], R, axis=1)
            if kind == 0:
                n = 1; a[0] = e[0]; b[0] = e[0]; ln = np.full(12, 1 + q % 3)
            elif kind <= 4:
                a[at] = e; b[at] = e; a[at - 1] = z; b[at - 1] = z
                if kind == 4: ln = np.full(12, R)
                else: n = P - grow + (0, 0, -1, 1)[kind]
            elif kind == 5:
                a[ix] = e[:, None]; b[ix] = e[:, None]; ln = rng.choice(np.array([1, 2, 3]), 12)
            else:
                bt = np.where(s % 2 == 0, e[:, None], z); a[ix] = bt; ln = R - np.arange(12) % 2
            d["pt"][q, g] = a; d["pu"][q, g] = b; d["pn"][q, g] = n
            d["bl"][q, g, cs] = ln; d["bt"][q, g, cs] = bt; d["bu"][q, g, cs] = rest[rng.integers(0, len(rest), (12, R))]; d["bu"][q, g, cs, ln - 1] = e
    return pack(d)
def setup_inputs_crowd(rng):
    d = parts(rng); x = d["x"]; sh = int(rng.integers(0, 8)); nb = P // R
    full = min(nb, B); at = R * (np.arange(full) * (nb - 1) // (full - 1)); ix = at[:, None] + np.arange(R)
    for g in range(8):
        kind = (g + sh) % 8
        if kind == 3: continue
        if kind >= 4:
            nm = rng.permutation(M); e, rest = nm[:full], nm[full:]
            lo = 1 if kind == 6 or P - full * R + 3 * full // 2 > 280 else 3
            for q in range(N):
                x[q, g, e] = signs(rng, full, 16); d["th"][q, g] = 3600
                cs = rng.permutation(np.append(1 + rng.permutation(B - 2)[:full - 2], [0, B - 1]))
                d["bk"][q, g] = -1; d["bk"][q, g, e] = cs
                a = rest[rng.integers(0, len(rest), P)]; b = rest[rng.integers(0, len(rest), P)]
                if kind <= 5:
                    a[at] = e; b[at] = e; ln = np.full(full, R)
                else:
                    a[ix] = e[:, None]; b[ix] = e[:, None]; ln = lo + np.arange(full) % 2
                d["pt"][q, g] = a; d["pu"][q, g] = b; d["pn"][q, g] = P
                d["bl"][q, g, cs] = ln; d["bt"][q, g, cs] = e[:, None]; d["bu"][q, g, cs] = rest[rng.integers(0, len(rest), (full, R))]; d["bu"][q, g, cs, ln - 1] = e
            continue
        nm = rng.permutation(M)[:4]
        for q in range(N):
            x[q, g, nm] = signs(rng, 4, 16); cs = rng.permutation(B)[:3]; ln = rng.choice(np.array([2, 3, R - 1, R]), 3)
            d["bk"][q, g, nm] = np.append(cs, -1); d["bl"][q, g, cs] = ln; d["bt"][q, g, cs] = nm[:3, None]; d["bu"][q, g, cs, ln - 1] = nm[:3]
            w = np.zeros(nb, np.int64)
            if kind == 1: w[int(rng.choice(np.array([0, nb - 1, int(rng.integers(0, nb))])))] = 1
            if kind == 2: w = rng.integers(0, 3, nb)
            t = np.where(np.arange(P) % 2 == 0, nm[np.repeat(w, R)], nm[3])
            d["pt"][q, g] = t; d["pu"][q, g] = t; d["pn"][q, g] = P
    return pack(d)
def filler(rng, d, q, g, th, rest):
    d["th"][q, g] = th; d["pn"][q, g] = P; d["bk"][q, g] = -1
    d["pu"][q, g] = rest[rng.integers(0, len(rest), P)]; d["pt"][q, g] = rest[np.add.accumulate(rng.integers(1, len(rest), P)) % len(rest)]
def near(rng, a, n):
    i = rng.permutation(16)[:n]; y = np.array(a); y[i] = np.where(a[i] == 15, 14, a[i] + 1)
    return y
def lay(rng, n):
    s = np.arange(R); n = n[:, None]
    return np.sort(np.where(s < n, s, rng.integers(0, R, (len(n), R)) % n), axis=1)
def clones(rng, d, g):
    nm = rng.permutation(M); a = nm[:12 * R].reshape(12, R); b = nm[12 * R:24 * R].reshape(12, R); rest = nm[24 * R:]
    h = [int(v) for v in rng.integers(9, R + 1, 4)]; late = int(rng.integers(8, h[3]))
    na = np.array([3, 3, 2, h[0], h[1], R, h[2], R, h[3], 2, 1, 3]); nb = np.array([3, 2, 3, h[0], h[1], R, h[2], R, h[3], 1, 2, 3])
    for q in range(N):
        filler(rng, d, q, g, 3600, rest)
        x = rng.integers(-15, 16, (12, R, 16)); x[:3, 1] = x[:3, 0]; x[3, h[0] - 1] = x[3, h[0] - 2]; x[11, 1:3] = 0; y = np.array(x)
        y[1, 1] = x[1, 2]; x[2, 1] = y[2, 2]; x[9, 1] = 0; y[10, 1] = 0
        y[6, h[2] - 1] = near(rng, x[6, h[2] - 1], 17 - NEED); y[7, R - 1] = near(rng, x[7, R - 1], 16 - NEED); y[8, late] = near(rng, x[8, late], 17 - NEED)
        d["x"][q, g, a] = x; d["x"][q, g, b] = y; cs = rng.permutation(B)[:12]
        d["bk"][q, g, a[:, 0]] = cs; d["bk"][q, g, b[:, 0]] = cs
        ix = R * rng.permutation(P // R)[:12][:, None] + np.arange(R)
        d["pt"][q, g, ix] = np.take_along_axis(a, lay(rng, na), 1)
        d["bt"][q, g, cs] = np.take_along_axis(b, lay(rng, nb), 1); d["bu"][q, g, cs] = rest[rng.integers(0, len(rest), (12, R))]; d["bl"][q, g, cs] = R
def bound(rng, d, g, sg, ths):
    nm = rng.permutation(M); e, z, w, l, rest = nm[:16], nm[16:32], nm[32:96], nm[96:160], nm[160:]
    i = np.arange(16); pc = i & 1; bc = (i >> 1) & 1; s = np.arange(R); o = int(rng.integers(0, 4))
    for q in range(N):
        th = ths[(q + o) % 4]; filler(rng, d, q, g, th, rest)
        k = int(rng.integers(0, 16)); v = signs(rng, 16); v[k] = 1; up = sg * v; up[k] = th - sg * 3375; lo = np.array(up); lo[k] = up[k] - 1
        d["x"][q, g, e] = v; d["x"][q, g, w] = up; d["x"][q, g, l] = lo
        cs = rng.permutation(B)[:16]; d["bk"][q, g, e] = cs; at = R * rng.permutation(P // R)[:16]; t = np.where(s == 0, e[:, None], z[:, None])
        d["pt"][q, g, at[:, None] + s] = t; d["pu"][q, g, at] = np.where(pc == 1, l[rng.integers(0, 64, 16)], w[rng.integers(0, 64, 16)])
        d["bt"][q, g, cs] = t; d["bl"][q, g, cs] = np.where(bc == 1, R, 1)
        u = rest[rng.integers(0, len(rest), (16, R))]; u[:, 0] = np.where(bc == 1, l[rng.integers(0, 64, 16)], w[rng.integers(0, 64, 16)]); d["bu"][q, g, cs] = u
def singles(rng, d, g):
    pr = rng.permutation(M // 2); side = rng.integers(0, 2, 12); e = 2 * pr[:12] + side; y = 2 * pr[:12] + 1 - side
    rest = (2 * pr[12:, None] + np.arange(2)).reshape(-1)
    for q in range(N):
        filler(rng, d, q, g, -3600, rest)
        at = R * np.append(P // R - 1, rng.permutation(P // R - 1)[:11]) + R - 1; cs = rng.permutation(B)[:12]
        d["pt"][q, g, at] = e; d["pt"][q, g, at - 1] = y; d["pu"][q, g, at - 1] = y
        d["bk"][q, g, e] = cs; d["bl"][q, g, cs] = 1; d["bt"][q, g, cs, 0] = e; d["bu"][q, g, cs, 0] = rest[rng.integers(0, len(rest), 12)]
def setup_inputs_edge(rng):
    d = parts(rng, mode="near", alts=(HALF, HALF, HALF, HALF + 1)); x = d["x"]; sh = int(rng.integers(0, 8))
    m = rng.random((N, 8, P)) < 0.04; m[..., 0] = False; d["pt"] = np.where(m, np.roll(d["pt"], 1, axis=-1), d["pt"])
    for q in range(N):
        for g in range(8):
            if (g + sh) % 8 >= 4: continue
            u, t = d["pu"][q, g], d["pt"][q, g]; v = np.add.reduce(x[q, g][u] * x[q, g][t], axis=1)[:-1]
            v = np.unique(v[t[1:] != t[:-1]]); v = v[(v > 1026) & (v < 1300)]; w = v[np.isin(v - 1, v)]
            if len(w): d["th"][q, g] = rng.choice(w)
            elif len(v): d["th"][q, g] = rng.choice(v)
    for g in range(8):
        kind = (g + sh) % 8
        if kind == 4: clones(rng, d, g)
        elif kind == 5: bound(rng, d, g, -1, (-3375, -3371, -3372, -3378))
        elif kind == 6: bound(rng, d, g, 1, (3376, 3372, 3373, 3377))
        elif kind == 7: singles(rng, d, g)
    return pack(d)
def check_inputs(d):
    bad = []
    for k, lo, hi in (("tones", -15, 15), ("pu", 0, M - 1), ("pt", 0, M - 1), ("pn", 1, P), ("bu", 0, M - 1), ("bt", 0, M - 1), ("bl", 1, R), ("bk", -1, B - 1), ("th", -3600, 3600)):
        a = np.asarray(d[k]).astype(np.float32)
        if not np.all((a >= lo) & (a <= hi)): bad.append("range of " + k)
        elif k == "tones" and np.any(a != np.rint(a)): bad.append("whole numbers in tones")
        elif k == "tones" and np.any((a == 0) & np.signbit(a)): bad.append("-0.0 in tones")
    return bad
def tone_numbers(t, head):
    new = np.array(head); new[1:] |= t[1:] != t[:-1]; cnt = np.add.accumulate(new.astype(np.int64))
    return cnt - cnt[np.maximum.accumulate(np.where(head, np.arange(len(t)), 0))]
def visit(x, u, t, bu, bt, bl, bk, th):
    n = len(t); j = np.arange(n); s = np.arange(R)
    score = np.add.reduce(x[u] * x[t], axis=1)
    end = (j % R == R - 1) | (j == n - 1); end[:-1] |= (t[1:] != t[:-1]) & (score[:-1] >= th)
    head = np.ones(n, bool); head[1:] = end[:-1]
    first = np.flatnonzero(head); last = np.flatnonzero(end); size = last - first + 1
    k = tone_numbers(t, head)
    bh = np.zeros((B, R), bool); bh[:, 0] = True; kb = tone_numbers(bt.reshape(-1), bh.reshape(-1)).reshape(B, R)
    ci, si = np.nonzero(s < bl[:, None]); key = np.zeros((B, R), np.int64); key[ci, kb[ci, si]] = bt[ci, si]
    tones_of = kb[np.arange(B), bl - 1] + 1
    c = bk[t[first]]; c0 = np.maximum(c, 0)
    agree = np.add.reduce((x[t] == x[key[np.repeat(c0, size), k]]).astype(np.int64), axis=1) >= NEED
    match = (c >= 0) & (k[last] + 1 == tones_of[c0]) & (np.minimum.reduceat(agree.astype(np.int64), first) == 1)
    o = np.flatnonzero(match); o = o[np.unique(first[o] // R, return_index=True)[1]]
    o = o[np.unique(c[o], return_index=True)[1]]
    begin = np.array(first); length = np.array(size); begin[o] = n + c[o] * R; length[o] = bl[c[o]]
    before = np.add.accumulate(length) - length; src = (np.repeat(begin - before, length) + np.arange(np.sum(length)))[:P]
    nu = np.concatenate([u, bu.reshape(-1)])[src]; nt = np.concatenate([t, bt.reshape(-1)])[src]
    ix = np.minimum(first[o][:, None] + s, n - 1); bu, bt, bl = np.array(bu), np.array(bt), np.array(bl)
    bu[c[o]] = u[ix]; bt[c[o]] = t[ix]; bl[c[o]] = size[o]
    return nu, nt, bu, bt, bl
def reference(tones, pu, pt, pn, bu, bt, bl, bk, th):
    x = np.ascontiguousarray(tones.astype(np.float32).reshape(N, 8, 16, M).transpose(0, 1, 3, 2)).astype(np.int64)
    lu = np.stack([gentries(a) for a in pu]).astype(np.int64); lt = np.stack([gentries(a) for a in pt]).astype(np.int64)
    piece = {(r, g): (lu[r, g, :pn[r, g, 0]], lt[r, g, :pn[r, g, 0]]) for r in range(N) for g in range(8)}
    u = bu.astype(np.int64).reshape(N, 8, B, R); t = bt.astype(np.int64).reshape(N, 8, B, R); ln = bl.astype(np.int64); pt_ = bk.astype(np.int64)
    for v in range(VI):
        for q in range(N):
            r = (q - HO * v) % N
            for g in range(8):
                a, b, u[q, g], t[q, g], ln[q, g] = visit(x[q, g], piece[r, g][0], piece[r, g][1], u[q, g], t[q, g], ln[q, g], pt_[q, g], int(th[q, g, 0]))
                piece[r, g] = (a, b)
    fu = np.full((N, 8, P), -1, np.int64); ft = np.full((N, 8, P), -1, np.int64)
    for q in range(N):
        for g in range(8):
            a, b = piece[(q - HO * (VI - 1)) % N, g]; fu[q, g, :len(a)] = a; ft[q, g, :len(b)] = b
    live = np.arange(R) < ln[..., None]
    return {"yu": np.stack([gtable(a) for a in fu]).astype(np.float32), "yt": np.stack([gtable(a) for a in ft]).astype(np.float32),
            "zu": np.where(live, u, -1).reshape(N, 8, B * R).astype(np.float32), "zt": np.where(live, t, -1).reshape(N, 8, B * R).astype(np.float32)}

@@ -1,0 +1,665 @@
+from concourse.mybir import AluOpType as ALU, AxisListType as AX, ActivationFunctionType as ACT
+
+F, BF, I, U = "float32", "bfloat16", "int32", "uint16"
+KA, XA, KB, XB, KEND = 4128, 8256, 11328, 15456, 18528
+ZC = 13312
+DUM = 6144
+KSPL, XSPL, ESPL, ZSPL, CV, KV = (2560, 1536, 1536), 2048, ((3072, 0), (3072, 0), 2304), 4096, 768, (512, 1536)
+NS1, XC1, U1 = 3, 3072, 256
+NTV0 = 20
+SB = {
+    "TON": ([128, 4096], BF), "BIG": ([128, KEND], BF), "WN": ([128, ZC + 16], BF), "PR": ([128, 3072], BF),
+    "CW": ([128, 3072], BF), "A1": ([128, 6240], BF), "A2": ([128, 6240], BF), "SC": ([128, 3072], BF),
+    "EW": ([128, 3072], BF), "XR": ([128, 3072], BF), "TH": ([128, 8192], BF), "KS": ([128, 32], F),
+    "IN0": ([128, 408], U), "IN1": ([128, 408], U), "IN2": ([128, 408], U), "SD0": ([128, 408], U), "SD1": ([128, 408], U),
+    "LU": ([128, 192], I), "LT": ([128, 192], I), "L3": ([128, 768], I), "LB": ([128, 256], I), "LS": ([128, 144], I),
+    "H4": ([128, 1024], I), "ST": ([128, 1792], BF), "LSF": ([128, 144], F), "E8": ([128, 256], F),
+    "IB": ([128, 128], BF), "IF": ([128, 128], F), "NB": ([128, 128], BF), "NS": ([128, 128], BF), "EA": ([128, 128], BF),
+    "EB": ([128, 128], BF), "PS": ([128, 128], BF), "SH1": ([128, 128], F), "SH2": ([128, 128], F),
+    "ON": ([128, 256], BF), "ONF": ([128, 128], F), "G8F": ([128, 8], F), "G8": ([128, 8], BF), "SEL": ([128, 64], BF),
+    "G4": ([128, 8], BF), "MS": ([128, 144], BF), "MU": ([128, 144], BF), "MT": ([128, 144], BF), "MP": ([128, 136], BF),
+    "WB": ([128, 240], BF), "COL": ([128, 32], F), "CI": ([128, 16], I), "BC": ([128, 64], U), "BCF": ([128, 64], F),
+    "MI": ([128, 256], F), "QM": ([128, 256], BF), "QN": ([128, 128], BF), "JB": ([128, 256], F), "SI": ([128, 256], F),
+    "SG": ([128, 256], BF), "W8": ([128, 256], BF), "CC1": ([128, 128], BF), "TRI": ([128, 128], BF), "K16": ([128, 192], BF),
+    "JO": ([128, 192], F), "DF": ([128, 256], F), "THS": ([128, 256], F), "TMP": ([128, 256], F), "RR": ([128, 128], F),
+    "OF": ([128, 200], F), "NO": ([128, 192], BF), "NQ": ([128, 272], BF), "IV": ([128, 272], BF), "THX": ([128, 256], F),
+    "NE": ([128, 272], BF), "EN": ([128, 272], BF), "N4": ([128, 8, 2, 16], BF), "K4": ([128, 8, 2, 16], BF),
+    "C4": ([128, 8, 2, 16], BF), "P2": ([128, 256], BF), "X2": ([128, 256], F), "HC": ([128, 256], BF),
+    "KP": ([128, 256], BF), "NP": ([128, 256], BF), "CP": ([128, 256], BF), "SP": ([128, 256], F),
+    "KK": ([128, 256], BF), "CK": ([128, 256], BF),
+    "LN": ([128, 256], BF), "GG": ([128, 256], BF), "OX": ([128, 192], U),
+    "OD": ([128, 192], U), "FS": ([128, 256], BF), "OK": ([128, 256], BF), "VL": ([128, 256], F), "MX": ([128, 256], F),
+    "MI8": ([128, 48], I), "SM": ([128, 192], F), "SL2": ([128, 48], BF), "SQ": ([128, 64], BF), "OH": ([128, 1024], BF), "LC": ([128, 128], BF),
+    "OC": ([128, 8], U), "TBC": ([128, 128], BF), "TBW": ([128, 144], BF), "GT": ([128, 128], BF), "QQ": ([128, 256], BF), "Q3": ([128, 128], BF),
+    "QV": ([128, 192], BF), "ZV": ([128, 96], BF), "LP": ([128, 256], F), "OP": ([128, 16], U), "OS": ([128, 192], U),
+    "NV": ([128, 192], BF), "TT": ([128, 256], BF), "OK2": ([128, 256], U), "OB": ([128, 256], U),
+    "OE": ([128, 8], U), "EV": ([128, 128], BF), "YO": ([128, 384], F), "ZO": ([128, 512], F),
+}
+SCRATCH = {k: ("sbuf", v[0], v[1]) for k, v in SB.items()}
+for _b in range(8):
+    SCRATCH["B%d" % _b] = ("psum", [128, 512], F)
+SEMAPHORES = ["qV", "qS", "qP", "qG", "sent"] + ["d%d" % k for k in range(48)] + ["r%d" % k for k in range(6)]
+
+
+def rank_program(g, core, T, topo):
+    rank = T.rank_of(core)
+    if rank is None:
+        return
+    nxt, prv = T.cores[(rank + 3) % 8], T.cores[(rank - 3) % 8]
+    Q = {"V": g.vector, "S": g.scalar, "P": g.tensor, "G": g, "Y": g.sync}
+    cnt = {"qV": 0, "qS": 0, "qP": 0, "qG": 0}
+    seen = {k: {} for k in Q}
+    hist = {}
+    nd = [0]
+    fin = {}
+
+    def a(n, c0=None, c1=None, p=128, st=1, p0=0, ps=1):
+        w = SB[n][0][1] if n in SB else 512
+        c0 = 0 if c0 is None else c0
+        c1 = w if c1 is None else c1
+        t = T[n]
+        ap = t[p0:p0 + p, c0:c1:st] if st > 1 else (t[p0::ps, c0:c1] if ps > 1 else t[p0:p0 + p, c0:c1])
+        return (ap, [(n, c0, c1, st)])
+
+    def a4(n, h=None, p=96):
+        return (T[n][0:p] if h is None else T[n][0:p, :, h, :], [(n, 0, 256, 1)])
+
+    def ind(w, o):
+        return (w[0].indirect(o[0]), w[1] + o[1])
+
+    def ext(ap):
+        return (ap, [])
+
+    def wait(q, kind, reads, writes):
+        need = {}
+        for rs, isw in ((reads, False), (writes, True)):
+            for (n, c0, c1, st) in rs:
+                ps = n not in SB
+                for (h0, h1, hw, hq, sem, val, hs) in hist.get(n, []):
+                    apart = h1 <= c0 or c1 <= h0 or not (hw or isw) or (st > 1 and hs == st and (c0 - h0) % st != 0)
+                    if hq == kind and (hq == "P" or (hq == "D" and n == "WN")):
+                        continue
+                    if apart and not (ps and hq != kind):
+                        continue
+                    need[sem] = max(need.get(sem, 0), val)
+        for sem, val in need.items():
+            if seen[q].get(sem, 0) < val:
+                Q[q].wait_ge(T.sem[sem], val)
+                seen[q][sem] = val
+
+    def note(rd, wr, q, sem, val):
+        for rs, isw in ((rd, False), (wr, True)):
+            for (n, c0, c1, st) in rs:
+                h = hist.setdefault(n, [])
+                h[:] = [e for e in h if not (e[4] == sem and e[2] == isw and c0 <= e[0] and e[1] <= c1 and
+                                             (st == 1 or q == "P" or (e[6] == st and (c0 - e[0]) % st == 0)))]
+                h.append((c0, c1, isw, q, sem, val, 1 if q == "P" else st))
+
+    def issue(q, fn, reads, writes, dma=False):
+        rd = [r for x in reads for r in x[1]]
+        wr = [r for x in writes for r in x[1]]
+        wait(q, "D" if dma else q, rd, wr)
+        ins = fn()
+        if dma:
+            sem, val = "d%d" % nd[0], 16
+            nd[0] += 1
+            ins.then_inc(T.sem[sem], 16)
+        else:
+            sem = "q" + q
+            cnt[sem] += 1
+            val = cnt[sem]
+            ins.then_inc(T.sem[sem], 1)
+        fin[sem] = val
+        note(rd, wr, "D" if dma else q, sem, val)
+
+    def sc(x):
+        return x[0] if isinstance(x, tuple) else x
+
+    def tl(*xs):
+        return [x for x in xs if isinstance(x, tuple)]
+
+    def cp(o, i):
+        issue("V", lambda: g.vector.tensor_copy(o[0], i[0]), [i], [o])
+
+    def tt(o, x, y, op):
+        issue("V", lambda: g.vector.tensor_tensor(o[0], x[0], y[0], op), [x, y], [o])
+
+    def ts(o, x, s1, op0, s2=None, op1=None):
+        if op1 is None:
+            issue("V", lambda: g.vector.tensor_scalar(o[0], x[0], sc(s1), None, op0), tl(x, s1), [o])
+        else:
+            issue("V", lambda: g.vector.tensor_scalar(o[0], x[0], sc(s1), sc(s2), op0, op1), tl(x, s1, s2), [o])
+
+    def scan(o, d0, d1, init, op0, op1):
+        issue("V", lambda: g.vector.tensor_tensor_scan(o[0], d0[0], d1[0], sc(init), op0, op1), tl(d0, d1, init), [o])
+
+    def ms(o, v):
+        issue("V", lambda: g.vector.memset(o[0], v), [], [o])
+
+    def red(o, i):
+        issue("V", lambda: g.vector.tensor_reduce(o[0], i[0], AX.X, ALU.add), [i], [o])
+
+    def sq(o, i):
+        issue("S", lambda: g.scalar.activation(o[0], i[0], ACT.Copy), [i], [o])
+
+    def sa(o, i, scale, bias=0.0, f=ACT.Identity):
+        issue("S", lambda: g.scalar.activation(o[0], i[0], f, bias=sc(bias), scale=sc(scale)), tl(i, scale, bias), [o])
+
+    def gat(q, o, i):
+        (cp if q == "V" else sq)(o, i)
+
+    def mm(o, l, r, s0=True, s1=True):
+        issue("P", lambda: g.tensor.matmul(o[0], l[0], r[0], s0, s1), [l, r], [o])
+
+    def acc(o, prs):
+        for k, (l, r) in enumerate(prs):
+            mm(o, l, r, k == 0, k == len(prs) - 1)
+
+    def io(o, pat, base=0, cm=0, fl=True):
+        if fl:
+            issue("G", lambda: g.iota(o[0], pat, base, cm, allow_small_or_imprecise_dtypes=True), [], [o])
+        else:
+            issue("G", lambda: g.iota(o[0], pat, base, cm), [], [o])
+
+    def sel(o, i, pat, op, base, cm):
+        issue("G", lambda: g.affine_select(o[0], i[0], pat, op, 0.0, base, cm), [i], [o])
+
+    def dma(q, o, i):
+        issue(q, lambda: Q[q].dma_start(o[0], i[0]), [i], [o], dma=True)
+
+    col = lambda k, p=128: a("COL", k, k + 1, p)
+    sm = lambda c, w=8, p=96: a("SM", c, c + w, p)
+    mi = lambda c, w=8: a("MI8", c, c + w, 96)
+    ch = lambda n, c: a(n, 1024 * c, 1024 * c + 1024)
+    bc16 = lambda: a("BC", 0, 8)
+    bc32 = lambda: a("BC", 16, 32)
+    i96 = a("IB", 0, 96, 96)
+
+    def steps(W, ks, q):
+        for k in ks:
+            o = a("TH", 256 * k, 256 * k + 2 * W)
+            if q == "V":
+                ts(o, a("TT", 0, 2 * W), float(k), ALU.is_lt)
+            else:
+                sa(o, a("TT", 0, 2 * W), -1.0, a("KS", k, k + 1), ACT.Sign)
+
+    def counts(W, bank, ks, q):
+        for k in ks:
+            for hf in range(2):
+                mm(a(bank, 128 * hf + 2 * (k % 16) + k // 16, 128 * hf + 128, W, 32), a("TH", 256 * k + W * hf, 256 * k + W * hf + W),
+                   a("G4", 0, 4) if q == "V" else a("G4", 4, 8))
+
+    def w2b(bank, wide, c, rhs):
+        for s in range(32):
+            mm(a(bank, s, 256, 32, 32, 32 * c), a(wide, 1024 * c + s, 1024 * c + 1024, st=32), rhs)
+
+    def rebuild(v, lo, hi, q):
+        w = (a("BIG", KB, XB), a("BIG", KA, KB), a("BIG", KB, KEND))[v]
+        K = (KA, KB, KA)[v]
+        gat(q, a("BIG", K + 32 + lo, K + 32 + hi), ind(w, a("OK2", lo // 16, hi // 16)))
+
+    dma("Y", a("LS", 0, 128, 8), ext(T.bl[:]))
+    for k in range(8):
+        dma("SY"[k % 2], a("LB", 32 * k, 32 * k + 32), ext(T.bt[k, :]))
+    dma("S", a("LT"), ext(T.pt[:]))
+    dma("Y", a("L3", 256, 512), ext(T.bt[:]))
+    dma("S", a("LS", 128, 136, 1), ext(T.pn[:]))
+    dma("Y", a("LS", 136, 144, 1), ext(T.th[:]))
+    dma("S", a("TON", 2048, 4096), ext(T.tones[:, 2048:4096]))
+    dma("Y", a("TON", 0, 2048), ext(T.tones[:, 0:2048]))
+    dma("S", a("L3", 512, 768), ext(T.bk[:]))
+    dma("Y", a("LU"), ext(T.pu[:]))
+    dma("Y", a("L3", 0, 256), ext(T.bu[:]))
+
+    ms(a("ONF"), 1.0)
+    ms(a("ON"), 1.0)
+    io(a("CI", 0, 1), [[0, 1]], 0, 1, False)
+    io(a("SI"), [[0, 8], [1, 32]])
+    io(a("E8", p=8), [[1, 8], [0, 32]], 0, -1)
+    sel(a("IF"), a("ONF"), [[-1, 128]], ALU.is_equal, 0, 1)
+    sel(a("SEL"), a("ON", 0, 64), [[-1, 8], [-16, 8]], ALU.is_equal, 0, 1)
+    io(a("BCF", 0, 16), [[1, 16]])
+    io(a("BCF", 16, 32), [[1, 8], [0, 2]])
+    io(a("BCF", 32, 48), [[0, 2], [1, 8]])
+    sel(a("SH1"), a("ONF"), [[-1, 128]], ALU.is_equal, -1, 1)
+    io(a("MI"), [[0, 16], [1, 16]])
+    io(a("SP"), [[0, 8], [1, 16], [16, 2]])
+    io(a("ST", 1280, 1536), [[1, 4], [0, 64]])
+    io(a("ST", 1536, 1792), [[0, 4], [1, 64]])
+    io(a("K16"), [[16, 192]])
+    io(a("RR"), [[0, 8], [1, 16]])
+    io(a("WN", 0, 4096), [[0, 4096]])
+    io(a("BIG", 0, KA), [[0, KA]], 99)
+    io(a("CC1"), [[1, 128]], 1)
+    sel(a("TRI"), a("ON", 0, 128), [[1, 128]], ALU.is_gt, 0, -1)
+    io(a("A1", 0, 3072), [[0, 3072]])
+    io(a("A2", 0, 3072), [[0, 3072]])
+    for k, (s, m) in enumerate(((0, 15), (4, 15), (5, 15), (3, 31), (0, 1), (0, 7), (1, 127))):
+        ts(a("CI", 1 + k, 2 + k), a("CI", 0, 1), s, ALU.arith_shift_right, m, ALU.bitwise_and)
+    cp(a("COL", 0, 8), a("CI", 0, 8))
+    sa(col(9), col(1), 4.0)
+    sa(col(24), col(0), 32.0)
+    sa(col(25), col(0), 32.0, 32.0)
+    sa(a("KS"), a("SI", 0, 32), 1.0, -0.5)
+    sa(a("IB"), a("IF"), 1.0)
+    sa(a("JB"), a("SI"), 1.0, col(24))
+    sa(a("NS"), a("IF"), -16384.0)
+    sa(a("PS"), a("IF"), 16384.0)
+    sa(a("NB"), a("IF"), -float(2 ** 25))
+    sa(a("EA"), a("IF"), float(KA))
+    sa(a("EB"), a("IF"), float(KB))
+    sa(a("W8"), a("SI"), -float(2 ** 19), 31.0 * 2 ** 19)
+    sa(col(8), col(0), 1.0, float(DUM))
+    for v in range(3):
+        sa(col(16 + v), col(1), 1.0, float(4096 + 3072 * v))
+    sa(col(19), col(6), 512.0, col(4))
+    sa(col(26), col(4), 1.0, 2.0)
+    sa(col(27), col(0), 1.0, 129.0)
+    ts(a("G8F"), a("SI", 0, 8), col(2), ALU.is_equal)
+    cp(a("G8"), a("G8F"))
+    ts(a("G4", 0, 4), a("SI", 0, 4), col(3), ALU.is_equal)
+    ts(a("G4", 4, 8), a("SI", 0, 4), col(3), ALU.is_equal, 0.5, ALU.mult)
+    ts(a("SG"), a("SI"), 0.0, ALU.is_gt)
+    ts(a("E8", p=8), a("E8", p=8), 0.0, ALU.is_equal)
+    ms(a("NQ", 0, 16), 0.0)
+    ms(a("TBC"), 0.0)
+    ms(a("SM"), 0.0)
+
+    def first_book():
+        cp(a("LSF", 0, 128, 8), a("LS", 0, 128, 8))
+        mm(a("B0", 0, 256), a("LSF", 0, 128, 8), a("E8", p=8))
+        tt(a("NQ", 1, 256), a("LB", 1, 256), a("LB", 0, 255), ALU.not_equal)
+        tt(a("OK"), a("B0", 0, 256), a("SI"), ALU.is_gt)
+        cp(a("TBC", 2, 128, st=16), a("B0", 0, 256, st=32))
+        tt(a("FS"), a("OK"), a("NQ", 0, 256), ALU.mult)
+        scan(a("HC"), a("FS"), a("SG"), 0.0, ALU.add, ALU.mult)
+        for hf in range(2):
+            mm(a("B2", 128 * hf, 128 * hf + 128), a("HC", 128 * hf, 128 * hf + 128), a("IB"))
+        ts(sm(0, p=128), a("HC", 31, 256, st=32), col(25), ALU.add)
+        cp(a("TT"), a("B2", 0, 256))
+        steps(128, range(32 - NTV0), "S")
+        steps(128, range(32 - NTV0, 32), "V")
+        counts(128, "B3", range(32 - NTV0, 32), "V")
+        counts(128, "B3", range(32 - NTV0), "S")
+
+    ts(col(10), col(1), 2.0, ALU.min, 8.0, ALU.mult)
+    ts(col(11), col(1), 4.0, ALU.max, 5.0, ALU.min)
+    ts(col(11), col(11), -4.0, ALU.add, 8.0, ALU.mult)
+    ts(col(12), col(1), 4.0, ALU.is_ge, 8.0, ALU.mult)
+    ts(a("BCF", 48, 56), a("BCF", 0, 8), col(11), ALU.add, col(12), ALU.add)
+    ts(a("BCF", 32, 48), a("BCF", 32, 48), col(10), ALU.add)
+    ts(a("BCF", 48, 56), a("BCF", 48, 56), col(10), ALU.add)
+    cp(a("BC", 0, 56), a("BCF", 0, 56))
+    ms(a("SH1", 15, 128, st=16), 0.0)
+    ms(a("SH2"), 0.0)
+    ms(a("NE", 0, 16), 0.0)
+    ms(a("EN", 0, 16), 1.0)
+    ms(a("IV", 256, 272), 0.0)
+    ms(a("OF", 192, 200), 0.0)
+    ms(a("BIG", KA, KA + 32), 0.0)
+    ms(a("BIG", KB + 4096, XB), 0.0)
+    tt(a("SH1"), a("SH1"), a("IF"), ALU.subtract)
+    cp(a("SH2", 15, 128, st=16), a("SEL", 0, 8))
+    ts(a("MI"), a("MI"), col(1), ALU.is_equal)
+    ts(col(11), col(1), 0.0, ALU.is_equal, 63.0, ALU.mult)
+    ts(col(12), col(5), -63.0, ALU.mult, 64.0, ALU.add)
+    ts(a("TMP", 0, 96), a("ONF", 0, 96), 0.25, ALU.mult)
+    ms(a("TMP", 128, 224), 0.0)
+    ts(col(13), col(1), 2.0, ALU.is_lt, col(12), ALU.mult)
+    ts(col(14), col(1), 4.0, ALU.is_lt, col(12), ALU.mult)
+    scan(a("VL", 0, 96), a("TMP", 0, 96), a("TMP", 128, 224), float(2 ** 96), ALU.mult, ALU.add)
+    ts(col(11), col(11), 1.0, ALU.add)
+    tt(col(14), col(14), col(13), ALU.subtract)
+    tt(a("VL", 128, 224), a("VL", 0, 96), a("IF", 0, 96), ALU.mult)
+    ts(a("TMP"), a("SI"), 31.0, ALU.is_equal, -3.0 * 16384, ALU.mult)
+    red(col(20), a("VL", 128, 224))
+    for n in ("MS", "MU", "MT", "MP", "WB", "TBW", "SQ", "ZV"):
+        sa(a(n), a("ON", 0, SB[n][0][1]), 0.0)
+    sa(a("TBW", 0, 1), a("ONF", 0, 1), float(2 ** 98))
+    sa(col(15), col(5), -1.0)
+    sa(col(22), col(5), 32.0)
+    sa(a("JO"), a("K16"), 1.0, col(1))
+    sa(a("WN", ZC, ZC + 16), a("ONF", 0, 16), col(15))
+    sa(a("TBC", 0, 128, st=16), a("ONF", 0, 8), col(7))
+    sa(a("TBC", 1, 128, st=16), a("ONF", 0, 8), col(22))
+    sa(a("MS", 15, 143, st=16), a("G8F"), col(11))
+    sa(a("MU", 15, 143, st=16), a("G8F"), col(13))
+    sa(a("MT", 15, 143, st=16), a("G8F"), col(14))
+    sa(a("MP", 7, 71, st=8), a("G8F"), col(13))
+    sa(a("MP", 71, 135, st=8), a("G8F"), col(14))
+    sa(a("WB", 115, 116), col(20), 1.0)
+    sa(col(21), col(20), 2.0)
+    sa(a("SL2", 0, 32), a("SEL", 0, 32), 1.0)
+    for c in (32, 40):
+        sa(a("SL2", c, c + 8), a("SEL", 24, 32), 1.0)
+    first_book()
+    ts(a("ST", 1280, 1536), a("ST", 1280, 1536), col(9), ALU.add)
+
+    def pointers(v, lo, hi, q):
+        for c in range(3):
+            l, h = max(lo, 1024 * c), min(hi, 1024 * c + 1024)
+            if l < h:
+                o = 136 * c + 64 - 64 * c
+                gat(q, a("CW", l, h), ind(a("WN", 0, 4096), a("IN%d" % v, o + l // 16, o + h // 16)))
+
+    tt(a("LP", 0, 128), ind(sm(0, p=128), bc16()), a("MI", 0, 128), ALU.mult)
+    mm(a("B2", 0, 8), a("LP", 0, 128), a("G8F"))
+    for c in range(3):
+        cp(a("IN0", 136 * c + 64, 136 * c + 128), a("LT", 64 * c, 64 * c + 64))
+    ts(a("DF"), a("SP"), float(32 - NTV0), ALU.is_lt, 256.0, ALU.mult)
+    cp(a("OE"), a("B2", 0, 8))
+    cp(a("OB"), a("L3", 256, 512))
+    cp(a("LSF", 128, 144, 1), a("LS", 128, 144, 1))
+    mm(a("B5", 0, 16), a("ONF", p=1), a("LSF", 128, 144, 1))
+    ts(a("QM", 0, 128), a("RR"), 2.0, ALU.is_lt)
+    ts(a("QM", 128, 256), a("RR"), col(26), ALU.is_equal, -1.0, ALU.mult)
+    ts(a("QN"), a("RR"), 4.0, ALU.is_ge)
+    ts(a("LC"), a("RR"), 3.0, ALU.is_lt)
+    ts(sm(8, p=128), a("B5", 8, 16), 16384.0, ALU.add)
+    cp(a("IN0", 128, 136), a("B5", 0, 8))
+    tt(a("QM", 128, 256), a("QM", 128, 256), a("QM", 0, 128), ALU.subtract)
+    tt(a("QN"), a("QN"), a("LC"), ALU.subtract)
+    tt(a("THS"), ind(sm(8, p=128), bc32()), a("TMP"), ALU.add)
+    ts(a("VL"), a("B3", 0, 256), 16.0, ALU.mult, col(19), ALU.add)
+    tt(a("X2"), a("VL"), a("DF"), ALU.add)
+    for h in range(2):
+        mm(a("B6", 128 * h, 128 * h + 128), a("X2", h, 256, st=2), a("IF"))
+
+    def book_digits():
+        ts(a("H4", 0, 512), a("L3", 0, 512), 6, ALU.arith_shift_right)
+        ts(a("H4", 512, 1024), a("L3", 0, 512), 63, ALU.bitwise_and)
+        cp(a("ST", 0, 1024), a("H4"))
+        for r, c in ((0, 0), (1, 512), (2, 256), (3, 768)):
+            dma("Y", a("WN", 0, 4096, p0=r, ps=16), a("ST", c, c + 256))
+
+    for v in range(3):
+        IN, SD = "IN%d" % v, "SD%d" % v
+        R = 4096 + 3072 * v
+        K = (KA, KB, KA)[v]
+        XC = (XA, XB, XA)[v]
+        ou = lambda c: a(IN, 136 * c, 136 * c + 64)
+        ot = lambda c: a(IN, 136 * c + 64, 136 * c + 128)
+        for c in range(3):
+            sq(ch("XR", c), ind(a("TON"), ot(c)))
+        if v == 0:
+            gat("V", a("BIG", KB + XSPL, KB + XSPL + 1024), ind(a("TON"), a("OB", XSPL // 16, XSPL // 16 + 64)))
+            ts(a("ST", 1024, 1280), a("L3", 512, 768), 1.0, ALU.add, 32.0, ALU.mult)
+            for r, c in ((6, 1280), (7, 1536), (4, 1024)):
+                dma("Y", a("WN", 0, 4096, p0=r, ps=16), a("ST", c, c + 256))
+            gat("V", a("BIG", KB + XSPL + 1024, KB + 4096), ind(a("TON"), a("OB", XSPL // 16 + 64, 256)))
+            for c in range(3):
+                cp(ou(c), a("LU", 64 * c, 64 * c + 64))
+            for h in range(2):
+                cp(a("OK2", h, 256, st=2), a("B6", 128 * h, 128 * h + 128))
+            gat("S", a("BIG", KB, KB + XSPL), ind(a("TON"), a("OB", 0, XSPL // 16)))
+            sa(a("DF"), a("SP"), 1.0, col(25))
+        else:
+            pointers(v, 0, CV, "V")
+        cp(sm(128, p=128), a(IN, 128, 136))
+        tt(a("IV", 0, 256), ind(sm(128, p=128), bc32()), a("JB"), ALU.is_le)
+        tt(ch("PR", 0), ind(a("TON"), ou(0)), ch("XR", 0), ALU.mult)
+        w2b("B0", "PR", 0, a("G8"))
+        for c in range(3):
+            cp(a("OF", 64 * c, 64 * c + 64), ot(c))
+        acc(a("B3", 0, 192), [(a("SH1"), a("OF", 0, 192)), (a("SH2"), a("OF", 1, 193))])
+        pointers(v, CV if v > 0 else 0, 3072, "S")
+        tt(a("PR", 1024, 1536), ind(a("TON"), a(IN, 136, 168)), a("XR", 1024, 1536), ALU.mult)
+        ts(a("NO"), a("B3", 0, 192), 0.0, ALU.not_equal)
+        for gg in range(8):
+            for h in range(2):
+                mm(a("B4", 32 * gg + 16 * h, 32 * gg + 16 * h + 16, 96), a("NO", h, 192, st=2), a("IB", 16 * gg, 16 * gg + 16))
+        tt(a("PR", 1536, 2048), ind(a("TON"), a(IN, 168, 200)), a("XR", 1536, 2048), ALU.mult)
+        cp(a("NQ", 1, 257, 96), a("B4", 0, 256, 96))
+        acc(a("B3", 0, 256, 96), [(a("NS", 0, 96, 96), a("NQ", 1, 257, 96)), (a("NS", 0, 96, 96), a("IV", 1, 257, 96)),
+                                  (a("NS", 0, 96, 96), a("IV", 1, 257, 96))])
+        w2b("B0", "PR", 1, a("G8"))
+        if v < 2:
+            scan(a("GG", p=96), a("NQ", 0, 256, 96), a("SG", p=96), 0.0, ALU.add, ALU.mult)
+            for hf in range(2):
+                mm(a("B5", 96 * hf, 96 * hf + 96), a("GG", 128 * hf, 128 * hf + 128, 96), i96)
+        tt(ch("PR", 2), ind(a("TON"), ou(2)), ch("XR", 2), ALU.mult)
+        w2b("B1", "CW", 0, a("SEL", 32, 40))
+        w2b("B0", "PR", 2, a("G8"))
+        tt(a("THX", p=96), a("B3", 0, 256, 96), a("THS", p=96), ALU.add)
+        for c in range(1, 3):
+            w2b("B1", "CW", c, a("SEL", 32, 40))
+        if v == 0:
+            rebuild(0, 0, KSPL[0], "S")
+            rebuild(0, KSPL[0], 4096, "V")
+        sq(a("EV"), ind(a("BIG", K, K + 4128), a("OE")))
+        if v > 0:
+            cp(ind(a("BIG", 0, KA), a("OE")), a("EV"))
+        if v < 2:
+            sq(a("TT", 0, 192), a("B5", 0, 192))
+            steps(96, range(1, NS1), "S")
+        s0 = a("B0", 0, 256, 96)
+        cont = a("NE", 0, 256, 96)
+        tt(a("NE", 1, 257, 96), s0, a("THX", p=96), ALU.is_lt)
+        tt(a("EN", 1, 257, 96), s0, a("THX", p=96), ALU.is_ge)
+        sq(a4("N4"), a("NE", 1, 257, 96))
+        scan(a("KK", p=96), a("NQ", 0, 256, 96), cont, 0.0, ALU.add, ALU.mult)
+        sq(a4("K4"), a("KK", p=96))
+        tt(a("HC", p=96), a("B1", 0, 256, 96), a("EN", 0, 256, 96), ALU.mult)
+        scan(a("CK", p=96), cont, a("HC", p=96), 0.0, ALU.mult, ALU.add)
+        half = lambda n, h: a(n, 128 * h, 128 * h + 128, 96)
+        for h in range(2):
+            cp(half("NP", h), a4("N4", h))
+        cp(a4("C4"), a("CK", p=96))
+        for h in range(2):
+            cp(half("KP", h), a4("K4", h))
+        for h in range(2):
+            cp(half("CP", h), a4("C4", h))
+            acc(a("B4", 96 * h, 96 * h + 96),
+                [(half("KP", h), i96), (half("NP", h), a("EB" if v == 1 else "EA", 0, 96, 96)), (half("CP", h), i96)])
+        scan(a("LN", p=96), a("ON", p=96), cont, 0.0, ALU.add, ALU.mult)
+        if v == 0:
+            cp(ind(a("BIG", 0, KA), a("OE")), a("EV"))
+        if v < 2:
+            steps(96, range(NS1, 32), "S")
+        for h in range(2):
+            cp(a("OD", h, 192, st=2), a("B4", 96 * h, 96 * h + 96))
+        acc(a("B3", 0, 256, 96), [(i96, a("W8", p=96)), (i96, a("CK", p=96)), (i96, a("LN", p=96))] +
+            ([(a("PS", 0, 96, 96), a("GG", p=96)), (a("NS", 0, 96, 96), a("KK", p=96))] if v < 2 else []) +
+            [(a("NB", 0, 96, 96), a("NE", 1, 257, 96)), (a("NB", 0, 96, 96), a("IV", 0, 256, 96))])
+        for c in range(3):
+            tt(ch("PR", c), ind(a("BIG", 0, K + 4128), a("OD", 64 * c, 64 * c + 64)), ch("XR", c), ALU.not_equal)
+            if v < 2:
+                counts(96, "B0", ((range(8), range(8, 20), range(20, 32)), (range(20), range(20, 32), ()))[v][c], "S")
+            if v < 2 and c == 2 - v:
+                sq(a("WN", R, R + U1), ind(a("WN", 0, 4096), a(IN, 0, U1 // 16)))
+                sq(a("P2", p=96), a("B0", 0, 256, 96))
+                sq(a("WN", R + U1, R + 1024), ind(a("WN", 0, 4096), a(IN, U1 // 16, 64)))
+            w2b("B2", "PR", c, a("G8"))
+        for h in range(2 if v < 2 else 0):
+            acc(a("B1", 96 * h, 96 * h + 96), [(a("IB"), a("K16", 0, 192, st=2)), (a("P2", h, 256, 96, 2), i96)])
+        for c in range(1 if v < 2 else 0, 3):
+            sq(a("WN", R + 1024 * c, R + 1024 * c + 1024), ind(a("WN", 0, 4096), ou(c)))
+        for r in range(2):
+            dma("Y", a("WN", R, R + 3072, p0=r, ps=16), a("WN", R, R + 3072, p0=6 + r, ps=16))
+            dma("G", a("WN", R, R + 3072, p0=2 + r, ps=16), a("CW", p0=6 + r, ps=16))
+        if v == 0:
+            book_digits()
+        else:
+            tt(a("TBC"), a("B7", 128, 256), a("TBC"), ALU.add)
+
+        def compact():
+            for h in range(2):
+                ts(a("OX", h, 192, st=2), a("B1", 96 * h, 96 * h + 96), 16.0, ALU.add, 3071.0, ALU.min)
+            sq(a("BIG", XC, XC + XC1), ind(a("XR"), a("OX", 0, XC1 // 16)))
+
+        scan(a("FS", p=96), cont, a("B2", 0, 256, 96), 0.0, ALU.mult, ALU.max)
+        if v < 2:
+            compact()
+        ts(a("OK", p=96), a("FS", p=96), 6.5, ALU.is_lt)
+        tt(a("VL", p=96), a("B3", 0, 256, 96), a("OK", p=96), ALU.mult)
+        scan(a("MX", p=96), a("SG", p=96), a("VL", p=96), 0.0, ALU.mult, ALU.max)
+        cp(mi(32), a("MX", 31, 256, 96, 32))
+        ts(mi(8), mi(32), 5, ALU.arith_shift_right, 255, ALU.bitwise_and)
+        ts(mi(0), mi(32), 31, ALU.bitwise_and)
+        ts(mi(16), mi(32), 19, ALU.arith_shift_right)
+        ts(mi(24), mi(32), 14, ALU.arith_shift_right, 31, ALU.bitwise_and)
+        cp(sm(0, 32), mi(0, 32))
+        tt(a("LC"), ind(sm(8, p=128), bc16()), a("MI", 0, 128), ALU.mult)
+        mm(a("B4", 0, 6), a("LC", p=96), a("G8", 0, 6, 96))
+        for gg in range(8):
+            ts(a("OH", 128 * gg, 128 * gg + 128, 96), a("CC1", p=96), sm(8 + gg, 1), ALU.is_equal)
+        acc(a("B5", 0, 128), [(a("TBC"), a("IB"))] +
+            [(a("WB", 112 - 16 * gg, 240 - 16 * gg, 96), a("OH", 128 * gg, 128 * gg + 128, 96)) for gg in range(8)])
+        cp(a("OC", 0, 6), a("B4", 0, 6))
+        ts(sm(56), sm(0), 1.0, ALU.add)
+        tt(sm(72), sm(56), sm(16), ALU.add)
+        cp(a("TBW", 1, 129), a("B5", 0, 128))
+        ts(sm(64), sm(72), -1.0, ALU.mult, col(25, 96), ALU.add)
+        cp(a("GT", 0, 96), ind(a("TBW"), a("OC", 0, 6)))
+        mm(a("B4", 0, 48, 96), a("GT", 0, 96), a("SL2"))
+        ts(mi(32), sm(64), float(R), ALU.add)
+        ts(mi(0), mi(32), 6, ALU.arith_shift_right)
+        ts(mi(8), mi(32), 63, ALU.bitwise_and)
+        ts(sm(160, 24), a("B4", 24, 48, 96), col(21, 96), ALU.is_lt)
+        cp(sm(40, 16), mi(0, 16))
+        ts(sm(104), sm(160), -16384.0, ALU.mult, 16384.0, ALU.add)
+        tt(sm(80, 24), a("B4", 0, 24, 96), sm(40, 24), ALU.subtract)
+        tt(sm(104), sm(104), sm(64), ALU.add)
+        tt(a("SQ", 0, 24, 96), sm(80, 24), sm(160, 24), ALU.mult)
+        mm(a("B5", 0, 8, 96), a("TRI", 0, 96, 96), a("SQ", 16, 24, 96))
+        mm(a("B5", 8, 16), a("ON", 0, 128, 96), a("SQ", 16, 24, 96))
+        tt(sm(32), a("B4", 16, 24, 96), sm(104), ALU.add)
+        if v < 2:
+            tt(a("QQ"), ind(a("SQ", 0, 32), a("BC", 32, 48)), a("QM"), ALU.mult)
+        tt(sm(112), a("B5", 0, 8, 96), sm(104), ALU.add)
+        tt(sm(120), a("B5", 0, 8, 96), sm(32), ALU.add)
+        tt(sm(136, p=128), a("B5", 8, 16), sm(128, p=128), ALU.add)
+        top = R + 3071 if v < 2 else ZC
+        win = a("WN", 0, R + 3072 if v < 2 else ZC + 16)
+        new = lambda q, lo, hi: gat(q, a("EW", lo, hi), ind(win, a("OS", lo // 16, hi // 16)))
+
+        def book_table():
+            tt(a("Q3"), ind(a("SQ", 0, 48), a("BC", 48, 56)), a("QN"), ALU.mult)
+            for gg in range(8):
+                mm(a("B7", 128 + 16 * gg, 144 + 16 * gg), a("OH", 128 * gg, 128 * gg + 128, 96), a("Q3", 16 * gg, 16 * gg + 16, 96))
+
+        def book(q, lo, hi):
+            for l in range(lo, hi, 512):
+                gat(q, a("TH", l, l + 512), ind(win, a("OK2", l // 16, l // 16 + 32)))
+
+        if v == 2:
+            book_table()
+            tt(a("TBC"), a("B7", 128, 256), a("TBC"), ALU.add)
+            ts(sm(0, p=128), a("TBC", 0, 128, st=16), 64.0, ALU.mult, -float(ZC), ALU.add)
+            cp(sm(8, p=128), a("TBC", 2, 128, st=16))
+            tt(sm(0, p=128), sm(0, p=128), a("TBC", 1, 128, st=16), ALU.add)
+            tt(a("MX"), ind(sm(8, p=128), bc32()), a("SP"), ALU.is_gt)
+            tt(a("VL"), ind(sm(0, p=128), bc32()), a("SP"), ALU.add)
+            tt(a("X2"), a("VL"), a("MX"), ALU.mult)
+            for h in range(2):
+                mm(a("B3", 128 * h, 128 * h + 128), a("X2", h, 256, st=2), a("IF"))
+        ts(sm(112, 16), sm(112, 16), col(8, 96), ALU.min)
+        tt(a("LP"), ind(sm(112, 16, 128), a("BC", 0, 16)), a("MI"), ALU.mult)
+        for k in range(2):
+            mm(a("B4", 6 * k, 6 * k + 6), a("LP", 128 * k, 128 * k + 128, 96), a("G8F", 0, 6, 96))
+        if v == 2:
+            for h in range(2):
+                ts(a("OK2", h, 256, st=2), a("B3", 128 * h, 128 * h + 128), float(ZC), ALU.add)
+            book("S", 0, ZSPL)
+            tt(a("QQ"), ind(a("SQ", 0, 32), a("BC", 32, 48)), a("QM"), ALU.mult)
+        for k in range(2):
+            mm(a("B6", 96 * k, 96 * k + 96), a("QQ", 128 * k, 128 * k + 128, 96), i96)
+        if v == 2:
+            tt(sm(144, p=128), sm(136, p=128), a("G8F"), ALU.mult)
+            red(sm(152, 1, 128), sm(144, p=128))
+        cp(a("OP", 0, 12), a("B4", 0, 12))
+        cp(a("QV"), a("B6", 0, 192))
+        if v == 2:
+            ts(a("NV"), a("JO"), sm(152, 1, 128), ALU.is_ge)
+        cp(ind(a("A1"), a("OP", 0, 6)), a("QV", 0, 96))
+        cp(ind(a("A2"), a("OP", 6, 12)), a("QV", 96, 192))
+        def source(c):
+            ts(a("OS", 64 * c, 64 * c + 64), a("B%d" % (0, 2, 7)[c], 0, 64), col(16 + v), ALU.add, float(top), ALU.min)
+
+        for c in range(3):
+            scan(ch("SC", c), ch("A1", c), ch("A2", c), 0.0 if c == 0 else a("SC", 1024 * c - 1, 1024 * c), ALU.add, ALU.add)
+            acc(a("B%d" % (0, 2, 7)[c], 0, 64), [(a("IB"), a("K16", 64 * c, 64 * c + 64))] +
+                ([(a("PS"), a("NV", 64 * c, 64 * c + 64))] if v == 2 else []) +
+                [(a("MS", 15 - i, 143 - i), a("SC", 1024 * c + i, 1024 * c + 1024, st=16)) for i in range(16)])
+            if c > 0:
+                source(c - 1)
+        if v < 2:
+            e0, e1 = ESPL[v]
+            if e1:
+                new("V", 0, 1024)
+            else:
+                new("S", 0, 1024)
+            ts(a(SD, 128, 136), sm(136, p=128), 3072.0, ALU.min)
+            ts(sm(144), sm(8), -1.0, ALU.mult, col(27, 96), ALU.add)
+            tt(a("SQ", 32, 40, 96), sm(24), sm(160), ALU.mult)
+            source(2)
+            tt(a("SQ", 24, 32, 96), sm(144), sm(160), ALU.mult)
+            new("S", 1024, min(e0, 2048))
+            if e0 > 2048:
+                new("S", 2048, e0)
+            if XC1 < 3072:
+                sq(a("BIG", XC + XC1, XC + 3072), ind(a("XR"), a("OX", XC1 // 16, 192)))
+            book_table()
+            rid, pid, _ = topo.addr(nxt)
+
+            def names(c):
+                for k, m in enumerate(("MU", "MT")):
+                    acc(a("B%d" % (3, 6, 4)[c], 64 * k, 64 * k + 64),
+                        [(a(m, 15 - i, 143 - i), a("EW", 1024 * c + i, 1024 * c + 1024, st=16)) for i in range(16)])
+
+            def send(c):
+                end = 136 * c + (136 if c == 0 else 128)
+                src, dst, sem = a(SD, 136 * c, end), a("IN%d" % (v + 1), 136 * c, end), "r%d" % (3 * v + c)
+                cp(a(SD, 136 * c, 136 * c + 128), a("B%d" % (3, 6, 4)[c], 0, 128))
+                wait("G", "D", src[1], [])
+                g.remote_dma(dst[0], src[0], T.sem[sem], T.sem["sent"], pid, rid, topo.mask(core, nxt))
+                fin["sent"] = fin.get("sent", 0) + len(topo.engines(core, nxt))
+                fin[sem] = len(topo.engines(prv, core))
+                note([], dst[1], "D", sem, fin[sem])
+
+            ts(sm(144, p=128), a("B7", 132, 256, st=16), 32.0, ALU.mult)
+            names(0)
+            tt(sm(144, p=128), a("B7", 133, 256, st=16), sm(144, p=128), ALU.add)
+            tt(a("X2"), ind(sm(144, p=128), bc32()), a("DF"), ALU.add)
+            for h in range(2):
+                mm(a("B2", 128 * h, 128 * h + 128), a("X2", h, 256, st=2), a("IF"))
+            if e0 < 2048:
+                new("V", e0, 2048)
+            if e0 < 3072:
+                new("V", max(e0, 2048), 3072)
+            send(0)
+            for h in range(2):
+                ts(a("OK2", h, 256, st=2), a("B2", 128 * h, 128 * h + 128), 7199.0, ALU.min)
+            names(1)
+            names(2)
+            k0 = KSPL[v + 1]
+            rebuild(v + 1, 0, k0, "S")
+            rebuild(v + 1, k0, k0 + KV[0], "V")
+            send(1)
+            rebuild(v + 1, k0 + KV[0], k0 + KV[1], "V")
+            send(2)
+            rebuild(v + 1, k0 + KV[1], 4096, "V")
+            io(a("A1", 0, 3072), [[0, 3072]])
+            io(a("A2", 0, 3072), [[0, 3072]])
+        else:
+            new("V", 0, 1024)
+            source(2)
+            acc(a("B6"), [(a("MP", 7 - i, 135 - i), a("TH", 512 * i, 512 * i + 512)) for i in range(8)])
+            new("V", 1024, 2048)
+            new("S", ESPL[2], 3072)
+            sq(a("ZO"), a("B6"))
+            dma("Y", ext(T.zu[:]), a("ZO", p=64))
+            dma("Y", ext(T.zt[:]), a("ZO", p=64, p0=64))
+            new("V", 2048, ESPL[2])
+            for c in range(3):
+                for lo in range(2):
+                    acc(a("B%d" % (3, 4, 5)[c], 64 * lo, 64 * lo + 64),
+                        [(a("MP", 7 - i, 135 - i), a("EW", 1024 * c + 2 * i + lo, 1024 * c + 1024, st=16)) for i in range(8)])
+            for c in range(3):
+                for lo in range(2):
+                    gat("SSV"[c], a("YO", 192 * lo + 64 * c, 192 * lo + 64 * c + 64), a("B%d" % (3, 4, 5)[c], 64 * lo, 64 * lo + 64))
+            dma("Y", ext(T.yu[:]), a("YO", p=64))
+            dma("S", ext(T.yt[:]), a("YO", p=64, p0=64))
+    for sem, val in fin.items():
+        if seen["G"].get(sem, 0) < val:
+            g.wait_ge(T.sem[sem], val)

@@ -3,42 +3,114 @@ from concourse.mybir import AluOpType as ALU, AxisListType as AX, ActivationFunc
 F, BF, I, U = "float32", "bfloat16", "int32", "uint16"
 KA, XA, KB, XB, KEND = 4128, 8256, 11328, 15456, 18528
 ZC = 13312
-DUM = 6144
-KSPL, XSPL, ESPL, ZSPL, CV, KV = (2560, 1536, 1536), 2048, ((3072, 0), (3072, 0), 2304), 4096, 768, (512, 1536)
-NS1, XC1, U1 = 3, 3072, 256
-NTV0 = 20
+A2 = 6144
+GP = 512
+PARTS = ((0, 64), (64, 32))
+CY, PC, GA, SCA, CALL, SAME, HAND, LDMA, RDMA, RCALL = 0.83e-3, 0.45e-3, 1.3e-3, 3.2e-3, 0.05, 0.03, 0.1, 2.0, 3.0, 0.8
+HOLD, LAG, DEPTH = 0.3, 0.7, 3
 SB = {
-    "TON": ([128, 4096], BF), "BIG": ([128, KEND], BF), "WN": ([128, ZC + 16], BF), "PR": ([128, 3072], BF),
-    "CW": ([128, 3072], BF), "A1": ([128, 6240], BF), "A2": ([128, 6240], BF), "SC": ([128, 3072], BF),
-    "EW": ([128, 3072], BF), "XR": ([128, 3072], BF), "TH": ([128, 8192], BF), "KS": ([128, 32], F),
-    "IN0": ([128, 408], U), "IN1": ([128, 408], U), "IN2": ([128, 408], U), "SD0": ([128, 408], U), "SD1": ([128, 408], U),
-    "LU": ([128, 192], I), "LT": ([128, 192], I), "L3": ([128, 768], I), "LB": ([128, 256], I), "LS": ([128, 144], I),
-    "H4": ([128, 1024], I), "ST": ([128, 1792], BF), "LSF": ([128, 144], F), "E8": ([128, 256], F),
-    "IB": ([128, 128], BF), "IF": ([128, 128], F), "NB": ([128, 128], BF), "NS": ([128, 128], BF), "EA": ([128, 128], BF),
-    "EB": ([128, 128], BF), "PS": ([128, 128], BF), "SH1": ([128, 128], F), "SH2": ([128, 128], F),
-    "ON": ([128, 256], BF), "ONF": ([128, 128], F), "G8F": ([128, 8], F), "G8": ([128, 8], BF), "SEL": ([128, 64], BF),
-    "G4": ([128, 8], BF), "MS": ([128, 144], BF), "MU": ([128, 144], BF), "MT": ([128, 144], BF), "MP": ([128, 136], BF),
-    "WB": ([128, 240], BF), "COL": ([128, 32], F), "CI": ([128, 16], I), "BC": ([128, 64], U), "BCF": ([128, 64], F),
-    "MI": ([128, 256], F), "QM": ([128, 256], BF), "QN": ([128, 128], BF), "JB": ([128, 256], F), "SI": ([128, 256], F),
-    "SG": ([128, 256], BF), "W8": ([128, 256], BF), "CC1": ([128, 128], BF), "TRI": ([128, 128], BF), "K16": ([128, 192], BF),
-    "JO": ([128, 192], F), "DF": ([128, 256], F), "THS": ([128, 256], F), "TMP": ([128, 256], F), "RR": ([128, 128], F),
-    "OF": ([128, 200], F), "NO": ([128, 192], BF), "NQ": ([128, 272], BF), "IV": ([128, 272], BF), "THX": ([128, 256], F),
-    "NE": ([128, 272], BF), "EN": ([128, 272], BF), "N4": ([128, 8, 2, 16], BF), "K4": ([128, 8, 2, 16], BF),
-    "C4": ([128, 8, 2, 16], BF), "P2": ([128, 256], BF), "X2": ([128, 256], F), "HC": ([128, 256], BF),
-    "KP": ([128, 256], BF), "NP": ([128, 256], BF), "CP": ([128, 256], BF), "SP": ([128, 256], F),
-    "KK": ([128, 256], BF), "CK": ([128, 256], BF),
-    "LN": ([128, 256], BF), "GG": ([128, 256], BF), "OX": ([128, 192], U),
-    "OD": ([128, 192], U), "FS": ([128, 256], BF), "OK": ([128, 256], BF), "VL": ([128, 256], F), "MX": ([128, 256], F),
-    "MI8": ([128, 48], I), "SM": ([128, 192], F), "SL2": ([128, 48], BF), "SQ": ([128, 64], BF), "OH": ([128, 1024], BF), "LC": ([128, 128], BF),
-    "OC": ([128, 8], U), "TBC": ([128, 128], BF), "TBW": ([128, 144], BF), "GT": ([128, 128], BF), "QQ": ([128, 256], BF), "Q3": ([128, 128], BF),
-    "QV": ([128, 192], BF), "ZV": ([128, 96], BF), "LP": ([128, 256], F), "OP": ([128, 16], U), "OS": ([128, 192], U),
-    "NV": ([128, 192], BF), "TT": ([128, 256], BF), "OK2": ([128, 256], U), "OB": ([128, 256], U),
-    "OE": ([128, 8], U), "EV": ([128, 128], BF), "YO": ([128, 384], F), "ZO": ([128, 512], F),
+    "TON": ([128, 4096], BF), "PT": ([128, 4096], BF), "BIG": ([128, KEND], BF), "WN": ([128, ZC + 16], BF),
+    "PR": ([128, 3072], BF), "SC": ([128, 3072], BF), "XR": ([128, 3072], BF),
+    "EW": ([128, 3072], BF), "A": ([128, 2 * A2], BF), "TH": ([128, 8192], BF),
+    "IN0": ([128, 392], U), "IN1": ([128, 392], U), "IN2": ([128, 392], U), "SD0": ([128, 392], U), "SD1": ([128, 392], U),
+    "SG0": ([128, 384], BF), "SG1": ([128, 384], BF), "SR0": ([128, 1024], BF), "SR1": ([128, 384], BF), "SR2": ([128, 384], BF),
+    "NQ": ([128, 272], BF),
+    "UT": ([128, 256], F), "ZB": ([128, 2064], BF),
+    "L2": ([128, 384], I), "L3": ([128, 768], I), "LB": ([128, 256], I), "LS": ([128, 136], I), "LSF": ([128, 272], F),
+    "LF0": ([128, 192], F), "ST": ([128, 1792], BF), "HL2": ([128, 1024], BF),
+    "ON": ([128, 256], BF), "ONF": ([128, 256], F), "IF": ([128, 128], F),
+    "IB": ([128, 128], BF), "PS": ([128, 128], BF), "NS": ([128, 128], BF), "NB": ([128, 128], BF), "NI": ([128, 128], BF),
+    "P32": ([128, 128], BF), "EA": ([128, 128], BF), "EB": ([128, 128], BF), "I3": ([128, 128], BF),
+    "E8": ([128, 512], F), "SI": ([128, 256], F), "SG": ([128, 256], BF),
+    "KS": ([128, 32], F), "G4": ([128, 32], BF), "G8": ([128, 16], BF), "G8F": ([128, 16], F), "G8T": ([128, 256], F),
+    "G8B": ([128, 16], BF), "ROW": ([128, 3840], BF), "ROF": ([128, 912], F), "JO": ([128, 576], F),
+    "COL": ([128, 16], F), "CI": ([128, 8], I), "BC": ([128, 80], U), "BCF": ([128, 112], F),
+    "MI": ([128, 128], BF), "M6": ([128, 640], BF), "RR": ([128, 128], F),
+    "R6": ([128, 24], BF), "T12": ([128, 48], BF), "PM": ([128, 96], BF), "PMT": ([128, 96], BF), "CC1": ([128, 128], BF),
+    "SL2": ([128, 80], BF), "MS": ([128, 144], BF), "MU": ([128, 144], BF), "MT": ([128, 144], BF), "MP": ([128, 144], BF),
+    "WB": ([128, 240], BF), "SQ3": ([128, 384], BF), "THL": ([128, 96], F), "TMP": ([128, 384], F),
+    "NE": ([128, 272], BF), "N12": ([128, 192], BF), "SH32": ([128, 128], BF),
+    "CK": ([128, 256], BF), "KK": ([128, 256], BF), "LN": ([128, 256], BF), "GG": ([128, 256], BF), "FS": ([128, 256], BF),
+    "MX": ([128, 256], F), "OK": ([128, 256], BF), "TT": ([128, 512], BF), "P2": ([128, 256], BF),
+    "NB0": ([128, 272], BF), "HC": ([128, 256], BF),
+    "MI8": ([128, 40], I), "SM": ([128, 48], BF), "SF": ([128, 16], F), "TK": ([128, 40], BF), "SQ": ([128, 64], BF),
+    "OH": ([128, 1024], BF), "LC": ([128, 384], BF), "LP": ([128, 128], F), "PB": ([128, 256], BF), "QQ": ([128, 256], BF),
+    "Z3": ([128, 192], BF), "TB": ([128, 128], BF), "TBW": ([128, 144], BF), "GT": ([128, 96], BF), "QV": ([128, 192], BF),
+    "OC": ([128, 8], U), "OP": ([128, 16], U), "OD": ([128, 192], U), "OX": ([128, 192], U), "OS": ([128, 192], U),
+    "OK2": ([128, 256], U), "OB": ([128, 256], U), "OE": ([128, 8], U), "EV": ([128, 128], BF),
+    "NV": ([128, 256], BF), "YO": ([128, 384], F), "ZO": ([128, 512], F),
 }
-SCRATCH = {k: ("sbuf", v[0], v[1]) for k, v in SB.items()}
+POOL = {}
+for _p, _names in (("CB", "IB NI PS NS NB P32 EA EB I3 MI CC1 PM PMT R6 T12 SL2 G4 G8 MS MU MT MP WB"),
+                   ("CF", "IF RR E8 SI KS G8F G8T THL")):
+    _o = 0
+    for _n in _names.split():
+        POOL[_n] = (_p, _o)
+        _o += (SB[_n][0][1] + 15) // 16 * 16
+    SB[_p] = ([128, _o], SB[_n][1])
+SCRATCH = {k: ("sbuf", v[0], v[1]) for k, v in SB.items() if k not in POOL}
 for _b in range(8):
     SCRATCH["B%d" % _b] = ("psum", [128, 512], F)
-SEMAPHORES = ["qV", "qS", "qP", "qG", "sent"] + ["d%d" % k for k in range(48)] + ["r%d" % k for k in range(6)]
+SEMAPHORES = ["qV", "qS", "qP", "qG", "sent"] + ["d%d" % k for k in range(32)] + ["r%d" % k for k in range(10)]
+AID = ({}, {}, {0: "B7", 1: "B6", 2: "B7", 3: "B6", 5: "B7"})
+PLAN = {}
+
+
+def arrange(ops):
+    n = len(ops)
+    after = [[] for _ in ops]
+    for k, o in enumerate(ops):
+        for j in o["deps"]:
+            after[j].append(k)
+    prio = [0.0] * n
+    for k in range(n - 1, -1, -1):
+        prio[k] = max(prio[j] for j in after[k]) + 1e-4 if ops[k]["lazy"] and after[k] else -k
+    left = [len(o["deps"]) for o in ops]
+    est, on = [0.0] * n, [None] * n
+    free = {q: 0.0 for q in "VSPGY"}
+    ready = {q: set() for q in "VSPGYE"}
+    for k, o in enumerate(ops):
+        if not left[k]:
+            ready[o["q"]].add(k)
+    order, dma_free = [], 0.0
+    while len(order) < n:
+        best = None
+        for q in "PSVGY":
+            c = ready[q] | ready["E"] if q in "VS" else ready[q]
+            if c:
+                t = max(free[q], min(est[k] for k in c))
+                if best is None or t < best[0]:
+                    best = (t, q, c)
+        t, q, c = best
+        cost = lambda k: ops[k]["cost"][q == "V"]
+        x = max((k for k in c if est[k] <= t), key=lambda k: (prio[k], -k))
+        mine = lambda k, e: ops[k]["q"] == q or (ops[k]["q"] == "E" and q in "VS" and free["S" if q == "V" else "V"] > e)
+        soon = [est[k] for k in c if t < est[k] and prio[k] > prio[x] and mine(k, est[k])]
+        for r in "PVS" if q in "VS" else ():
+            front = [(p, max(est[p], free[r], t)) for p in ready[r] if r != q and prio[p] > prio[x]]
+            for _ in range(DEPTH):
+                front = [(k, max(e + cost(p) + 1.5 * HAND, est[k])) for p, e in front for k in after[p]
+                         if left[k] == 1 and prio[k] > prio[x] and e < t + cost(x)]
+                soon += [e for k, e in front if mine(k, e)]
+        if soon and min(soon) < t + (0.7 if ops[x]["lazy"] else HOLD) * cost(x):
+            free[q] = min(soon)
+            continue
+        o = ops[x]
+        ready[o["q"]].remove(x)
+        on[x] = q
+        free[q] = t + cost(x)
+        end = free[q] + o["lat"]
+        if o["move"]:
+            dma_free = end = max(end, dma_free) + o["move"]
+        order.append(x)
+        for j in after[x]:
+            r = ops[j]["q"]
+            gap = (0.0 if q == "P" else SAME) if q == r else (2 * HAND if "P" in (q, r) else HAND)
+            est[j] = max(est[j], end + gap + (LAG if ops[j]["lazy"] and r == "P" != q else 0.0))
+            left[j] -= 1
+            if not left[j]:
+                ready[r].add(j)
+    return order, on
 
 
 def rank_program(g, core, T, topo):
@@ -47,70 +119,70 @@ def rank_program(g, core, T, topo):
         return
     nxt, prv = T.cores[(rank + 3) % 8], T.cores[(rank - 3) % 8]
     Q = {"V": g.vector, "S": g.scalar, "P": g.tensor, "G": g, "Y": g.sync}
-    cnt = {"qV": 0, "qS": 0, "qP": 0, "qG": 0}
-    seen = {k: {} for k in Q}
-    hist = {}
-    nd = [0]
-    fin = {}
+    ops, hist, nd, lazy, who = [], {}, [0], [False], {}
 
     def a(n, c0=None, c1=None, p=128, st=1, p0=0, ps=1):
         w = SB[n][0][1] if n in SB else 512
         c0 = 0 if c0 is None else c0
         c1 = w if c1 is None else c1
-        t = T[n]
-        ap = t[p0:p0 + p, c0:c1:st] if st > 1 else (t[p0::ps, c0:c1] if ps > 1 else t[p0:p0 + p, c0:c1])
-        return (ap, [(n, c0, c1, st)])
-
-    def a4(n, h=None, p=96):
-        return (T[n][0:p] if h is None else T[n][0:p, :, h, :], [(n, 0, 256, 1)])
+        t, o = (T[POOL[n][0]], POOL[n][1]) if n in POOL else (T[n], 0)
+        ap = t[p0:p0 + p, o + c0:o + c1:st] if st > 1 else (t[p0::ps, o + c0:o + c1] if ps > 1 else t[p0:p0 + p, o + c0:o + c1])
+        return (ap, [(n, c0, c1, st)], (c1 - c0 + st - 1) // st, False)
 
     def ind(w, o):
-        return (w[0].indirect(o[0]), w[1] + o[1])
+        return (w[0].indirect(o[0]), w[1] + o[1], 16 * o[2], True)
 
     def ext(ap):
-        return (ap, [])
+        return (ap, [], 0, False)
 
-    def wait(q, kind, reads, writes):
-        need = {}
-        for rs, isw in ((reads, False), (writes, True)):
-            for (n, c0, c1, st) in rs:
-                ps = n not in SB
-                for (h0, h1, hw, hq, sem, val, hs) in hist.get(n, []):
-                    apart = h1 <= c0 or c1 <= h0 or not (hw or isw) or (st > 1 and hs == st and (c0 - h0) % st != 0)
-                    if hq == kind and (hq == "P" or (hq == "D" and n == "WN")):
+    def kind(x):
+        n = x[1][0][0]
+        return SB[n][1] if n in SB else "psum"
+
+    def issue(q, fn, reads, writes, cost, lat=0.0, move=0.0, sem=None, after=()):
+        k, deps = len(ops), set(after)
+        rw = [(r, False) for x in reads for r in x[1]] + [(r, True) for x in writes for r in x[1]]
+        for (n, c0, c1, st), isw in rw:
+            for (h0, h1, hw, j, hs) in hist.get(n, []):
+                if n in SB:
+                    if h1 <= c0 or c1 <= h0 or not (hw or isw) or (st > 1 and hs == st and (c0 - h0) % st != 0):
                         continue
-                    if apart and not (ps and hq != kind):
+                    if move and ops[j]["move"] and hw and isw:
                         continue
-                    need[sem] = max(need.get(sem, 0), val)
-        for sem, val in need.items():
-            if seen[q].get(sem, 0) < val:
-                Q[q].wait_ge(T.sem[sem], val)
-                seen[q][sem] = val
+                deps.add(j)
+        for (n, c0, c1, st), isw in rw:
+            h = hist.setdefault(n, [])
+            if n not in SB:
+                h[:] = []
+            elif isw and st == 1 and not move:
+                h[:] = [e for e in h if not (c0 <= e[0] and e[1] <= c1)]
+            h.append((c0, c1, isw, k, st))
+        deps.discard(k)
+        ops.append({"q": q, "fn": fn, "deps": deps, "cost": cost if isinstance(cost, tuple) else (cost, cost), "lat": lat,
+                    "move": move, "sem": sem, "lazy": lazy[0]})
+        return ops[k]
 
-    def note(rd, wr, q, sem, val):
-        for rs, isw in ((rd, False), (wr, True)):
-            for (n, c0, c1, st) in rs:
-                h = hist.setdefault(n, [])
-                h[:] = [e for e in h if not (e[4] == sem and e[2] == isw and c0 <= e[0] and e[1] <= c1 and
-                                             (st == 1 or q == "P" or (e[6] == st and (c0 - e[0]) % st == 0)))]
-                h.append((c0, c1, isw, q, sem, val, 1 if q == "P" else st))
+    def price(o, ins, f=1.0):
+        if o[3]:
+            return CALL + SCA * o[2]
+        if ins and ins[0][3]:
+            return CALL + GA * o[2]
+        if f < 2 and all(kind(x) in (BF, U) for x in [o] + ins[:2] if x[2] > 1):
+            f = 0.5
+        return CALL + CY * max(64, f * o[2])
 
-    def issue(q, fn, reads, writes, dma=False):
-        rd = [r for x in reads for r in x[1]]
-        wr = [r for x in writes for r in x[1]]
-        wait(q, "D" if dma else q, rd, wr)
-        ins = fn()
-        if dma:
-            sem, val = "d%d" % nd[0], 16
-            nd[0] += 1
-            ins.then_inc(T.sem[sem], 16)
-        else:
-            sem = "q" + q
-            cnt[sem] += 1
-            val = cnt[sem]
-            ins.then_inc(T.sem[sem], 1)
-        fin[sem] = val
-        note(rd, wr, "D" if dma else q, sem, val)
+    def both(o, i):
+        return (CALL + (GA * o[2] if i[3] else CY * max(64, o[2])), price(o, [i]))
+
+    def dmas(items, move, after=(), q="Y"):
+        sem = "d%d" % nd[0]
+        nd[0] += 1
+
+        def fn(q):
+            for o, i in items:
+                Q[q].dma_start(o[0], i[0]).then_inc(T.sem[sem], 16)
+        issue(q, fn, [i for o, i in items], [o for o, i in items], CALL * len(items), LDMA, move, (sem, 16 * len(items)), after)
+        return len(ops) - 1
 
     def sc(x):
         return x[0] if isinstance(x, tuple) else x
@@ -119,547 +191,579 @@ def rank_program(g, core, T, topo):
         return [x for x in xs if isinstance(x, tuple)]
 
     def cp(o, i):
-        issue("V", lambda: g.vector.tensor_copy(o[0], i[0]), [i], [o])
+        issue("V", lambda q: g.vector.tensor_copy(o[0], i[0]), [i], [o], price(o, [i]))
 
     def tt(o, x, y, op):
-        issue("V", lambda: g.vector.tensor_tensor(o[0], x[0], y[0], op), [x, y], [o])
+        issue("V", lambda q: g.vector.tensor_tensor(o[0], x[0], y[0], op), [x, y], [o],
+              price(o, [x, y], 1.0 if "psum" in (kind(x), kind(y)) else 2.0))
 
     def ts(o, x, s1, op0, s2=None, op1=None):
         if op1 is None:
-            issue("V", lambda: g.vector.tensor_scalar(o[0], x[0], sc(s1), None, op0), tl(x, s1), [o])
+            issue("V", lambda q: g.vector.tensor_scalar(o[0], x[0], sc(s1), None, op0), tl(x, s1), [o], price(o, [x]))
         else:
-            issue("V", lambda: g.vector.tensor_scalar(o[0], x[0], sc(s1), sc(s2), op0, op1), tl(x, s1, s2), [o])
+            issue("V", lambda q: g.vector.tensor_scalar(o[0], x[0], sc(s1), sc(s2), op0, op1), tl(x, s1, s2), [o], price(o, [x]))
 
     def scan(o, d0, d1, init, op0, op1):
-        issue("V", lambda: g.vector.tensor_tensor_scan(o[0], d0[0], d1[0], sc(init), op0, op1), tl(d0, d1, init), [o])
+        issue("V", lambda q: g.vector.tensor_tensor_scan(o[0], d0[0], d1[0], sc(init), op0, op1), tl(d0, d1, init), [o],
+              price(o, [d0, d1]))
 
     def ms(o, v):
-        issue("V", lambda: g.vector.memset(o[0], v), [], [o])
+        issue("V", lambda q: g.vector.memset(o[0], v), [], [o], price(o, []))
 
     def red(o, i):
-        issue("V", lambda: g.vector.tensor_reduce(o[0], i[0], AX.X, ALU.add), [i], [o])
+        issue("V", lambda q: g.vector.tensor_reduce(o[0], i[0], AX.X, ALU.add), [i], [o], CALL + CY * max(64, i[2]))
 
-    def sq(o, i):
-        issue("S", lambda: g.scalar.activation(o[0], i[0], ACT.Copy), [i], [o])
+    def relu(o, i, scale, bias=0.0):
+        issue("S", lambda q: g.scalar.activation(o[0], i[0], ACT.Relu, bias=sc(bias), scale=scale), tl(i, bias), [o],
+              CALL + CY * max(64, o[2]))
 
-    def sa(o, i, scale, bias=0.0, f=ACT.Identity):
-        issue("S", lambda: g.scalar.activation(o[0], i[0], f, bias=sc(bias), scale=sc(scale)), tl(i, scale, bias), [o])
+    def ec(o, i, q="E"):
+        issue(q, lambda q: g.vector.tensor_copy(o[0], i[0]) if q == "V" else g.scalar.activation(o[0], i[0], ACT.Copy),
+              [i], [o], both(o, i))
 
-    def gat(q, o, i):
-        (cp if q == "V" else sq)(o, i)
+    def es(o, i, scale, bias=0.0, q="E"):
+        issue(q, lambda q: g.vector.tensor_scalar(o[0], i[0], sc(scale), sc(bias), ALU.mult, ALU.add) if q == "V" else
+              g.scalar.activation(o[0], i[0], ACT.Identity, bias=sc(bias), scale=sc(scale)), tl(i, scale, bias), [o], both(o, i))
+
+    def gather(out, o0, win, offs, n, q="E"):
+        for l in range(0, n, GP):
+            ec(a(out, o0 + l, o0 + l + GP), ind(win, a(offs, l // 16, (l + GP) // 16)), q)
+
+    def mms(items):
+        def fn(q):
+            for o, l, r, s0, s1 in items:
+                ins = g.tensor.matmul(o[0], l[0], (r if isinstance(r, tuple) else r(None))[0], s0, s1)
+            return ins
+        rs = [r if isinstance(r, tuple) else r("V") for o, l, r, s0, s1 in items]
+        issue("P", fn, [x[1] for x in items] + rs, [x[0] for x in items],
+              sum(PC * max(min(64, x[1][2]), r[2] if isinstance(x[2], tuple) else 4) * (4 if kind(x[1]) == F else 1)
+                  for x, r in zip(items, rs)))
 
     def mm(o, l, r, s0=True, s1=True):
-        issue("P", lambda: g.tensor.matmul(o[0], l[0], r[0], s0, s1), [l, r], [o])
+        mms([(o, l, r, s0, s1)])
 
-    def acc(o, prs):
-        for k, (l, r) in enumerate(prs):
-            mm(o, l, r, k == 0, k == len(prs) - 1)
+    def more(o, l, r, last=False):
+        mm(o, l, r, False, last)
 
-    def io(o, pat, base=0, cm=0, fl=True):
-        if fl:
-            issue("G", lambda: g.iota(o[0], pat, base, cm, allow_small_or_imprecise_dtypes=True), [], [o])
+    def acc(o, prs, close=True):
+        mms([(o, l, r, k == 0, close and k == len(prs) - 1) for k, (l, r) in enumerate(prs)])
+
+    def io(o, pat, base=0, cm=0):
+        if kind(o) == I:
+            issue("G", lambda q: g.iota(o[0], pat, base, cm), [], [o], 0.13 + 2 * CY * o[2])
         else:
-            issue("G", lambda: g.iota(o[0], pat, base, cm), [], [o])
+            issue("G", lambda q: g.iota(o[0], pat, base, cm, allow_small_or_imprecise_dtypes=True), [], [o], 0.13 + 2 * CY * o[2])
 
-    def sel(o, i, pat, op, base, cm):
-        issue("G", lambda: g.affine_select(o[0], i[0], pat, op, 0.0, base, cm), [i], [o])
+    def sel(o, i, pat, op, base, cm, fill=0.0):
+        issue("G", lambda q: g.affine_select(o[0], i[0], pat, op, fill, base, cm), [i], [o], 0.17 + 2 * CY * o[2])
 
-    def dma(q, o, i):
-        issue(q, lambda: Q[q].dma_start(o[0], i[0]), [i], [o], dma=True)
+    def put(o, i, pat, base, v):
+        sel(o, i, [[-s, n] for s, n in pat], ALU.not_equal, -base, 1, v)
+
+    def band(o, tmp, i, pat, lo, hi):
+        sel(tmp, i, [[-s, n] for s, n in pat], ALU.is_ge, -lo, 1)
+        sel(o, tmp, pat, ALU.is_ge, hi, -1)
+
+    def clear(first, after=None):
+        for o in (0, A2):
+            for l in range(o, o + 3072, 1024):
+                if first:
+                    ec(a("A", l, l + 1024), a("ZB", 0, 1024), "S")
+                else:
+                    io(a("A", l, l + 1024), [[0, 1024]])
+                    ops[-1]["deps"].add(after)
 
     col = lambda k, p=128: a("COL", k, k + 1, p)
-    sm = lambda c, w=8, p=96: a("SM", c, c + w, p)
     mi = lambda c, w=8: a("MI8", c, c + w, 96)
-    ch = lambda n, c: a(n, 1024 * c, 1024 * c + 1024)
-    bc16 = lambda: a("BC", 0, 8)
-    bc32 = lambda: a("BC", 16, 32)
+    sm = lambda c, w=8, p=96: a("SM", c, c + w, p)
     i96 = a("IB", 0, 96, 96)
+    s96 = lambda n: a(n, 0, 96, 96)
+    one = lambda m: a("ON", 0, m, 1)
+    nil = lambda m, p=128: a("ZB", 0, m, p)
+    row = lambda k, n=256, o=0: a("ROW", 256 * k + o, 256 * k + o + n, 1)
+    bar = lambda n, h: a(n, h, 256, 96, 2)
+    lis = lambda n, h, o=0: a(n, o + h, o + 192, 128, 2)
 
-    def steps(W, ks, q):
-        for k in ks:
-            o = a("TH", 256 * k, 256 * k + 2 * W)
-            if q == "V":
-                ts(o, a("TT", 0, 2 * W), float(k), ALU.is_lt)
-            else:
-                sa(o, a("TT", 0, 2 * W), -1.0, a("KS", k, k + 1), ACT.Sign)
+    def count(W, bank, w0, q):
+        for k in range(16):
+            o, x, b = a("TH", 512 * k, 512 * k + 4 * W), a("TT", 0, 4 * W), a("KS", k, k + 1)
+            op = issue(q, lambda q, o=o, x=x, b=b, k=k:
+                       g.vector.tensor_scalar(o[0], x[0], float(k), 0.5, ALU.is_lt, ALU.subtract) if q == "V" else
+                       g.scalar.activation(o[0], x[0], ACT.Sign, bias=b[0], scale=-2.0),
+                       [x, b], [o], (CALL + CY * 4 * W, CALL + CY * 2 * W))
+            wt = lambda q, op=op: a("G4", w0, w0 + 8) if q else (a("G4", w0, w0 + 4) if op["q"] == "V" else a("G4", w0 + 4, w0 + 8))
+            mms([(a(bank, 128 * (j % 2) + 2 * k + j // 2, 128 * (j % 2) + 128, W, 32),
+                  a("TH", 512 * k + W * j, 512 * k + W * j + W), wt, True, True) for j in range(4)])
 
-    def counts(W, bank, ks, q):
-        for k in ks:
-            for hf in range(2):
-                mm(a(bank, 128 * hf + 2 * (k % 16) + k // 16, 128 * hf + 128, W, 32), a("TH", 256 * k + W * hf, 256 * k + W * hf + W),
-                   a("G4", 0, 4) if q == "V" else a("G4", 4, 8))
+    def turn(src, W):
+        eye = a("IB", 0, W, W)
+        mms([(a("B6", 0, 4 * W), one(128), row(13, 4 * W, 256 - 2 * W), True, False)] +
+            [(a("B6", W * j, W * j + W), a(src, 128 * (j % 2), 128 * (j % 2) + 128, W), eye, False, j == 3) for j in range(4)])
+        ec(a("TT", 0, 4 * W), a("B6", 0, 4 * W))
 
-    def w2b(bank, wide, c, rhs):
-        for s in range(32):
-            mm(a(bank, s, 256, 32, 32, 32 * c), a(wide, 1024 * c + s, 1024 * c + 1024, st=32), rhs)
+    def w2b(bank, wide, c, rhs, open_):
+        mms([(a(bank, s, 256, 32, 32, 32 * c), a(wide[0], wide[1] + 1024 * c + s, wide[1] + 1024 * c + 1024, st=32), rhs,
+              not open_, not open_) for s in range(32)])
 
-    def rebuild(v, lo, hi, q):
-        w = (a("BIG", KB, XB), a("BIG", KA, KB), a("BIG", KB, KEND))[v]
+    def rebuild(v):
         K = (KA, KB, KA)[v]
-        gat(q, a("BIG", K + 32 + lo, K + 32 + hi), ind(w, a("OK2", lo // 16, hi // 16)))
+        gather("BIG", K + 32, (a("WN", 0, 4096), a("BIG", KA, KB), a("BIG", KB, KEND))[v], "OK2", 4096)
+        ec(a("EV"), ind(a("BIG", K, K + 4128), a("OE")))
+        cp(ind(a("BIG", 0, KA), a("OE")), a("EV"))
 
-    dma("Y", a("LS", 0, 128, 8), ext(T.bl[:]))
-    for k in range(8):
-        dma("SY"[k % 2], a("LB", 32 * k, 32 * k + 32), ext(T.bt[k, :]))
-    dma("S", a("LT"), ext(T.pt[:]))
-    dma("Y", a("L3", 256, 512), ext(T.bt[:]))
-    dma("S", a("LS", 128, 136, 1), ext(T.pn[:]))
-    dma("Y", a("LS", 136, 144, 1), ext(T.th[:]))
-    dma("S", a("TON", 2048, 4096), ext(T.tones[:, 2048:4096]))
-    dma("Y", a("TON", 0, 2048), ext(T.tones[:, 0:2048]))
-    dma("S", a("L3", 512, 768), ext(T.bk[:]))
-    dma("Y", a("LU"), ext(T.pu[:]))
-    dma("Y", a("L3", 0, 256), ext(T.bu[:]))
+    for q, items, move in (("Y", [(a("LB", 32 * k, 32 * k + 32), ext(T.bt[k, :])) for k in range(4)], 1.0),
+                           ("S", [(a("LB", 32 * k, 32 * k + 32), ext(T.bt[k, :])) for k in range(4, 8)], 1.0),
+                           ("Y", [(a("L2", 0, 192), ext(T.pt[:]))], 0.5),
+                           ("S", [(a("L3", 512, 768), ext(T.bk[:]))], 0.6),
+                           ("Y", [(a("L3", 256, 512), ext(T.bt[:]))], 0.6),
+                           ("S", [(a("L2", 192, 384), ext(T.pu[:]))], 0.5),
+                           ("Y", [(a("TON", 0, 2048), ext(T.tones[:, 0:2048]))], 1.8),
+                           ("S", [(a("TON", 2048, 4096), ext(T.tones[:, 2048:4096]))], 1.8),
+                           ("Y", [(a("LS", 0, 128, 8), ext(T.bl[:])), (a("LS", 128, 129, 8), ext(T.pn[:]))], 0.1),
+                           ("S", [(a("LS", 129, 130, 8), ext(T.th[:])), (a("L3", 0, 256), ext(T.bu[:]))], 0.6)):
+        dmas(items, move, q=q)
 
-    ms(a("ONF"), 1.0)
+    ms(a("ZB", 0, 1024), 0.0)
     ms(a("ON"), 1.0)
-    io(a("CI", 0, 1), [[0, 1]], 0, 1, False)
+    ms(a("ONF"), 1.0)
+    ms(a("PT"), 0.0)
+    ms(a("BIG", 0, KA), 99.0)
+    lazy[0] = True
+    clear(True)
+    diag = [[1, 128]]
+    sel(a("IF"), a("ONF", 0, 128), [[-1, 128]], ALU.is_equal, 0, 1)
+    put(a("IB"), nil(128), diag, 0, 1.0)
+    for n, v in (("NI", -1.0), ("PS", 16384.0), ("P32", 32768.0), ("EA", float(KA)), ("EB", float(KB)),
+                 ("NS", -16384.0), ("NB", -float(2 ** 25))):
+        es(a(n), a("IB"), v)
+    sel(a("I3"), a("IB"), [[0, 8], [-1, 16]], ALU.is_ge, 2, 0)
     io(a("SI"), [[0, 8], [1, 32]])
-    io(a("E8", p=8), [[1, 8], [0, 32]], 0, -1)
-    sel(a("IF"), a("ONF"), [[-1, 128]], ALU.is_equal, 0, 1)
-    sel(a("SEL"), a("ON", 0, 64), [[-1, 8], [-16, 8]], ALU.is_equal, 0, 1)
-    io(a("BCF", 0, 16), [[1, 16]])
-    io(a("BCF", 16, 32), [[1, 8], [0, 2]])
-    io(a("BCF", 32, 48), [[0, 2], [1, 8]])
-    sel(a("SH1"), a("ONF"), [[-1, 128]], ALU.is_equal, -1, 1)
-    io(a("MI"), [[0, 16], [1, 16]])
-    io(a("SP"), [[0, 8], [1, 16], [16, 2]])
+    sel(a("SG"), a("ON"), [[0, 8], [1, 32]], ALU.is_gt, 0, 0)
+    io(a("KS"), [[2, 32]], -1)
+    sel(a("E8", 0, 256, 8), a("ONF", p=8), [[1, 8], [0, 32]], ALU.is_equal, 0, -1)
+    put(a("E8", 256, 512, 8), nil(256, 8), [[1, 8], [0, 32]], 0, -1.0)
+    io(a("G4", 0, 8), [[-8, 2], [0, 4]], 16)
+    io(a("G4", 8, 16), [[-1, 2], [0, 4]], 2)
+    band(a("G4", 0, 16), a("G4", 16, 32), a("G4", 0, 16), [[0, 4], [32, 4]], 0, 30)
+    grp = [[16, 8]]
+    band(a("G8F", 0, 8), a("G8F", 8, 16), a("ONF", 0, 8), grp, 0, 15)
+    band(a("G8", 0, 8), a("G8", 8, 16), a("ON", 0, 8), grp, 0, 15)
+    sel(a("G8T", 0, 128, 8), a("ONF", 0, 128, 8), [[1, 8], [0, 16]], ALU.is_equal, 0, -1)
+    sel(a("G8T", 128, 256, 8), a("ONF", 0, 128, 8), [[1, 128]], ALU.is_equal, -2, -16)
+    for lo, hi, r, s in ((0, 24, 0, 1), (24, 40, 2, 0), (40, 80, 3, 0)):
+        put(a("SL2", lo, hi), nil(hi - lo), [[s, (hi - lo) // 8], [16, 8]], r, 1.0)
+    io(a("CC1"), [[1, 128]], 1)
+    io(a("RR"), [[0, 8], [1, 16]])
+    io(row(1), [[0, 256]], -16384)
+    io(a("ROW", 256 + 31, 512, 1, 32), [[0, 8]], 32768)
+    io(row(2), [[0, 256]], -6 * 64)
+    io(row(13, 512), [[-16, 2], [0, 256]])
+    es(a("G8B", 0, 8), a("G8", 0, 8), float(2 ** 25))
+    io(row(3), [[0, 8], [-1, 32]], 31)
+    io(row(4, 192), [[64, 96], [0, 2]])
+    io(row(5), [[0, 128], [16, 2]])
+    io(row(6), [[0, 128], [-16, 2]])
+    io(row(7), [[16, 256]])
+    io(row(8, 128), [[0, 8], [1, 16]])
+    io(row(8, 96, 128), [[0, 96]], 2 ** 19)
+    io(row(9), [[0, 256]], -1)
+    for v in range(3):
+        io(row(10 + v // 2, 96, 128 * (v % 2)), [[-1, 48], [0, 2]], -64 - 48 * v)
+    io(row(11, 96, 128), [[0, 48], [-32, 2]], -31)
+    for k in range(2):
+        sel(row(12, 96, 128 * k), nil(96, 1), [[0, 6], [1 - 2 * k, 2], [0, 8]], ALU.is_equal, k, 0, float(2 ** 99))
+    io(a("ROF", 0, 256, 1), [[1, 16], [512, 8], [0, 2]])
+    io(a("ROF", 256, 268, 1), [[A2 + 1, 2], [32, 6]], 31)
+    sel(a("ROF", 272, 528, 1), a("ONF", p=1), [[-1, 2], [0, 8], [1, 16]], ALU.is_equal, 0, 0)
+    io(a("ROF", 528, 656, 1), [[1, 64], [0, 2]])
+    io(a("ROF", 656, 784, 1), [[0, 64], [32, 2]])
+    io(a("ROF", 784, 912, 1), [[0, 8], [192, 16]])
+    sel(a("M6", 0, 128), a("ON", 0, 128), [[0, 8], [6, 16]], ALU.is_gt, 0, -1)
+    band(a("M6", 128, 384), a("M6", 384, 640), a("ON"), [[0, 16], [6, 16]], 0, 5)
+    put(a("PM"), nil(96), [[1, 6], [6, 16]], 0, 1.0)
+    put(a("PMT"), nil(96), [[1, 16], [16, 6]], 0, 1.0)
+    sel(a("T12", 0, 12), a("ON", 0, 12), [[16, 2], [16, 6]], ALU.is_gt, 0, -1)
+    io(a("T12", 12, 24), [[0, 12]], -1)
+    band(a("T12", 12, 24), a("T12", 24, 36), a("T12", 12, 24), [[0, 2], [16, 6]], 0, 15)
+    mm(a("B4", 0, 24, 96), a("PMT", p=96), a("T12", 0, 24, 96))
+    ec(a("R6", p=96), a("B4", 0, 24, 96))
+    five = ("MS", "MU", "MT", "MP", "WB")
+    ec((T.CB[:, POOL["MS"][1]:POOL["MS"][1] + 816], [a(n)[1][0] for n in five], 816, False), nil(816))
+    for n in ("TBW", "SM", "SQ"):
+        ec(a(n), nil(SB[n][0][1]))
+    put(a("MS", 15, 143, st=16), a("G8", 0, 8), grp, 0, 64.0)
+    for n, r, o in (("MU", 0, 7), ("MT", 2, 71)):
+        for x in (a(n, 15, 143, st=16), a("MP", o, o + 64, st=8)):
+            put(x, nil(8), grp, r, 1.0)
+            put(x, x, grp, r + 1, 1.0)
+    for k, rows in enumerate((((14, -1.0), (15, 32.0)), ((0, 64.0), (1, 1.0)), ((2, 1.0),))):
+        x = a("SQ3", 128 * k, 128 * k + 128)
+        for j, (r, v) in enumerate(rows):
+            put(x, x if j else nil(128), [[16, 8], [0, 16]], r, v)
+    ms(a("TBW", 0, 1), float(2 ** 98))
+    for n in ("NB0", "NE"):
+        ec(a(n, 0, 16), nil(16))
+    ec(a("NQ", 0, 257, st=256), nil(2))
+    for o in (KA, KB):
+        ec(a("BIG", o, o + 32), nil(32))
+    for n in ("SD0", "SD1"):
+        ms(a(n, 0, 8), 0)
+    ms(a("WN", ZC, ZC + 16), -0.5)
+    io(a("CI", 0, 1), [[0, 1]], 0, 1)
+    ts(a("CI", 1, 2), a("CI", 0, 1), 15, ALU.bitwise_and)
+    cp(col(0), a("CI", 1, 2))
+    io(col(1), [[0, 1]], 32, 32)
+    io(col(2), [[0, 1]], -129, -1)
+    ts(a("MI"), a("RR"), col(0), ALU.is_equal)
+    io(a("JO", 0, 192), [[16, 96], [0, 2]], 1)
+    io(a("JO", 192, 384), [[0, 96], [1, 2]], -1)
+    io(a("JO", 384, 576), [[16, 192]], 1)
+    es(a("JO", 384, 576), a("JO", 384, 576), 1.0, col(0))
+    ts(a("JO", 0, 192), a("JO", 0, 192), col(0), ALU.add, 2.0, ALU.mult)
+    tt(a("JO", 0, 192), a("JO", 0, 192), a("JO", 192, 384), ALU.add)
+    put(a("SH32"), nil(128), diag, 1, 32768.0)
+    ms(a("TMP", 0, 96), 0.25)
+    scan(a("TMP", 256, 352), a("TMP", 0, 96), a("ONF", 0, 96), float(2 ** 96), ALU.mult, ALU.mult)
+    tt(a("TMP", 128, 224), a("TMP", 256, 352), a("IF", 0, 96), ALU.mult)
+    red(col(3), a("TMP", 128, 224))
+    es(col(4), col(3), 2.0)
+    es(a("WB", 115, 116), col(3), 1.0)
+    io(a("BCF", 0, 32), [[1, 32]])
+    io(a("BCF", 32, 48), [[0, 2], [1, 8]], 16)
+    io(a("BCF", 80, 104), [[0, 24]], 7)
+    for o, picks in ((80, ((16, 0, 0), (16, 1, 8))), (88, ((16, 0, 0), (16, 1, 8), (18, 2, 24), (18, 3, 32))),
+                     (96, ((16, 0, 0), (16, 1, 8), (16, 2, 16), (16, 14, 40), (16, 15, 48)))):
+        for s, r, v in picks:
+            put(a("BCF", o, o + 8), a("BCF", o, o + 8), [[s, 8]], r, v - 49.0)
+        red(col(5 + (o - 80) // 8), a("BCF", o, o + 8))
+    es(a("BCF", 48, 56), a("BCF", 0, 8), 1.0, col(5))
+    es(a("BCF", 56, 64), a("BCF", 0, 8), 1.0, col(6))
+    io(a("BCF", 64, 76), [[0, 12]], 56)
+    for o in range(2):
+        es(a("BCF", 64 + 2 * o, 76, st=3), a("BCF", o, 8, st=2), 1.0, col(7))
+    cp(a("BC", 0, 16), a("BCF", 0, 16))
+    cp(a("BC", 16, 76), a("BCF", 16, 76))
+
+    lazy[0] = False
+    tt(a("NB0", 1, 256), a("LB", 1, 256), a("LB", 0, 255), ALU.not_equal)
+    scan(a("HC"), a("NB0", 0, 256), a("SG"), 0.0, ALU.add, ALU.mult)
+    turn("HC", 128)
+    ts(a("ST", 1024, 1280), a("L3", 512, 768), 1.0, ALU.add, 32.0, ALU.mult)
+    lazy[0] = True
     io(a("ST", 1280, 1536), [[1, 4], [0, 64]])
     io(a("ST", 1536, 1792), [[0, 4], [1, 64]])
-    io(a("K16"), [[16, 192]])
-    io(a("RR"), [[0, 8], [1, 16]])
-    io(a("WN", 0, 4096), [[0, 4096]])
-    io(a("BIG", 0, KA), [[0, KA]], 99)
-    io(a("CC1"), [[1, 128]], 1)
-    sel(a("TRI"), a("ON", 0, 128), [[1, 128]], ALU.is_gt, 0, -1)
-    io(a("A1", 0, 3072), [[0, 3072]])
-    io(a("A2", 0, 3072), [[0, 3072]])
-    for k, (s, m) in enumerate(((0, 15), (4, 15), (5, 15), (3, 31), (0, 1), (0, 7), (1, 127))):
-        ts(a("CI", 1 + k, 2 + k), a("CI", 0, 1), s, ALU.arith_shift_right, m, ALU.bitwise_and)
-    cp(a("COL", 0, 8), a("CI", 0, 8))
-    sa(col(9), col(1), 4.0)
-    sa(col(24), col(0), 32.0)
-    sa(col(25), col(0), 32.0, 32.0)
-    sa(a("KS"), a("SI", 0, 32), 1.0, -0.5)
-    sa(a("IB"), a("IF"), 1.0)
-    sa(a("JB"), a("SI"), 1.0, col(24))
-    sa(a("NS"), a("IF"), -16384.0)
-    sa(a("PS"), a("IF"), 16384.0)
-    sa(a("NB"), a("IF"), -float(2 ** 25))
-    sa(a("EA"), a("IF"), float(KA))
-    sa(a("EB"), a("IF"), float(KB))
-    sa(a("W8"), a("SI"), -float(2 ** 19), 31.0 * 2 ** 19)
-    sa(col(8), col(0), 1.0, float(DUM))
-    for v in range(3):
-        sa(col(16 + v), col(1), 1.0, float(4096 + 3072 * v))
-    sa(col(19), col(6), 512.0, col(4))
-    sa(col(26), col(4), 1.0, 2.0)
-    sa(col(27), col(0), 1.0, 129.0)
-    ts(a("G8F"), a("SI", 0, 8), col(2), ALU.is_equal)
-    cp(a("G8"), a("G8F"))
-    ts(a("G4", 0, 4), a("SI", 0, 4), col(3), ALU.is_equal)
-    ts(a("G4", 4, 8), a("SI", 0, 4), col(3), ALU.is_equal, 0.5, ALU.mult)
-    ts(a("SG"), a("SI"), 0.0, ALU.is_gt)
-    ts(a("E8", p=8), a("E8", p=8), 0.0, ALU.is_equal)
-    ms(a("NQ", 0, 16), 0.0)
-    ms(a("TBC"), 0.0)
-    ms(a("SM"), 0.0)
-
-    def first_book():
-        cp(a("LSF", 0, 128, 8), a("LS", 0, 128, 8))
-        mm(a("B0", 0, 256), a("LSF", 0, 128, 8), a("E8", p=8))
-        tt(a("NQ", 1, 256), a("LB", 1, 256), a("LB", 0, 255), ALU.not_equal)
-        tt(a("OK"), a("B0", 0, 256), a("SI"), ALU.is_gt)
-        cp(a("TBC", 2, 128, st=16), a("B0", 0, 256, st=32))
-        tt(a("FS"), a("OK"), a("NQ", 0, 256), ALU.mult)
-        scan(a("HC"), a("FS"), a("SG"), 0.0, ALU.add, ALU.mult)
-        for hf in range(2):
-            mm(a("B2", 128 * hf, 128 * hf + 128), a("HC", 128 * hf, 128 * hf + 128), a("IB"))
-        ts(sm(0, p=128), a("HC", 31, 256, st=32), col(25), ALU.add)
-        cp(a("TT"), a("B2", 0, 256))
-        steps(128, range(32 - NTV0), "S")
-        steps(128, range(32 - NTV0, 32), "V")
-        counts(128, "B3", range(32 - NTV0, 32), "V")
-        counts(128, "B3", range(32 - NTV0), "S")
-
-    ts(col(10), col(1), 2.0, ALU.min, 8.0, ALU.mult)
-    ts(col(11), col(1), 4.0, ALU.max, 5.0, ALU.min)
-    ts(col(11), col(11), -4.0, ALU.add, 8.0, ALU.mult)
-    ts(col(12), col(1), 4.0, ALU.is_ge, 8.0, ALU.mult)
-    ts(a("BCF", 48, 56), a("BCF", 0, 8), col(11), ALU.add, col(12), ALU.add)
-    ts(a("BCF", 32, 48), a("BCF", 32, 48), col(10), ALU.add)
-    ts(a("BCF", 48, 56), a("BCF", 48, 56), col(10), ALU.add)
-    cp(a("BC", 0, 56), a("BCF", 0, 56))
-    ms(a("SH1", 15, 128, st=16), 0.0)
-    ms(a("SH2"), 0.0)
-    ms(a("NE", 0, 16), 0.0)
-    ms(a("EN", 0, 16), 1.0)
-    ms(a("IV", 256, 272), 0.0)
-    ms(a("OF", 192, 200), 0.0)
-    ms(a("BIG", KA, KA + 32), 0.0)
-    ms(a("BIG", KB + 4096, XB), 0.0)
-    tt(a("SH1"), a("SH1"), a("IF"), ALU.subtract)
-    cp(a("SH2", 15, 128, st=16), a("SEL", 0, 8))
-    ts(a("MI"), a("MI"), col(1), ALU.is_equal)
-    ts(col(11), col(1), 0.0, ALU.is_equal, 63.0, ALU.mult)
-    ts(col(12), col(5), -63.0, ALU.mult, 64.0, ALU.add)
-    ts(a("TMP", 0, 96), a("ONF", 0, 96), 0.25, ALU.mult)
-    ms(a("TMP", 128, 224), 0.0)
-    ts(col(13), col(1), 2.0, ALU.is_lt, col(12), ALU.mult)
-    ts(col(14), col(1), 4.0, ALU.is_lt, col(12), ALU.mult)
-    scan(a("VL", 0, 96), a("TMP", 0, 96), a("TMP", 128, 224), float(2 ** 96), ALU.mult, ALU.add)
-    ts(col(11), col(11), 1.0, ALU.add)
-    tt(col(14), col(14), col(13), ALU.subtract)
-    tt(a("VL", 128, 224), a("VL", 0, 96), a("IF", 0, 96), ALU.mult)
-    ts(a("TMP"), a("SI"), 31.0, ALU.is_equal, -3.0 * 16384, ALU.mult)
-    red(col(20), a("VL", 128, 224))
-    for n in ("MS", "MU", "MT", "MP", "WB", "TBW", "SQ", "ZV"):
-        sa(a(n), a("ON", 0, SB[n][0][1]), 0.0)
-    sa(a("TBW", 0, 1), a("ONF", 0, 1), float(2 ** 98))
-    sa(col(15), col(5), -1.0)
-    sa(col(22), col(5), 32.0)
-    sa(a("JO"), a("K16"), 1.0, col(1))
-    sa(a("WN", ZC, ZC + 16), a("ONF", 0, 16), col(15))
-    sa(a("TBC", 0, 128, st=16), a("ONF", 0, 8), col(7))
-    sa(a("TBC", 1, 128, st=16), a("ONF", 0, 8), col(22))
-    sa(a("MS", 15, 143, st=16), a("G8F"), col(11))
-    sa(a("MU", 15, 143, st=16), a("G8F"), col(13))
-    sa(a("MT", 15, 143, st=16), a("G8F"), col(14))
-    sa(a("MP", 7, 71, st=8), a("G8F"), col(13))
-    sa(a("MP", 71, 135, st=8), a("G8F"), col(14))
-    sa(a("WB", 115, 116), col(20), 1.0)
-    sa(col(21), col(20), 2.0)
-    sa(a("SL2", 0, 32), a("SEL", 0, 32), 1.0)
-    for c in (32, 40):
-        sa(a("SL2", c, c + 8), a("SEL", 24, 32), 1.0)
-    first_book()
-    ts(a("ST", 1280, 1536), a("ST", 1280, 1536), col(9), ALU.add)
-
-    def pointers(v, lo, hi, q):
+    es(col(10), col(0), 256.0)
+    es(a("ST", 1280, 1536), a("ST", 1280, 1536), 64.0, col(10))
+    lazy[0] = False
+    dmas([(a("PT", p0=r, ps=16), a("ST", c, c + 256)) for r, c in ((0, 1024), (2, 1280), (3, 1536))], 0.9)
+    for l in range(2):
         for c in range(3):
-            l, h = max(lo, 1024 * c), min(hi, 1024 * c + 1024)
-            if l < h:
-                o = 136 * c + 64 - 64 * c
-                gat(q, a("CW", l, h), ind(a("WN", 0, 4096), a("IN%d" % v, o + l // 16, o + h // 16)))
-
-    tt(a("LP", 0, 128), ind(sm(0, p=128), bc16()), a("MI", 0, 128), ALU.mult)
-    mm(a("B2", 0, 8), a("LP", 0, 128), a("G8F"))
-    for c in range(3):
-        cp(a("IN0", 136 * c + 64, 136 * c + 128), a("LT", 64 * c, 64 * c + 64))
-    ts(a("DF"), a("SP"), float(32 - NTV0), ALU.is_lt, 256.0, ALU.mult)
-    cp(a("OE"), a("B2", 0, 8))
+            cp(a("IN0", 128 * c + 8 + 64 * l, 128 * c + 72 + 64 * l), a("L2", 192 * l + 64 * c, 192 * l + 64 * c + 64))
     cp(a("OB"), a("L3", 256, 512))
-    cp(a("LSF", 128, 144, 1), a("LS", 128, 144, 1))
-    mm(a("B5", 0, 16), a("ONF", p=1), a("LSF", 128, 144, 1))
-    ts(a("QM", 0, 128), a("RR"), 2.0, ALU.is_lt)
-    ts(a("QM", 128, 256), a("RR"), col(26), ALU.is_equal, -1.0, ALU.mult)
-    ts(a("QN"), a("RR"), 4.0, ALU.is_ge)
-    ts(a("LC"), a("RR"), 3.0, ALU.is_lt)
-    ts(sm(8, p=128), a("B5", 8, 16), 16384.0, ALU.add)
-    cp(a("IN0", 128, 136), a("B5", 0, 8))
-    tt(a("QM", 128, 256), a("QM", 128, 256), a("QM", 0, 128), ALU.subtract)
-    tt(a("QN"), a("QN"), a("LC"), ALU.subtract)
-    tt(a("THS"), ind(sm(8, p=128), bc32()), a("TMP"), ALU.add)
-    ts(a("VL"), a("B3", 0, 256), 16.0, ALU.mult, col(19), ALU.add)
-    tt(a("X2"), a("VL"), a("DF"), ALU.add)
-    for h in range(2):
-        mm(a("B6", 128 * h, 128 * h + 128), a("X2", h, 256, st=2), a("IF"))
+    count(128, "B3", 0, "E")
+    ec(a("P2"), a("B3", 0, 256))
+    mm(a("B7", 0, 256), a("ONF", 0, 128, 1), a("ROF", 0, 256, 1), True, False)
+    mms([(a("B7", h, 256, st=2), a("P2", h, 256, st=2), a("IB"), False, h == 1) for h in range(2)])
+    ts(a("OK2"), a("B7", 0, 256), 248.0, ALU.add)
+    ec(a("HL2", 512, 1024), nil(512))
+    cp(a("LF0"), a("L2", 192, 384))
+    mms([(a("B5", 32 * gg + 16 * h, 32 * gg + 16 * h + 16, 96), lis("LF0", h), a("IF", 16 * gg, 16 * gg + 16), True, True)
+         for gg in range(8) for h in range(2)])
+    ec(a("HL2", 0, 256, 96), a("B5", 0, 256, 96))
+    tt(a("HL2", 256, 512, 96), a("B5", 0, 256, 96), a("HL2", 0, 256, 96), ALU.subtract)
+    for hf, bank in enumerate(("B5", "B4")):
+        for c in range(3):
+            mms([(a(bank, s, 512, 32, 32, 32 * c), a("HL2", s, 1024, 32, 32, 32 * c),
+                  a("IB", 32 * c + 16 * hf, 32 * c + 16 * hf + 16, 32, p0=32 * c), True, True) for s in range(32)])
+        ec(a("SR0", 512 * hf, 512 * hf + 512, 96), a(bank, p=96))
+    lazy[0] = True
+    cp(a("LSF", 0, 130, 8), a("LS", 0, 130, 8))
+    mm(a("B0", 300, 301), a("G8T", 0, 128, 8), a("LSF", 128, 129, 8))
+    cp(a("IN0", 7, 8), a("B0", 300, 301))
+    es(a("THL", p=8), a("ONF", 0, 96, 8), a("LSF", 129, 130, 8))
+    mm(a("B0", 0, 256), a("LSF", 0, 128, 8), a("E8", 0, 256, 8))
+    tt(a("OK"), a("B0", 0, 256), a("SI"), ALU.is_gt)
+    tt(a("FS"), a("OK"), a("NB0", 0, 256), ALU.mult)
+    scan(a("KK"), a("FS"), a("SG"), 0.0, ALU.add, ALU.mult)
+    es(a("SF", 0, 8), a("KK", 31, 256, st=32), 1.0, col(1))
+    tt(a("LP"), ind(a("SF", 0, 8), a("BC", 0, 8)), a("MI"), ALU.mult)
+    mm(a("B6", 0, 8), a("LP"), a("G8F", 0, 8))
+    cp(a("OE"), a("B6", 0, 8))
+    es(a("LSF", 136, 264, 8), a("LSF", 0, 128, 8), 1.0, -1.0)
+    acc(a("B7", 0, 128), [(a("G8T", 128, 256, 8), a("LSF", 136, 264, 8)), (a("ROF", 272, 400, 1), a("ROF", 528, 656, 1)),
+                          (a("ROF", 400, 528, 1), a("ROF", 656, 784, 1))])
+    ec(a("TB"), a("B7", 0, 128))
+    cp(a("ST", 0, 512), a("L3", 0, 512))
+    tt(a("ST", 512, 1024), a("L3", 0, 512), a("ST", 0, 512), ALU.subtract)
+    lazy[0] = False
 
-    def book_digits():
-        ts(a("H4", 0, 512), a("L3", 0, 512), 6, ALU.arith_shift_right)
-        ts(a("H4", 512, 1024), a("L3", 0, 512), 63, ALU.bitwise_and)
-        cp(a("ST", 0, 1024), a("H4"))
-        for r, c in ((0, 0), (1, 512), (2, 256), (3, 768)):
-            dma("Y", a("WN", 0, 4096, p0=r, ps=16), a("ST", c, c + 256))
+    def upper_rows(v):
+        if v == 0:
+            dmas([(a("WN", 4096 + 1024 * c, 5120 + 1024 * c, p0=r, ps=16), a("SR0", p=8, p0=32 * c + 8 * r))
+                  for r in range(2) for c in range(3)], 0.6)
+        else:
+            dmas([(a("WN", 4096 + 3072 * v, 7168 + 3072 * v, p0=r, ps=16), a("SR%d" % v, p=64, p0=64 * r)) for r in range(2)], 0.5)
+
+    rid, pid, _ = topo.addr(nxt)
+    sent = [0]
+
+    def remote(dst, src, sem, move):
+        sent[0] += len(topo.engines(core, nxt))
+        issue("G", lambda q: g.remote_dma(dst[0], src[0], T.sem[sem], T.sem["sent"], pid, rid, topo.mask(core, nxt)),
+              [src], [dst], RCALL + (2.0 if sem == "r0" else 0.0), RDMA - RCALL + move, 0.0, (sem, len(topo.engines(prv, core))))
 
     for v in range(3):
-        IN, SD = "IN%d" % v, "SD%d" % v
+        IN, SD, SR = "IN%d" % v, "SD%d" % v, "SR%d" % v
         R = 4096 + 3072 * v
         K = (KA, KB, KA)[v]
         XC = (XA, XB, XA)[v]
-        ou = lambda c: a(IN, 136 * c, 136 * c + 64)
-        ot = lambda c: a(IN, 136 * c + 64, 136 * c + 128)
-        for c in range(3):
-            sq(ch("XR", c), ind(a("TON"), ot(c)))
-        if v == 0:
-            gat("V", a("BIG", KB + XSPL, KB + XSPL + 1024), ind(a("TON"), a("OB", XSPL // 16, XSPL // 16 + 64)))
-            ts(a("ST", 1024, 1280), a("L3", 512, 768), 1.0, ALU.add, 32.0, ALU.mult)
-            for r, c in ((6, 1280), (7, 1536), (4, 1024)):
-                dma("Y", a("WN", 0, 4096, p0=r, ps=16), a("ST", c, c + 256))
-            gat("V", a("BIG", KB + XSPL + 1024, KB + 4096), ind(a("TON"), a("OB", XSPL // 16 + 64, 256)))
-            for c in range(3):
-                cp(ou(c), a("LU", 64 * c, 64 * c + 64))
+        CW, PR, SC = ("WN", R), ("PR", 0), ("SC", 0)
+        wd = lambda n, lo, hi: a(n[0], n[1] + lo, n[1] + hi)
+        XR = ("XR", 0)
+        nb = col(8)
+        names_of = lambda up, lo, hi: a(IN, 8 + 64 * (up + lo // 1024) + lo // 16, 8 + 64 * (up + lo // 1024) + hi // 16)
+        cont, new = a("NE", 0, 256, 96), a("NQ", 0, 256, 96)
+        s0, s1, s3, s5 = [a("B%d" % k, 0, 256, 96) for k in (0, 1, 3, 5)]
+
+        def slots(p0, p):
+            at = lambda n, lo, hi, st=1: a(n, lo, hi, p, st, p0)
+            eye = lambda n: at(n, p0, p0 + p)
+            out = lambda h: a("B4", 2 * p0 + p * h, 2 * p0 + p * h + p)
+            more(at("B0", 0, 256), eye("PS"), at("NQ", 1, 257), True)
+            mm(a("B4", 2 * p0, 2 * (p0 + p)), a("ON", 0, 128, 1, p0=p0), a("ZB", 0, 2 * p, 1, p0=p0), True, False)
+            ts(at("NE", 1, 257), at("B0", 0, 256), 0.0, ALU.is_lt)
+            more(at("B1", 0, 256), eye("NS"), at("NE", 0, 256), True)
+            mms([(out(h), at("NE", 1 + h, 257, 2), eye("EB" if v == 1 else "EA"), False, False) for h in range(2)])
+            scan(at("KK", 0, 256), at("NQ", 0, 256), at("NE", 0, 256), 0.0, ALU.add, ALU.mult)
+            mms([(out(h), at("KK", h, 256, 2), eye("IB"), False, False) for h in range(2)])
+            scan(at("CK", 0, 256), at("NE", 0, 256), at("B1", 0, 256), 0.0, ALU.mult, ALU.max)
+            mms([(out(h), at("CK", h, 256, 2), eye("IB"), False, h == 1) for h in range(2)])
+            cp(a("OD", 2 * p0, 2 * (p0 + p)), a("B4", 2 * p0, 2 * (p0 + p)))
+
+        def changes(p0, p):
+            ec(a("UT", p=p, p0=p0), a("B2", 0, 256, p, p0=p0))
+            tt(a("NQ", 1, 256, p, p0=p0), a("B2", 1, 256, p, p0=p0), a("UT", 0, 255, p, p0=p0), ALU.not_equal)
+
+        def differ(c):
+            p0, p = PARTS[c // 2]
             for h in range(2):
-                cp(a("OK2", h, 256, st=2), a("B6", 128 * h, 128 * h + 128))
-            gat("S", a("BIG", KB, KB + XSPL), ind(a("TON"), a("OB", 0, XSPL // 16)))
-            sa(a("DF"), a("SP"), 1.0, col(25))
-        else:
-            pointers(v, 0, CV, "V")
-        cp(sm(128, p=128), a(IN, 128, 136))
-        tt(a("IV", 0, 256), ind(sm(128, p=128), bc32()), a("JB"), ALU.is_le)
-        tt(ch("PR", 0), ind(a("TON"), ou(0)), ch("XR", 0), ALU.mult)
-        w2b("B0", "PR", 0, a("G8"))
-        for c in range(3):
-            cp(a("OF", 64 * c, 64 * c + 64), ot(c))
-        acc(a("B3", 0, 192), [(a("SH1"), a("OF", 0, 192)), (a("SH2"), a("OF", 1, 193))])
-        pointers(v, CV if v > 0 else 0, 3072, "S")
-        tt(a("PR", 1024, 1536), ind(a("TON"), a(IN, 136, 168)), a("XR", 1024, 1536), ALU.mult)
-        ts(a("NO"), a("B3", 0, 192), 0.0, ALU.not_equal)
-        for gg in range(8):
-            for h in range(2):
-                mm(a("B4", 32 * gg + 16 * h, 32 * gg + 16 * h + 16, 96), a("NO", h, 192, st=2), a("IB", 16 * gg, 16 * gg + 16))
-        tt(a("PR", 1536, 2048), ind(a("TON"), a(IN, 168, 200)), a("XR", 1536, 2048), ALU.mult)
-        cp(a("NQ", 1, 257, 96), a("B4", 0, 256, 96))
-        acc(a("B3", 0, 256, 96), [(a("NS", 0, 96, 96), a("NQ", 1, 257, 96)), (a("NS", 0, 96, 96), a("IV", 1, 257, 96)),
-                                  (a("NS", 0, 96, 96), a("IV", 1, 257, 96))])
-        w2b("B0", "PR", 1, a("G8"))
-        if v < 2:
-            scan(a("GG", p=96), a("NQ", 0, 256, 96), a("SG", p=96), 0.0, ALU.add, ALU.mult)
-            for hf in range(2):
-                mm(a("B5", 96 * hf, 96 * hf + 96), a("GG", 128 * hf, 128 * hf + 128, 96), i96)
-        tt(ch("PR", 2), ind(a("TON"), ou(2)), ch("XR", 2), ALU.mult)
-        w2b("B1", "CW", 0, a("SEL", 32, 40))
-        w2b("B0", "PR", 2, a("G8"))
-        tt(a("THX", p=96), a("B3", 0, 256, 96), a("THS", p=96), ALU.add)
-        for c in range(1, 3):
-            w2b("B1", "CW", c, a("SEL", 32, 40))
+                l, o = 1024 * c + 512 * h, p0 + p * h + 32 * c
+                key, own = ind(a("BIG", 0, K + 4128), a("OD", o, o + 32)), a("XR", 1024 * c + h, 1024 * c + 1024, st=2)
+                bank = AID[v].get(2 * c + h)
+                if bank:
+                    ec(wd(SC, l, l + 512), key, "S")
+                    acc(a(bank), [(a("NI"), own), (a("IB"), wd(SC, l, l + 512))])
+                    ts(wd(PR, l, l + 512), a(bank), 0.0, ALU.not_equal)
+                else:
+                    tt(wd(PR, l, l + 512), key, own, ALU.not_equal)
+                mms([(a("B5", 2 * i + h, 256, 32, 32, 32 * c), a(PR[0], PR[1] + l + i, PR[1] + l + 512, st=16), a("G8B", 0, 8),
+                      False, h == 1 and i == 15) for i in range(16)])
+
+        ts(nb, a(IN, 7, 8), -1.0, ALU.mult)
+        relu(a("N12"), a("JO", 0, 192), 1.0, nb)
         if v == 0:
-            rebuild(0, 0, KSPL[0], "S")
-            rebuild(0, KSPL[0], 4096, "V")
-        sq(a("EV"), ind(a("BIG", K, K + 4128), a("OE")))
-        if v > 0:
-            cp(ind(a("BIG", 0, KA), a("OE")), a("EV"))
+            gather("WN", 0, a("TON"), "OB", 4096)
+            rebuild(0)
+            dmas([(a("WN", 0, 4096, p0=r, ps=16), a("ST", c, c + 256)) for r, c in ((0, 0), (1, 512), (2, 256), (3, 768))], 1.2)
+        mms([(s0, a("THL", p=8), a("E8", 256, 512, 8), True, False), (s0, one(96), row(1), False, False)])
+        mms([(bar("B0", h), lis("N12", 1 - h), a("SH32" if h else "P32"), False, False) for h in range(2)])
+        mm(s1, one(96), nil(256, 1), True, False)
+        mm(s5, row(8, 96, 128), row(2), True, False)
+        for c in range(3):
+            pieces = range(1024 * c, 1024 * c + 1024, GP)
+
+            def tones():
+                for l in pieces:
+                    ec(wd(XR, l, l + GP), ind(a("TON"), names_of(0, l, l + GP)), "SESESS"[l // GP])
+                for l in pieces:
+                    tt(wd(PR, l, l + GP), ind(a("TON"), names_of(1, l, l + GP)), wd(XR, l, l + GP), ALU.mult)
+
+            if c < 2:
+                tones()
+            else:
+                slots(*PARTS[0])
+            for l in pieces:
+                ec(wd(CW, l, l + GP), ind(a("PT"), names_of(0, l, l + GP)), "S")
+            w2b("B2", CW, c, a("MT", 15, 143, st=16), False)
+            if c:
+                changes(*PARTS[c - 1])
+            if c == 2:
+                if v < 2:
+                    scan(a("GG", p=96), new, a("SG", p=96), 0.0, ALU.add, ALU.mult)
+                    turn("GG", 96)
+                tones()
+            w2b("B1", CW, c, a("SL2", 0, 8), True)
+            w2b("B0", PR, c, a("G8", 0, 8), True)
+        upper_rows(v)
+        slots(*PARTS[1])
+        differ(0)
+        lazy[0] = True
         if v < 2:
-            sq(a("TT", 0, 192), a("B5", 0, 192))
-            steps(96, range(1, NS1), "S")
-        s0 = a("B0", 0, 256, 96)
-        cont = a("NE", 0, 256, 96)
-        tt(a("NE", 1, 257, 96), s0, a("THX", p=96), ALU.is_lt)
-        tt(a("EN", 1, 257, 96), s0, a("THX", p=96), ALU.is_ge)
-        sq(a4("N4"), a("NE", 1, 257, 96))
-        scan(a("KK", p=96), a("NQ", 0, 256, 96), cont, 0.0, ALU.add, ALU.mult)
-        sq(a4("K4"), a("KK", p=96))
-        tt(a("HC", p=96), a("B1", 0, 256, 96), a("EN", 0, 256, 96), ALU.mult)
-        scan(a("CK", p=96), cont, a("HC", p=96), 0.0, ALU.mult, ALU.add)
-        half = lambda n, h: a(n, 128 * h, 128 * h + 128, 96)
-        for h in range(2):
-            cp(half("NP", h), a4("N4", h))
-        cp(a4("C4"), a("CK", p=96))
-        for h in range(2):
-            cp(half("KP", h), a4("K4", h))
-        for h in range(2):
-            cp(half("CP", h), a4("C4", h))
-            acc(a("B4", 96 * h, 96 * h + 96),
-                [(half("KP", h), i96), (half("NP", h), a("EB" if v == 1 else "EA", 0, 96, 96)), (half("CP", h), i96)])
+            count(96, "B7", 8, "S")
+            mm(a("B6", 0, 192), one(128), row(4, 192), True, False)
+            lazy[0] = False
+            ec(a("P2", p=96), a("B7", 0, 256, 96), "S")
+            mms([(lis("B6", h), bar("P2", h), i96, False, h == 1) for h in range(2)])
+            ts(a("OX"), a("B6", 0, 192), 0.5, ALU.mult, 15.5, ALU.add)
+            lazy[0] = True
+            gather("BIG", XC, a("XR"), "OX", 3072, "S")
         scan(a("LN", p=96), a("ON", p=96), cont, 0.0, ALU.add, ALU.mult)
-        if v == 0:
-            cp(ind(a("BIG", 0, KA), a("OE")), a("EV"))
-        if v < 2:
-            steps(96, range(NS1, 32), "S")
-        for h in range(2):
-            cp(a("OD", h, 192, st=2), a("B4", 96 * h, 96 * h + 96))
-        acc(a("B3", 0, 256, 96), [(i96, a("W8", p=96)), (i96, a("CK", p=96)), (i96, a("LN", p=96))] +
-            ([(a("PS", 0, 96, 96), a("GG", p=96)), (a("NS", 0, 96, 96), a("KK", p=96))] if v < 2 else []) +
-            [(a("NB", 0, 96, 96), a("NE", 1, 257, 96)), (a("NB", 0, 96, 96), a("IV", 0, 256, 96))])
-        for c in range(3):
-            tt(ch("PR", c), ind(a("BIG", 0, K + 4128), a("OD", 64 * c, 64 * c + 64)), ch("XR", c), ALU.not_equal)
-            if v < 2:
-                counts(96, "B0", ((range(8), range(8, 20), range(20, 32)), (range(20), range(20, 32), ()))[v][c], "S")
-            if v < 2 and c == 2 - v:
-                sq(a("WN", R, R + U1), ind(a("WN", 0, 4096), a(IN, 0, U1 // 16)))
-                sq(a("P2", p=96), a("B0", 0, 256, 96))
-                sq(a("WN", R + U1, R + 1024), ind(a("WN", 0, 4096), a(IN, U1 // 16, 64)))
-            w2b("B2", "PR", c, a("G8"))
-        for h in range(2 if v < 2 else 0):
-            acc(a("B1", 96 * h, 96 * h + 96), [(a("IB"), a("K16", 0, 192, st=2)), (a("P2", h, 256, 96, 2), i96)])
-        for c in range(1 if v < 2 else 0, 3):
-            sq(a("WN", R + 1024 * c, R + 1024 * c + 1024), ind(a("WN", 0, 4096), ou(c)))
-        for r in range(2):
-            dma("Y", a("WN", R, R + 3072, p0=r, ps=16), a("WN", R, R + 3072, p0=6 + r, ps=16))
-            dma("G", a("WN", R, R + 3072, p0=2 + r, ps=16), a("CW", p0=6 + r, ps=16))
-        if v == 0:
-            book_digits()
-        else:
-            tt(a("TBC"), a("B7", 128, 256), a("TBC"), ALU.add)
-
-        def compact():
-            for h in range(2):
-                ts(a("OX", h, 192, st=2), a("B1", 96 * h, 96 * h + 96), 16.0, ALU.add, 3071.0, ALU.min)
-            sq(a("BIG", XC, XC + XC1), ind(a("XR"), a("OX", 0, XC1 // 16)))
-
-        scan(a("FS", p=96), cont, a("B2", 0, 256, 96), 0.0, ALU.mult, ALU.max)
-        if v < 2:
-            compact()
-        ts(a("OK", p=96), a("FS", p=96), 6.5, ALU.is_lt)
-        tt(a("VL", p=96), a("B3", 0, 256, 96), a("OK", p=96), ALU.mult)
-        scan(a("MX", p=96), a("SG", p=96), a("VL", p=96), 0.0, ALU.mult, ALU.max)
+        mms([(s3, row(8, 96, 128), row(3), True, False)] +
+            [(bar("B3", h), lis("N12", h), a("NB"), False, False) for h in range(2)])
+        for l, r in (([(s96("PS"), a("GG", p=96)), (s96("NS"), a("KK", p=96))] if v < 2 else []) +
+                     [(s96("NB"), a("NE", 1, 257, 96)), (i96, a("CK", p=96))]):
+            more(s3, l, r)
+        more(s3, i96, a("LN", p=96), True)
+        d0 = lambda lo, hi: a("B0", lo, hi, 96)
+        mm(a("B4", 0, 128), a("I3"), a("TB"), True, False)
+        mms([(d0(0, 80), one(96), nil(80, 1), True, False), (d0(0, 8), row(10 + v // 2, 96, 128 * (v % 2)), one(8), False, False),
+             (d0(8, 16), row(11, 96, 128), one(8), False, False), (d0(64, 72), row(12, 96), one(8), False, False),
+             (d0(72, 80), row(12, 96, 128), one(8), False, False)])
+        acc(a("B2", 0, 12), [(a("ONF", 0, 128, 1), a("ROF", 256, 268, 1)), (a("ROF", 784, 912, 1), a("ONF", 0, 12, 1))], False)
+        lazy[0] = False
+        differ(1)
+        differ(2)
+        scan(a("FS", p=96), cont, s5, 0.0, ALU.mult, ALU.max)
+        tt(a("UT", p=96), s3, a("FS", p=96), ALU.subtract)
+        scan(a("MX", p=96), a("SG", p=96), a("UT", p=96), 0.0, ALU.mult, ALU.max)
         cp(mi(32), a("MX", 31, 256, 96, 32))
-        ts(mi(8), mi(32), 5, ALU.arith_shift_right, 255, ALU.bitwise_and)
-        ts(mi(0), mi(32), 31, ALU.bitwise_and)
-        ts(mi(16), mi(32), 19, ALU.arith_shift_right)
-        ts(mi(24), mi(32), 14, ALU.arith_shift_right, 31, ALU.bitwise_and)
-        cp(sm(0, 32), mi(0, 32))
-        tt(a("LC"), ind(sm(8, p=128), bc16()), a("MI", 0, 128), ALU.mult)
-        mm(a("B4", 0, 6), a("LC", p=96), a("G8", 0, 6, 96))
+        ts(mi(0), mi(32), 5, ALU.arith_shift_right, 255, ALU.bitwise_and)
+        cp(sm(0), mi(0))
+        tt(a("LC", 0, 128), ind(a("SM", 0, 8), a("BC", 0, 8)), a("MI"), ALU.mult)
+        mm(a("B1", 0, 6), a("LC", 0, 128, 96), a("G8", 0, 6, 96))
         for gg in range(8):
-            ts(a("OH", 128 * gg, 128 * gg + 128, 96), a("CC1", p=96), sm(8 + gg, 1), ALU.is_equal)
-        acc(a("B5", 0, 128), [(a("TBC"), a("IB"))] +
-            [(a("WB", 112 - 16 * gg, 240 - 16 * gg, 96), a("OH", 128 * gg, 128 * gg + 128, 96)) for gg in range(8)])
-        cp(a("OC", 0, 6), a("B4", 0, 6))
-        ts(sm(56), sm(0), 1.0, ALU.add)
-        tt(sm(72), sm(56), sm(16), ALU.add)
-        cp(a("TBW", 1, 129), a("B5", 0, 128))
-        ts(sm(64), sm(72), -1.0, ALU.mult, col(25, 96), ALU.add)
-        cp(a("GT", 0, 96), ind(a("TBW"), a("OC", 0, 6)))
-        mm(a("B4", 0, 48, 96), a("GT", 0, 96), a("SL2"))
-        ts(mi(32), sm(64), float(R), ALU.add)
-        ts(mi(0), mi(32), 6, ALU.arith_shift_right)
-        ts(mi(8), mi(32), 63, ALU.bitwise_and)
-        ts(sm(160, 24), a("B4", 24, 48, 96), col(21, 96), ALU.is_lt)
-        cp(sm(40, 16), mi(0, 16))
-        ts(sm(104), sm(160), -16384.0, ALU.mult, 16384.0, ALU.add)
-        tt(sm(80, 24), a("B4", 0, 24, 96), sm(40, 24), ALU.subtract)
-        tt(sm(104), sm(104), sm(64), ALU.add)
-        tt(a("SQ", 0, 24, 96), sm(80, 24), sm(160, 24), ALU.mult)
-        mm(a("B5", 0, 8, 96), a("TRI", 0, 96, 96), a("SQ", 16, 24, 96))
-        mm(a("B5", 8, 16), a("ON", 0, 128, 96), a("SQ", 16, 24, 96))
-        tt(sm(32), a("B4", 16, 24, 96), sm(104), ALU.add)
+            ts(a("OH", 128 * gg, 128 * gg + 128, 96), a("CC1", p=96), sm(gg, 1), ALU.is_equal)
+            more(a("B4", 0, 128), a("WB", 112 - 16 * gg, 240 - 16 * gg, 96), a("OH", 128 * gg, 128 * gg + 128, 96), gg == 7)
+        cp(a("OC", 0, 6), a("B1", 0, 6))
+        ec(a("TBW", 1, 129), a("B4", 0, 128))
+        ts(mi(8), mi(32), 19, ALU.arith_shift_right)
+        ts(mi(16), mi(32), 31, ALU.bitwise_and)
         if v < 2:
-            tt(a("QQ"), ind(a("SQ", 0, 32), a("BC", 32, 48)), a("QM"), ALU.mult)
-        tt(sm(112), a("B5", 0, 8, 96), sm(104), ALU.add)
-        tt(sm(120), a("B5", 0, 8, 96), sm(32), ALU.add)
-        tt(sm(136, p=128), a("B5", 8, 16), sm(128, p=128), ALU.add)
+            ts(mi(24), mi(32), 14, ALU.arith_shift_right, 31, ALU.bitwise_and)
+        cp(sm(8, 24 if v < 2 else 16), mi(8, 24 if v < 2 else 16))
+        mms([(d0(8, 16), i96, sm(8), False, False), (d0(8, 16), i96, sm(16), False, False)] +
+            [(d0(c, c + 8), s96("NI"), sm(16), False, False) for c in (16, 24, 32)])
+        ec(a("GT"), ind(a("TBW"), a("OC", 0, 6)))
+        more(d0(0, 80), a("GT"), a("SL2"), True)
+        tt(a("LC", 128, 384), ind(a("SM", 0, 32), a("BC", 8, 24)), a("M6", 128, 384), ALU.mult)
+        mms([(a("B2", 0, 12), a("LC", 128, 256, 96), a("R6", 12, 24, 96), False, False),
+             (a("B2", 0, 6), a("LC", 256, 384, 96), a("R6", 12, 18, 96), False, False)])
+        ts(a("TK", p=96), d0(40, 80), col(4, 96), ALU.is_lt)
+        tt(a("SQ", 0, 40, 96), d0(0, 40), a("TK", p=96), ALU.mult)
+        tt(a("PB"), ind(a("SQ", 0, 24), a("BC", 32, 48)), a("M6", 0, 256), ALU.mult)
+        ec(a("QQ", 0, 128), ind(a("SQ"), a("BC", 48, 56)))
+        es(a("QQ", 128, 256), ind(a("SQ"), a("BC", 56, 64)), -1.0)
+        mms([(a("B2", 0, 12), a("PB", 0, 128, 96), a("ON", 0, 12, 96), False, False),
+             (a("B2", 0, 12), a("PB", 128, 256, 96), a("R6", 0, 12, 96), False, True)])
+        mms([(a("B5", 96 * k, 96 * k + 96), a("QQ", 128 * k, 128 * k + 128, 96), a("PM", p=96), True, True) for k in range(2)])
+        cp(a("OP", 0, 12), a("B2", 0, 12))
+        ec(a("QV"), a("B5", 0, 192))
+        cp(ind(a("A"), a("OP", 0, 12)), a("QV"))
+        mm(a("B3", 0, 1, 8), a("SQ", 16, 24, 96), a("ON", 0, 1, 96))
+        ec(a("SF", 8, 9, 8), a("B3", 0, 1, 8))
+        mm(a("B3", 2, 3), a("G8T", 0, 128, 8), a("SF", 8, 9, 8))
         top = R + 3071 if v < 2 else ZC
         win = a("WN", 0, R + 3072 if v < 2 else ZC + 16)
-        new = lambda q, lo, hi: gat(q, a("EW", lo, hi), ind(win, a("OS", lo // 16, hi // 16)))
-
-        def book_table():
-            tt(a("Q3"), ind(a("SQ", 0, 48), a("BC", 48, 56)), a("QN"), ALU.mult)
-            for gg in range(8):
-                mm(a("B7", 128 + 16 * gg, 144 + 16 * gg), a("OH", 128 * gg, 128 * gg + 128, 96), a("Q3", 16 * gg, 16 * gg + 16, 96))
-
-        def book(q, lo, hi):
-            for l in range(lo, hi, 512):
-                gat(q, a("TH", l, l + 512), ind(win, a("OK2", l // 16, l // 16 + 32)))
-
         if v == 2:
-            book_table()
-            tt(a("TBC"), a("B7", 128, 256), a("TBC"), ALU.add)
-            ts(sm(0, p=128), a("TBC", 0, 128, st=16), 64.0, ALU.mult, -float(ZC), ALU.add)
-            cp(sm(8, p=128), a("TBC", 2, 128, st=16))
-            tt(sm(0, p=128), sm(0, p=128), a("TBC", 1, 128, st=16), ALU.add)
-            tt(a("MX"), ind(sm(8, p=128), bc32()), a("SP"), ALU.is_gt)
-            tt(a("VL"), ind(sm(0, p=128), bc32()), a("SP"), ALU.add)
-            tt(a("X2"), a("VL"), a("MX"), ALU.mult)
-            for h in range(2):
-                mm(a("B3", 128 * h, 128 * h + 128), a("X2", h, 256, st=2), a("IF"))
-        ts(sm(112, 16), sm(112, 16), col(8, 96), ALU.min)
-        tt(a("LP"), ind(sm(112, 16, 128), a("BC", 0, 16)), a("MI"), ALU.mult)
-        for k in range(2):
-            mm(a("B4", 6 * k, 6 * k + 6), a("LP", 128 * k, 128 * k + 128, 96), a("G8F", 0, 6, 96))
-        if v == 2:
-            for h in range(2):
-                ts(a("OK2", h, 256, st=2), a("B3", 128 * h, 128 * h + 128), float(ZC), ALU.add)
-            book("S", 0, ZSPL)
-            tt(a("QQ"), ind(a("SQ", 0, 32), a("BC", 32, 48)), a("QM"), ALU.mult)
-        for k in range(2):
-            mm(a("B6", 96 * k, 96 * k + 96), a("QQ", 128 * k, 128 * k + 128, 96), i96)
-        if v == 2:
-            tt(sm(144, p=128), sm(136, p=128), a("G8F"), ALU.mult)
-            red(sm(152, 1, 128), sm(144, p=128))
-        cp(a("OP", 0, 12), a("B4", 0, 12))
-        cp(a("QV"), a("B6", 0, 192))
-        if v == 2:
-            ts(a("NV"), a("JO"), sm(152, 1, 128), ALU.is_ge)
-        cp(ind(a("A1"), a("OP", 0, 6)), a("QV", 0, 96))
-        cp(ind(a("A2"), a("OP", 6, 12)), a("QV", 96, 192))
-        def source(c):
-            ts(a("OS", 64 * c, 64 * c + 64), a("B%d" % (0, 2, 7)[c], 0, 64), col(16 + v), ALU.add, float(top), ALU.min)
+            es(col(9), a("B3", 2, 3), -1.0, nb)
+            relu(a("NV", 0, 192), a("JO", 384, 576), 1.0, col(9))
 
-        for c in range(3):
-            scan(ch("SC", c), ch("A1", c), ch("A2", c), 0.0 if c == 0 else a("SC", 1024 * c - 1, 1024 * c), ALU.add, ALU.add)
-            acc(a("B%d" % (0, 2, 7)[c], 0, 64), [(a("IB"), a("K16", 64 * c, 64 * c + 64))] +
-                ([(a("PS"), a("NV", 64 * c, 64 * c + 64))] if v == 2 else []) +
-                [(a("MS", 15 - i, 143 - i), a("SC", 1024 * c + i, 1024 * c + 1024, st=16)) for i in range(16)])
-            if c > 0:
-                source(c - 1)
-        if v < 2:
-            e0, e1 = ESPL[v]
-            if e1:
-                new("V", 0, 1024)
+        def table():
+            if v < 2:
+                es(sm(32), sm(0), 1.0, col(2, 96))
+                tt(a("SQ", 40, 56, 96), sm(24, 16), a("TK", 0, 16, 96), ALU.mult)
+            es(a("Z3"), ind(a("SQ"), a("BC", 64, 76)), -1.0)
+            mms([(a("B3", 128, 256), a("I3"), a("TB"), True, False)] +
+                [(a("B3", 128, 256, 32, p0=32 * (gg // 2)), a("Z3", 48 * (gg // 2) + 16 * (gg % 2), 48 * (gg // 2) + 16 * (gg % 2) + 32, 96),
+                  a("OH", 128 * gg, 128 * gg + 128, 96), False, gg % 2 == 1) for gg in range(8)])
+            ec(a("TB"), a("B3", 128, 256))
+            pick = lambda bank, k, close: [(a(bank, h, 256, st=2), a("SQ3", 128 * k, 128 * k + 128), a("TB"), False, close and h == 1)
+                                           for h in range(2)]
+            acc(a("B0", 0, 256), [(one(128), row(7 if v < 2 else 5)), (row(8, 128), one(256))], False)
+            if v < 2:
+                mms(pick("B0", 0, True))
+                ts(a("OK2"), a("B0", 0, 256), 32.0, ALU.add, 7199.0, ALU.min)
             else:
-                new("S", 0, 1024)
-            ts(a(SD, 128, 136), sm(136, p=128), 3072.0, ALU.min)
-            ts(sm(144), sm(8), -1.0, ALU.mult, col(27, 96), ALU.add)
-            tt(a("SQ", 32, 40, 96), sm(24), sm(160), ALU.mult)
-            source(2)
-            tt(a("SQ", 24, 32, 96), sm(144), sm(160), ALU.mult)
-            new("S", 1024, min(e0, 2048))
-            if e0 > 2048:
-                new("S", 2048, e0)
-            if XC1 < 3072:
-                sq(a("BIG", XC + XC1, XC + 3072), ind(a("XR"), a("OX", XC1 // 16, 192)))
-            book_table()
-            rid, pid, _ = topo.addr(nxt)
+                acc(a("B4", 0, 256), [(one(128), row(6)), (row(8, 128), row(9))], False)
+                mms(pick("B4", 2, True))
+                mms(pick("B0", 1, False))
+                relu(a("OK"), a("B4", 0, 256), -1.0)
+                more(a("B0", 0, 256), a("PS"), a("OK"), True)
+                ts(a("OK2"), a("B0", 0, 256), float(ZC), ALU.min)
 
-            def names(c):
-                for k, m in enumerate(("MU", "MT")):
-                    acc(a("B%d" % (3, 6, 4)[c], 64 * k, 64 * k + 64),
-                        [(a(m, 15 - i, 143 - i), a("EW", 1024 * c + i, 1024 * c + 1024, st=16)) for i in range(16)])
-
-            def send(c):
-                end = 136 * c + (136 if c == 0 else 128)
-                src, dst, sem = a(SD, 136 * c, end), a("IN%d" % (v + 1), 136 * c, end), "r%d" % (3 * v + c)
-                cp(a(SD, 136 * c, 136 * c + 128), a("B%d" % (3, 6, 4)[c], 0, 128))
-                wait("G", "D", src[1], [])
-                g.remote_dma(dst[0], src[0], T.sem[sem], T.sem["sent"], pid, rid, topo.mask(core, nxt))
-                fin["sent"] = fin.get("sent", 0) + len(topo.engines(core, nxt))
-                fin[sem] = len(topo.engines(prv, core))
-                note([], dst[1], "D", sem, fin[sem])
-
-            ts(sm(144, p=128), a("B7", 132, 256, st=16), 32.0, ALU.mult)
-            names(0)
-            tt(sm(144, p=128), a("B7", 133, 256, st=16), sm(144, p=128), ALU.add)
-            tt(a("X2"), ind(sm(144, p=128), bc32()), a("DF"), ALU.add)
-            for h in range(2):
-                mm(a("B2", 128 * h, 128 * h + 128), a("X2", h, 256, st=2), a("IF"))
-            if e0 < 2048:
-                new("V", e0, 2048)
-            if e0 < 3072:
-                new("V", max(e0, 2048), 3072)
-            send(0)
-            for h in range(2):
-                ts(a("OK2", h, 256, st=2), a("B2", 128 * h, 128 * h + 128), 7199.0, ALU.min)
-            names(1)
-            names(2)
-            k0 = KSPL[v + 1]
-            rebuild(v + 1, 0, k0, "S")
-            rebuild(v + 1, k0, k0 + KV[0], "V")
-            send(1)
-            rebuild(v + 1, k0 + KV[0], k0 + KV[1], "V")
-            send(2)
-            rebuild(v + 1, k0 + KV[1], 4096, "V")
-            io(a("A1", 0, 3072), [[0, 3072]])
-            io(a("A2", 0, 3072), [[0, 3072]])
+        if v == 2:
+            table()
+        for c in range(3):
+            scan(wd(SC, 1024 * c, 1024 * c + 1024), a("A", 1024 * c, 1024 * c + 1024), a("A", A2 + 1024 * c, A2 + 1024 * c + 1024),
+                 0.0 if c == 0 else wd(SC, 1024 * c - 1, 1024 * c), ALU.add, ALU.add)
+            bank = a(("B6", "B7", "B1")[c], 0, 64)
+            acc(bank, [(one(128), row(7, 64, 64 * c)), (row(8, 128), one(64))], False)
+            mms([(bank, a("MS", 15 - i, 143 - i), a(SC[0], SC[1] + 1024 * c + i, SC[1] + 1024 * c + 1024, st=16), False,
+                  i == 15 and v < 2) for i in range(16)])
+            if v == 2:
+                more(bank, a("PS"), a("NV", 64 * c, 64 * c + 64), True)
+        for c in range(3):
+            ts(a("OS", 64 * c, 64 * c + 64), a(("B6", "B7", "B1")[c], 0, 64), float(R), ALU.add, float(top), ALU.min)
+        if v < 2:
+            ts(a(SD, 7, 8), a("B3", 2, 3), nb, ALU.subtract, 3072.0, ALU.min)
+            table()
+        gather("EW", 0, win, "OS", 3072)
+        if v < 2:
+            nx, SG_ = v + 1, "SG%d" % v
+            for c in range(3):
+                bank = ("B2", "B5", "B4")[c]
+                for o, m in ((0, "MT"), (64, "MU")):
+                    acc(a(bank, o, o + 64), [(a(m, 15 - i, 143 - i), a("EW", 1024 * c + i, 1024 * c + 1024, st=16)) for i in range(16)])
+                cp(a(SD, 128 * c + 8, 128 * c + 136), a(bank, 0, 128))
+                lo = 128 * c + 8 if c else 0
+                remote(a("IN%d" % nx, lo, 128 * c + 136), a(SD, lo, 128 * c + 136), "r%d" % (5 * v + c), 0.4)
+            dmas([(a(SG_, p=64, p0=64 * r), a("EW", p0=r, ps=16)) for r in range(2)], 0.5, [len(ops) - 2])
+            remote(a("SR%d" % nx), a(SG_), "r%d" % (5 * v + 3), 0.8)
+            lazy[0] = True
+            clear(False, len(ops) - 1)
+            rebuild(nx)
+            lazy[0] = False
         else:
-            new("V", 0, 1024)
-            source(2)
-            acc(a("B6"), [(a("MP", 7 - i, 135 - i), a("TH", 512 * i, 512 * i + 512)) for i in range(8)])
-            new("V", 1024, 2048)
-            new("S", ESPL[2], 3072)
-            sq(a("ZO"), a("B6"))
-            dma("Y", ext(T.zu[:]), a("ZO", p=64))
-            dma("Y", ext(T.zt[:]), a("ZO", p=64, p0=64))
-            new("V", 2048, ESPL[2])
             for c in range(3):
+                bank = ("B3", "B4", "B5")[c]
                 for lo in range(2):
-                    acc(a("B%d" % (3, 4, 5)[c], 64 * lo, 64 * lo + 64),
+                    acc(a(bank, 64 * lo, 64 * lo + 64),
                         [(a("MP", 7 - i, 135 - i), a("EW", 1024 * c + 2 * i + lo, 1024 * c + 1024, st=16)) for i in range(8)])
-            for c in range(3):
                 for lo in range(2):
-                    gat("SSV"[c], a("YO", 192 * lo + 64 * c, 192 * lo + 64 * c + 64), a("B%d" % (3, 4, 5)[c], 64 * lo, 64 * lo + 64))
-            dma("Y", ext(T.yu[:]), a("YO", p=64))
-            dma("S", ext(T.yt[:]), a("YO", p=64, p0=64))
+                    ec(a("YO", 192 * lo + 64 * c, 192 * lo + 64 * c + 64), a(bank, 64 * lo, 64 * lo + 64))
+            dmas([(ext(T.yu[:]), a("YO", p=64)), (ext(T.yt[:]), a("YO", p=64, p0=64))], 0.7)
+            gather("TH", 0, win, "OK2", 4096)
+            for i in range(8):
+                mm(a("B2"), a("MP", 7 - i, 135 - i), a("TH", 512 * i, 512 * i + 512), i == 0, i == 7)
+            ec(a("ZO"), a("B2"))
+            dmas([(ext(T.zu[:]), a("ZO", p=64))], 0.5)
+            dmas([(ext(T.zt[:]), a("ZO", p=64, p0=64))], 0.5, q="S")
+
+    if not PLAN:
+        PLAN["order"], PLAN["on"] = arrange(ops)
+    order = PLAN["order"]
+    cnt, fin, seen = {}, {"sent": sent[0]}, {q: {} for q in Q}
+    for k in order:
+        o = ops[k]
+        o["q"], o["own"] = PLAN["on"][k], o["sem"] is None
+        if o["own"]:
+            cnt[o["q"]] = cnt.get(o["q"], 0) + 1
+            o["sem"] = ("q" + o["q"], cnt[o["q"]])
+        fin[o["sem"][0]] = o["sem"][1]
+    for k in order:
+        o = ops[k]
+        q, need = o["q"], {}
+        for d in o["deps"]:
+            if not (q == ops[d]["q"] == "P"):
+                sem, val = ops[d]["sem"]
+                need[sem] = max(need.get(sem, 0), val)
+        for sem, val in need.items():
+            if seen[q].get(sem, 0) < val:
+                Q[q].wait_ge(T.sem[sem], val)
+                seen[q][sem] = val
+        ins = o["fn"](q)
+        if o["own"]:
+            ins.then_inc(T.sem[o["sem"][0]], 1)
     for sem, val in fin.items():
         if seen["G"].get(sem, 0) < val:
             g.wait_ge(T.sem[sem], val)

@@ -1,48 +1,58 @@
+import numpy as np
 from concourse.mybir import AluOpType as ALU, AxisListType as AX, ActivationFunctionType as ACT
 
 F, BF, I, U = "float32", "bfloat16", "int32", "uint16"
 KA, XA, KB, XB, KEND = 4128, 8256, 11328, 15456, 18528
 ZC = 13312
-A2 = 6144
+A2 = 12288
+AV = (6144, 3072, 0)
 GP = 512
 PARTS = ((0, 64), (64, 32))
-CY, PC, GA, SCA, CALL, SAME, HAND, LDMA, RDMA, RCALL = 0.83e-3, 0.45e-3, 1.3e-3, 3.2e-3, 0.05, 0.03, 0.1, 2.0, 3.0, 0.8
+CY, PC, GA, SCA, CALL, SAME, HAND, LDMA, RDMA, RCALL = 0.87e-3, 0.44e-3, 1.25e-3, 3.2e-3, 0.05, 0.11, 0.12, 2.0, 2.6, 0.55
 HOLD, LAG, DEPTH = 0.3, 0.7, 3
+RULE, SHARE, CQ, LZ = 0, 1.0, "S", False
+PASSES, LEAN, PHAND = 8, 0.0, 0.26
+LOADS = "bt pt t0 t1 bk bl pu l8 bu"
+XQ, WQ, EQ, OQ, EARLY = "EEEEEE", "EEEEEE", ("E", "E"), "S", True
+RQ, TQ, FILL, TWICE, GR, GW = ("E", "E"), "E", True, False, 1024, 512
+ROUNDS, ALSO = 1200, ((1.0, (1.0, 1.3, 1.4, 1.0)), (1.0, (1.3, 1.3, 1.0, 1.2)), (1.0, (1.0, 1.0, 1.4, 1.6)))
 SB = {
     "TON": ([128, 4096], BF), "PT": ([128, 4096], BF), "BIG": ([128, KEND], BF), "WN": ([128, ZC + 16], BF),
-    "PR": ([128, 3072], BF), "SC": ([128, 3072], BF), "XR": ([128, 3072], BF),
-    "EW": ([128, 3072], BF), "A": ([128, 2 * A2], BF), "TH": ([128, 8192], BF),
+    "PR": ([128, 3072], BF), "SC": ([128, 3072], BF),
+    "EW": ([128, 3072], BF), "A": ([128, 2 * A2], BF), "TH": ([128, 4096], BF),
     "IN0": ([128, 392], U), "IN1": ([128, 392], U), "IN2": ([128, 392], U), "SD0": ([128, 392], U), "SD1": ([128, 392], U),
     "SG0": ([128, 384], BF), "SG1": ([128, 384], BF), "SR0": ([128, 1024], BF), "SR1": ([128, 384], BF), "SR2": ([128, 384], BF),
-    "NQ": ([128, 272], BF),
-    "UT": ([128, 256], F), "ZB": ([128, 2064], BF),
-    "L2": ([128, 384], I), "L3": ([128, 768], I), "LB": ([128, 256], I), "LS": ([128, 136], I), "LSF": ([128, 272], F),
+    "NQ": ([128, 512], BF), "LT": ([128, 192], F), "NL": ([128, 192], BF), "DF": ([128, 384], F), "MN": ([128, 864], BF),
+    "UT": ([128, 256], F), "ZB": ([128, 1024], BF),
+    "L2": ([128, 384], I), "L3": ([128, 768], I), "LB": ([128, 8], I), "LBF": ([128, 32], F), "LS": ([128, 136], I), "LSF": ([128, 272], F),
     "LF0": ([128, 192], F), "ST": ([128, 1792], BF), "HL2": ([128, 1024], BF),
     "ON": ([128, 256], BF), "ONF": ([128, 256], F), "IF": ([128, 128], F),
     "IB": ([128, 128], BF), "PS": ([128, 128], BF), "NS": ([128, 128], BF), "NB": ([128, 128], BF), "NI": ([128, 128], BF),
     "P32": ([128, 128], BF), "EA": ([128, 128], BF), "EB": ([128, 128], BF), "I3": ([128, 128], BF),
-    "E8": ([128, 512], F), "SI": ([128, 256], F), "SG": ([128, 256], BF),
-    "KS": ([128, 32], F), "G4": ([128, 32], BF), "G8": ([128, 16], BF), "G8F": ([128, 16], F), "G8T": ([128, 256], F),
-    "G8B": ([128, 16], BF), "ROW": ([128, 3840], BF), "ROF": ([128, 912], F), "JO": ([128, 576], F),
-    "COL": ([128, 16], F), "CI": ([128, 8], I), "BC": ([128, 80], U), "BCF": ([128, 112], F),
-    "MI": ([128, 128], BF), "M6": ([128, 640], BF), "RR": ([128, 128], F),
-    "R6": ([128, 24], BF), "T12": ([128, 48], BF), "PM": ([128, 96], BF), "PMT": ([128, 96], BF), "CC1": ([128, 128], BF),
-    "SL2": ([128, 80], BF), "MS": ([128, 144], BF), "MU": ([128, 144], BF), "MT": ([128, 144], BF), "MP": ([128, 144], BF),
-    "WB": ([128, 240], BF), "SQ3": ([128, 384], BF), "THL": ([128, 96], F), "TMP": ([128, 384], F),
+    "E8": ([128, 256], F), "SG": ([128, 256], BF),
+    "IS": ([128, 128], BF), "N63": ([128, 128], BF), "I16": ([128, 128], BF), "CAP": ([128, 256], BF), "IL": ([128, 128], BF),
+    "FY": ([128, 256], BF), "RM": ([128, 512], BF), "YY": ([128, 256], BF),
+    "G4": ([128, 160], BF), "G8": ([128, 16], BF), "G8T": ([128, 256], F),
+    "G8B": ([128, 16], BF), "ROW": ([128, 4608], BF), "ROF": ([128, 912], F), "JO": ([128, 576], F),
+    "COL": ([128, 16], F), "CI": ([128, 8], I), "BC": ([128, 96], U), "BCF": ([128, 128], F),
+    "MI": ([128, 128], BF), "M6": ([128, 384], BF), "RR": ([128, 128], F),
+    "R6": ([128, 32], BF), "OH2": ([128, 1024], BF), "P19": ([128, 128], BF), "T12": ([128, 48], BF), "PM": ([128, 96], BF), "PMT": ([128, 96], BF), "CC1": ([128, 128], BF),
+    "SL2": ([128, 128], BF), "MS": ([128, 144], BF), "MU": ([128, 144], BF), "MT": ([128, 144], BF), "MP": ([128, 144], BF),
+    "WB": ([128, 240], BF), "SQ3": ([128, 512], BF), "THL": ([128, 96], F), "TMP": ([128, 384], F),
     "NE": ([128, 272], BF), "N12": ([128, 192], BF), "SH32": ([128, 128], BF),
-    "CK": ([128, 256], BF), "KK": ([128, 256], BF), "LN": ([128, 256], BF), "GG": ([128, 256], BF), "FS": ([128, 256], BF),
-    "MX": ([128, 256], F), "OK": ([128, 256], BF), "TT": ([128, 512], BF), "P2": ([128, 256], BF),
-    "NB0": ([128, 272], BF), "HC": ([128, 256], BF),
-    "MI8": ([128, 40], I), "SM": ([128, 48], BF), "SF": ([128, 16], F), "TK": ([128, 40], BF), "SQ": ([128, 64], BF),
-    "OH": ([128, 1024], BF), "LC": ([128, 384], BF), "LP": ([128, 128], F), "PB": ([128, 256], BF), "QQ": ([128, 256], BF),
+    "CK": ([128, 256], BF), "KK": ([128, 256], BF), "LN": ([128, 256], BF), "FS": ([128, 256], BF),
+    "MX": ([128, 256], F), "OK": ([128, 256], BF), "TT": ([128, 512], BF), "P2": ([128, 528], BF),
+    "NB0": ([128, 272], BF),
+    "MI8": ([128, 40], I), "SM": ([128, 48], BF), "SF": ([128, 16], F), "TK": ([128, 64], F), "SQ": ([128, 80], BF),
+    "OH": ([128, 1024], BF), "LC": ([128, 384], BF), "PB": ([128, 256], BF), "QQ": ([128, 256], BF),
     "Z3": ([128, 192], BF), "TB": ([128, 128], BF), "TBW": ([128, 144], BF), "GT": ([128, 96], BF), "QV": ([128, 192], BF),
-    "OC": ([128, 8], U), "OP": ([128, 16], U), "OD": ([128, 192], U), "OX": ([128, 192], U), "OS": ([128, 192], U),
+    "OC": ([128, 8], U), "OP": ([128, 16], U), "OD": ([128, 192], U), "OS": ([128, 192], U),
     "OK2": ([128, 256], U), "OB": ([128, 256], U), "OE": ([128, 8], U), "EV": ([128, 128], BF),
     "NV": ([128, 256], BF), "YO": ([128, 384], F), "ZO": ([128, 512], F),
 }
 POOL = {}
-for _p, _names in (("CB", "IB NI PS NS NB P32 EA EB I3 MI CC1 PM PMT R6 T12 SL2 G4 G8 MS MU MT MP WB"),
-                   ("CF", "IF RR E8 SI KS G8F G8T THL")):
+for _p, _names in (("CB", "IB NI PS NS NB P32 EA EB IS N63 I16 P19 CAP IL I3 MI CC1 PM PMT R6 T12 SL2 G4 G8 MS MU MT MP WB"),
+                   ("CF", "IF RR E8 G8T THL")):
     _o = 0
     for _n in _names.split():
         POOL[_n] = (_p, _o)
@@ -52,7 +62,8 @@ SCRATCH = {k: ("sbuf", v[0], v[1]) for k, v in SB.items() if k not in POOL}
 for _b in range(8):
     SCRATCH["B%d" % _b] = ("psum", [128, 512], F)
 SEMAPHORES = ["qV", "qS", "qP", "qG", "sent"] + ["d%d" % k for k in range(32)] + ["r%d" % k for k in range(10)]
-AID = ({}, {}, {0: "B7", 1: "B6", 2: "B7", 3: "B6", 5: "B7"})
+LOW = 2.0 ** -93
+AID = 3 * ({0: "B7", 2: "B6"},)
 PLAN = {}
 
 
@@ -64,7 +75,12 @@ def arrange(ops):
             after[j].append(k)
     prio = [0.0] * n
     for k in range(n - 1, -1, -1):
-        prio[k] = max(prio[j] for j in after[k]) + 1e-4 if ops[k]["lazy"] and after[k] else -k
+        if RULE:
+            o = ops[k]
+            prio[k] = (max([prio[j] + (0.0 if o["q"] == ops[j]["q"] == "P" else HAND) for j in after[k]] + [0.0]) +
+                       min(o["cost"]) * (SHARE if o["cost"][0] > 0.5 else 1.0) + o["lat"] + o["move"])
+        else:
+            prio[k] = max(prio[j] for j in after[k]) + 1e-4 if ops[k]["lazy"] and after[k] else -k
     left = [len(o["deps"]) for o in ops]
     est, on = [0.0] * n, [None] * n
     free = {q: 0.0 for q in "VSPGY"}
@@ -113,6 +129,101 @@ def arrange(ops):
     return order, on
 
 
+def settle(ops):
+    n = len(ops)
+    before = [sorted(o["deps"] | o["behind"]) for o in ops]
+    after = [[] for _ in ops]
+    for k in range(n):
+        for j in before[k]:
+            after[j].append(k)
+    tail = [o["lat"] + o["move"] for o in ops]
+    way = ["R" if o["q"] == "G" else "D" for o in ops]
+
+    def sweep(rank, back):
+        src, dst = (after, before) if back else (before, after)
+        left = [len(x) for x in src]
+        ready = [(rank[k], k) for k in range(n) if not left[k]]
+        slots = {q: [] for q in "VSPGYDR"}
+        t0, t1, on = [0.0] * n, [0.0] * n, [None] * n
+
+        def fit(q, t, d):
+            x = slots[q]
+            i = len(x)
+            while i and x[i - 1][1] > t:
+                i -= 1
+            while i < len(x) and x[i][0] < t + d:
+                t = x[i][1]
+                i += 1
+            return t, i
+        while ready:
+            k = min(ready)
+            ready.remove(k)
+            k = k[1]
+            o, best = ops[k], None
+            for q in ("VS" if o["q"] == "E" else o["q"]):
+                t = max([t0[j] + 1e-3 if j in o["behind"] else
+                         t1[j] + ((0.0 if q == "P" else SAME) if on[j] == q else (PHAND if "P" == (q if back else on[j]) else HAND))
+                         for j in src[k]] + [0.0])
+                d = o["cost"][q == "V"]
+                if back:
+                    t += tail[k]
+                t, i = fit(q, t, d)
+                key = t + d + (lean[0] * d if q == "V" else 0.0)
+                if best is None or key < best[0]:
+                    best = (key, q, t, d, i)
+            _, q, t, d, i = best
+            on[k], t0[k], t1[k] = q, t, t + d
+            slots[q].insert(i, (t, t + d))
+            if not back:
+                t1[k] += o["lat"]
+                if o["move"]:
+                    m, i = fit(way[k], t1[k], o["move"])
+                    slots[way[k]].insert(i, (m, m + o["move"]))
+                    t1[k] = m + o["move"]
+            for j in dst[k]:
+                left[j] -= 1
+                if not left[j]:
+                    ready.append((rank[j], j))
+        return t0, t1, on
+
+    rank = [0.0] * n
+    for k in range(n - 1, -1, -1):
+        rank[k] = min(rank[j] for j in after[k]) - 1e-4 if ops[k]["lazy"] and after[k] else k
+    def replay(order, on, slow, pe, hand, far):
+        end, free = [0.0] * n, {q: 0.0 for q in "VSPGYDR"}
+        for k in order:
+            o, q = ops[k], on[k]
+            t = max([free[q]] + [end[j] + (0.0 if q == on[j] == "P" else hand * (PHAND if on[j] == "P" else HAND)) for j in o["deps"]])
+            free[q] = t + o["cost"][q == "V"] * (pe if q == "P" else slow)
+            end[k] = free[q] + o["lat"] * far
+            if o["move"]:
+                free[way[k]] = end[k] = max(end[k], free[way[k]]) + o["move"] * far
+        return max(end)
+
+    def mixed(r):
+        x = (np.arange(n + 4, dtype=np.uint64) + np.uint64(r * 7919 * 4096 + 1)) * np.uint64(0x9E3779B97F4A7C15)
+        x = (x ^ (x >> np.uint64(31))) * np.uint64(0xBF58476D1CE4E5B9)
+        return (x >> np.uint64(40)).astype(float) / 2 ** 24
+
+    kept, lean = None, [LEAN]
+    for r in range(PASSES + 2 * ROUNDS):
+        if r >= PASSES and (r - PASSES) % 2 == 0:
+            t, u = np.array(kept[1]), mixed(r)
+            lo = u[n] * kept[3]
+            rank = list(t + ((t > lo) & (t < lo + 3 + 12 * u[n + 1])) * (u[:n] - 0.5) * (1.0, 2.8, 5.0)[int(3 * u[n + 2])])
+            lean[0] = (0.0, 0.1, 0.3)[int(3 * u[n + 3])]
+        rank[:len(LOADS.split())] = range(-len(LOADS.split()) - 999, -999)
+        t0, t1, on = sweep(rank, False)
+        order = sorted(range(n), key=lambda k: (t0[k], k))
+        worth = max(t1) + sum(w * replay(order, on, *x) for w, x in ALSO)
+        if kept is None or worth < kept[0]:
+            kept = (worth, t0, on, max(t1), order)
+        if r < PASSES or (r - PASSES) % 2 == 0:
+            rank = [-x for x in sweep([-x for x in t1], True)[1]]
+    PLAN["time"] = kept[3]
+    return kept[4], kept[2]
+
+
 def rank_program(g, core, T, topo):
     rank = T.rank_of(core)
     if rank is None:
@@ -159,7 +270,7 @@ def rank_program(g, core, T, topo):
             h.append((c0, c1, isw, k, st))
         deps.discard(k)
         ops.append({"q": q, "fn": fn, "deps": deps, "cost": cost if isinstance(cost, tuple) else (cost, cost), "lat": lat,
-                    "move": move, "sem": sem, "lazy": lazy[0]})
+                    "move": move, "sem": sem, "lazy": lazy[0], "behind": set(), "name": (rw[-1][0][:2], rw[0][0][:2]) if rw else ()})
         return ops[k]
 
     def price(o, ins, f=1.0):
@@ -225,9 +336,9 @@ def rank_program(g, core, T, topo):
         issue(q, lambda q: g.vector.tensor_scalar(o[0], i[0], sc(scale), sc(bias), ALU.mult, ALU.add) if q == "V" else
               g.scalar.activation(o[0], i[0], ACT.Identity, bias=sc(bias), scale=sc(scale)), tl(i, scale, bias), [o], both(o, i))
 
-    def gather(out, o0, win, offs, n, q="E"):
-        for l in range(0, n, GP):
-            ec(a(out, o0 + l, o0 + l + GP), ind(win, a(offs, l // 16, (l + GP) // 16)), q)
+    def gather(out, o0, win, offs, n, q="E", gp=GP):
+        for l in range(0, n, gp):
+            ec(a(out, o0 + l, o0 + l + gp), ind(win, a(offs, l // 16, (l + gp) // 16)), q[l // gp % len(q)])
 
     def mms(items):
         def fn(q):
@@ -264,15 +375,6 @@ def rank_program(g, core, T, topo):
         sel(tmp, i, [[-s, n] for s, n in pat], ALU.is_ge, -lo, 1)
         sel(o, tmp, pat, ALU.is_ge, hi, -1)
 
-    def clear(first, after=None):
-        for o in (0, A2):
-            for l in range(o, o + 3072, 1024):
-                if first:
-                    ec(a("A", l, l + 1024), a("ZB", 0, 1024), "S")
-                else:
-                    io(a("A", l, l + 1024), [[0, 1024]])
-                    ops[-1]["deps"].add(after)
-
     col = lambda k, p=128: a("COL", k, k + 1, p)
     mi = lambda c, w=8: a("MI8", c, c + w, 96)
     sm = lambda c, w=8, p=96: a("SM", c, c + w, p)
@@ -284,83 +386,99 @@ def rank_program(g, core, T, topo):
     bar = lambda n, h: a(n, h, 256, 96, 2)
     lis = lambda n, h, o=0: a(n, o + h, o + 192, 128, 2)
 
-    def count(W, bank, w0, q):
-        for k in range(16):
-            o, x, b = a("TH", 512 * k, 512 * k + 4 * W), a("TT", 0, 4 * W), a("KS", k, k + 1)
-            op = issue(q, lambda q, o=o, x=x, b=b, k=k:
-                       g.vector.tensor_scalar(o[0], x[0], float(k), 0.5, ALU.is_lt, ALU.subtract) if q == "V" else
-                       g.scalar.activation(o[0], x[0], ACT.Sign, bias=b[0], scale=-2.0),
-                       [x, b], [o], (CALL + CY * 4 * W, CALL + CY * 2 * W))
-            wt = lambda q, op=op: a("G4", w0, w0 + 8) if q else (a("G4", w0, w0 + 4) if op["q"] == "V" else a("G4", w0 + 4, w0 + 8))
-            mms([(a(bank, 128 * (j % 2) + 2 * k + j // 2, 128 * (j % 2) + 128, W, 32),
-                  a("TH", 512 * k + W * j, 512 * k + W * j + W), wt, True, True) for j in range(4)])
+    def count(W, gs, tb, cb, q="E"):
+        n, off = 16 * gs, gs - 8
+        if off:
+            mms([(a(tb, W * j, W * j + W), a("YY", 128 * (j % 2), 128 * (j % 2) + 128, W), a("IS" if j // 2 else "IB", 0, W, W), True, True)
+                 for j in range(4)])
+            ec(a("TT", 0, 4 * W), a(tb, 0, 4 * W))
+        else:
+            for j in range(2):
+                mms([(a(tb, W * j + m, W * j + W, 32, 8, 32 * g4), a("YY", 32 * m, 32 * m + 32),
+                      a("IB", 64 * j + 16 * g4, 64 * j + 16 * g4 + 16), True, True) for g4 in range(4) for m in range(8)])
+            ec(a("TT", 0, 2 * W), a(tb, 0, 2 * W))
+            es(a("TT", 2 * W, 4 * W), a("TT", 0, 2 * W), 64.0 ** -16)
+        sums, again = a(cb, 0, n, W), a(tb, 0, n, W)
+        mms([(x, one(W), row(13, n) if off else nil(n, 1), True, False) for x in ((sums, again) if TWICE else (sums,))])
+        for k in range(8):
+            o, x, hi = a("TH", 512 * k, 512 * k + 4 * W), a("TT", 0, 4 * W), LOW * 64.0 ** (2 * k + 1)
+            op = issue(q, lambda q, o=o, x=x, hi=hi:
+                       g.vector.tensor_scalar(o[0], x[0], hi, hi, ALU.min, ALU.subtract) if q == "V" else
+                       g.scalar.activation(o[0], x[0], ACT.Relu, bias=hi, scale=-1.0),
+                       [x], [o], (CALL + CY * 4 * W, CALL + CY * 2 * W))
+            wt = lambda q, op=op, k=k: a("G4", 0, 64) if q else a("G4", 4 * k + 32 * (op["q"] == "V"), 4 * k + 32 * (op["q"] == "V") + 4)
+            for b in (cb, tb) if TWICE else (cb,):
+                mms([(a(b, off + k + 4 * gs * j, 4 * gs * (j + 1), W, gs), a("TH", 512 * k + W * j, 512 * k + W * j + W), wt,
+                      False, b == cb and k == 7 and j == 3) for j in range(4)])
+        es(a("P2", 1, 2 * n, W, 2), sums, 1.0 / 64, 128.25)
+        if TWICE:
+            more(again, a("N63", 0, W, W), a("P2", 1, 2 * n, W, 2), True)
+            es(a("P2", 0, 2 * n, W, 2), again, 1.0, 8192.0)
+        else:
+            es(a("UT", 0, n, W), a("P2", 1, 2 * n, W, 2), 63.0, -8192.0)
+            tt(a("P2", 0, 2 * n, W, 2), sums, a("UT", 0, n, W), ALU.subtract)
 
-    def turn(src, W):
-        eye = a("IB", 0, W, W)
-        mms([(a("B6", 0, 4 * W), one(128), row(13, 4 * W, 256 - 2 * W), True, False)] +
-            [(a("B6", W * j, W * j + W), a(src, 128 * (j % 2), 128 * (j % 2) + 128, W), eye, False, j == 3) for j in range(4)])
-        ec(a("TT", 0, 4 * W), a("B6", 0, 4 * W))
-
-    def w2b(bank, wide, c, rhs, open_):
+    def w2b(bank, wide, c, rhs, close):
         mms([(a(bank, s, 256, 32, 32, 32 * c), a(wide[0], wide[1] + 1024 * c + s, wide[1] + 1024 * c + 1024, st=32), rhs,
-              not open_, not open_) for s in range(32)])
+              False, close and s == 31) for s in range(32)])
 
     def rebuild(v):
         K = (KA, KB, KA)[v]
-        gather("BIG", K + 32, (a("WN", 0, 4096), a("BIG", KA, KB), a("BIG", KB, KEND))[v], "OK2", 4096)
+        gather("BIG", K + 32, (a("WN", 0, 4096), a("BIG", KA, KB), a("BIG", KB, KEND))[v], "OK2", 4096, RQ[v > 0], GR)
         ec(a("EV"), ind(a("BIG", K, K + 4128), a("OE")))
         cp(ind(a("BIG", 0, KA), a("OE")), a("EV"))
 
-    for q, items, move in (("Y", [(a("LB", 32 * k, 32 * k + 32), ext(T.bt[k, :])) for k in range(4)], 1.0),
-                           ("S", [(a("LB", 32 * k, 32 * k + 32), ext(T.bt[k, :])) for k in range(4, 8)], 1.0),
-                           ("Y", [(a("L2", 0, 192), ext(T.pt[:]))], 0.5),
-                           ("S", [(a("L3", 512, 768), ext(T.bk[:]))], 0.6),
-                           ("Y", [(a("L3", 256, 512), ext(T.bt[:]))], 0.6),
-                           ("S", [(a("L2", 192, 384), ext(T.pu[:]))], 0.5),
-                           ("Y", [(a("TON", 0, 2048), ext(T.tones[:, 0:2048]))], 1.8),
-                           ("S", [(a("TON", 2048, 4096), ext(T.tones[:, 2048:4096]))], 1.8),
-                           ("Y", [(a("LS", 0, 128, 8), ext(T.bl[:])), (a("LS", 128, 129, 8), ext(T.pn[:]))], 0.1),
-                           ("S", [(a("LS", 129, 130, 8), ext(T.th[:])), (a("L3", 0, 256), ext(T.bu[:]))], 0.6)):
-        dmas(items, move, q=q)
+    loads = {"bt": ([(a("L3", 256, 512), ext(T.bt[:]))], 0.6), "pt": ([(a("L2", 0, 192), ext(T.pt[:]))], 0.5),
+             "bk": ([(a("L3", 512, 768), ext(T.bk[:]))], 0.6), "pu": ([(a("L2", 192, 384), ext(T.pu[:]))], 0.5),
+             "t0": ([(a("TON", 0, 2048), ext(T.tones[:, 0:2048]))], 1.8), "t1": ([(a("TON", 2048, 4096), ext(T.tones[:, 2048:4096]))], 1.8),
+             "bl": ([(a("LS", 0, 128, 8), ext(T.bl[:])), (a("LS", 128, 129, 8), ext(T.pn[:])), (a("LS", 129, 130, 8), ext(T.th[:]))], 0.1),
+             "l8": ([(a("LB", 0, 8), ext(T.bl[:]))], 0.25), "bu": ([(a("L3", 0, 256), ext(T.bu[:]))], 0.6)}
+    for k, n in enumerate(LOADS.split()):
+        tones_in = dmas(*loads[n], q="YS"[k % 2])
 
     ms(a("ZB", 0, 1024), 0.0)
     ms(a("ON"), 1.0)
     ms(a("ONF"), 1.0)
     ms(a("PT"), 0.0)
-    ms(a("BIG", 0, KA), 99.0)
+    if FILL:
+        ms(a("SC", 0, KA // 4), 99.0)
+    else:
+        ms(a("BIG", 0, KA), 99.0)
     lazy[0] = True
-    clear(True)
     diag = [[1, 128]]
     sel(a("IF"), a("ONF", 0, 128), [[-1, 128]], ALU.is_equal, 0, 1)
     put(a("IB"), nil(128), diag, 0, 1.0)
     for n, v in (("NI", -1.0), ("PS", 16384.0), ("P32", 32768.0), ("EA", float(KA)), ("EB", float(KB)),
-                 ("NS", -16384.0), ("NB", -float(2 ** 25))):
+                 ("NS", -16384.0), ("NB", -float(2 ** 25)), ("IS", 64.0 ** -16), ("N63", -63.0), ("I16", 16.0),
+                 ("P19", float(2 ** 19)), ("IL", LOW / 2)):
         es(a(n), a("IB"), v)
     sel(a("I3"), a("IB"), [[0, 8], [-1, 16]], ALU.is_ge, 2, 0)
-    io(a("SI"), [[0, 8], [1, 32]])
     sel(a("SG"), a("ON"), [[0, 8], [1, 32]], ALU.is_gt, 0, 0)
-    io(a("KS"), [[2, 32]], -1)
-    sel(a("E8", 0, 256, 8), a("ONF", p=8), [[1, 8], [0, 32]], ALU.is_equal, 0, -1)
-    put(a("E8", 256, 512, 8), nil(256, 8), [[1, 8], [0, 32]], 0, -1.0)
-    io(a("G4", 0, 8), [[-8, 2], [0, 4]], 16)
-    io(a("G4", 8, 16), [[-1, 2], [0, 4]], 2)
-    band(a("G4", 0, 16), a("G4", 16, 32), a("G4", 0, 16), [[0, 4], [32, 4]], 0, 30)
+    sel(a("CAP"), nil(256), [[0, 8], [1, 32]], ALU.is_equal, 0, 0, float(2 ** 99))
+    sel(a("CAP"), a("CAP"), [[0, 8], [1, 32]], ALU.is_gt, 0, 0, LOW)
+    put(a("E8", p=8), nil(256, 8), [[1, 8], [0, 32]], 0, -1.0)
+    sel(a("G4", 64, 96), a("ON", 0, 32), [[0, 8], [1, 4]], ALU.is_gt, 0, 0, 64.0 ** -2)
+    ms(col(11), 64.0 ** 2 / LOW / 2 ** 20)
+    scan(a("G4", 96, 128), a("G4", 64, 96), a("ON", 0, 32), col(11), ALU.mult, ALU.mult)
+    band(a("G4", 96, 128), a("G4", 128, 160), a("G4", 96, 128), [[0, 8], [32, 4]], 0, 30)
+    es(a("G4", 0, 32), a("G4", 96, 128), float(2 ** 20))
+    es(a("G4", 32, 64), a("G4", 96, 128), -float(2 ** 20))
     grp = [[16, 8]]
-    band(a("G8F", 0, 8), a("G8F", 8, 16), a("ONF", 0, 8), grp, 0, 15)
     band(a("G8", 0, 8), a("G8", 8, 16), a("ON", 0, 8), grp, 0, 15)
     sel(a("G8T", 0, 128, 8), a("ONF", 0, 128, 8), [[1, 8], [0, 16]], ALU.is_equal, 0, -1)
     sel(a("G8T", 128, 256, 8), a("ONF", 0, 128, 8), [[1, 128]], ALU.is_equal, -2, -16)
-    for lo, hi, r, s in ((0, 24, 0, 1), (24, 40, 2, 0), (40, 80, 3, 0)):
+    ec(a("SL2", 40, 64), nil(24))
+    for lo, hi, r, s in ((0, 24, 0, 1), (24, 40, 2, 0), (64, 128, 3, 0)):
         put(a("SL2", lo, hi), nil(hi - lo), [[s, (hi - lo) // 8], [16, 8]], r, 1.0)
     io(a("CC1"), [[1, 128]], 1)
     io(a("RR"), [[0, 8], [1, 16]])
     io(row(1), [[0, 256]], -16384)
     io(a("ROW", 256 + 31, 512, 1, 32), [[0, 8]], 32768)
     io(row(2), [[0, 256]], -6 * 64)
-    io(row(13, 512), [[-16, 2], [0, 256]])
+    io(row(13), [[0, 16], [-1984, 2], [0, 8]], 1984)
     es(a("G8B", 0, 8), a("G8", 0, 8), float(2 ** 25))
     io(row(3), [[0, 8], [-1, 32]], 31)
-    io(row(4, 192), [[64, 96], [0, 2]])
+    io(row(4, 96), [[-1, 96]], -129)
     io(row(5), [[0, 128], [16, 2]])
     io(row(6), [[0, 128], [-16, 2]])
     io(row(7), [[16, 256]])
@@ -373,20 +491,21 @@ def rank_program(g, core, T, topo):
     for k in range(2):
         sel(row(12, 96, 128 * k), nil(96, 1), [[0, 6], [1 - 2 * k, 2], [0, 8]], ALU.is_equal, k, 0, float(2 ** 99))
     io(a("ROF", 0, 256, 1), [[1, 16], [512, 8], [0, 2]])
-    io(a("ROF", 256, 268, 1), [[A2 + 1, 2], [32, 6]], 31)
+    io(a("ROF", 256, 268, 1), [[1, 2], [32, 6]], 31)
     sel(a("ROF", 272, 528, 1), a("ONF", p=1), [[-1, 2], [0, 8], [1, 16]], ALU.is_equal, 0, 0)
     io(a("ROF", 528, 656, 1), [[1, 64], [0, 2]])
     io(a("ROF", 656, 784, 1), [[0, 64], [32, 2]])
     io(a("ROF", 784, 912, 1), [[0, 8], [192, 16]])
     sel(a("M6", 0, 128), a("ON", 0, 128), [[0, 8], [6, 16]], ALU.is_gt, 0, -1)
-    band(a("M6", 128, 384), a("M6", 384, 640), a("ON"), [[0, 16], [6, 16]], 0, 5)
+    band(a("M6", 128, 384), a("PB"), a("ON"), [[0, 16], [6, 16]], 0, 5)
     put(a("PM"), nil(96), [[1, 6], [6, 16]], 0, 1.0)
     put(a("PMT"), nil(96), [[1, 16], [16, 6]], 0, 1.0)
     sel(a("T12", 0, 12), a("ON", 0, 12), [[16, 2], [16, 6]], ALU.is_gt, 0, -1)
     io(a("T12", 12, 24), [[0, 12]], -1)
     band(a("T12", 12, 24), a("T12", 24, 36), a("T12", 12, 24), [[0, 2], [16, 6]], 0, 15)
     mm(a("B4", 0, 24, 96), a("PMT", p=96), a("T12", 0, 24, 96))
-    ec(a("R6", p=96), a("B4", 0, 24, 96))
+    ec(a("R6", 0, 24, 96), a("B4", 0, 24, 96))
+    es(a("R6", 24, 30, 96), a("B4", 12, 18, 96), -1.0)
     five = ("MS", "MU", "MT", "MP", "WB")
     ec((T.CB[:, POOL["MS"][1]:POOL["MS"][1] + 816], [a(n)[1][0] for n in five], 816, False), nil(816))
     for n in ("TBW", "SM", "SQ"):
@@ -396,14 +515,32 @@ def rank_program(g, core, T, topo):
         for x in (a(n, 15, 143, st=16), a("MP", o, o + 64, st=8)):
             put(x, nil(8), grp, r, 1.0)
             put(x, x, grp, r + 1, 1.0)
-    for k, rows in enumerate((((14, -1.0), (15, 32.0)), ((0, 64.0), (1, 1.0)), ((2, 1.0),))):
+    for k, rows in ((2, ((0, 64.0), (1, 1.0))), (3, ((2, 1.0),))):
         x = a("SQ3", 128 * k, 128 * k + 128)
         for j, (r, v) in enumerate(rows):
             put(x, x if j else nil(128), [[16, 8], [0, 16]], r, v)
+    for h in range(2):
+        x = a("SQ3", 128 * h, 128 * h + 128)
+        io(x, [[0, 8], [1, 16]], 16 * h + 128)
+        sel(x, x, [[-16, 8], [0, 16]], ALU.is_equal, -14, 1)
+        put(x, x, [[16, 8], [0, 16]], 15, 32.0)
+        put(x, x, [[32, 4], [-16, 2], [0, 16]], 30, 159.0)
     ms(a("TBW", 0, 1), float(2 ** 98))
     for n in ("NB0", "NE"):
         ec(a(n, 0, 16), nil(16))
-    ec(a("NQ", 0, 257, st=256), nil(2))
+    put(a("DF", 128, 256), a("IF"), diag, -1, -1.0)
+    ec(a("DF", 128, 256, st=16), a("IF", 0, 128, st=16))
+    ec(a("DF", 0, 128), a("DF", 128, 256))
+    ec(a("DF", 0, 128, st=16), nil(8))
+    ec(a("DF", 256, 384), nil(128))
+    put(a("DF", 256, 384, st=16), nil(8), grp, 15, -1.0)
+    put(a("MN", 0, 288), nil(288), [[16, 9], [1000, 2], [1, 16]], -1000, 1.0)
+    es(a("MN", 288, 576), a("MN", 0, 288), 63.0)
+    es(a("MN", 576, 864), a("MN", 0, 288), 16384.0)
+    io(row(16), [[0, 8], [1, 32]], -159)
+    io(row(17), [[0, 8], [1, 32]], 64)
+    ec(row(14), nil(256, 1))
+    ec(row(15), a("SG", p=1))
     for o in (KA, KB):
         ec(a("BIG", o, o + 32), nil(32))
     for n in ("SD0", "SD1"):
@@ -412,8 +549,6 @@ def rank_program(g, core, T, topo):
     io(a("CI", 0, 1), [[0, 1]], 0, 1)
     ts(a("CI", 1, 2), a("CI", 0, 1), 15, ALU.bitwise_and)
     cp(col(0), a("CI", 1, 2))
-    io(col(1), [[0, 1]], 32, 32)
-    io(col(2), [[0, 1]], -129, -1)
     ts(a("MI"), a("RR"), col(0), ALU.is_equal)
     io(a("JO", 0, 192), [[16, 96], [0, 2]], 1)
     io(a("JO", 192, 384), [[0, 96], [1, 2]], -1)
@@ -430,24 +565,27 @@ def rank_program(g, core, T, topo):
     es(a("WB", 115, 116), col(3), 1.0)
     io(a("BCF", 0, 32), [[1, 32]])
     io(a("BCF", 32, 48), [[0, 2], [1, 8]], 16)
-    io(a("BCF", 80, 104), [[0, 24]], 7)
+    io(a("BCF", 80, 104), [[0, 24]], 8)
     for o, picks in ((80, ((16, 0, 0), (16, 1, 8))), (88, ((16, 0, 0), (16, 1, 8), (18, 2, 24), (18, 3, 32))),
                      (96, ((16, 0, 0), (16, 1, 8), (16, 2, 16), (16, 14, 40), (16, 15, 48)))):
         for s, r, v in picks:
-            put(a("BCF", o, o + 8), a("BCF", o, o + 8), [[s, 8]], r, v - 49.0)
+            put(a("BCF", o, o + 8), a("BCF", o, o + 8), [[s, 8]], r, v - 56.0)
         red(col(5 + (o - 80) // 8), a("BCF", o, o + 8))
     es(a("BCF", 48, 56), a("BCF", 0, 8), 1.0, col(5))
     es(a("BCF", 56, 64), a("BCF", 0, 8), 1.0, col(6))
-    io(a("BCF", 64, 76), [[0, 12]], 56)
+    io(a("BCF", 64, 76), [[0, 12]], 64)
     for o in range(2):
         es(a("BCF", 64 + 2 * o, 76, st=3), a("BCF", o, 8, st=2), 1.0, col(7))
+    io(a("BCF", 112, 128), [[1, 8], [0, 2]])
     cp(a("BC", 0, 16), a("BCF", 0, 16))
     cp(a("BC", 16, 76), a("BCF", 16, 76))
+    cp(a("BC", 80, 96), a("BCF", 112, 128))
 
     lazy[0] = False
-    tt(a("NB0", 1, 256), a("LB", 1, 256), a("LB", 0, 255), ALU.not_equal)
-    scan(a("HC"), a("NB0", 0, 256), a("SG"), 0.0, ALU.add, ALU.mult)
-    turn("HC", 128)
+    tt(a("NB0", 1, 256), a("L3", 257, 512), a("L3", 256, 511), ALU.not_equal)
+    es(a("FY"), a("NB0", 0, 256), 63.0, 1.0)
+    scan(a("YY"), a("FY"), a("CAP"), LOW, ALU.mult, ALU.min)
+    count(128, 8, "B6", "B3")
     ts(a("ST", 1024, 1280), a("L3", 512, 768), 1.0, ALU.add, 32.0, ALU.mult)
     lazy[0] = True
     io(a("ST", 1280, 1536), [[1, 4], [0, 64]])
@@ -455,16 +593,21 @@ def rank_program(g, core, T, topo):
     es(col(10), col(0), 256.0)
     es(a("ST", 1280, 1536), a("ST", 1280, 1536), 64.0, col(10))
     lazy[0] = False
-    dmas([(a("PT", p0=r, ps=16), a("ST", c, c + 256)) for r, c in ((0, 1024), (2, 1280), (3, 1536))], 0.9)
+    last = dmas([(a("PT", p0=r, ps=16), a("ST", c, c + 256)) for r, c in ((0, 1024), (2, 1280), (3, 1536))], 1.2)
+    for items, move in (([(a("BIG", l, l + KA // 4), a("SC", 0, KA // 4)) for l in range(0, KA if FILL else 0, KA // 4)], 4.0),
+                        ([(a("A", o + l, o + l + 1024), a("ZB")) for o in (AV[0], AV[0] + A2) for l in range(0, 3072, 1024)], 6.0)):
+        if items:
+            ops[dmas(items, move)]["behind"].add(last)
+            last = len(ops) - 1
     for l in range(2):
         for c in range(3):
             cp(a("IN0", 128 * c + 8 + 64 * l, 128 * c + 72 + 64 * l), a("L2", 192 * l + 64 * c, 192 * l + 64 * c + 64))
     cp(a("OB"), a("L3", 256, 512))
-    count(128, "B3", 0, "E")
-    ec(a("P2"), a("B3", 0, 256))
     mm(a("B7", 0, 256), a("ONF", 0, 128, 1), a("ROF", 0, 256, 1), True, False)
-    mms([(a("B7", h, 256, st=2), a("P2", h, 256, st=2), a("IB"), False, h == 1) for h in range(2)])
-    ts(a("OK2"), a("B7", 0, 256), 248.0, ALU.add)
+    mms([(a("B7", h, 256, st=2), a("P2", 128 * h, 128 * h + 128), a("I16"), False, h == 1) for h in range(2)])
+    ts(a("OK2"), a("B7", 0, 256), -2048.0, ALU.add)
+    ms(a("P2", 512, 528), 159.0)
+    lazy[0] = True
     ec(a("HL2", 512, 1024), nil(512))
     cp(a("LF0"), a("L2", 192, 384))
     mms([(a("B5", 32 * gg + 16 * h, 32 * gg + 16 * h + 16, 96), lis("LF0", h), a("IF", 16 * gg, 16 * gg + 16), True, True)
@@ -481,20 +624,22 @@ def rank_program(g, core, T, topo):
     mm(a("B0", 300, 301), a("G8T", 0, 128, 8), a("LSF", 128, 129, 8))
     cp(a("IN0", 7, 8), a("B0", 300, 301))
     es(a("THL", p=8), a("ONF", 0, 96, 8), a("LSF", 129, 130, 8))
-    mm(a("B0", 0, 256), a("LSF", 0, 128, 8), a("E8", 0, 256, 8))
-    tt(a("OK"), a("B0", 0, 256), a("SI"), ALU.is_gt)
-    tt(a("FS"), a("OK"), a("NB0", 0, 256), ALU.mult)
+    acc(a("B0", 0, 256), [(one(128), row(17)), (a("NI"), a("FY"))])
+    ec(a("OK"), a("B0", 0, 256))
+    cp(a("LBF", 0, 8), a("LB"))
+    tt(a("FS"), ind(a("LBF", 0, 8), a("BC", 80, 96)), a("OK"), ALU.is_gt)
     scan(a("KK"), a("FS"), a("SG"), 0.0, ALU.add, ALU.mult)
-    es(a("SF", 0, 8), a("KK", 31, 256, st=32), 1.0, col(1))
-    tt(a("LP"), ind(a("SF", 0, 8), a("BC", 0, 8)), a("MI"), ALU.mult)
-    mm(a("B6", 0, 8), a("LP"), a("G8F", 0, 8))
-    cp(a("OE"), a("B6", 0, 8))
+    io(a("LBF", 8, 16), [[32, 8]], 32)
+    es(a("LBF", 8, 16), a("LBF", 8, 16), 1.0, col(10))
+    tt(a("LBF", 16, 24), a("KK", 31, 256, st=32), a("LBF", 8, 16), ALU.add)
+    cp(a("OE"), a("LBF", 16, 24))
     es(a("LSF", 136, 264, 8), a("LSF", 0, 128, 8), 1.0, -1.0)
     acc(a("B7", 0, 128), [(a("G8T", 128, 256, 8), a("LSF", 136, 264, 8)), (a("ROF", 272, 400, 1), a("ROF", 528, 656, 1)),
                           (a("ROF", 400, 528, 1), a("ROF", 656, 784, 1))])
     ec(a("TB"), a("B7", 0, 128))
-    cp(a("ST", 0, 512), a("L3", 0, 512))
-    tt(a("ST", 512, 1024), a("L3", 0, 512), a("ST", 0, 512), ALU.subtract)
+    for l in range(0, 512, 128):
+        cp(a("ST", l, l + 128), a("L3", l, l + 128))
+        tt(a("ST", 512 + l, 640 + l), a("L3", l, l + 128), a("ST", l, l + 128), ALU.subtract)
     lazy[0] = False
 
     def upper_rows(v):
@@ -505,12 +650,14 @@ def rank_program(g, core, T, topo):
             dmas([(a("WN", 4096 + 3072 * v, 7168 + 3072 * v, p0=r, ps=16), a("SR%d" % v, p=64, p0=64 * r)) for r in range(2)], 0.5)
 
     rid, pid, _ = topo.addr(nxt)
-    sent = [0]
+    sent, calls = [0], []
 
     def remote(dst, src, sem, move):
         sent[0] += len(topo.engines(core, nxt))
         issue("G", lambda q: g.remote_dma(dst[0], src[0], T.sem[sem], T.sem["sent"], pid, rid, topo.mask(core, nxt)),
-              [src], [dst], RCALL + (2.0 if sem == "r0" else 0.0), RDMA - RCALL + move, 0.0, (sem, len(topo.engines(prv, core))))
+              [src], [dst], RCALL + (2.0 if sem == "r0" else 0.0), RDMA - RCALL, move, (sem, len(topo.engines(prv, core))))
+        ops[-1]["behind"].update(calls[-1:])
+        calls.append(len(ops) - 1)
 
     for v in range(3):
         IN, SD, SR = "IN%d" % v, "SD%d" % v, "SR%d" % v
@@ -519,7 +666,7 @@ def rank_program(g, core, T, topo):
         XC = (XA, XB, XA)[v]
         CW, PR, SC = ("WN", R), ("PR", 0), ("SC", 0)
         wd = lambda n, lo, hi: a(n[0], n[1] + lo, n[1] + hi)
-        XR = ("XR", 0)
+        XR = ("BIG", XC)
         nb = col(8)
         names_of = lambda up, lo, hi: a(IN, 8 + 64 * (up + lo // 1024) + lo // 16, 8 + 64 * (up + lo // 1024) + hi // 16)
         cont, new = a("NE", 0, 256, 96), a("NQ", 0, 256, 96)
@@ -529,7 +676,6 @@ def rank_program(g, core, T, topo):
             at = lambda n, lo, hi, st=1: a(n, lo, hi, p, st, p0)
             eye = lambda n: at(n, p0, p0 + p)
             out = lambda h: a("B4", 2 * p0 + p * h, 2 * p0 + p * h + p)
-            more(at("B0", 0, 256), eye("PS"), at("NQ", 1, 257), True)
             mm(a("B4", 2 * p0, 2 * (p0 + p)), a("ON", 0, 128, 1, p0=p0), a("ZB", 0, 2 * p, 1, p0=p0), True, False)
             ts(at("NE", 1, 257), at("B0", 0, 256), 0.0, ALU.is_lt)
             more(at("B1", 0, 256), eye("NS"), at("NE", 0, 256), True)
@@ -541,14 +687,27 @@ def rank_program(g, core, T, topo):
             cp(a("OD", 2 * p0, 2 * (p0 + p)), a("B4", 2 * p0, 2 * (p0 + p)))
 
         def changes(p0, p):
-            ec(a("UT", p=p, p0=p0), a("B2", 0, 256, p, p0=p0))
-            tt(a("NQ", 1, 256, p, p0=p0), a("B2", 1, 256, p, p0=p0), a("UT", 0, 255, p, p0=p0), ALU.not_equal)
+            lo, hi = 2 * p0, 2 * (p0 + p)
+            for l in range(lo, hi, 64):
+                cp(a("LT", l, l + 64), names_of(0, 16 * l, 16 * l + 1024))
+            mms([(a("B3", lo, hi, st=2), a("DF", 0, 128), a("LT", lo, hi, st=2), True, True),
+                 (a("B3", lo + 1, hi, st=2), a("DF", 128, 256), a("LT", lo + 1, hi, st=2), True, False),
+                 (a("B3", lo + 1, hi, st=2), a("DF", 256, 384), a("LT", lo, hi, st=2), False, True)])
+            ts(a("NL", lo, hi), a("B3", lo, hi), 0.0, ALU.not_equal)
+            turned = lambda bank, o, k, sh, last: [(a(bank, o, o + 256, p, p0=p0), a("NL", lo + h, hi, st=2),
+                                                    a("MN", 288 * k + 16 - 16 * h + sh, 288 * k + 272 - 16 * h + sh), False, last and h == 1)
+                                                   for h in range(2)]
+            mms(turned("B0", 0, 2, 1, False))
+            both_ = 512 if v < 2 else 256
+            mms([(a("B2", 0, both_, p, p0=p0), a("ON", 0, p, 1), a("ROW", 256 * 14, 256 * 14 + both_, 1), True, False)] +
+                turned("B2", 0, 0, 0, v == 2) + (turned("B2", 256, 1, 0, True) if v < 2 else []))
+            ec(a("NQ", 0, both_, p, p0=p0), a("B2", 0, both_, p, p0=p0), "S")
 
         def differ(c):
-            p0, p = PARTS[c // 2]
+            p0, p = [x for x in PARTS if x[0] <= 32 * c][-1]
             for h in range(2):
                 l, o = 1024 * c + 512 * h, p0 + p * h + 32 * c
-                key, own = ind(a("BIG", 0, K + 4128), a("OD", o, o + 32)), a("XR", 1024 * c + h, 1024 * c + 1024, st=2)
+                key, own = ind(a("BIG", 0, K + 4128), a("OD", o, o + 32)), a("BIG", XC + 1024 * c + h, XC + 1024 * c + 1024, st=2)
                 bank = AID[v].get(2 * c + h)
                 if bank:
                     ec(wd(SC, l, l + 512), key, "S")
@@ -562,63 +721,47 @@ def rank_program(g, core, T, topo):
         ts(nb, a(IN, 7, 8), -1.0, ALU.mult)
         relu(a("N12"), a("JO", 0, 192), 1.0, nb)
         if v == 0:
-            gather("WN", 0, a("TON"), "OB", 4096)
+            lazy[0] = True
+            gather("WN", 0, a("TON"), "OB", 4096, RQ[0], GR)
             rebuild(0)
-            dmas([(a("WN", 0, 4096, p0=r, ps=16), a("ST", c, c + 256)) for r, c in ((0, 0), (1, 512), (2, 256), (3, 768))], 1.2)
-        mms([(s0, a("THL", p=8), a("E8", 256, 512, 8), True, False), (s0, one(96), row(1), False, False)])
+            dmas([(a("WN", 0, 4096, p0=r, ps=16), a("ST", c, c + 256)) for r, c in ((0, 0), (1, 512), (2, 256), (3, 768))], 1.6)
+            lazy[0] = False
+        mms([(s0, a("THL", p=8), a("E8", p=8), True, False), (s0, one(96), row(1), False, False)])
         mms([(bar("B0", h), lis("N12", 1 - h), a("SH32" if h else "P32"), False, False) for h in range(2)])
         mm(s1, one(96), nil(256, 1), True, False)
         mm(s5, row(8, 96, 128), row(2), True, False)
-        for c in range(3):
-            pieces = range(1024 * c, 1024 * c + 1024, GP)
-
-            def tones():
+        for p0, p in PARTS:
+            thirds = range(p0 // 32, (p0 + p) // 32)
+            changes(p0, p)
+            for c in thirds:
+                pieces = range(1024 * c, 1024 * c + 1024, GP)
                 for l in pieces:
-                    ec(wd(XR, l, l + GP), ind(a("TON"), names_of(0, l, l + GP)), "SESESS"[l // GP])
+                    ec(wd(XR, l, l + GP), ind(a("TON"), names_of(0, l, l + GP)), XQ[l // GP])
                 for l in pieces:
                     tt(wd(PR, l, l + GP), ind(a("TON"), names_of(1, l, l + GP)), wd(XR, l, l + GP), ALU.mult)
-
-            if c < 2:
-                tones()
-            else:
-                slots(*PARTS[0])
-            for l in pieces:
-                ec(wd(CW, l, l + GP), ind(a("PT"), names_of(0, l, l + GP)), "S")
-            w2b("B2", CW, c, a("MT", 15, 143, st=16), False)
-            if c:
-                changes(*PARTS[c - 1])
-            if c == 2:
-                if v < 2:
-                    scan(a("GG", p=96), new, a("SG", p=96), 0.0, ALU.add, ALU.mult)
-                    turn("GG", 96)
-                tones()
-            w2b("B1", CW, c, a("SL2", 0, 8), True)
-            w2b("B0", PR, c, a("G8", 0, 8), True)
+                w2b("B0", PR, c, a("G8", 0, 8), True)
+            for c in thirds:
+                for l in range(1024 * c, 1024 * c + 1024, GW):
+                    ec(wd(CW, l, l + GW), ind(a("PT"), names_of(0, l, l + GW)), WQ[l // GW])
+                w2b("B1", CW, c, a("SL2", 0, 8), False)
+            slots(p0, p)
+        lazy[0] = True
         upper_rows(v)
-        slots(*PARTS[1])
+        lazy[0] = False
         differ(0)
         lazy[0] = True
-        if v < 2:
-            count(96, "B7", 8, "S")
-            mm(a("B6", 0, 192), one(128), row(4, 192), True, False)
-            lazy[0] = False
-            ec(a("P2", p=96), a("B7", 0, 256, 96), "S")
-            mms([(lis("B6", h), bar("P2", h), i96, False, h == 1) for h in range(2)])
-            ts(a("OX"), a("B6", 0, 192), 0.5, ALU.mult, 15.5, ALU.add)
-            lazy[0] = True
-            gather("BIG", XC, a("XR"), "OX", 3072, "S")
         scan(a("LN", p=96), a("ON", p=96), cont, 0.0, ALU.add, ALU.mult)
         mms([(s3, row(8, 96, 128), row(3), True, False)] +
             [(bar("B3", h), lis("N12", h), a("NB"), False, False) for h in range(2)])
-        for l, r in (([(s96("PS"), a("GG", p=96)), (s96("NS"), a("KK", p=96))] if v < 2 else []) +
-                     [(s96("NB"), a("NE", 1, 257, 96)), (i96, a("CK", p=96))]):
+        for l, r in ((s96("NB"), a("NE", 1, 257, 96)), (i96, a("CK", p=96)), (s96("P19"), a("LN", p=96))):
             more(s3, l, r)
         more(s3, i96, a("LN", p=96), True)
         d0 = lambda lo, hi: a("B0", lo, hi, 96)
         mm(a("B4", 0, 128), a("I3"), a("TB"), True, False)
-        mms([(d0(0, 80), one(96), nil(80, 1), True, False), (d0(0, 8), row(10 + v // 2, 96, 128 * (v % 2)), one(8), False, False),
-             (d0(8, 16), row(11, 96, 128), one(8), False, False), (d0(64, 72), row(12, 96), one(8), False, False),
-             (d0(72, 80), row(12, 96, 128), one(8), False, False)])
+        mms([(d0(0, 128), one(96), nil(128, 1), True, False), (d0(0, 8), row(10 + v // 2, 96, 128 * (v % 2)), one(8), False, False),
+             (d0(8, 16), row(11, 96, 128), one(8), False, False), (d0(88, 96), row(12, 96), one(8), False, False),
+             (d0(96, 104), row(12, 96, 128), one(8), False, False), (d0(40, 48), one(96), one(8), False, False),
+             (d0(48, 56), row(4, 96), one(8), False, False)])
         acc(a("B2", 0, 12), [(a("ONF", 0, 128, 1), a("ROF", 256, 268, 1)), (a("ROF", 784, 912, 1), a("ONF", 0, 12, 1))], False)
         lazy[0] = False
         differ(1)
@@ -629,6 +772,15 @@ def rank_program(g, core, T, topo):
         cp(mi(32), a("MX", 31, 256, 96, 32))
         ts(mi(0), mi(32), 5, ALU.arith_shift_right, 255, ALU.bitwise_and)
         cp(sm(0), mi(0))
+        if v < 2:
+            es(sm(32), a("MX", 31, 256, 96, 32), 2.0 ** -19, 128.0, "S")
+            ec(a("RM", 0, 256), ind(a("SM", 32, 48), a("BC", 80, 96)), "S")
+            acc(a("B7", 0, 256, 96), [(one(96), row(16)), (i96, a("RM", 0, 256, 96))])
+            issue("S", lambda q: g.scalar.activation(T.RM[0:96, 256:512], T.B7[0:96, 0:256], ACT.Sign, bias=0.5, scale=1.0),
+                  [a("B7", 0, 256)], [a("RM", 256, 512)], CALL + CY * 256)
+            acc(a("B7", 256, 512, 96), [(s96("IL"), a("ON", p=96)), (s96("IL"), a("RM", 256, 512, 96))])
+            scan(a("YY", p=96), a("NQ", 256, 512, 96), a("B7", 256, 512, 96), 0.0, ALU.mult, ALU.max)
+            count(96, 16, "B7", "B6", CQ)
         tt(a("LC", 0, 128), ind(a("SM", 0, 8), a("BC", 0, 8)), a("MI"), ALU.mult)
         mm(a("B1", 0, 6), a("LC", 0, 128, 96), a("G8", 0, 6, 96))
         for gg in range(8):
@@ -638,18 +790,16 @@ def rank_program(g, core, T, topo):
         ec(a("TBW", 1, 129), a("B4", 0, 128))
         ts(mi(8), mi(32), 19, ALU.arith_shift_right)
         ts(mi(16), mi(32), 31, ALU.bitwise_and)
-        if v < 2:
-            ts(mi(24), mi(32), 14, ALU.arith_shift_right, 31, ALU.bitwise_and)
-        cp(sm(8, 24 if v < 2 else 16), mi(8, 24 if v < 2 else 16))
-        mms([(d0(8, 16), i96, sm(8), False, False), (d0(8, 16), i96, sm(16), False, False)] +
+        cp(sm(8, 16), mi(8, 16))
+        mms([(d0(c, c + 8), i96, sm(k), False, False) for c, k in ((8, 8), (48, 0))] +
             [(d0(c, c + 8), s96("NI"), sm(16), False, False) for c in (16, 24, 32)])
         ec(a("GT"), ind(a("TBW"), a("OC", 0, 6)))
-        more(d0(0, 80), a("GT"), a("SL2"), True)
+        more(d0(0, 128), a("GT"), a("SL2"), True)
         tt(a("LC", 128, 384), ind(a("SM", 0, 32), a("BC", 8, 24)), a("M6", 128, 384), ALU.mult)
         mms([(a("B2", 0, 12), a("LC", 128, 256, 96), a("R6", 12, 24, 96), False, False),
-             (a("B2", 0, 6), a("LC", 256, 384, 96), a("R6", 12, 18, 96), False, False)])
-        ts(a("TK", p=96), d0(40, 80), col(4, 96), ALU.is_lt)
-        tt(a("SQ", 0, 40, 96), d0(0, 40), a("TK", p=96), ALU.mult)
+             (a("B2", 6, 12), a("LC", 256, 384, 96), a("R6", 24, 30, 96), False, False)])
+        ts(a("TK", p=96), d0(64, 128), col(4, 96), ALU.is_lt)
+        tt(a("SQ", 0, 64, 96), d0(0, 64), a("TK", p=96), ALU.mult)
         tt(a("PB"), ind(a("SQ", 0, 24), a("BC", 32, 48)), a("M6", 0, 256), ALU.mult)
         ec(a("QQ", 0, 128), ind(a("SQ"), a("BC", 48, 56)))
         es(a("QQ", 128, 256), ind(a("SQ"), a("BC", 56, 64)), -1.0)
@@ -658,7 +808,8 @@ def rank_program(g, core, T, topo):
         mms([(a("B5", 96 * k, 96 * k + 96), a("QQ", 128 * k, 128 * k + 128, 96), a("PM", p=96), True, True) for k in range(2)])
         cp(a("OP", 0, 12), a("B2", 0, 12))
         ec(a("QV"), a("B5", 0, 192))
-        cp(ind(a("A"), a("OP", 0, 12)), a("QV"))
+        for k in range(2):
+            cp(ind(a("A", AV[v] + A2 * k, AV[v] + A2 * k + 6144), a("OP", 6 * k, 6 * k + 6)), a("QV", 96 * k, 96 * k + 96))
         mm(a("B3", 0, 1, 8), a("SQ", 16, 24, 96), a("ON", 0, 1, 96))
         ec(a("SF", 8, 9, 8), a("B3", 0, 1, 8))
         mm(a("B3", 2, 3), a("G8T", 0, 128, 8), a("SF", 8, 9, 8))
@@ -669,45 +820,59 @@ def rank_program(g, core, T, topo):
             relu(a("NV", 0, 192), a("JO", 384, 576), 1.0, col(9))
 
         def table():
-            if v < 2:
-                es(sm(32), sm(0), 1.0, col(2, 96))
-                tt(a("SQ", 40, 56, 96), sm(24, 16), a("TK", 0, 16, 96), ALU.mult)
             es(a("Z3"), ind(a("SQ"), a("BC", 64, 76)), -1.0)
             mms([(a("B3", 128, 256), a("I3"), a("TB"), True, False)] +
                 [(a("B3", 128, 256, 32, p0=32 * (gg // 2)), a("Z3", 48 * (gg // 2) + 16 * (gg % 2), 48 * (gg // 2) + 16 * (gg % 2) + 32, 96),
                   a("OH", 128 * gg, 128 * gg + 128, 96), False, gg % 2 == 1) for gg in range(8)])
             ec(a("TB"), a("B3", 128, 256))
-            pick = lambda bank, k, close: [(a(bank, h, 256, st=2), a("SQ3", 128 * k, 128 * k + 128), a("TB"), False, close and h == 1)
+            pick = lambda bank, k, close: [(a(bank, h, 256, st=2), a("SQ3", 128 * k(h), 128 * k(h) + 128), a("TB"), False, close and h == 1)
                                            for h in range(2)]
-            acc(a("B0", 0, 256), [(one(128), row(7 if v < 2 else 5)), (row(8, 128), one(256))], False)
             if v < 2:
-                mms(pick("B0", 0, True))
-                ts(a("OK2"), a("B0", 0, 256), 32.0, ALU.add, 7199.0, ALU.min)
+                for gg in range(8):
+                    es(a("OH2", 128 * gg, 128 * gg + 128, 96), a("OH", 128 * gg, 128 * gg + 128, 96), a("TK", gg, gg + 1, 96), q=OQ)
+                acc(a("B7", 0, 256), [(one(128), row(7)), (row(8, 128), one(256))], False)
+                mms(pick("B7", lambda h: h, False))
+                for h in range(2):
+                    first = lambda gg: 32 * (8 * h + gg) + 16 * (1 - gg % 2)
+                    mms([(a("B7", h, 256, 32, 2, 32 * (gg // 2)), a("P2", first(gg), first(gg) + 32, 96),
+                          a("OH2", 128 * gg, 128 * gg + 128, 96), False, h == 1 and gg % 2 == 1) for gg in range(8)])
+                ts(a("OK2"), a("B7", 0, 256), 32.0, ALU.add, 7199.0, ALU.min)
             else:
+                acc(a("B0", 0, 256), [(one(128), row(5)), (row(8, 128), one(256))], False)
                 acc(a("B4", 0, 256), [(one(128), row(6)), (row(8, 128), row(9))], False)
-                mms(pick("B4", 2, True))
-                mms(pick("B0", 1, False))
+                mms(pick("B4", lambda h: 3, True))
+                mms(pick("B0", lambda h: 2, False))
                 relu(a("OK"), a("B4", 0, 256), -1.0)
                 more(a("B0", 0, 256), a("PS"), a("OK"), True)
                 ts(a("OK2"), a("B0", 0, 256), float(ZC), ALU.min)
 
         if v == 2:
             table()
+        srcs = ("B0", "B1", "B4") if v < 2 else ("B6", "B7", "B1")
         for c in range(3):
-            scan(wd(SC, 1024 * c, 1024 * c + 1024), a("A", 1024 * c, 1024 * c + 1024), a("A", A2 + 1024 * c, A2 + 1024 * c + 1024),
+            o = AV[v] + 1024 * c
+            scan(wd(SC, 1024 * c, 1024 * c + 1024), a("A", o, o + 1024), a("A", A2 + o, A2 + o + 1024),
                  0.0 if c == 0 else wd(SC, 1024 * c - 1, 1024 * c), ALU.add, ALU.add)
-            bank = a(("B6", "B7", "B1")[c], 0, 64)
+            bank = a(srcs[c], 0, 64)
             acc(bank, [(one(128), row(7, 64, 64 * c)), (row(8, 128), one(64))], False)
             mms([(bank, a("MS", 15 - i, 143 - i), a(SC[0], SC[1] + 1024 * c + i, SC[1] + 1024 * c + 1024, st=16), False,
                   i == 15 and v < 2) for i in range(16)])
             if v == 2:
                 more(bank, a("PS"), a("NV", 64 * c, 64 * c + 64), True)
         for c in range(3):
-            ts(a("OS", 64 * c, 64 * c + 64), a(("B6", "B7", "B1")[c], 0, 64), float(R), ALU.add, float(top), ALU.min)
+            ts(a("OS", 64 * c, 64 * c + 64), a(srcs[c], 0, 64), float(R), ALU.add, float(top), ALU.min)
         if v < 2:
             ts(a(SD, 7, 8), a("B3", 2, 3), nb, ALU.subtract, 3072.0, ALU.min)
-            table()
-        gather("EW", 0, win, "OS", 3072)
+            if EARLY:
+                table()
+        if v == 2:
+            gather("TH", 0, win, "OK2", 4096, TQ)
+            for i in range(8):
+                mm(a("B2"), a("MP", 7 - i, 135 - i), a("TH", 512 * i, 512 * i + 512), i == 0, i == 7)
+            ec(a("ZO"), a("B2"))
+            dmas([(ext(T.zu[:]), a("ZO", p=64))], 0.5)
+            dmas([(ext(T.zt[:]), a("ZO", p=64, p0=64))], 0.5)
+        gather("EW", 0, win, "OS", 3072, EQ[v // 2])
         if v < 2:
             nx, SG_ = v + 1, "SG%d" % v
             for c in range(3):
@@ -716,11 +881,16 @@ def rank_program(g, core, T, topo):
                     acc(a(bank, o, o + 64), [(a(m, 15 - i, 143 - i), a("EW", 1024 * c + i, 1024 * c + 1024, st=16)) for i in range(16)])
                 cp(a(SD, 128 * c + 8, 128 * c + 136), a(bank, 0, 128))
                 lo = 128 * c + 8 if c else 0
-                remote(a("IN%d" % nx, lo, 128 * c + 136), a(SD, lo, 128 * c + 136), "r%d" % (5 * v + c), 0.4)
+                remote(a("IN%d" % nx, lo, 128 * c + 136), a(SD, lo, 128 * c + 136), "r%d" % (5 * v + c), 1.2)
             dmas([(a(SG_, p=64, p0=64 * r), a("EW", p0=r, ps=16)) for r in range(2)], 0.5, [len(ops) - 2])
-            remote(a("SR%d" % nx), a(SG_), "r%d" % (5 * v + 3), 0.8)
-            lazy[0] = True
-            clear(False, len(ops) - 1)
+            remote(a("SR%d" % nx), a(SG_), "r%d" % (5 * v + 3), 3.6)
+            for o in (AV[nx], AV[nx] + A2):
+                for l in range(o, o + 3072, 1024):
+                    io(a("A", l, l + 1024), [[0, 1024]])
+                    ops[-1]["behind"].add(calls[-1])
+            if not EARLY:
+                table()
+            lazy[0] = LZ
             rebuild(nx)
             lazy[0] = False
         else:
@@ -732,15 +902,11 @@ def rank_program(g, core, T, topo):
                 for lo in range(2):
                     ec(a("YO", 192 * lo + 64 * c, 192 * lo + 64 * c + 64), a(bank, 64 * lo, 64 * lo + 64))
             dmas([(ext(T.yu[:]), a("YO", p=64)), (ext(T.yt[:]), a("YO", p=64, p0=64))], 0.7)
-            gather("TH", 0, win, "OK2", 4096)
-            for i in range(8):
-                mm(a("B2"), a("MP", 7 - i, 135 - i), a("TH", 512 * i, 512 * i + 512), i == 0, i == 7)
-            ec(a("ZO"), a("B2"))
-            dmas([(ext(T.zu[:]), a("ZO", p=64))], 0.5)
-            dmas([(ext(T.zt[:]), a("ZO", p=64, p0=64))], 0.5, q="S")
+
 
     if not PLAN:
-        PLAN["order"], PLAN["on"] = arrange(ops)
+        PLAN["ops"] = ops
+        PLAN["order"], PLAN["on"] = settle(ops) if PASSES else arrange(ops)
     order = PLAN["order"]
     cnt, fin, seen = {}, {"sent": sent[0]}, {q: {} for q in Q}
     for k in order:

@@ -1,132 +1,73 @@
 import numpy as np
 from concourse.mybir import AluOpType as ALU, AxisListType as AX, ActivationFunctionType as ACT
 
-F, BF, I, U = "float32", "bfloat16", "int32", "uint16"
+F, BF, I, U, H = "float32", "bfloat16", "int32", "uint16", "float16"
 KA, XA, KB, XB, KEND = 4128, 8256, 11328, 15456, 18528
-ZC = 13312
-A2 = 12288
-AV = (6144, 3072, 0)
+AV = (768, 384, 0)
 GP = 512
 PARTS = ((0, 64), (64, 32))
+MAGIC = 1.5 * 2 ** 23
 CY, PC, GA, SCA, CALL, SAME, HAND, LDMA, RDMA, RCALL = 0.87e-3, 0.44e-3, 1.25e-3, 3.2e-3, 0.05, 0.11, 0.12, 2.0, 2.6, 0.55
-HOLD, LAG, DEPTH = 0.3, 0.7, 3
-RULE, SHARE, CQ, LZ = 0, 1.0, "S", False
-PASSES, LEAN, PHAND = 8, 0.0, 0.26
+PASSES, LEAN, PHAND, FIRST = 8, 0.0, 0.26, 2.0
 LOADS = "bt pt t0 t1 bk bl pu l8 bu"
-XQ, WQ, EQ, OQ, EARLY = "EEEEEE", "EEEEEE", ("E", "E"), "S", True
-RQ, TQ, FILL, TWICE, GR, GW = ("E", "E"), "E", True, False, 1024, 512
+XQ, WQ, OQ, CQ, RQ, GR, GW, LZ, AHEAD = "EEEEEE", "EEEEEE", "E", "E", ("E", "E"), 1024, 512, False, True
+WAIT = (0, 6, 6)
 ROUNDS, ALSO = 1200, ((1.0, (1.0, 1.3, 1.4, 1.0)), (1.0, (1.3, 1.3, 1.0, 1.2)), (1.0, (1.0, 1.0, 1.4, 1.6)))
 SB = {
-    "TON": ([128, 4096], BF), "PT": ([128, 4096], BF), "BIG": ([128, KEND], BF), "WN": ([128, ZC + 16], BF),
-    "PR": ([128, 3072], BF), "SC": ([128, 3072], BF),
-    "EW": ([128, 3072], BF), "A": ([128, 2 * A2], BF), "TH": ([128, 4096], BF),
+    "TON": ([128, 4096], BF), "PT": ([128, 4096], BF), "BIG": ([128, KEND], BF), "WN": ([128, 4096], BF),
+    "PR": ([128, 3072], BF), "SC": ([128, 3072], BF), "CW": ([128, 3072], BF), "TH": ([128, 4096], BF),
+    "W": ([128, 13344], F), "A": ([128, 1344], BF), "SE": ([128, 384], BF), "XM": ([128, 384], BF),
+    "G1": ([128, 384], F), "SN": ([128, 384], F), "YI": ([128, 1344], I), "HT": ([128, 384], H),
+    "LIN": ([128, 192], F), "LIB": ([128, 256], F), "HF": ([128, 48], F), "AD": ([128, 784], BF), "XL": ([128, 128], F),
+    "OX": ([128, 16], U), "CD": ([128, 256], F), "CA": ([128, 256], BF), "MY": ([128, 256], BF), "TRI": ([128, 192], BF),
     "IN0": ([128, 392], U), "IN1": ([128, 392], U), "IN2": ([128, 392], U), "SD0": ([128, 392], U), "SD1": ([128, 392], U),
-    "SG0": ([128, 384], BF), "SG1": ([128, 384], BF), "SR0": ([128, 1024], BF), "SR1": ([128, 384], BF), "SR2": ([128, 384], BF),
-    "NQ": ([128, 512], BF), "LT": ([128, 192], F), "NL": ([128, 192], BF), "DF": ([128, 384], F), "MN": ([128, 864], BF),
+    "NQ": ([128, 512], BF), "NL": ([128, 192], BF), "DF": ([128, 384], BF), "MN": ([128, 864], BF),
     "UT": ([128, 256], F), "ZB": ([128, 1024], BF),
     "L2": ([128, 384], I), "L3": ([128, 768], I), "LB": ([128, 8], I), "LBF": ([128, 32], F), "LS": ([128, 136], I), "LSF": ([128, 272], F),
-    "LF0": ([128, 192], F), "ST": ([128, 1792], BF), "HL2": ([128, 1024], BF),
-    "ON": ([128, 256], BF), "ONF": ([128, 256], F), "IF": ([128, 128], F),
-    "IB": ([128, 128], BF), "PS": ([128, 128], BF), "NS": ([128, 128], BF), "NB": ([128, 128], BF), "NI": ([128, 128], BF),
-    "P32": ([128, 128], BF), "EA": ([128, 128], BF), "EB": ([128, 128], BF), "I3": ([128, 128], BF),
+    "ST": ([128, 256], BF),
+    "ON": ([128, 256], BF), "ONF": ([128, 256], F),
+    "IB": ([128, 128], BF), "NS": ([128, 128], BF), "NB": ([128, 128], BF), "NI": ([128, 128], BF),
+    "P32": ([128, 128], BF), "EA": ([128, 128], BF), "EB": ([128, 128], BF), "I3": ([128, 128], BF), "I4K": ([128, 128], BF),
     "E8": ([128, 256], F), "SG": ([128, 256], BF),
-    "IS": ([128, 128], BF), "N63": ([128, 128], BF), "I16": ([128, 128], BF), "CAP": ([128, 256], BF), "IL": ([128, 128], BF),
+    "IS": ([128, 128], BF), "I16": ([128, 128], BF), "CAP": ([128, 256], BF), "IL": ([128, 128], BF),
     "FY": ([128, 256], BF), "RM": ([128, 512], BF), "YY": ([128, 256], BF),
     "G4": ([128, 160], BF), "G8": ([128, 16], BF), "G8T": ([128, 256], F),
-    "G8B": ([128, 16], BF), "ROW": ([128, 4608], BF), "ROF": ([128, 912], F), "JO": ([128, 576], F),
-    "COL": ([128, 16], F), "CI": ([128, 8], I), "BC": ([128, 96], U), "BCF": ([128, 128], F),
+    "G8B": ([128, 16], BF), "ROW": ([128, 5632], BF), "ROF": ([128, 1040], F), "JO": ([128, 384], F),
+    "COL": ([128, 16], F), "CI": ([128, 8], I), "BC": ([128, 144], U), "BCF": ([128, 176], F),
     "MI": ([128, 128], BF), "M6": ([128, 384], BF), "RR": ([128, 128], F),
-    "R6": ([128, 32], BF), "OH2": ([128, 1024], BF), "P19": ([128, 128], BF), "T12": ([128, 48], BF), "PM": ([128, 96], BF), "PMT": ([128, 96], BF), "CC1": ([128, 128], BF),
-    "SL2": ([128, 128], BF), "MS": ([128, 144], BF), "MU": ([128, 144], BF), "MT": ([128, 144], BF), "MP": ([128, 144], BF),
-    "WB": ([128, 240], BF), "SQ3": ([128, 512], BF), "THL": ([128, 96], F), "TMP": ([128, 384], F),
+    "R6": ([128, 48], BF), "OH2": ([128, 1024], BF), "PL": ([128, 128], BF), "P5": ([128, 128], BF), "P15": ([128, 128], BF),
+    "N15": ([128, 128], BF), "N9": ([128, 128], BF), "T12": ([128, 48], BF), "PM": ([128, 96], BF), "PMT": ([128, 96], BF), "CC1": ([128, 128], BF),
+    "SL2": ([128, 160], BF), "MS": ([128, 144], BF), "MB": ([128, 144], BF),
+    "WB": ([128, 240], BF), "SQ3": ([128, 384], BF), "THL": ([128, 96], F), "TMP": ([128, 192], BF),
     "NE": ([128, 272], BF), "N12": ([128, 192], BF), "SH32": ([128, 128], BF),
     "CK": ([128, 256], BF), "KK": ([128, 256], BF), "LN": ([128, 256], BF), "FS": ([128, 256], BF),
     "MX": ([128, 256], F), "OK": ([128, 256], BF), "TT": ([128, 512], BF), "P2": ([128, 528], BF),
     "NB0": ([128, 272], BF),
-    "MI8": ([128, 40], I), "SM": ([128, 48], BF), "SF": ([128, 16], F), "TK": ([128, 64], F), "SQ": ([128, 80], BF),
+    "SM": ([128, 48], BF), "SF": ([128, 16], F), "TK": ([128, 80], F), "SQ": ([128, 112], BF),
     "OH": ([128, 1024], BF), "LC": ([128, 384], BF), "PB": ([128, 256], BF), "QQ": ([128, 256], BF),
     "Z3": ([128, 192], BF), "TB": ([128, 128], BF), "TBW": ([128, 144], BF), "GT": ([128, 96], BF), "QV": ([128, 192], BF),
-    "OC": ([128, 8], U), "OP": ([128, 16], U), "OD": ([128, 192], U), "OS": ([128, 192], U),
+    "OC": ([128, 8], U), "OP": ([128, 16], U), "OD": ([128, 192], U), "OS": ([128, 32], U),
     "OK2": ([128, 256], U), "OB": ([128, 256], U), "OE": ([128, 8], U), "EV": ([128, 128], BF),
-    "NV": ([128, 256], BF), "YO": ([128, 384], F), "ZO": ([128, 512], F),
+    "NV": ([128, 192], BF), "YO": ([128, 384], F), "ZO": ([128, 512], F),
 }
 POOL = {}
-for _p, _names in (("CB", "IB NI PS NS NB P32 EA EB IS N63 I16 P19 CAP IL I3 MI CC1 PM PMT R6 T12 SL2 G4 G8 MS MU MT MP WB"),
-                   ("CF", "IF RR E8 G8T THL")):
+for _p, _names in (("CB", "IB NI NS NB P32 EA EB IS I16 PL P5 P15 N15 N9 CAP IL I3 I4K MI CC1 PM PMT R6 T12 SL2 G4 G8 CA MY TRI MS MB WB"),
+                   ("CF", "RR E8 G8T THL CD")):
     _o = 0
     for _n in _names.split():
         POOL[_n] = (_p, _o)
         _o += (SB[_n][0][1] + 15) // 16 * 16
     SB[_p] = ([128, _o], SB[_n][1])
 SCRATCH = {k: ("sbuf", v[0], v[1]) for k, v in SB.items() if k not in POOL}
+SB["DL"] = ([8, 13328], F)
+SCRATCH["DL"] = ("dram",) + SB["DL"]
 for _b in range(8):
     SCRATCH["B%d" % _b] = ("psum", [128, 512], F)
 SEMAPHORES = ["qV", "qS", "qP", "qG", "sent"] + ["d%d" % k for k in range(32)] + ["r%d" % k for k in range(10)]
 LOW = 2.0 ** -93
-AID = 3 * ({0: "B7", 2: "B6"},)
+AID = 3 * ({1: "B7", 3: "B6"},)
+ALONE = (True, True, True)
 PLAN = {}
-
-
-def arrange(ops):
-    n = len(ops)
-    after = [[] for _ in ops]
-    for k, o in enumerate(ops):
-        for j in o["deps"]:
-            after[j].append(k)
-    prio = [0.0] * n
-    for k in range(n - 1, -1, -1):
-        if RULE:
-            o = ops[k]
-            prio[k] = (max([prio[j] + (0.0 if o["q"] == ops[j]["q"] == "P" else HAND) for j in after[k]] + [0.0]) +
-                       min(o["cost"]) * (SHARE if o["cost"][0] > 0.5 else 1.0) + o["lat"] + o["move"])
-        else:
-            prio[k] = max(prio[j] for j in after[k]) + 1e-4 if ops[k]["lazy"] and after[k] else -k
-    left = [len(o["deps"]) for o in ops]
-    est, on = [0.0] * n, [None] * n
-    free = {q: 0.0 for q in "VSPGY"}
-    ready = {q: set() for q in "VSPGYE"}
-    for k, o in enumerate(ops):
-        if not left[k]:
-            ready[o["q"]].add(k)
-    order, dma_free = [], 0.0
-    while len(order) < n:
-        best = None
-        for q in "PSVGY":
-            c = ready[q] | ready["E"] if q in "VS" else ready[q]
-            if c:
-                t = max(free[q], min(est[k] for k in c))
-                if best is None or t < best[0]:
-                    best = (t, q, c)
-        t, q, c = best
-        cost = lambda k: ops[k]["cost"][q == "V"]
-        x = max((k for k in c if est[k] <= t), key=lambda k: (prio[k], -k))
-        mine = lambda k, e: ops[k]["q"] == q or (ops[k]["q"] == "E" and q in "VS" and free["S" if q == "V" else "V"] > e)
-        soon = [est[k] for k in c if t < est[k] and prio[k] > prio[x] and mine(k, est[k])]
-        for r in "PVS" if q in "VS" else ():
-            front = [(p, max(est[p], free[r], t)) for p in ready[r] if r != q and prio[p] > prio[x]]
-            for _ in range(DEPTH):
-                front = [(k, max(e + cost(p) + 1.5 * HAND, est[k])) for p, e in front for k in after[p]
-                         if left[k] == 1 and prio[k] > prio[x] and e < t + cost(x)]
-                soon += [e for k, e in front if mine(k, e)]
-        if soon and min(soon) < t + (0.7 if ops[x]["lazy"] else HOLD) * cost(x):
-            free[q] = min(soon)
-            continue
-        o = ops[x]
-        ready[o["q"]].remove(x)
-        on[x] = q
-        free[q] = t + cost(x)
-        end = free[q] + o["lat"]
-        if o["move"]:
-            dma_free = end = max(end, dma_free) + o["move"]
-        order.append(x)
-        for j in after[x]:
-            r = ops[j]["q"]
-            gap = (0.0 if q == "P" else SAME) if q == r else (2 * HAND if "P" in (q, r) else HAND)
-            est[j] = max(est[j], end + gap + (LAG if ops[j]["lazy"] and r == "P" != q else 0.0))
-            left[j] -= 1
-            if not left[j]:
-                ready[r].add(j)
-    return order, on
 
 
 def settle(ops):
@@ -137,6 +78,10 @@ def settle(ops):
         for j in before[k]:
             after[j].append(k)
     tail = [o["lat"] + o["move"] for o in ops]
+    loose = ([o["behind"] - o["deps"] for o in ops], [set() for _ in ops])
+    for k in range(n):
+        for j in loose[0][k]:
+            loose[1][j].add(k)
     way = ["R" if o["q"] == "G" else "D" for o in ops]
 
     def sweep(rank, back):
@@ -161,12 +106,16 @@ def settle(ops):
             k = k[1]
             o, best = ops[k], None
             for q in ("VS" if o["q"] == "E" else o["q"]):
-                t = max([t0[j] + 1e-3 if j in o["behind"] else
-                         t1[j] + ((0.0 if q == "P" else SAME) if on[j] == q else (PHAND if "P" == (q if back else on[j]) else HAND))
-                         for j in src[k]] + [0.0])
+                t = max([t1[j] + ((0.0 if q == "P" else SAME) if on[j] == q else (PHAND if "P" == (q if back else on[j]) else HAND))
+                         for j in src[k] if not loose[back][k] or j not in loose[back][k]] + [0.0])
                 d = o["cost"][q == "V"]
                 if back:
+                    if o["move"]:
+                        t, i = fit(way[k], t, o["move"])
+                        slots[way[k]].insert(i, (t, t + o["move"]))
                     t += tail[k]
+                for j in loose[back][k]:
+                    t = max(t, t0[j] + 1e-3)
                 t, i = fit(q, t, d)
                 key = t + d + (lean[0] * d if q == "V" else 0.0)
                 if best is None or key < best[0]:
@@ -220,7 +169,7 @@ def settle(ops):
             kept = (worth, t0, on, max(t1), order)
         if r < PASSES or (r - PASSES) % 2 == 0:
             rank = [-x for x in sweep([-x for x in t1], True)[1]]
-    PLAN["time"] = kept[3]
+    PLAN["time"], PLAN["worth"] = kept[3], kept[0]
     return kept[4], kept[2]
 
 
@@ -230,7 +179,7 @@ def rank_program(g, core, T, topo):
         return
     nxt, prv = T.cores[(rank + 3) % 8], T.cores[(rank - 3) % 8]
     Q = {"V": g.vector, "S": g.scalar, "P": g.tensor, "G": g, "Y": g.sync}
-    ops, hist, nd, lazy, who = [], {}, [0], [False], {}
+    ops, hist, nd, lazy = [], {}, [0], [False]
 
     def a(n, c0=None, c1=None, p=128, st=1, p0=0, ps=1):
         w = SB[n][0][1] if n in SB else 512
@@ -278,7 +227,7 @@ def rank_program(g, core, T, topo):
             return CALL + SCA * o[2]
         if ins and ins[0][3]:
             return CALL + GA * o[2]
-        if f < 2 and all(kind(x) in (BF, U) for x in [o] + ins[:2] if x[2] > 1):
+        if f < 2 and all(kind(x) in (BF, U, H) for x in [o] + ins[:2] if x[2] > 1):
             f = 0.5
         return CALL + CY * max(64, f * o[2])
 
@@ -324,9 +273,12 @@ def rank_program(g, core, T, topo):
     def red(o, i):
         issue("V", lambda q: g.vector.tensor_reduce(o[0], i[0], AX.X, ALU.add), [i], [o], CALL + CY * max(64, i[2]))
 
-    def relu(o, i, scale, bias=0.0):
-        issue("S", lambda q: g.scalar.activation(o[0], i[0], ACT.Relu, bias=sc(bias), scale=scale), tl(i, bias), [o],
+    def act(o, i, f, scale=1.0, bias=0.0):
+        issue("S", lambda q: g.scalar.activation(o[0], i[0], f, bias=sc(bias), scale=scale), tl(i, bias), [o],
               CALL + CY * max(64, o[2]))
+
+    def relu(o, i, scale, bias=0.0):
+        act(o, i, ACT.Relu, scale, bias)
 
     def ec(o, i, q="E"):
         issue(q, lambda q: g.vector.tensor_copy(o[0], i[0]) if q == "V" else g.scalar.activation(o[0], i[0], ACT.Copy),
@@ -335,6 +287,11 @@ def rank_program(g, core, T, topo):
     def es(o, i, scale, bias=0.0, q="E"):
         issue(q, lambda q: g.vector.tensor_scalar(o[0], i[0], sc(scale), sc(bias), ALU.mult, ALU.add) if q == "V" else
               g.scalar.activation(o[0], i[0], ACT.Identity, bias=sc(bias), scale=sc(scale)), tl(i, scale, bias), [o], both(o, i))
+
+    def fill(o, v):
+        z = a("ZB", 0, o[2])
+        issue("E", lambda q: g.vector.memset(o[0], v) if q == "V" else g.scalar.activation(o[0], z[0], ACT.Identity, bias=v, scale=1.0),
+              [z], [o], both(o, z))
 
     def gather(out, o0, win, offs, n, q="E", gp=GP):
         for l in range(0, n, gp):
@@ -376,13 +333,12 @@ def rank_program(g, core, T, topo):
         sel(o, tmp, pat, ALU.is_ge, hi, -1)
 
     col = lambda k, p=128: a("COL", k, k + 1, p)
-    mi = lambda c, w=8: a("MI8", c, c + w, 96)
     sm = lambda c, w=8, p=96: a("SM", c, c + w, p)
     i96 = a("IB", 0, 96, 96)
     s96 = lambda n: a(n, 0, 96, 96)
     one = lambda m: a("ON", 0, m, 1)
     nil = lambda m, p=128: a("ZB", 0, m, p)
-    row = lambda k, n=256, o=0: a("ROW", 256 * k + o, 256 * k + o + n, 1)
+    row = lambda k, n=256, o=0, st=1: a("ROW", 256 * k + o, 256 * k + o + n, 1, st)
     bar = lambda n, h: a(n, h, 256, 96, 2)
     lis = lambda n, h, o=0: a(n, o + h, o + 192, 128, 2)
 
@@ -398,8 +354,8 @@ def rank_program(g, core, T, topo):
                       a("IB", 64 * j + 16 * g4, 64 * j + 16 * g4 + 16), True, True) for g4 in range(4) for m in range(8)])
             ec(a("TT", 0, 2 * W), a(tb, 0, 2 * W))
             es(a("TT", 2 * W, 4 * W), a("TT", 0, 2 * W), 64.0 ** -16)
-        sums, again = a(cb, 0, n, W), a(tb, 0, n, W)
-        mms([(x, one(W), row(13, n) if off else nil(n, 1), True, False) for x in ((sums, again) if TWICE else (sums,))])
+        sums = a(cb, 0, n, W)
+        mm(sums, one(W), row(13, n) if off else nil(n, 1), True, False)
         for k in range(8):
             o, x, hi = a("TH", 512 * k, 512 * k + 4 * W), a("TT", 0, 4 * W), LOW * 64.0 ** (2 * k + 1)
             op = issue(q, lambda q, o=o, x=x, hi=hi:
@@ -407,16 +363,11 @@ def rank_program(g, core, T, topo):
                        g.scalar.activation(o[0], x[0], ACT.Relu, bias=hi, scale=-1.0),
                        [x], [o], (CALL + CY * 4 * W, CALL + CY * 2 * W))
             wt = lambda q, op=op, k=k: a("G4", 0, 64) if q else a("G4", 4 * k + 32 * (op["q"] == "V"), 4 * k + 32 * (op["q"] == "V") + 4)
-            for b in (cb, tb) if TWICE else (cb,):
-                mms([(a(b, off + k + 4 * gs * j, 4 * gs * (j + 1), W, gs), a("TH", 512 * k + W * j, 512 * k + W * j + W), wt,
-                      False, b == cb and k == 7 and j == 3) for j in range(4)])
+            mms([(a(cb, off + k + 4 * gs * j, 4 * gs * (j + 1), W, gs), a("TH", 512 * k + W * j, 512 * k + W * j + W), wt,
+                  False, k == 7 and j == 3) for j in range(4)])
         es(a("P2", 1, 2 * n, W, 2), sums, 1.0 / 64, 128.25)
-        if TWICE:
-            more(again, a("N63", 0, W, W), a("P2", 1, 2 * n, W, 2), True)
-            es(a("P2", 0, 2 * n, W, 2), again, 1.0, 8192.0)
-        else:
-            es(a("UT", 0, n, W), a("P2", 1, 2 * n, W, 2), 63.0, -8192.0)
-            tt(a("P2", 0, 2 * n, W, 2), sums, a("UT", 0, n, W), ALU.subtract)
+        es(a("UT", 0, n, W), a("P2", 1, 2 * n, W, 2), 63.0, -8192.0)
+        tt(a("P2", 0, 2 * n, W, 2), sums, a("UT", 0, n, W), ALU.subtract)
 
     def w2b(bank, wide, c, rhs, close):
         mms([(a(bank, s, 256, 32, 32, 32 * c), a(wide[0], wide[1] + 1024 * c + s, wide[1] + 1024 * c + 1024, st=32), rhs,
@@ -424,9 +375,12 @@ def rank_program(g, core, T, topo):
 
     def rebuild(v):
         K = (KA, KB, KA)[v]
-        gather("BIG", K + 32, (a("WN", 0, 4096), a("BIG", KA, KB), a("BIG", KB, KEND))[v], "OK2", 4096, RQ[v > 0], GR)
+        gather("BIG", K + 32, (a("WN"), a("BIG", KA, KB), a("BIG", KB, KEND))[v], "OK2", 4096, RQ[v > 0], GR)
         ec(a("EV"), ind(a("BIG", K, K + 4128), a("OE")))
         cp(ind(a("BIG", 0, KA), a("OE")), a("EV"))
+
+    def spread(lo, n, move):
+        return dmas([(a("W", 16 - r + lo, 16 - r + lo + n, p0=r, ps=16), a("DL", lo, lo + n, 8)) for r in range(16)], move)
 
     loads = {"bt": ([(a("L3", 256, 512), ext(T.bt[:]))], 0.6), "pt": ([(a("L2", 0, 192), ext(T.pt[:]))], 0.5),
              "bk": ([(a("L3", 512, 768), ext(T.bk[:]))], 0.6), "pu": ([(a("L2", 192, 384), ext(T.pu[:]))], 0.5),
@@ -434,23 +388,21 @@ def rank_program(g, core, T, topo):
              "bl": ([(a("LS", 0, 128, 8), ext(T.bl[:])), (a("LS", 128, 129, 8), ext(T.pn[:])), (a("LS", 129, 130, 8), ext(T.th[:]))], 0.1),
              "l8": ([(a("LB", 0, 8), ext(T.bl[:]))], 0.25), "bu": ([(a("L3", 0, 256), ext(T.bu[:]))], 0.6)}
     for k, n in enumerate(LOADS.split()):
-        tones_in = dmas(*loads[n], q="YS"[k % 2])
+        dmas(*loads[n], q="YS"[k % 2])
 
     ms(a("ZB", 0, 1024), 0.0)
     ms(a("ON"), 1.0)
     ms(a("ONF"), 1.0)
-    ms(a("PT"), 0.0)
-    if FILL:
-        ms(a("SC", 0, KA // 4), 99.0)
-    else:
-        ms(a("BIG", 0, KA), 99.0)
+    for l in range(0, 4096, 1024):
+        fill(a("PT", l, l + 1024), 0.0)
+    ms(a("SC", 0, KA // 4), 99.0)
     lazy[0] = True
     diag = [[1, 128]]
-    sel(a("IF"), a("ONF", 0, 128), [[-1, 128]], ALU.is_equal, 0, 1)
     put(a("IB"), nil(128), diag, 0, 1.0)
-    for n, v in (("NI", -1.0), ("PS", 16384.0), ("P32", 32768.0), ("EA", float(KA)), ("EB", float(KB)),
-                 ("NS", -16384.0), ("NB", -float(2 ** 25)), ("IS", 64.0 ** -16), ("N63", -63.0), ("I16", 16.0),
-                 ("P19", float(2 ** 19)), ("IL", LOW / 2)):
+    for n, v in (("NI", -1.0), ("P32", 32768.0), ("EA", float(KA)), ("EB", float(KB)), ("I4K", 4096.0),
+                 ("NS", -16384.0), ("NB", -float(2 ** 25)), ("IS", 64.0 ** -16), ("I16", 16.0),
+                 ("PL", 2.0 ** 15 + 2 ** 9), ("P5", 2.0 ** -5), ("P15", 2.0 ** -15), ("N15", -2.0 ** -15), ("N9", -2.0 ** -9),
+                 ("IL", LOW / 2)):
         es(a(n), a("IB"), v)
     sel(a("I3"), a("IB"), [[0, 8], [-1, 16]], ALU.is_ge, 2, 0)
     sel(a("SG"), a("ON"), [[0, 8], [1, 32]], ALU.is_gt, 0, 0)
@@ -467,35 +419,44 @@ def rank_program(g, core, T, topo):
     band(a("G8", 0, 8), a("G8", 8, 16), a("ON", 0, 8), grp, 0, 15)
     sel(a("G8T", 0, 128, 8), a("ONF", 0, 128, 8), [[1, 8], [0, 16]], ALU.is_equal, 0, -1)
     sel(a("G8T", 128, 256, 8), a("ONF", 0, 128, 8), [[1, 128]], ALU.is_equal, -2, -16)
-    ec(a("SL2", 40, 64), nil(24))
-    for lo, hi, r, s in ((0, 24, 0, 1), (24, 40, 2, 0), (64, 128, 3, 0)):
+    for lo, hi in ((40, 80), (144, 160)):
+        ec(a("SL2", lo, hi), nil(hi - lo))
+    for lo, hi, r, s in ((0, 24, 0, 1), (24, 40, 2, 0), (80, 144, 3, 0)):
         put(a("SL2", lo, hi), nil(hi - lo), [[s, (hi - lo) // 8], [16, 8]], r, 1.0)
     io(a("CC1"), [[1, 128]], 1)
     io(a("RR"), [[0, 8], [1, 16]])
     io(row(1), [[0, 256]], -16384)
     io(a("ROW", 256 + 31, 512, 1, 32), [[0, 8]], 32768)
-    io(row(2), [[0, 256]], -6 * 64)
+    io(row(2), [[0, 256]], -6 * 1024)
     io(row(13), [[0, 16], [-1984, 2], [0, 8]], 1984)
     es(a("G8B", 0, 8), a("G8", 0, 8), float(2 ** 25))
     io(row(3), [[0, 8], [-1, 32]], 31)
     io(row(4, 96), [[-1, 96]], -129)
-    io(row(5), [[0, 128], [16, 2]])
-    io(row(6), [[0, 128], [-16, 2]])
+    io(row(5, 24), [[256, 24]])
+    io(row(5, 24, 32), [[0, 24]], 16)
+    io(row(5, 16, 64), [[16, 2], [0, 8]], -111)
+    sel(row(5, 16, 80), nil(16, 1), [[1, 2], [0, 8]], ALU.is_gt, 0, 0, 14.5)
+    sel(row(5, 16, 80), row(5, 16, 80), [[-1, 2], [0, 8]], ALU.is_ge, 0, 0, 0.5)
+    io(row(5, 128, 128), [[0, 128]], 4096)
+    io(row(6), [[-16, 2], [0, 128]], 1)
     io(row(7), [[16, 256]])
     io(row(8, 128), [[0, 8], [1, 16]])
-    io(row(8, 96, 128), [[0, 96]], 2 ** 19)
+    io(row(8, 96, 128), [[0, 96]], 2 ** 15)
     io(row(9), [[0, 256]], -1)
     for v in range(3):
         io(row(10 + v // 2, 96, 128 * (v % 2)), [[-1, 48], [0, 2]], -64 - 48 * v)
     io(row(11, 96, 128), [[0, 48], [-32, 2]], -31)
     for k in range(2):
         sel(row(12, 96, 128 * k), nil(96, 1), [[0, 6], [1 - 2 * k, 2], [0, 8]], ALU.is_equal, k, 0, float(2 ** 99))
+    es(row(18, 384), nil(384, 1), 1.0, -2.0 ** 26)
+    io(row(20, 128), [[0, 8], [16, 16]])
     io(a("ROF", 0, 256, 1), [[1, 16], [512, 8], [0, 2]])
-    io(a("ROF", 256, 268, 1), [[1, 2], [32, 6]], 31)
+    io(a("ROF", 256, 268, 1), [[34, 2], [128, 6]], 79)
     sel(a("ROF", 272, 528, 1), a("ONF", p=1), [[-1, 2], [0, 8], [1, 16]], ALU.is_equal, 0, 0)
     io(a("ROF", 528, 656, 1), [[1, 64], [0, 2]])
     io(a("ROF", 656, 784, 1), [[0, 64], [32, 2]])
-    io(a("ROF", 784, 912, 1), [[0, 8], [192, 16]])
+    io(a("ROF", 784, 912, 1), [[0, 8], [768, 16]])
+    es(a("ROF", 912, 1040, 1), a("ONF", 0, 128, 1), 1.0 / 32)
     sel(a("M6", 0, 128), a("ON", 0, 128), [[0, 8], [6, 16]], ALU.is_gt, 0, -1)
     band(a("M6", 128, 384), a("PB"), a("ON"), [[0, 16], [6, 16]], 0, 5)
     put(a("PM"), nil(96), [[1, 6], [6, 16]], 0, 1.0)
@@ -504,32 +465,46 @@ def rank_program(g, core, T, topo):
     io(a("T12", 12, 24), [[0, 12]], -1)
     band(a("T12", 12, 24), a("T12", 24, 36), a("T12", 12, 24), [[0, 2], [16, 6]], 0, 15)
     mm(a("B4", 0, 24, 96), a("PMT", p=96), a("T12", 0, 24, 96))
-    ec(a("R6", 0, 24, 96), a("B4", 0, 24, 96))
-    es(a("R6", 24, 30, 96), a("B4", 12, 18, 96), -1.0)
-    five = ("MS", "MU", "MT", "MP", "WB")
-    ec((T.CB[:, POOL["MS"][1]:POOL["MS"][1] + 816], [a(n)[1][0] for n in five], 816, False), nil(816))
-    for n in ("TBW", "SM", "SQ"):
+    es(a("R6", 0, 12, 96), a("B4", 0, 12, 96), 2.0 ** -4)
+    es(a("R6", 12, 24, 96), a("B4", 12, 24, 96), 2.0 ** -19)
+    es(a("R6", 24, 30, 96), a("B4", 12, 18, 96), -2.0 ** -13)
+    es(a("R6", 32, 44), a("ON", 0, 12), 1.0 / 16)
+    three = ("MS", "MB", "WB")
+    ec((T.CB[:, POOL["MS"][1]:POOL["MS"][1] + 528], [a(n)[1][0] for n in three], 528, False), nil(528))
+    for n in ("TBW", "SM", "SQ", "HF"):
         ec(a(n), nil(SB[n][0][1]))
-    put(a("MS", 15, 143, st=16), a("G8", 0, 8), grp, 0, 64.0)
-    for n, r, o in (("MU", 0, 7), ("MT", 2, 71)):
-        for x in (a(n, 15, 143, st=16), a("MP", o, o + 64, st=8)):
-            put(x, nil(8), grp, r, 1.0)
-            put(x, x, grp, r + 1, 1.0)
-    for k, rows in ((2, ((0, 64.0), (1, 1.0))), (3, ((2, 1.0),))):
-        x = a("SQ3", 128 * k, 128 * k + 128)
-        for j, (r, v) in enumerate(rows):
-            put(x, x if j else nil(128), [[16, 8], [0, 16]], r, v)
+    ec(a("AD", 768, 784), nil(16))
+    es(a("SQ", 88, 96), a("ON", 0, 8), 1.0)
+    es(a("SQ", 96, 104), a("ON", 0, 8), -1.0)
+    x = a("MS", 15, 143, st=16)
+    for j, (r, v) in enumerate(((0, 64.0), (14, -16.0), (15, 0.0))):
+        put(x, x if j else a("G8", 0, 8), grp, r, v)
+    x = a("MB", 15, 143, st=16)
+    put(x, nil(8), grp, 0, 64.0)
+    put(x, x, grp, 1, 1.0)
+    rows = [[16, 8], [0, 16]]
+    put(a("SQ3", 256, 384), nil(128), rows, 2, 1.0)
     for h in range(2):
         x = a("SQ3", 128 * h, 128 * h + 128)
         io(x, [[0, 8], [1, 16]], 16 * h + 128)
         sel(x, x, [[-16, 8], [0, 16]], ALU.is_equal, -14, 1)
-        put(x, x, [[16, 8], [0, 16]], 15, 32.0)
+        put(x, x, rows, 15, 32.0)
         put(x, x, [[32, 4], [-16, 2], [0, 16]], 30, 159.0)
+    x = a("MY", 0, 128)
+    sel(x, nil(128), rows, ALU.is_gt, 2, -1, -2.0 ** 26)
+    sel(x, x, rows, ALU.is_ge, 13, -1)
+    put(x, x, rows, 14, 2.0 ** 31)
+    put(a("MY", 128, 256), nil(128), rows, 15, 2.0 ** 26)
+    sel(a("TRI", 0, 96), a("ON", 0, 96), [[1, 96]], ALU.is_gt, 0, -1)
+    sel(a("TRI", 96, 192), a("ON", 0, 96), [[1, 96]], ALU.is_ge, 0, -1)
+    for h in range(2):
+        es(a("CA", 128 * h, 128 * h + 128), a("RR"), 16.0, -112.0)
+        es(a("CD", 128 * h, 128 * h + 128), a("RR"), 1.0, MAGIC)
     ms(a("TBW", 0, 1), float(2 ** 98))
     for n in ("NB0", "NE"):
         ec(a(n, 0, 16), nil(16))
-    put(a("DF", 128, 256), a("IF"), diag, -1, -1.0)
-    ec(a("DF", 128, 256, st=16), a("IF", 0, 128, st=16))
+    put(a("DF", 128, 256), a("IB"), diag, -1, -1.0)
+    ec(a("DF", 128, 256, st=16), a("IB", 0, 128, st=16))
     ec(a("DF", 0, 128), a("DF", 128, 256))
     ec(a("DF", 0, 128, st=16), nil(8))
     ec(a("DF", 256, 384), nil(128))
@@ -545,81 +520,71 @@ def rank_program(g, core, T, topo):
         ec(a("BIG", o, o + 32), nil(32))
     for n in ("SD0", "SD1"):
         ms(a(n, 0, 8), 0)
-    ms(a("WN", ZC, ZC + 16), -0.5)
+    ec(a("W", 0, 16), nil(16))
     io(a("CI", 0, 1), [[0, 1]], 0, 1)
     ts(a("CI", 1, 2), a("CI", 0, 1), 15, ALU.bitwise_and)
     cp(col(0), a("CI", 1, 2))
+    es(col(1), col(0), 2.0)
+    ts(col(2), col(0), 15.0, ALU.is_equal, -16384.0, ALU.mult)
+    es(col(10), col(0), 256.0)
     ts(a("MI"), a("RR"), col(0), ALU.is_equal)
-    io(a("JO", 0, 192), [[16, 96], [0, 2]], 1)
-    io(a("JO", 192, 384), [[0, 96], [1, 2]], -1)
-    io(a("JO", 384, 576), [[16, 192]], 1)
-    es(a("JO", 384, 576), a("JO", 384, 576), 1.0, col(0))
-    ts(a("JO", 0, 192), a("JO", 0, 192), col(0), ALU.add, 2.0, ALU.mult)
-    tt(a("JO", 0, 192), a("JO", 0, 192), a("JO", 192, 384), ALU.add)
+    io(a("JO", 0, 192), [[32, 96], [1, 2]], 1)
+    io(a("JO", 192, 384), [[16, 192]])
     put(a("SH32"), nil(128), diag, 1, 32768.0)
-    ms(a("TMP", 0, 96), 0.25)
-    scan(a("TMP", 256, 352), a("TMP", 0, 96), a("ONF", 0, 96), float(2 ** 96), ALU.mult, ALU.mult)
-    tt(a("TMP", 128, 224), a("TMP", 256, 352), a("IF", 0, 96), ALU.mult)
-    red(col(3), a("TMP", 128, 224))
-    es(col(4), col(3), 2.0)
-    es(a("WB", 115, 116), col(3), 1.0)
+    es(a("TMP", 0, 96, 1), a("ON", 0, 96, 1), 0.25)
+    scan(a("TMP", 96, 192, 1), a("TMP", 0, 96, 1), a("ON", 0, 96, 1), float(2 ** 96), ALU.mult, ALU.mult)
+    mm(a("B5", 0, 1, 96), a("TMP", 96, 192, 1), one(1))
+    es(col(4, 96), a("B5", 0, 1, 96), 2.0)
+    ec(a("WB", 115, 116, 96), a("B5", 0, 1, 96))
+    ec(a("MX"), nil(256))
+    for o in AV:
+        es(a("A", o, o + 384), nil(384), 1.0, col(2))
     io(a("BCF", 0, 32), [[1, 32]])
     io(a("BCF", 32, 48), [[0, 2], [1, 8]], 16)
-    io(a("BCF", 80, 104), [[0, 24]], 8)
-    for o, picks in ((80, ((16, 0, 0), (16, 1, 8))), (88, ((16, 0, 0), (16, 1, 8), (18, 2, 24), (18, 3, 32))),
+    io(a("BCF", 80, 104), [[0, 24]], 10)
+    for o, picks in ((80, ((16, 0, 0), (16, 1, 8), (16, 14, 88), (16, 15, 64))),
+                     (88, ((16, 0, 0), (16, 1, 8), (18, 2, 24), (18, 3, 32), (16, 14, 96), (16, 15, 72))),
                      (96, ((16, 0, 0), (16, 1, 8), (16, 2, 16), (16, 14, 40), (16, 15, 48)))):
         for s, r, v in picks:
-            put(a("BCF", o, o + 8), a("BCF", o, o + 8), [[s, 8]], r, v - 56.0)
+            put(a("BCF", o, o + 8), a("BCF", o, o + 8), [[s, 8]], r, v - 70.0)
         red(col(5 + (o - 80) // 8), a("BCF", o, o + 8))
     es(a("BCF", 48, 56), a("BCF", 0, 8), 1.0, col(5))
     es(a("BCF", 56, 64), a("BCF", 0, 8), 1.0, col(6))
-    io(a("BCF", 64, 76), [[0, 12]], 64)
+    io(a("BCF", 64, 76), [[0, 12]], 80)
     for o in range(2):
         es(a("BCF", 64 + 2 * o, 76, st=3), a("BCF", o, 8, st=2), 1.0, col(7))
     io(a("BCF", 112, 128), [[1, 8], [0, 2]])
+    io(a("BCF", 128, 144), [[16, 2], [32, 4], [128, 2]])
+    es(a("BCF", 128, 144), a("BCF", 128, 144), 1.0, col(0))
+    io(a("BCF", 144, 160), [[32, 8], [0, 2]], 31)
+    io(a("BCF", 160, 162), [[0, 2]], 0, 1)
     cp(a("BC", 0, 16), a("BCF", 0, 16))
     cp(a("BC", 16, 76), a("BCF", 16, 76))
     cp(a("BC", 80, 96), a("BCF", 112, 128))
+    cp(a("BC", 96, 130), a("BCF", 128, 162))
 
     lazy[0] = False
     tt(a("NB0", 1, 256), a("L3", 257, 512), a("L3", 256, 511), ALU.not_equal)
     es(a("FY"), a("NB0", 0, 256), 63.0, 1.0)
     scan(a("YY"), a("FY"), a("CAP"), LOW, ALU.mult, ALU.min)
     count(128, 8, "B6", "B3")
-    ts(a("ST", 1024, 1280), a("L3", 512, 768), 1.0, ALU.add, 32.0, ALU.mult)
-    lazy[0] = True
-    io(a("ST", 1280, 1536), [[1, 4], [0, 64]])
-    io(a("ST", 1536, 1792), [[0, 4], [1, 64]])
-    es(col(10), col(0), 256.0)
-    es(a("ST", 1280, 1536), a("ST", 1280, 1536), 64.0, col(10))
-    lazy[0] = False
-    last = dmas([(a("PT", p0=r, ps=16), a("ST", c, c + 256)) for r, c in ((0, 1024), (2, 1280), (3, 1536))], 1.2)
-    for items, move in (([(a("BIG", l, l + KA // 4), a("SC", 0, KA // 4)) for l in range(0, KA if FILL else 0, KA // 4)], 4.0),
-                        ([(a("A", o + l, o + l + 1024), a("ZB")) for o in (AV[0], AV[0] + A2) for l in range(0, 3072, 1024)], 6.0)):
-        if items:
-            ops[dmas(items, move)]["behind"].add(last)
-            last = len(ops) - 1
+    es(a("ST"), a("L3", 512, 768), 32.0, 32.0)
+    last = dmas([(a("PT", p0=0, ps=16), a("ST"))], 0.4)
+    ops[dmas([(a("BIG", l, l + KA // 4), a("SC", 0, KA // 4)) for l in range(0, KA, KA // 4)], 4.0)]["behind"].add(last)
+    last = len(ops) - 1
     for l in range(2):
-        for c in range(3):
-            cp(a("IN0", 128 * c + 8 + 64 * l, 128 * c + 72 + 64 * l), a("L2", 192 * l + 64 * c, 192 * l + 64 * c + 64))
+        cp(a("IN0", 8 + 192 * l, 200 + 192 * l), a("L2", 192 * l, 192 * l + 192))
     cp(a("OB"), a("L3", 256, 512))
     mm(a("B7", 0, 256), a("ONF", 0, 128, 1), a("ROF", 0, 256, 1), True, False)
     mms([(a("B7", h, 256, st=2), a("P2", 128 * h, 128 * h + 128), a("I16"), False, h == 1) for h in range(2)])
     ts(a("OK2"), a("B7", 0, 256), -2048.0, ALU.add)
     ms(a("P2", 512, 528), 159.0)
     lazy[0] = True
-    ec(a("HL2", 512, 1024), nil(512))
-    cp(a("LF0"), a("L2", 192, 384))
-    mms([(a("B5", 32 * gg + 16 * h, 32 * gg + 16 * h + 16, 96), lis("LF0", h), a("IF", 16 * gg, 16 * gg + 16), True, True)
-         for gg in range(8) for h in range(2)])
-    ec(a("HL2", 0, 256, 96), a("B5", 0, 256, 96))
-    tt(a("HL2", 256, 512, 96), a("B5", 0, 256, 96), a("HL2", 0, 256, 96), ALU.subtract)
-    for hf, bank in enumerate(("B5", "B4")):
-        for c in range(3):
-            mms([(a(bank, s, 512, 32, 32, 32 * c), a("HL2", s, 1024, 32, 32, 32 * c),
-                  a("IB", 32 * c + 16 * hf, 32 * c + 16 * hf + 16, 32, p0=32 * c), True, True) for s in range(32)])
-        ec(a("SR0", 512 * hf, 512 * hf + 512, 96), a(bank, p=96))
-    lazy[0] = True
+    es(a("LIB"), a("L3", 0, 256), 4096.0)
+    tt(a("LIB"), a("LIB"), a("L3", 256, 512), ALU.add)
+    dmas([(a("DL", 0, 4096, 8), a("LIB"))] + [(a("DL", 7168 + 3072 * v, 7184 + 3072 * v, 8), a("ONF", 0, 16, 8)) for v in range(3)], 0.6)
+    book = spread(0, 4096, 7.3)
+    ops[book]["behind"].add(last)
     cp(a("LSF", 0, 130, 8), a("LS", 0, 130, 8))
     mm(a("B0", 300, 301), a("G8T", 0, 128, 8), a("LSF", 128, 129, 8))
     cp(a("IN0", 7, 8), a("B0", 300, 301))
@@ -637,17 +602,7 @@ def rank_program(g, core, T, topo):
     acc(a("B7", 0, 128), [(a("G8T", 128, 256, 8), a("LSF", 136, 264, 8)), (a("ROF", 272, 400, 1), a("ROF", 528, 656, 1)),
                           (a("ROF", 400, 528, 1), a("ROF", 656, 784, 1))])
     ec(a("TB"), a("B7", 0, 128))
-    for l in range(0, 512, 128):
-        cp(a("ST", l, l + 128), a("L3", l, l + 128))
-        tt(a("ST", 512 + l, 640 + l), a("L3", l, l + 128), a("ST", l, l + 128), ALU.subtract)
     lazy[0] = False
-
-    def upper_rows(v):
-        if v == 0:
-            dmas([(a("WN", 4096 + 1024 * c, 5120 + 1024 * c, p0=r, ps=16), a("SR0", p=8, p0=32 * c + 8 * r))
-                  for r in range(2) for c in range(3)], 0.6)
-        else:
-            dmas([(a("WN", 4096 + 3072 * v, 7168 + 3072 * v, p0=r, ps=16), a("SR%d" % v, p=64, p0=64 * r)) for r in range(2)], 0.5)
 
     rid, pid, _ = topo.addr(nxt)
     sent, calls = [0], []
@@ -655,20 +610,21 @@ def rank_program(g, core, T, topo):
     def remote(dst, src, sem, move):
         sent[0] += len(topo.engines(core, nxt))
         issue("G", lambda q: g.remote_dma(dst[0], src[0], T.sem[sem], T.sem["sent"], pid, rid, topo.mask(core, nxt)),
-              [src], [dst], RCALL + (2.0 if sem == "r0" else 0.0), RDMA - RCALL, move, (sem, len(topo.engines(prv, core))))
+              [src], [dst], RCALL + (0.0 if calls else FIRST), RDMA - RCALL, move, (sem, len(topo.engines(prv, core))))
         ops[-1]["behind"].update(calls[-1:])
         calls.append(len(ops) - 1)
 
     for v in range(3):
-        IN, SD, SR = "IN%d" % v, "SD%d" % v, "SR%d" % v
+        IN, SD = "IN%d" % v, "SD%d" % v
         R = 4096 + 3072 * v
         K = (KA, KB, KA)[v]
         XC = (XA, XB, XA)[v]
-        CW, PR, SC = ("WN", R), ("PR", 0), ("SC", 0)
+        CW, PR, SC = ("CW", 0), ("PR", 0), ("SC", 0)
         wd = lambda n, lo, hi: a(n[0], n[1] + lo, n[1] + hi)
         XR = ("BIG", XC)
         nb = col(8)
-        names_of = lambda up, lo, hi: a(IN, 8 + 64 * (up + lo // 1024) + lo // 16, 8 + 64 * (up + lo // 1024) + hi // 16)
+        base = lambda up, lo: 8 + (64 * (up + lo // 1024) if v else 192 * up)
+        names_of = lambda up, lo, hi: a(IN, base(up, lo) + lo // 16, base(up, lo) + hi // 16)
         cont, new = a("NE", 0, 256, 96), a("NQ", 0, 256, 96)
         s0, s1, s3, s5 = [a("B%d" % k, 0, 256, 96) for k in (0, 1, 3, 5)]
 
@@ -689,10 +645,10 @@ def rank_program(g, core, T, topo):
         def changes(p0, p):
             lo, hi = 2 * p0, 2 * (p0 + p)
             for l in range(lo, hi, 64):
-                cp(a("LT", l, l + 64), names_of(0, 16 * l, 16 * l + 1024))
-            mms([(a("B3", lo, hi, st=2), a("DF", 0, 128), a("LT", lo, hi, st=2), True, True),
-                 (a("B3", lo + 1, hi, st=2), a("DF", 128, 256), a("LT", lo + 1, hi, st=2), True, False),
-                 (a("B3", lo + 1, hi, st=2), a("DF", 256, 384), a("LT", lo, hi, st=2), False, True)])
+                ts(a("HT", l, l + 64), names_of(0, 16 * l, 16 * l + 1024), -2048.0, ALU.add)
+            mms([(a("B3", lo, hi, st=2), a("DF", 0, 128), a("HT", lo, hi, st=2), True, True),
+                 (a("B3", lo + 1, hi, st=2), a("DF", 128, 256), a("HT", lo + 1, hi, st=2), True, False),
+                 (a("B3", lo + 1, hi, st=2), a("DF", 256, 384), a("HT", lo, hi, st=2), False, True)])
             ts(a("NL", lo, hi), a("B3", lo, hi), 0.0, ALU.not_equal)
             turned = lambda bank, o, k, sh, last: [(a(bank, o, o + 256, p, p0=p0), a("NL", lo + h, hi, st=2),
                                                     a("MN", 288 * k + 16 - 16 * h + sh, 288 * k + 272 - 16 * h + sh), False, last and h == 1)
@@ -712,19 +668,22 @@ def rank_program(g, core, T, topo):
                 if bank:
                     ec(wd(SC, l, l + 512), key, "S")
                     acc(a(bank), [(a("NI"), own), (a("IB"), wd(SC, l, l + 512))])
-                    ts(wd(PR, l, l + 512), a(bank), 0.0, ALU.not_equal)
+                    if ALONE[v]:
+                        act(wd(SC, l, l + 512), a(bank), ACT.Sign)
+                        act(wd(PR, l, l + 512), wd(SC, l, l + 512), ACT.Abs)
+                    else:
+                        ts(wd(PR, l, l + 512), a(bank), 0.0, ALU.not_equal)
                 else:
                     tt(wd(PR, l, l + 512), key, own, ALU.not_equal)
                 mms([(a("B5", 2 * i + h, 256, 32, 32, 32 * c), a(PR[0], PR[1] + l + i, PR[1] + l + 512, st=16), a("G8B", 0, 8),
                       False, h == 1 and i == 15) for i in range(16)])
 
-        ts(nb, a(IN, 7, 8), -1.0, ALU.mult)
-        relu(a("N12"), a("JO", 0, 192), 1.0, nb)
+        ts(col(13), a(IN, 7, 8), -1.0, ALU.mult, col(1), ALU.add)
+        relu(a("N12"), a("JO", 0, 192), 1.0, col(13))
         if v == 0:
             lazy[0] = True
             gather("WN", 0, a("TON"), "OB", 4096, RQ[0], GR)
             rebuild(0)
-            dmas([(a("WN", 0, 4096, p0=r, ps=16), a("ST", c, c + 256)) for r, c in ((0, 0), (1, 512), (2, 256), (3, 768))], 1.6)
             lazy[0] = False
         mms([(s0, a("THL", p=8), a("E8", p=8), True, False), (s0, one(96), row(1), False, False)])
         mms([(bar("B0", h), lis("N12", 1 - h), a("SH32" if h else "P32"), False, False) for h in range(2)])
@@ -744,40 +703,53 @@ def rank_program(g, core, T, topo):
                 for l in range(1024 * c, 1024 * c + 1024, GW):
                     ec(wd(CW, l, l + GW), ind(a("PT"), names_of(0, l, l + GW)), WQ[l // GW])
                 w2b("B1", CW, c, a("SL2", 0, 8), False)
+            k = len(ops)
             slots(p0, p)
+            if WAIT[0] is not None:
+                ops[k + 1]["behind"].add(book)
         lazy[0] = True
-        upper_rows(v)
+        for c in range(3):
+            ts(a("HT", 192 + 64 * c, 256 + 64 * c), names_of(1, 1024 * c, 1024 * c + 1024), -2048.0, ALU.add)
+        for gg in range(8):
+            o = lambda b: a("B2", 96 * (gg % 2) + 16 * b, 96 * (gg % 2) + 16 * b + 16, 32, p0=32 * (gg // 2))
+            mms([(o(b), a("HT", 192 * k + b, 192 * k + 192, st=6), a(("IB", "I4K")[k], 16 * gg, 16 * gg + 16), k == 0, k == 1)
+                 for b in range(6) for k in range(2)])
+        es(a("LIN"), a("B2", 0, 192), 1.0, 2048.0 * 4097)
+        dmas([(a("DL", R, R + 3072, p0=h, ps=2), a("LIN", 96 * h, 96 * h + 96)) for h in range(2)], 0.5)
+        spread(R, 3088, 5.5)
         lazy[0] = False
+        ahead = len(ops) - 1
         differ(0)
+        if WAIT[v] is not None:
+            ops[ahead + 1 + WAIT[v]]["behind"].add(ahead)
         lazy[0] = True
+        ts(nb, a(IN, 7, 8), -1.0, ALU.mult, *((col(0), ALU.add) if v == 2 else ()))
         scan(a("LN", p=96), a("ON", p=96), cont, 0.0, ALU.add, ALU.mult)
         mms([(s3, row(8, 96, 128), row(3), True, False)] +
             [(bar("B3", h), lis("N12", h), a("NB"), False, False) for h in range(2)])
-        for l, r in ((s96("NB"), a("NE", 1, 257, 96)), (i96, a("CK", p=96)), (s96("P19"), a("LN", p=96))):
-            more(s3, l, r)
-        more(s3, i96, a("LN", p=96), True)
+        more(s3, s96("NB"), a("NE", 1, 257, 96))
+        more(s3, s96("P5"), a("CK", p=96))
+        more(s3, s96("PL"), a("LN", p=96), True)
         d0 = lambda lo, hi: a("B0", lo, hi, 96)
         mm(a("B4", 0, 128), a("I3"), a("TB"), True, False)
-        mms([(d0(0, 128), one(96), nil(128, 1), True, False), (d0(0, 8), row(10 + v // 2, 96, 128 * (v % 2)), one(8), False, False),
-             (d0(8, 16), row(11, 96, 128), one(8), False, False), (d0(88, 96), row(12, 96), one(8), False, False),
-             (d0(96, 104), row(12, 96, 128), one(8), False, False), (d0(40, 48), one(96), one(8), False, False),
-             (d0(48, 56), row(4, 96), one(8), False, False)])
-        acc(a("B2", 0, 12), [(a("ONF", 0, 128, 1), a("ROF", 256, 268, 1)), (a("ROF", 784, 912, 1), a("ONF", 0, 12, 1))], False)
+        mms([(d0(0, 160), one(96), nil(160, 1), True, False), (d0(0, 8), row(10 + v // 2, 96, 128 * (v % 2)), one(8), False, False),
+             (d0(8, 16), row(11, 96, 128), one(8), False, False), (d0(104, 112), row(12, 96), one(8), False, False),
+             (d0(112, 120), row(12, 96, 128), one(8), False, False), (d0(40, 48), one(96), one(8), False, False),
+             (d0(48, 56), row(4, 96), one(8), False, False), (d0(64, 80), one(96), row(5, 16, 80), False, False)])
+        acc(a("B2", 0, 12), [(a("ROF", 912, 1040, 1), a("ROF", 256, 268, 1)), (a("ROF", 784, 912, 1), a("ROF", 912, 924, 1))], False)
         lazy[0] = False
         differ(1)
         differ(2)
         scan(a("FS", p=96), cont, s5, 0.0, ALU.mult, ALU.max)
         tt(a("UT", p=96), s3, a("FS", p=96), ALU.subtract)
         scan(a("MX", p=96), a("SG", p=96), a("UT", p=96), 0.0, ALU.mult, ALU.max)
-        cp(mi(32), a("MX", 31, 256, 96, 32))
-        ts(mi(0), mi(32), 5, ALU.arith_shift_right, 255, ALU.bitwise_and)
-        cp(sm(0), mi(0))
+        offer, high = a("MX", 31, 256, 96, 32), a("SF", 0, 8, 96)
+        ts(high, offer, MAGIC * 2 ** 9, ALU.add, MAGIC * 2 ** 9, ALU.subtract)
+        tt(sm(0), offer, high, ALU.subtract)
         if v < 2:
-            es(sm(32), a("MX", 31, 256, 96, 32), 2.0 ** -19, 128.0, "S")
-            ec(a("RM", 0, 256), ind(a("SM", 32, 48), a("BC", 80, 96)), "S")
+            es(a("RM", 0, 256), ind(a("MX"), a("BC", 112, 128)), 2.0 ** -15, 128.0, "S")
             acc(a("B7", 0, 256, 96), [(one(96), row(16)), (i96, a("RM", 0, 256, 96))])
-            issue("S", lambda q: g.scalar.activation(T.RM[0:96, 256:512], T.B7[0:96, 0:256], ACT.Sign, bias=0.5, scale=1.0),
-                  [a("B7", 0, 256)], [a("RM", 256, 512)], CALL + CY * 256)
+            act(a("RM", 256, 512, 96), a("B7", 0, 256, 96), ACT.Sign, 1.0, 0.5)
             acc(a("B7", 256, 512, 96), [(s96("IL"), a("ON", p=96)), (s96("IL"), a("RM", 256, 512, 96))])
             scan(a("YY", p=96), a("NQ", 256, 512, 96), a("B7", 256, 512, 96), 0.0, ALU.mult, ALU.max)
             count(96, 16, "B7", "B6", CQ)
@@ -788,36 +760,72 @@ def rank_program(g, core, T, topo):
             more(a("B4", 0, 128), a("WB", 112 - 16 * gg, 240 - 16 * gg, 96), a("OH", 128 * gg, 128 * gg + 128, 96), gg == 7)
         cp(a("OC", 0, 6), a("B1", 0, 6))
         ec(a("TBW", 1, 129), a("B4", 0, 128))
-        ts(mi(8), mi(32), 19, ALU.arith_shift_right)
-        ts(mi(16), mi(32), 31, ALU.bitwise_and)
-        cp(sm(8, 16), mi(8, 16))
-        mms([(d0(c, c + 8), i96, sm(k), False, False) for c, k in ((8, 8), (48, 0))] +
-            [(d0(c, c + 8), s96("NI"), sm(16), False, False) for c in (16, 24, 32)])
+        ts(sm(8), offer, MAGIC * 2 ** 15, ALU.add, MAGIC * 2 ** 15, ALU.subtract)
+        tt(sm(16), high, sm(8), ALU.subtract)
+        mms([(d0(c, c + 8), s96(m), sm(k), False, False) for c, m, k in
+             ((48, "IB", 0), (8, "P15", 8), (72, "P15", 8), (64, "N15", 8), (16, "N9", 16), (24, "N9", 16), (32, "N9", 16), (72, "N9", 16))])
+        lazy[0] = True
+        cut, at16 = a("B1", 0, 384), a("B4", 0, 16, 96)
+        mms([(cut, row(8, 128), row(18, 384), True, False), (a("B1", 0, 256), row(18, 128), row(7), False, False),
+             (a("B1", 256, 384), row(18, 128), row(7, 128), False, False), (a("B1", 256, 384), row(18, 128), row(5, 128, 128), False, False)])
+        mms([(at16, row(7, 192, 0, 2), one(16), True, False), (at16, one(96), row(5, 16, 64), False, False)])
+        lazy[0] = False
         ec(a("GT"), ind(a("TBW"), a("OC", 0, 6)))
-        more(d0(0, 128), a("GT"), a("SL2"), True)
+        more(d0(0, 160), a("GT"), a("SL2"), True)
         tt(a("LC", 128, 384), ind(a("SM", 0, 32), a("BC", 8, 24)), a("M6", 128, 384), ALU.mult)
         mms([(a("B2", 0, 12), a("LC", 128, 256, 96), a("R6", 12, 24, 96), False, False),
              (a("B2", 6, 12), a("LC", 256, 384, 96), a("R6", 24, 30, 96), False, False)])
-        ts(a("TK", p=96), d0(64, 128), col(4, 96), ALU.is_lt)
-        tt(a("SQ", 0, 64, 96), d0(0, 64), a("TK", p=96), ALU.mult)
+        ts(a("TK", p=96), d0(80, 160), col(4, 96), ALU.is_lt)
+        tt(a("SQ", 0, 80, 96), d0(0, 80), a("TK", p=96), ALU.mult)
         tt(a("PB"), ind(a("SQ", 0, 24), a("BC", 32, 48)), a("M6", 0, 256), ALU.mult)
         ec(a("QQ", 0, 128), ind(a("SQ"), a("BC", 48, 56)))
         es(a("QQ", 128, 256), ind(a("SQ"), a("BC", 56, 64)), -1.0)
-        mms([(a("B2", 0, 12), a("PB", 0, 128, 96), a("ON", 0, 12, 96), False, False),
+        mms([(a("B2", 0, 12), a("PB", 0, 128, 96), a("R6", 32, 44, 96), False, False),
              (a("B2", 0, 12), a("PB", 128, 256, 96), a("R6", 0, 12, 96), False, True)])
         mms([(a("B5", 96 * k, 96 * k + 96), a("QQ", 128 * k, 128 * k + 128, 96), a("PM", p=96), True, True) for k in range(2)])
-        cp(a("OP", 0, 12), a("B2", 0, 12))
+        ts(a("OP", 0, 12), a("B2", 0, 12), MAGIC, ALU.add, MAGIC, ALU.subtract)
         ec(a("QV"), a("B5", 0, 192))
-        for k in range(2):
-            cp(ind(a("A", AV[v] + A2 * k, AV[v] + A2 * k + 6144), a("OP", 6 * k, 6 * k + 6)), a("QV", 96 * k, 96 * k + 96))
+        cp(ind(a("A", AV[v], AV[v] + 576), a("OP", 0, 12)), a("QV"))
+        sq = lambda c: a("SQ", c, c + 8, 96)
+        mms([(a("B4", 0, 8, 96), a("TRI", 0, 96, 96), sq(16), False, False), (a("B4", 0, 8, 96), i96, sq(64), False, False),
+             (a("B4", 8, 16, 96), a("TRI", 96, 192, 96), sq(16), False, False), (a("B4", 8, 16, 96), s96("NI"), sq(72), False, True)])
         mm(a("B3", 0, 1, 8), a("SQ", 16, 24, 96), a("ON", 0, 1, 96))
         ec(a("SF", 8, 9, 8), a("B3", 0, 1, 8))
         mm(a("B3", 2, 3), a("G8T", 0, 128, 8), a("SF", 8, 9, 8))
-        top = R + 3071 if v < 2 else ZC
-        win = a("WN", 0, R + 3072 if v < 2 else ZC + 16)
+        win = a("W", 0, R + 3089)
         if v == 2:
-            es(col(9), a("B3", 2, 3), -1.0, nb)
-            relu(a("NV", 0, 192), a("JO", 384, 576), 1.0, col(9))
+            ts(col(9), a("B3", 2, 3), nb, ALU.subtract, 2.0 ** 25, ALU.mult)
+            relu(a("NV"), a("JO", 192, 384), -2.0 ** 25, col(9))
+            es(a("NV"), a("NV"), 1.0, -1.0, "S")
+        else:
+            ts(a(SD, 7, 8), a("B3", 2, 3), nb, ALU.subtract, 3072.0, ALU.min)
+            if AHEAD and v == 0:
+                remote(a("IN1", 0, 8), a(SD, 0, 8), "r9", 0.3)
+
+        own = a("A", AV[v], AV[v] + 384)
+        scan(a("SE"), own, nil(384), 0.0, ALU.add, ALU.add)
+        more(cut, a("MY", 128, 256), own)
+        more(cut, a("MY", 0, 128), a("SE"), True)
+        bank = a("B0", 0, 24)
+        acc(bank, [(one(128), row(5, 24)), (row(8, 128), row(5, 24, 32))], False)
+        mms([(bank, a("MS", 15 - i, 143 - i), a("SE", i, 384, st=16), False, i == 15) for i in range(16)])
+        ts(a("OS", 0, 24), bank, float(R + 16), ALU.add, float(R + 3088), ALU.min)
+        es(a("XM"), cut, -1.0, q="S")
+        hf = lambda c: a("HF", c, c + 16, 96)
+        ts(hf(0), at16, 1.0 / 256, ALU.mult, MAGIC, ALU.add)
+        ts(hf(32), hf(0), MAGIC, ALU.subtract, 256.0, ALU.mult)
+        tt(hf(16), at16, hf(32), ALU.subtract)
+        tt(a("AD", 512, 768), ind(a("HF", 0, 16), a("BC", 0, 16)), a("CD"), ALU.is_lt)
+        tt(a("AD", 0, 256), ind(a("HF", 16, 32), a("BC", 0, 16)), a("CA"), ALU.is_lt)
+        es(a("AD", 256, 512, 96), a("AD", 0, 256, 96), -1.0, 1.0, "S")
+        ad = lambda c: a("AD", c, c + 128, 96)
+        acc(a("B4", 0, 128), [(one(128), row(20, 128)), (row(8, 128), one(128)), (ad(0), ad(513)), (ad(128), ad(641)),
+                              (ad(256), ad(512)), (ad(384), ad(640))])
+        ec(a("XL"), a("B4", 0, 128))
+        cp(a("OX"), ind(a("XL"), a("BC", 128, 129)))
+        tt(a("G1"), ind(win, a("OS", 0, 24)), a("XM"), ALU.min)
+        scan(a("SN"), cut, a("G1"), 0.0, ALU.min, ALU.max)
+        piece = ind(a("SN"), a("OX", 0, 12))
 
         def table():
             es(a("Z3"), ind(a("SQ"), a("BC", 64, 76)), -1.0)
@@ -825,88 +833,59 @@ def rank_program(g, core, T, topo):
                 [(a("B3", 128, 256, 32, p0=32 * (gg // 2)), a("Z3", 48 * (gg // 2) + 16 * (gg % 2), 48 * (gg // 2) + 16 * (gg % 2) + 32, 96),
                   a("OH", 128 * gg, 128 * gg + 128, 96), False, gg % 2 == 1) for gg in range(8)])
             ec(a("TB"), a("B3", 128, 256))
-            pick = lambda bank, k, close: [(a(bank, h, 256, st=2), a("SQ3", 128 * k(h), 128 * k(h) + 128), a("TB"), False, close and h == 1)
-                                           for h in range(2)]
-            if v < 2:
-                for gg in range(8):
-                    es(a("OH2", 128 * gg, 128 * gg + 128, 96), a("OH", 128 * gg, 128 * gg + 128, 96), a("TK", gg, gg + 1, 96), q=OQ)
-                acc(a("B7", 0, 256), [(one(128), row(7)), (row(8, 128), one(256))], False)
-                mms(pick("B7", lambda h: h, False))
-                for h in range(2):
-                    first = lambda gg: 32 * (8 * h + gg) + 16 * (1 - gg % 2)
-                    mms([(a("B7", h, 256, 32, 2, 32 * (gg // 2)), a("P2", first(gg), first(gg) + 32, 96),
-                          a("OH2", 128 * gg, 128 * gg + 128, 96), False, h == 1 and gg % 2 == 1) for gg in range(8)])
-                ts(a("OK2"), a("B7", 0, 256), 32.0, ALU.add, 7199.0, ALU.min)
-            else:
-                acc(a("B0", 0, 256), [(one(128), row(5)), (row(8, 128), one(256))], False)
-                acc(a("B4", 0, 256), [(one(128), row(6)), (row(8, 128), row(9))], False)
-                mms(pick("B4", lambda h: 3, True))
-                mms(pick("B0", lambda h: 2, False))
-                relu(a("OK"), a("B4", 0, 256), -1.0)
-                more(a("B0", 0, 256), a("PS"), a("OK"), True)
-                ts(a("OK2"), a("B0", 0, 256), float(ZC), ALU.min)
 
-        if v == 2:
-            table()
-        srcs = ("B0", "B1", "B4") if v < 2 else ("B6", "B7", "B1")
-        for c in range(3):
-            o = AV[v] + 1024 * c
-            scan(wd(SC, 1024 * c, 1024 * c + 1024), a("A", o, o + 1024), a("A", A2 + o, A2 + o + 1024),
-                 0.0 if c == 0 else wd(SC, 1024 * c - 1, 1024 * c), ALU.add, ALU.add)
-            bank = a(srcs[c], 0, 64)
-            acc(bank, [(one(128), row(7, 64, 64 * c)), (row(8, 128), one(64))], False)
-            mms([(bank, a("MS", 15 - i, 143 - i), a(SC[0], SC[1] + 1024 * c + i, SC[1] + 1024 * c + 1024, st=16), False,
-                  i == 15 and v < 2) for i in range(16)])
-            if v == 2:
-                more(bank, a("PS"), a("NV", 64 * c, 64 * c + 64), True)
-        for c in range(3):
-            ts(a("OS", 64 * c, 64 * c + 64), a(srcs[c], 0, 64), float(R), ALU.add, float(top), ALU.min)
+        table()
         if v < 2:
-            ts(a(SD, 7, 8), a("B3", 2, 3), nb, ALU.subtract, 3072.0, ALU.min)
-            if EARLY:
-                table()
-        if v == 2:
-            gather("TH", 0, win, "OK2", 4096, TQ)
-            for i in range(8):
-                mm(a("B2"), a("MP", 7 - i, 135 - i), a("TH", 512 * i, 512 * i + 512), i == 0, i == 7)
-            ec(a("ZO"), a("B2"))
-            dmas([(ext(T.zu[:]), a("ZO", p=64))], 0.5)
-            dmas([(ext(T.zt[:]), a("ZO", p=64, p0=64))], 0.5)
-        gather("EW", 0, win, "OS", 3072, EQ[v // 2])
-        if v < 2:
-            nx, SG_ = v + 1, "SG%d" % v
+            for gg in range(8):
+                es(a("OH2", 128 * gg, 128 * gg + 128, 96), a("OH", 128 * gg, 128 * gg + 128, 96), a("TK", gg, gg + 1, 96), q=OQ)
+            acc(a("B7", 0, 256), [(one(128), row(7)), (row(8, 128), one(256))], False)
+            mms([(a("B7", h, 256, st=2), a("SQ3", 128 * h, 128 * h + 128), a("TB"), False, False) for h in range(2)])
+            for h in range(2):
+                first = lambda gg: 32 * (8 * h + gg) + 16 * (1 - gg % 2)
+                mms([(a("B7", h, 256, 32, 2, 32 * (gg // 2)), a("P2", first(gg), first(gg) + 32, 96),
+                      a("OH2", 128 * gg, 128 * gg + 128, 96), False, h == 1 and gg % 2 == 1) for gg in range(8)])
+            ts(a("OK2"), a("B7", 0, 256), 32.0, ALU.add, 7199.0, ALU.min)
+            nx = v + 1
+            cp(a("YI", 0, 192), piece)
             for c in range(3):
-                bank = ("B2", "B5", "B4")[c]
-                for o, m in ((0, "MT"), (64, "MU")):
-                    acc(a(bank, o, o + 64), [(a(m, 15 - i, 143 - i), a("EW", 1024 * c + i, 1024 * c + 1024, st=16)) for i in range(16)])
-                cp(a(SD, 128 * c + 8, 128 * c + 136), a(bank, 0, 128))
-                lo = 128 * c + 8 if c else 0
+                x, o = a("YI", 64 * c, 64 * c + 64), 192 + 128 * c
+                ts(a("YI", o, o + 64), x, 4095, ALU.bitwise_and)
+                ts(a("YI", o + 64, o + 128), x, 12, ALU.arith_shift_right)
+                cp(a(SD, 128 * c + 8, 128 * c + 136), a("YI", o, o + 128))
+                lo = 128 * c + 8 if c or (AHEAD and v == 0) else 0
                 remote(a("IN%d" % nx, lo, 128 * c + 136), a(SD, lo, 128 * c + 136), "r%d" % (5 * v + c), 1.2)
-            dmas([(a(SG_, p=64, p0=64 * r), a("EW", p0=r, ps=16)) for r in range(2)], 0.5, [len(ops) - 2])
-            remote(a("SR%d" % nx), a(SG_), "r%d" % (5 * v + 3), 3.6)
-            for o in (AV[nx], AV[nx] + A2):
-                for l in range(o, o + 3072, 1024):
-                    io(a("A", l, l + 1024), [[0, 1024]])
-                    ops[-1]["behind"].add(calls[-1])
-            if not EARLY:
-                table()
             lazy[0] = LZ
             rebuild(nx)
             lazy[0] = False
         else:
-            for c in range(3):
-                bank = ("B3", "B4", "B5")[c]
-                for lo in range(2):
-                    acc(a(bank, 64 * lo, 64 * lo + 64),
-                        [(a("MP", 7 - i, 135 - i), a("EW", 1024 * c + 2 * i + lo, 1024 * c + 1024, st=16)) for i in range(8)])
-                for lo in range(2):
-                    ec(a("YO", 192 * lo + 64 * c, 192 * lo + 64 * c + 64), a(bank, 64 * lo, 64 * lo + 64))
-            dmas([(ext(T.yu[:]), a("YO", p=64)), (ext(T.yt[:]), a("YO", p=64, p0=64))], 0.7)
-
+            def part(y, n, o, out):
+                ts(a("YI", y + n, y + 2 * n), a("YI", y, y + n), 12, ALU.arith_shift_right)
+                ts(a("YI", y + 2 * n, y + 3 * n), a("YI", y, y + n), 4095, ALU.bitwise_and)
+                ec(a(out, 0, n), a("YI", y + n, y + 2 * n))
+                tt(a(out, n, 2 * n), a("YI", y + 2 * n, y + 3 * n), a("YI", y, y + n), ALU.min)
+            mm(a("B6", 0, 8), one(128), nil(8, 1), True, False)
+            mms([(a("B6", k, 8, st=2), a("MB", 15 - i, 143 - i), a("TB", 64 * k + 4 * i, 64 * k + 4 * i + 4), False, k == 1 and i == 15)
+                 for k in range(2) for i in range(16)])
+            for h in range(2):
+                ts(a("OK2", 8 * h, 8 * h + 8), a("B6", 0, 8), 16.0 + 16 * h, ALU.add, float(R + 3088), ALU.min)
+            acc(a("B7", 0, 256), [(one(128), row(6)), (row(8, 128), row(9))], False)
+            mms([(a("B7", 128 * h + 32 * m, 128 * h + 32 * m + 32), a("SQ3", 256, 384), a("TB", m, 128, st=4), False, h == 1 and m == 3)
+                 for h in range(2) for m in range(4)])
+            relu(a("OK"), a("B7", 0, 256), 2.0 ** 25)
+            es(a("OK"), a("OK"), 1.0, -1.0, "S")
+            tt(a("UT"), ind(win, a("OK2", 0, 16)), a("OK"), ALU.min)
+            issue("V", lambda q: g.vector.transpose(T.MX[:], T.UT[:]), [a("UT")], [a("MX")], CALL + CY * 256)
+            cp(a("YI", 576, 832), ind(a("MX"), a("BC", 96, 112)))
+            part(576, 256, 0, "ZO")
+            dmas([(ext(z[h::2, :]), a("ZO", 256 * k + 128 * h, 256 * k + 128 * h + 128))
+                  for k, z in enumerate((T.zu, T.zt)) for h in range(2)], 1.0)
+            tt(a("YI", 0, 192), piece, a("NV"), ALU.min)
+            part(0, 192, 0, "YO")
+            dmas([(ext(T.yu[:]), a("YO", 0, 192)), (ext(T.yt[:]), a("YO", 192, 384))], 0.7)
 
     if not PLAN:
         PLAN["ops"] = ops
-        PLAN["order"], PLAN["on"] = settle(ops) if PASSES else arrange(ops)
+        PLAN["order"], PLAN["on"] = settle(ops)
     order = PLAN["order"]
     cnt, fin, seen = {}, {"sent": sent[0]}, {q: {} for q in Q}
     for k in order:

@@ -1,3 +1,4 @@
+import math
 import numpy as np
 from concourse.mybir import AluOpType as ALU, AxisListType as AX, ActivationFunctionType as ACT
 
@@ -11,47 +12,53 @@ CY, PC, GA, SCA, CALL, SAME, HAND, LDMA, RDMA, RCALL = 0.87e-3, 0.44e-3, 1.25e-3
 PASSES, LEAN, PHAND, FIRST = 8, 0.0, 0.26, 2.0
 LOADS = "bt pt t0 t1 bk bl pu l8 bu"
 XQ, WQ, OQ, CQ, RQ, GR, GW, LZ, AHEAD = "EEEEEE", "EEEEEE", "E", "E", ("E", "E"), 1024, 512, False, True
-WAIT = (0, 6, 6)
-ROUNDS, ALSO = 1200, ((1.0, (1.0, 1.3, 1.4, 1.0)), (1.0, (1.3, 1.3, 1.0, 1.2)), (1.0, (1.0, 1.0, 1.4, 1.6)))
+WAIT, MOVES = 0, 12000
+ROUNDS, ALSO = 1000, ((0.8, ((1.4, 1.0), 1.3, 1.3, 1.0, 1.1, 1.2)), (0.8, ((1.0, 1.4), 1.0, 1.0, 1.5, 1.0, 1.0)),
+                      (0.8, ((1.0, 1.0), 1.0, 1.4, 1.3, 0.75, 1.8)), (0.7, ((1.2, 1.2), 1.5, 2.0, 1.0, 1.25, 1.0)))
 SB = {
-    "TON": ([128, 4096], BF), "PT": ([128, 4096], BF), "BIG": ([128, KEND], BF), "WN": ([128, 4096], BF),
-    "PR": ([128, 3072], BF), "SC": ([128, 3072], BF), "CW": ([128, 3072], BF), "TH": ([128, 4096], BF),
+    "TON": ([128, 4096], BF), "BIG": ([128, KEND], BF), "PS": ([128, 6144], BF),
+    "T0": ([128, 512], BF), "PN": ([128, 192], F), "PD": ([128, 384], BF), "PK": ([128, 128], BF), "SB2": ([128, 272], BF),
     "W": ([128, 13344], F), "A": ([128, 1344], BF), "SE": ([128, 384], BF), "XM": ([128, 384], BF),
-    "G1": ([128, 384], F), "SN": ([128, 384], F), "YI": ([128, 1344], I), "HT": ([128, 384], H),
+    "G1": ([128, 384], F), "SN": ([128, 384], F), "YI": ([128, 896], I), "HT": ([128, 384], H),
     "LIN": ([128, 192], F), "LIB": ([128, 256], F), "HF": ([128, 48], F), "AD": ([128, 784], BF), "XL": ([128, 128], F),
     "OX": ([128, 16], U), "CD": ([128, 256], F), "CA": ([128, 256], BF), "MY": ([128, 256], BF), "TRI": ([128, 192], BF),
     "IN0": ([128, 392], U), "IN1": ([128, 392], U), "IN2": ([128, 392], U), "SD0": ([128, 392], U), "SD1": ([128, 392], U),
-    "NQ": ([128, 512], BF), "NL": ([128, 192], BF), "DF": ([128, 384], BF), "MN": ([128, 864], BF),
-    "UT": ([128, 256], F), "ZB": ([128, 1024], BF),
+    "NQ": ([128, 512], BF), "NL": ([128, 192], BF), "DF": ([128, 384], BF), "MN": ([128, 576], BF),
+    "UT": ([128, 256], F), "ZB": ([128, 528], BF),
     "L2": ([128, 384], I), "L3": ([128, 768], I), "LB": ([128, 8], I), "LBF": ([128, 32], F), "LS": ([128, 136], I), "LSF": ([128, 272], F),
     "ST": ([128, 256], BF),
     "ON": ([128, 256], BF), "ONF": ([128, 256], F),
     "IB": ([128, 128], BF), "NS": ([128, 128], BF), "NB": ([128, 128], BF), "NI": ([128, 128], BF),
     "P32": ([128, 128], BF), "EA": ([128, 128], BF), "EB": ([128, 128], BF), "I3": ([128, 128], BF), "I4K": ([128, 128], BF),
     "E8": ([128, 256], F), "SG": ([128, 256], BF),
-    "IS": ([128, 128], BF), "I16": ([128, 128], BF), "CAP": ([128, 256], BF), "IL": ([128, 128], BF),
+    "IS": ([128, 128], BF), "I16": ([128, 128], BF), "CAP": ([128, 256], BF),
     "FY": ([128, 256], BF), "RM": ([128, 512], BF), "YY": ([128, 256], BF),
     "G4": ([128, 160], BF), "G8": ([128, 16], BF), "G8T": ([128, 256], F),
     "G8B": ([128, 16], BF), "ROW": ([128, 5632], BF), "ROF": ([128, 1040], F), "JO": ([128, 384], F),
     "COL": ([128, 16], F), "CI": ([128, 8], I), "BC": ([128, 144], U), "BCF": ([128, 176], F),
-    "MI": ([128, 128], BF), "M6": ([128, 384], BF), "RR": ([128, 128], F),
-    "R6": ([128, 48], BF), "OH2": ([128, 1024], BF), "PL": ([128, 128], BF), "P5": ([128, 128], BF), "P15": ([128, 128], BF),
-    "N15": ([128, 128], BF), "N9": ([128, 128], BF), "T12": ([128, 48], BF), "PM": ([128, 96], BF), "PMT": ([128, 96], BF), "CC1": ([128, 128], BF),
+    "E6": ([128, 224], BF), "MI": ([128, 256], BF), "LC": ([128, 256], BF), "RR": ([128, 128], F),
+    "OH2": ([128, 1024], BF), "PL": ([128, 128], BF), "P5": ([128, 128], BF), "P15": ([128, 128], BF),
+    "N63": ([128, 128], BF), "N15": ([128, 128], BF), "N9": ([128, 128], BF), "CC1": ([128, 128], BF),
     "SL2": ([128, 160], BF), "MS": ([128, 144], BF), "MB": ([128, 144], BF),
     "WB": ([128, 240], BF), "SQ3": ([128, 384], BF), "THL": ([128, 96], F), "TMP": ([128, 192], BF),
     "NE": ([128, 272], BF), "N12": ([128, 192], BF), "SH32": ([128, 128], BF),
     "CK": ([128, 256], BF), "KK": ([128, 256], BF), "LN": ([128, 256], BF), "FS": ([128, 256], BF),
     "MX": ([128, 256], F), "OK": ([128, 256], BF), "TT": ([128, 512], BF), "P2": ([128, 528], BF),
     "NB0": ([128, 272], BF),
-    "SM": ([128, 48], BF), "SF": ([128, 16], F), "TK": ([128, 80], F), "SQ": ([128, 112], BF),
-    "OH": ([128, 1024], BF), "LC": ([128, 384], BF), "PB": ([128, 256], BF), "QQ": ([128, 256], BF),
+    "SM": ([128, 576], BF), "SF": ([128, 16], F), "TK": ([128, 80], F), "SQ": ([128, 112], BF),
+    "OH": ([128, 1024], BF), "QQ": ([128, 256], BF),
     "Z3": ([128, 192], BF), "TB": ([128, 128], BF), "TBW": ([128, 144], BF), "GT": ([128, 96], BF), "QV": ([128, 192], BF),
     "OC": ([128, 8], U), "OP": ([128, 16], U), "OD": ([128, 192], U), "OS": ([128, 32], U),
     "OK2": ([128, 256], U), "OB": ([128, 256], U), "OE": ([128, 8], U), "EV": ([128, 128], BF),
     "NV": ([128, 192], BF), "YO": ([128, 384], F), "ZO": ([128, 512], F),
 }
+PACK, SANY, QUART, AGAIN, FILLD = False, True, 1, False, False
+SB.update({"TP": ([128, 4096], F), "XF": ([128, 3072], F)} if PACK else {"PT": ([128, 4096], BF), "CW": ([128, 3072], BF)})
+LIES = {"PR": ("PS", 0, 3072), "SC": ("PS", 3072, 3072), "TH": ("PS", 0, 4096), "WN": ("BIG", KB + 32, 4096), "RW": ("BIG", KA + 32, 4096)}
+ZERO, STEP = 65.0 / 2048, 2.0 ** -20
+GDMA, GFIRST = 0.6, 1.5
 POOL = {}
-for _p, _names in (("CB", "IB NI NS NB P32 EA EB IS I16 PL P5 P15 N15 N9 CAP IL I3 I4K MI CC1 PM PMT R6 T12 SL2 G4 G8 CA MY TRI MS MB WB"),
+for _p, _names in (("CB", "IB NI NS NB P32 EA EB IS I16 PL P5 P15 N15 N9 CAP I3 I4K CC1 E6 SL2 G4 G8 CA MY TRI MS MB WB"),
                    ("CF", "RR E8 G8T THL CD")):
     _o = 0
     for _n in _names.split():
@@ -63,7 +70,7 @@ SB["DL"] = ([8, 13328], F)
 SCRATCH["DL"] = ("dram",) + SB["DL"]
 for _b in range(8):
     SCRATCH["B%d" % _b] = ("psum", [128, 512], F)
-SEMAPHORES = ["qV", "qS", "qP", "qG", "sent"] + ["d%d" % k for k in range(32)] + ["r%d" % k for k in range(10)]
+SEMAPHORES = ["qV", "qS", "qP", "qG", "sent"] + ["d%d" % k for k in range(48)] + ["r%d" % k for k in range(10)]
 LOW = 2.0 ** -93
 AID = 3 * ({1: "B7", 3: "B6"},)
 ALONE = (True, True, True)
@@ -82,7 +89,9 @@ def settle(ops):
     for k in range(n):
         for j in loose[0][k]:
             loose[1][j].add(k)
-    way = ["R" if o["q"] == "G" else "D" for o in ops]
+    hard = [[[j for j in x[k] if j not in y[k]] for k in range(n)] for x, y in zip((before, after), loose)]
+    gap = {p + q: (0.0 if q == "P" else SAME) if p == q else (PHAND if p == "P" else HAND) for p in "VSPGY" for q in "VSPGY"}
+    way = ["R" if o["sem"] and o["sem"][0][0] == "r" else "D" for o in ops]
 
     def sweep(rank, back):
         src, dst = (after, before) if back else (before, after)
@@ -106,8 +115,11 @@ def settle(ops):
             k = k[1]
             o, best = ops[k], None
             for q in ("VS" if o["q"] == "E" else o["q"]):
-                t = max([t1[j] + ((0.0 if q == "P" else SAME) if on[j] == q else (PHAND if "P" == (q if back else on[j]) else HAND))
-                         for j in src[k] if not loose[back][k] or j not in loose[back][k]] + [0.0])
+                t = 0.0
+                for j in hard[back][k]:
+                    e = t1[j] + (gap[q + on[j]] if back else gap[on[j] + q])
+                    if e > t:
+                        t = e
                 d = o["cost"][q == "V"]
                 if back:
                     if o["move"]:
@@ -138,19 +150,19 @@ def settle(ops):
     rank = [0.0] * n
     for k in range(n - 1, -1, -1):
         rank[k] = min(rank[j] for j in after[k]) - 1e-4 if ops[k]["lazy"] and after[k] else k
-    def replay(order, on, slow, pe, hand, far):
+    def replay(order, on, slow, pe, hand, far, ga, near):
         end, free = [0.0] * n, {q: 0.0 for q in "VSPGYDR"}
         for k in order:
             o, q = ops[k], on[k]
             t = max([free[q]] + [end[j] + (0.0 if q == on[j] == "P" else hand * (PHAND if on[j] == "P" else HAND)) for j in o["deps"]])
-            free[q] = t + o["cost"][q == "V"] * (pe if q == "P" else slow)
+            free[q] = t + o["cost"][q == "V"] * (pe if q == "P" else slow[q == "V"] * (ga if o["ga"] else 1.0))
             end[k] = free[q] + o["lat"] * far
             if o["move"]:
-                free[way[k]] = end[k] = max(end[k], free[way[k]]) + o["move"] * far
+                free[way[k]] = end[k] = max(end[k], free[way[k]]) + o["move"] * (far if way[k] == "R" else near)
         return max(end)
 
-    def mixed(r):
-        x = (np.arange(n + 4, dtype=np.uint64) + np.uint64(r * 7919 * 4096 + 1)) * np.uint64(0x9E3779B97F4A7C15)
+    def mixed(r, m=n + 4):
+        x = (np.arange(m, dtype=np.uint64) + np.uint64(r * 7919 * 4096 + 1)) * np.uint64(0x9E3779B97F4A7C15)
         x = (x ^ (x >> np.uint64(31))) * np.uint64(0xBF58476D1CE4E5B9)
         return (x >> np.uint64(40)).astype(float) / 2 ** 24
 
@@ -170,7 +182,87 @@ def settle(ops):
         if r < PASSES or (r - PASSES) % 2 == 0:
             rank = [-x for x in sweep([-x for x in t1], True)[1]]
     PLAN["time"], PLAN["worth"] = kept[3], kept[0]
-    return kept[4], kept[2]
+    return polish(ops, kept[4], kept[2], way, mixed)
+
+
+def polish(ops, order, on, way, mixed):
+    n = len(ops)
+    deps = [sorted(o["deps"]) for o in ops]
+    must = [o["deps"] | o["behind"] for o in ops]
+    cases = ((1.0, ((1.0, 1.0),) + 5 * (1.0,)),) + ALSO
+
+    def replay(order, on, slow, pe, hand, far, ga, near, why=None):
+        end, free, last = [0.0] * n, dict.fromkeys("VSPGYDR", 0.0), {}
+        hp, hh = hand * PHAND, hand * HAND
+        for k in order:
+            o, q = ops[k], on[k]
+            t, w = free[q], -1
+            for j in deps[k]:
+                e = end[j] + ((0.0 if q == "P" else hp) if on[j] == "P" else hh)
+                if e > t:
+                    t, w = e, j
+            if why:
+                why[k], last[q] = (w, False) if w >= 0 else (last.get(q), True), k
+            t += o["cost"][q == "V"] * (pe if q == "P" else slow[q == "V"] * (ga if o["ga"] else 1.0))
+            free[q] = t
+            if o["move"]:
+                t, x = t + o["lat"] * far, way[k]
+                if free[x] > t:
+                    t = free[x]
+                    if why:
+                        why[k] = (last.get(x), True)
+                last[x] = k
+                free[x] = t = t + o["move"] * (far if x == "R" else near)
+            end[k] = t
+        return end
+
+    worth = lambda order, on: sum(w * max(replay(order, on, *x)) for w, x in cases)
+    now, links = worth(order, on), None
+    kept = (now, order, on)
+    for r in range(MOVES):
+        u = mixed(10 ** 6 + r, 5)
+        if links is None:
+            why = [0] * n
+            end = replay(order, on, *cases[int(u[4] * len(cases))][1], why)
+            k, links, either = end.index(max(end)), [], []
+            while k is not None:
+                j, queued = why[k]
+                either += [k] * (ops[k]["q"] == "E")
+                links += [(j, k)] * (queued and j is not None)
+                k = j
+            place = {k: i for i, k in enumerate(order)}
+        order2, on2 = order, on
+        if u[0] < 0.3:
+            k = either[int(u[1] * len(either))]
+            on2 = on[:k] + ["S" if on[k] == "V" else "V"] + on[k + 1:]
+        else:
+            j, k = links[int(u[1] * len(links))]
+            lo, hi, up = place[j], place[k], u[0] < 0.65
+            for _ in range(int(u[2] * 3)):
+                far = [i for i in (range(lo - 1, -1, -1) if up else range(hi + 1, n)) if on[order[i]] == on[k]][:1]
+                lo, hi = (far[0] if far and up else lo), (far[0] if far and not up else hi)
+            if up:
+                need, moved = set(must[k]), {k}
+                for x in order[hi - 1:lo - 1 if lo else None:-1]:
+                    if x in need:
+                        need |= must[x]
+                        moved.add(x)
+            else:
+                moved = {j}
+                for x in order[lo + 1:hi + 1]:
+                    if must[x] & moved:
+                        moved.add(x)
+            if order[lo if up else hi] in moved or lo <= max(place[x] for x in range(len(LOADS.split()))):
+                continue
+            part = order[lo:hi + 1]
+            order2 = order[:lo] + [x for x in part if (x in moved) == up] + [x for x in part if (x in moved) != up] + order[hi + 1:]
+        w = worth(order2, on2)
+        if w < now or u[3] < math.exp((now - w) / (0.04 * (1 - r / MOVES) + 1e-3)):
+            order, on, now, links = order2, on2, w, None
+            if w < kept[0]:
+                kept = (w, order, on)
+    PLAN["time"], PLAN["worth"] = max(replay(kept[1], kept[2], *cases[0][1])), kept[0]
+    return kept[1], kept[2]
 
 
 def rank_program(g, core, T, topo):
@@ -179,12 +271,14 @@ def rank_program(g, core, T, topo):
         return
     nxt, prv = T.cores[(rank + 3) % 8], T.cores[(rank - 3) % 8]
     Q = {"V": g.vector, "S": g.scalar, "P": g.tensor, "G": g, "Y": g.sync}
-    ops, hist, nd, lazy = [], {}, [0], [False]
+    ops, hist, nd, lazy, cast = [], {}, [0], [False], []
 
     def a(n, c0=None, c1=None, p=128, st=1, p0=0, ps=1):
-        w = SB[n][0][1] if n in SB else 512
+        w = SB[n][0][1] if n in SB else (LIES[n][2] if n in LIES else 512)
         c0 = 0 if c0 is None else c0
         c1 = w if c1 is None else c1
+        if n in LIES:
+            n, c0, c1 = LIES[n][0], c0 + LIES[n][1], c1 + LIES[n][1]
         t, o = (T[POOL[n][0]], POOL[n][1]) if n in POOL else (T[n], 0)
         ap = t[p0:p0 + p, o + c0:o + c1:st] if st > 1 else (t[p0::ps, o + c0:o + c1] if ps > 1 else t[p0:p0 + p, o + c0:o + c1])
         return (ap, [(n, c0, c1, st)], (c1 - c0 + st - 1) // st, False)
@@ -219,7 +313,7 @@ def rank_program(g, core, T, topo):
             h.append((c0, c1, isw, k, st))
         deps.discard(k)
         ops.append({"q": q, "fn": fn, "deps": deps, "cost": cost if isinstance(cost, tuple) else (cost, cost), "lat": lat,
-                    "move": move, "sem": sem, "lazy": lazy[0], "behind": set(), "name": (rw[-1][0][:2], rw[0][0][:2]) if rw else ()})
+                    "move": move, "sem": sem, "ga": any(x[3] for x in reads + writes), "lazy": lazy[0], "behind": set(), "name": (rw[-1][0][:2], rw[0][0][:2]) if rw else ()})
         return ops[k]
 
     def price(o, ins, f=1.0):
@@ -241,7 +335,11 @@ def rank_program(g, core, T, topo):
         def fn(q):
             for o, i in items:
                 Q[q].dma_start(o[0], i[0]).then_inc(T.sem[sem], 16)
-        issue(q, fn, [i for o, i in items], [o for o, i in items], CALL * len(items), LDMA, move, (sem, 16 * len(items)), after)
+        cost = CALL * len(items)
+        if q == "G":
+            cost = GDMA * len(items) + (0.0 if cast else GFIRST)
+            cast.append(sem)
+        issue(q, fn, [i for o, i in items], [o for o, i in items], cost, LDMA, move, (sem, 16 * len(items)), after)
         return len(ops) - 1
 
     def sc(x):
@@ -251,7 +349,12 @@ def rank_program(g, core, T, topo):
         return [x for x in xs if isinstance(x, tuple)]
 
     def cp(o, i):
+        if SANY and not o[3]:
+            return ec(o, i)
         issue("V", lambda q: g.vector.tensor_copy(o[0], i[0]), [i], [o], price(o, [i]))
+
+    def shift(o, i, scale, bias):
+        es(o, i, scale, bias, "E" if SANY else "V")
 
     def tt(o, x, y, op):
         issue("V", lambda q: g.vector.tensor_tensor(o[0], x[0], y[0], op), [x, y], [o],
@@ -333,7 +436,8 @@ def rank_program(g, core, T, topo):
         sel(o, tmp, pat, ALU.is_ge, hi, -1)
 
     col = lambda k, p=128: a("COL", k, k + 1, p)
-    sm = lambda c, w=8, p=96: a("SM", c, c + w, p)
+    sm = lambda c: a("SM", 18 * c + 15, 18 * c + 143, 96, 16)
+    smi = lambda c, i: a("SM", 18 * c + 15 - i, 18 * c + 143 - i, 96)
     i96 = a("IB", 0, 96, 96)
     s96 = lambda n: a(n, 0, 96, 96)
     one = lambda m: a("ON", 0, m, 1)
@@ -344,6 +448,7 @@ def rank_program(g, core, T, topo):
 
     def count(W, gs, tb, cb, q="E"):
         n, off = 16 * gs, gs - 8
+        TH = "TH" if off or PACK else "PT"
         if off:
             mms([(a(tb, W * j, W * j + W), a("YY", 128 * (j % 2), 128 * (j % 2) + 128, W), a("IS" if j // 2 else "IB", 0, W, W), True, True)
                  for j in range(4)])
@@ -357,17 +462,21 @@ def rank_program(g, core, T, topo):
         sums = a(cb, 0, n, W)
         mm(sums, one(W), row(13, n) if off else nil(n, 1), True, False)
         for k in range(8):
-            o, x, hi = a("TH", 512 * k, 512 * k + 4 * W), a("TT", 0, 4 * W), LOW * 64.0 ** (2 * k + 1)
+            o, x, hi = a(TH, 512 * k, 512 * k + 4 * W), a("TT", 0, 4 * W), LOW * 64.0 ** (2 * k + 1)
             op = issue(q, lambda q, o=o, x=x, hi=hi:
                        g.vector.tensor_scalar(o[0], x[0], hi, hi, ALU.min, ALU.subtract) if q == "V" else
                        g.scalar.activation(o[0], x[0], ACT.Relu, bias=hi, scale=-1.0),
                        [x], [o], (CALL + CY * 4 * W, CALL + CY * 2 * W))
             wt = lambda q, op=op, k=k: a("G4", 0, 64) if q else a("G4", 4 * k + 32 * (op["q"] == "V"), 4 * k + 32 * (op["q"] == "V") + 4)
-            mms([(a(cb, off + k + 4 * gs * j, 4 * gs * (j + 1), W, gs), a("TH", 512 * k + W * j, 512 * k + W * j + W), wt,
+            mms([(a(cb, off + k + 4 * gs * j, 4 * gs * (j + 1), W, gs), a(TH, 512 * k + W * j, 512 * k + W * j + W), wt,
                   False, k == 7 and j == 3) for j in range(4)])
         es(a("P2", 1, 2 * n, W, 2), sums, 1.0 / 64, 128.25)
-        es(a("UT", 0, n, W), a("P2", 1, 2 * n, W, 2), 63.0, -8192.0)
-        tt(a("P2", 0, 2 * n, W, 2), sums, a("UT", 0, n, W), ALU.subtract)
+        if AGAIN:
+            more(sums, a("N63", 0, W, W), a("P2", 1, 2 * n, W, 2), True)
+            es(a("P2", 0, 2 * n, W, 2), sums, 1.0, 8192.0)
+        else:
+            es(a("UT", 0, n, W), a("P2", 1, 2 * n, W, 2), 63.0, -8192.0)
+            tt(a("P2", 0, 2 * n, W, 2), sums, a("UT", 0, n, W), ALU.subtract)
 
     def w2b(bank, wide, c, rhs, close):
         mms([(a(bank, s, 256, 32, 32, 32 * c), a(wide[0], wide[1] + 1024 * c + s, wide[1] + 1024 * c + 1024, st=32), rhs,
@@ -386,23 +495,38 @@ def rank_program(g, core, T, topo):
              "bk": ([(a("L3", 512, 768), ext(T.bk[:]))], 0.6), "pu": ([(a("L2", 192, 384), ext(T.pu[:]))], 0.5),
              "t0": ([(a("TON", 0, 2048), ext(T.tones[:, 0:2048]))], 1.8), "t1": ([(a("TON", 2048, 4096), ext(T.tones[:, 2048:4096]))], 1.8),
              "bl": ([(a("LS", 0, 128, 8), ext(T.bl[:])), (a("LS", 128, 129, 8), ext(T.pn[:])), (a("LS", 129, 130, 8), ext(T.th[:]))], 0.1),
+             "z": ([(a("T0", 0, 256), ext(T.tones[0::16, :]))], 0.4),
              "l8": ([(a("LB", 0, 8), ext(T.bl[:]))], 0.25), "bu": ([(a("L3", 0, 256), ext(T.bu[:]))], 0.6)}
     for k, n in enumerate(LOADS.split()):
         dmas(*loads[n], q="YS"[k % 2])
 
-    ms(a("ZB", 0, 1024), 0.0)
+    ms(a("ZB"), 0.0)
     ms(a("ON"), 1.0)
     ms(a("ONF"), 1.0)
-    for l in range(0, 4096, 1024):
-        fill(a("PT", l, l + 1024), 0.0)
-    ms(a("SC", 0, KA // 4), 99.0)
-    lazy[0] = True
+    if FILLD:
+        ms(a("SC", 1024, 1024 + KA // 4), 99.0)
     diag = [[1, 128]]
     put(a("IB"), nil(128), diag, 0, 1.0)
+    if PACK:
+        ec(a("PK", p=16), nil(128, 16))
+        x = a("PK", 0, 128, 16, 16)
+        put(x, x, [[1, 8]], 0, 1.0)
+        put(x, x, [[1, 8]], 8, STEP)
+        ts(a("T0", 0, 256), a("T0", 0, 256), 0.0, ALU.is_equal, ZERO, ALU.mult)
+        es(a("T0", 256, 512), a("L3", 512, 768), 1.0, -63.0)
+        last = dmas([(a("RW", p=8, p0=8 * k), a("T0", 256 * k, 256 * k + 256)) for k in range(2)], 0.8)
+        for j in range(8):
+            bank, l = a("B%d" % (0, 1, 2, 4, 5)[j % 5]), 512 * j
+            acc(bank, [(a("IB"), a("TON", l, l + 512)), (a("PK", p=16), a("RW", l, l + 512, 16))])
+            ec(a("TP", l, l + 512), bank)
+    lazy[0] = True
+    if PACK:
+        ec(a("SB2"), nil(272))
+        put(a("SB2", 1, 257, st=2), nil(128), diag, 0, 32 / STEP)
+        es(row(21), one(256), 2048.0)
     for n, v in (("NI", -1.0), ("P32", 32768.0), ("EA", float(KA)), ("EB", float(KB)), ("I4K", 4096.0),
                  ("NS", -16384.0), ("NB", -float(2 ** 25)), ("IS", 64.0 ** -16), ("I16", 16.0),
-                 ("PL", 2.0 ** 15 + 2 ** 9), ("P5", 2.0 ** -5), ("P15", 2.0 ** -15), ("N15", -2.0 ** -15), ("N9", -2.0 ** -9),
-                 ("IL", LOW / 2)):
+                 ("PL", 2.0 ** 15 + 2 ** 9), ("P5", 2.0 ** -5), ("P15", 2.0 ** -15), ("N15", -2.0 ** -15), ("N9", -2.0 ** -9)):
         es(a(n), a("IB"), v)
     sel(a("I3"), a("IB"), [[0, 8], [-1, 16]], ALU.is_ge, 2, 0)
     sel(a("SG"), a("ON"), [[0, 8], [1, 32]], ALU.is_gt, 0, 0)
@@ -451,28 +575,21 @@ def rank_program(g, core, T, topo):
     es(row(18, 384), nil(384, 1), 1.0, -2.0 ** 26)
     io(row(20, 128), [[0, 8], [16, 16]])
     io(a("ROF", 0, 256, 1), [[1, 16], [512, 8], [0, 2]])
-    io(a("ROF", 256, 268, 1), [[34, 2], [128, 6]], 79)
+    io(a("ROF", 256, 268, 1), [[34, 2], [2048, 6]], 79)
     sel(a("ROF", 272, 528, 1), a("ONF", p=1), [[-1, 2], [0, 8], [1, 16]], ALU.is_equal, 0, 0)
     io(a("ROF", 528, 656, 1), [[1, 64], [0, 2]])
     io(a("ROF", 656, 784, 1), [[0, 64], [32, 2]])
-    io(a("ROF", 784, 912, 1), [[0, 8], [768, 16]])
+    io(a("ROF", 784, 912, 1), [[0, 8], [128, 16]])
     es(a("ROF", 912, 1040, 1), a("ONF", 0, 128, 1), 1.0 / 32)
-    sel(a("M6", 0, 128), a("ON", 0, 128), [[0, 8], [6, 16]], ALU.is_gt, 0, -1)
-    band(a("M6", 128, 384), a("PB"), a("ON"), [[0, 16], [6, 16]], 0, 5)
-    put(a("PM"), nil(96), [[1, 6], [6, 16]], 0, 1.0)
-    put(a("PMT"), nil(96), [[1, 16], [16, 6]], 0, 1.0)
-    sel(a("T12", 0, 12), a("ON", 0, 12), [[16, 2], [16, 6]], ALU.is_gt, 0, -1)
-    io(a("T12", 12, 24), [[0, 12]], -1)
-    band(a("T12", 12, 24), a("T12", 24, 36), a("T12", 12, 24), [[0, 2], [16, 6]], 0, 15)
-    mm(a("B4", 0, 24, 96), a("PMT", p=96), a("T12", 0, 24, 96))
-    es(a("R6", 0, 12, 96), a("B4", 0, 12, 96), 2.0 ** -4)
-    es(a("R6", 12, 24, 96), a("B4", 12, 24, 96), 2.0 ** -19)
-    es(a("R6", 24, 30, 96), a("B4", 12, 18, 96), -2.0 ** -13)
-    es(a("R6", 32, 44), a("ON", 0, 12), 1.0 / 16)
+    sel(a("E6", 0, 192), nil(192), [[-1, 16], [-1, 2], [-16, 6]], ALU.is_ge, 0, 1, 2.0 ** -4)
+    for o, v in ((192, -2.0 ** -19), (198, -2.0 ** -19), (204, 2.0 ** -13)):
+        es(a("E6", o, o + 6), a("G8", 0, 6), v)
     three = ("MS", "MB", "WB")
     ec((T.CB[:, POOL["MS"][1]:POOL["MS"][1] + 528], [a(n)[1][0] for n in three], 528, False), nil(528))
-    for n in ("TBW", "SM", "SQ", "HF"):
+    for n in ("TBW", "SQ", "HF"):
         ec(a(n), nil(SB[n][0][1]))
+    for l in (0, 288):
+        ec(a("SM", l, l + 288), nil(288))
     ec(a("AD", 768, 784), nil(16))
     es(a("SQ", 88, 96), a("ON", 0, 8), 1.0)
     es(a("SQ", 96, 104), a("ON", 0, 8), -1.0)
@@ -510,12 +627,9 @@ def rank_program(g, core, T, topo):
     ec(a("DF", 256, 384), nil(128))
     put(a("DF", 256, 384, st=16), nil(8), grp, 15, -1.0)
     put(a("MN", 0, 288), nil(288), [[16, 9], [1000, 2], [1, 16]], -1000, 1.0)
-    es(a("MN", 288, 576), a("MN", 0, 288), 63.0)
-    es(a("MN", 576, 864), a("MN", 0, 288), 16384.0)
+    es(a("MN", 288, 576), a("MN", 0, 288), 16384.0)
     io(row(16), [[0, 8], [1, 32]], -159)
     io(row(17), [[0, 8], [1, 32]], 64)
-    ec(row(14), nil(256, 1))
-    ec(row(15), a("SG", p=1))
     for o in (KA, KB):
         ec(a("BIG", o, o + 32), nil(32))
     for n in ("SD0", "SD1"):
@@ -527,7 +641,6 @@ def rank_program(g, core, T, topo):
     es(col(1), col(0), 2.0)
     ts(col(2), col(0), 15.0, ALU.is_equal, -16384.0, ALU.mult)
     es(col(10), col(0), 256.0)
-    ts(a("MI"), a("RR"), col(0), ALU.is_equal)
     io(a("JO", 0, 192), [[32, 96], [1, 2]], 1)
     io(a("JO", 192, 384), [[16, 192]])
     put(a("SH32"), nil(128), diag, 1, 32768.0)
@@ -539,8 +652,10 @@ def rank_program(g, core, T, topo):
     ec(a("MX"), nil(256))
     for o in AV:
         es(a("A", o, o + 384), nil(384), 1.0, col(2))
-    io(a("BCF", 0, 32), [[1, 32]])
-    io(a("BCF", 32, 48), [[0, 2], [1, 8]], 16)
+    io(a("BCF", 0, 16), [[1, 16]])
+    io(a("BCF", 16, 32), [[144, 2], [16, 8]], 159)
+    for h in range(2):
+        ts(a("MI", 128 * h, 128 * h + 128), a("RR"), col(0), ALU.is_equal)
     io(a("BCF", 80, 104), [[0, 24]], 10)
     for o, picks in ((80, ((16, 0, 0), (16, 1, 8), (16, 14, 88), (16, 15, 64))),
                      (88, ((16, 0, 0), (16, 1, 8), (18, 2, 24), (18, 3, 32), (16, 14, 96), (16, 15, 72))),
@@ -559,7 +674,8 @@ def rank_program(g, core, T, topo):
     io(a("BCF", 144, 160), [[32, 8], [0, 2]], 31)
     io(a("BCF", 160, 162), [[0, 2]], 0, 1)
     cp(a("BC", 0, 16), a("BCF", 0, 16))
-    cp(a("BC", 16, 76), a("BCF", 16, 76))
+    cp(a("BC", 16, 32), a("BCF", 16, 32))
+    cp(a("BC", 48, 76), a("BCF", 48, 76))
     cp(a("BC", 80, 96), a("BCF", 112, 128))
     cp(a("BC", 96, 130), a("BCF", 128, 162))
 
@@ -568,27 +684,31 @@ def rank_program(g, core, T, topo):
     es(a("FY"), a("NB0", 0, 256), 63.0, 1.0)
     scan(a("YY"), a("FY"), a("CAP"), LOW, ALU.mult, ALU.min)
     count(128, 8, "B6", "B3")
-    es(a("ST"), a("L3", 512, 768), 32.0, 32.0)
-    last = dmas([(a("PT", p0=0, ps=16), a("ST"))], 0.4)
-    ops[dmas([(a("BIG", l, l + KA // 4), a("SC", 0, KA // 4)) for l in range(0, KA, KA // 4)], 4.0)]["behind"].add(last)
-    last = len(ops) - 1
+    if not PACK:
+        es(a("ST"), a("L3", 512, 768), 32.0, 32.0)
+        last = dmas([(a("PT", p0=0, ps=16), a("ST"))], 0.4)
+    if FILLD:
+        dmas([(a("BIG", l, l + KA // 4), a("SC", 1024, 1024 + KA // 4)) for l in range(0, KA, KA // 4)], 4.0)
+    lazy[0] = True
+    for l in range(0, 0 if FILLD else KA, KA // 8):
+        fill(a("BIG", l, l + KA // 8), 99.0)
+    lazy[0] = False
     for l in range(2):
         cp(a("IN0", 8 + 192 * l, 200 + 192 * l), a("L2", 192 * l, 192 * l + 192))
     cp(a("OB"), a("L3", 256, 512))
     mm(a("B7", 0, 256), a("ONF", 0, 128, 1), a("ROF", 0, 256, 1), True, False)
     mms([(a("B7", h, 256, st=2), a("P2", 128 * h, 128 * h + 128), a("I16"), False, h == 1) for h in range(2)])
-    ts(a("OK2"), a("B7", 0, 256), -2048.0, ALU.add)
+    shift(a("OK2"), a("B7", 0, 256), 1.0, -2048.0)
     ms(a("P2", 512, 528), 159.0)
     lazy[0] = True
-    es(a("LIB"), a("L3", 0, 256), 4096.0)
-    tt(a("LIB"), a("LIB"), a("L3", 256, 512), ALU.add)
+    es(a("B5", 0, 256), a("L3", 0, 256), 4096.0)
+    tt(a("LIB"), a("L3", 256, 512), a("B5", 0, 256), ALU.add)
     dmas([(a("DL", 0, 4096, 8), a("LIB"))] + [(a("DL", 7168 + 3072 * v, 7184 + 3072 * v, 8), a("ONF", 0, 16, 8)) for v in range(3)], 0.6)
     book = spread(0, 4096, 7.3)
-    ops[book]["behind"].add(last)
     cp(a("LSF", 0, 130, 8), a("LS", 0, 130, 8))
     mm(a("B0", 300, 301), a("G8T", 0, 128, 8), a("LSF", 128, 129, 8))
     cp(a("IN0", 7, 8), a("B0", 300, 301))
-    es(a("THL", p=8), a("ONF", 0, 96, 8), a("LSF", 129, 130, 8))
+    es(a("THL", p=8), a("ONF", 0, 96, 8), a("LSF", 129, 130, 8), -0.5)
     acc(a("B0", 0, 256), [(one(128), row(17)), (a("NI"), a("FY"))])
     ec(a("OK"), a("B0", 0, 256))
     cp(a("LBF", 0, 8), a("LB"))
@@ -621,7 +741,7 @@ def rank_program(g, core, T, topo):
         XC = (XA, XB, XA)[v]
         CW, PR, SC = ("CW", 0), ("PR", 0), ("SC", 0)
         wd = lambda n, lo, hi: a(n[0], n[1] + lo, n[1] + hi)
-        XR = ("BIG", XC)
+        XR = ("XF", 0) if PACK else ("BIG", XC)
         nb = col(8)
         base = lambda up, lo: 8 + (64 * (up + lo // 1024) if v else 192 * up)
         names_of = lambda up, lo, hi: a(IN, base(up, lo) + lo // 16, base(up, lo) + hi // 16)
@@ -644,8 +764,6 @@ def rank_program(g, core, T, topo):
 
         def changes(p0, p):
             lo, hi = 2 * p0, 2 * (p0 + p)
-            for l in range(lo, hi, 64):
-                ts(a("HT", l, l + 64), names_of(0, 16 * l, 16 * l + 1024), -2048.0, ALU.add)
             mms([(a("B3", lo, hi, st=2), a("DF", 0, 128), a("HT", lo, hi, st=2), True, True),
                  (a("B3", lo + 1, hi, st=2), a("DF", 128, 256), a("HT", lo + 1, hi, st=2), True, False),
                  (a("B3", lo + 1, hi, st=2), a("DF", 256, 384), a("HT", lo, hi, st=2), False, True)])
@@ -653,11 +771,10 @@ def rank_program(g, core, T, topo):
             turned = lambda bank, o, k, sh, last: [(a(bank, o, o + 256, p, p0=p0), a("NL", lo + h, hi, st=2),
                                                     a("MN", 288 * k + 16 - 16 * h + sh, 288 * k + 272 - 16 * h + sh), False, last and h == 1)
                                                    for h in range(2)]
-            mms(turned("B0", 0, 2, 1, False))
-            both_ = 512 if v < 2 else 256
-            mms([(a("B2", 0, both_, p, p0=p0), a("ON", 0, p, 1), a("ROW", 256 * 14, 256 * 14 + both_, 1), True, False)] +
-                turned("B2", 0, 0, 0, v == 2) + (turned("B2", 256, 1, 0, True) if v < 2 else []))
-            ec(a("NQ", 0, both_, p, p0=p0), a("B2", 0, both_, p, p0=p0), "S")
+            mms(turned("B0", 0, 1, 1, False))
+            x, y = turned("B2", 0, 0, 0, True)
+            mms([x[:3] + (True, False), y])
+            ec(a("NQ", 0, 256, p, p0=p0), a("B2", 0, 256, p, p0=p0))
 
         def differ(c):
             p0, p = [x for x in PARTS if x[0] <= 32 * c][-1]
@@ -667,7 +784,8 @@ def rank_program(g, core, T, topo):
                 bank = AID[v].get(2 * c + h)
                 if bank:
                     ec(wd(SC, l, l + 512), key, "S")
-                    acc(a(bank), [(a("NI"), own), (a("IB"), wd(SC, l, l + 512))])
+                    mm(a(bank), a("NI"), own, True, False)
+                    more(a(bank), a("IB"), wd(SC, l, l + 512), True)
                     if ALONE[v]:
                         act(wd(SC, l, l + 512), a(bank), ACT.Sign)
                         act(wd(PR, l, l + 512), wd(SC, l, l + 512), ACT.Abs)
@@ -678,52 +796,65 @@ def rank_program(g, core, T, topo):
                 mms([(a("B5", 2 * i + h, 256, 32, 32, 32 * c), a(PR[0], PR[1] + l + i, PR[1] + l + 512, st=16), a("G8B", 0, 8),
                       False, h == 1 and i == 15) for i in range(16)])
 
-        ts(col(13), a(IN, 7, 8), -1.0, ALU.mult, col(1), ALU.add)
+        shift(col(13), a(IN, 7, 8), -1.0, col(1))
         relu(a("N12"), a("JO", 0, 192), 1.0, col(13))
         if v == 0:
             lazy[0] = True
-            gather("WN", 0, a("TON"), "OB", 4096, RQ[0], GR)
+            gather("WN", 0, a("TP" if PACK else "TON"), "OB", 4096, RQ[0], GR)
             rebuild(0)
             lazy[0] = False
         mms([(s0, a("THL", p=8), a("E8", p=8), True, False), (s0, one(96), row(1), False, False)])
         mms([(bar("B0", h), lis("N12", 1 - h), a("SH32" if h else "P32"), False, False) for h in range(2)])
-        mm(s1, one(96), nil(256, 1), True, False)
+        mm(s1, one(96), row(21) if PACK else nil(256, 1), True, False)
         mm(s5, row(8, 96, 128), row(2), True, False)
+        for up in range(2):
+            for c in range(3):
+                shift(a("HT", 192 * up + 64 * c, 192 * up + 64 * c + 64), names_of(up, 1024 * c, 1024 * c + 1024), 1.0, -2048.0)
+        lazy[0] = True
+        for gg in range(8):
+            o = lambda b: a("B6", 96 * (gg % 2) + 16 * b, 96 * (gg % 2) + 16 * b + 16, 32, p0=32 * (gg // 2))
+            mms([(o(b), a("HT", 192 * k + b, 192 * k + 192, st=6), a(("IB", "I4K")[k], 16 * gg, 16 * gg + 16), k == 0, k == 1)
+                 for b in range(6) for k in range(2)])
+        es(a("LIN"), a("B6", 0, 192), 1.0, 2048.0 * 4097)
+        laid = dmas([(a("DL", R, R + 3072, p0=h, ps=2), a("LIN", 96 * h, 96 * h + 96)) for h in range(2)], 0.5)
+        spread(R, 3088, 5.5)
+        lazy[0] = False
         for p0, p in PARTS:
             thirds = range(p0 // 32, (p0 + p) // 32)
             changes(p0, p)
             for c in thirds:
                 pieces = range(1024 * c, 1024 * c + 1024, GP)
                 for l in pieces:
-                    ec(wd(XR, l, l + GP), ind(a("TON"), names_of(0, l, l + GP)), XQ[l // GP])
+                    ec(wd(XR, l, l + GP), ind(a("TP" if PACK else "TON"), names_of(0, l, l + GP)), XQ[l // GP])
+                if PACK:
+                    l = 1024 * c
+                    dmas([(a("PN", 64 * c, 64 * c + 64), a("XF", l, l + 1024, p0=0, ps=16))], 0.4)
+                    dmas([(a("BIG", XC + l, XC + l + 1024), a("XF", l, l + 1024))], 0.95, q="G")
                 for l in pieces:
                     tt(wd(PR, l, l + GP), ind(a("TON"), names_of(1, l, l + GP)), wd(XR, l, l + GP), ALU.mult)
                 w2b("B0", PR, c, a("G8", 0, 8), True)
-            for c in thirds:
+            for c in thirds if PACK else ():
+                x, r, d = a("PN", 64 * c, 64 * c + 64), a("PD", 192 + 64 * c, 256 + 64 * c), a("PD", 64 * c, 64 * c + 64)
+                ec(r, x)
+                tt(d, x, r, ALU.subtract)
+                mms([(a("B1", 32 * gg, 32 * gg + 32, 32, p0=32 * c), a("SB2", 1 + 32 * gg - h, 33 + 32 * gg - h),
+                      a("PD", 64 * c + 32 * h, 64 * c + 32 * h + 32), False, False) for gg in range(8) for h in range(2)])
+            for c in () if PACK else thirds:
                 for l in range(1024 * c, 1024 * c + 1024, GW):
                     ec(wd(CW, l, l + GW), ind(a("PT"), names_of(0, l, l + GW)), WQ[l // GW])
                 w2b("B1", CW, c, a("SL2", 0, 8), False)
             k = len(ops)
             slots(p0, p)
-            if WAIT[0] is not None:
-                ops[k + 1]["behind"].add(book)
+            if p0 == WAIT:
+                ops[k + 1]["behind"].add(laid)
         lazy[0] = True
-        for c in range(3):
-            ts(a("HT", 192 + 64 * c, 256 + 64 * c), names_of(1, 1024 * c, 1024 * c + 1024), -2048.0, ALU.add)
-        for gg in range(8):
-            o = lambda b: a("B2", 96 * (gg % 2) + 16 * b, 96 * (gg % 2) + 16 * b + 16, 32, p0=32 * (gg // 2))
-            mms([(o(b), a("HT", 192 * k + b, 192 * k + 192, st=6), a(("IB", "I4K")[k], 16 * gg, 16 * gg + 16), k == 0, k == 1)
-                 for b in range(6) for k in range(2)])
-        es(a("LIN"), a("B2", 0, 192), 1.0, 2048.0 * 4097)
-        dmas([(a("DL", R, R + 3072, p0=h, ps=2), a("LIN", 96 * h, 96 * h + 96)) for h in range(2)], 0.5)
-        spread(R, 3088, 5.5)
+        if v < 2:
+            es(a("NQ", 256, 512, 96), a("NQ", 0, 256, 96), 63.0, 1.0)
+            ec(a("NQ", 256, 512, 96, 32), nil(8, 96))
         lazy[0] = False
-        ahead = len(ops) - 1
         differ(0)
-        if WAIT[v] is not None:
-            ops[ahead + 1 + WAIT[v]]["behind"].add(ahead)
         lazy[0] = True
-        ts(nb, a(IN, 7, 8), -1.0, ALU.mult, *((col(0), ALU.add) if v == 2 else ()))
+        shift(nb, a(IN, 7, 8), -1.0, col(0) if v == 2 else 0.0)
         scan(a("LN", p=96), a("ON", p=96), cont, 0.0, ALU.add, ALU.mult)
         mms([(s3, row(8, 96, 128), row(3), True, False)] +
             [(bar("B3", h), lis("N12", h), a("NB"), False, False) for h in range(2)])
@@ -731,6 +862,9 @@ def rank_program(g, core, T, topo):
         more(s3, s96("P5"), a("CK", p=96))
         more(s3, s96("PL"), a("LN", p=96), True)
         d0 = lambda lo, hi: a("B0", lo, hi, 96)
+        cut, at16 = a("B1", 0, 384), a("B4", 0, 16, 96)
+        mms([(cut, row(8, 128), row(18, 384), True, False), (a("B1", 0, 256), row(18, 128), row(7), False, False),
+             (a("B1", 256, 384), row(18, 128), row(7, 128), False, False), (a("B1", 256, 384), row(18, 128), row(5, 128, 128), False, False)])
         mm(a("B4", 0, 128), a("I3"), a("TB"), True, False)
         mms([(d0(0, 160), one(96), nil(160, 1), True, False), (d0(0, 8), row(10 + v // 2, 96, 128 * (v % 2)), one(8), False, False),
              (d0(8, 16), row(11, 96, 128), one(8), False, False), (d0(104, 112), row(12, 96), one(8), False, False),
@@ -748,41 +882,38 @@ def rank_program(g, core, T, topo):
         tt(sm(0), offer, high, ALU.subtract)
         if v < 2:
             es(a("RM", 0, 256), ind(a("MX"), a("BC", 112, 128)), 2.0 ** -15, 128.0, "S")
-            acc(a("B7", 0, 256, 96), [(one(96), row(16)), (i96, a("RM", 0, 256, 96))])
+            mm(a("B7", 0, 256, 96), one(96), row(16), True, False)
+            more(a("B7", 0, 256, 96), i96, a("RM", 0, 256, 96), True)
             act(a("RM", 256, 512, 96), a("B7", 0, 256, 96), ACT.Sign, 1.0, 0.5)
-            acc(a("B7", 256, 512, 96), [(s96("IL"), a("ON", p=96)), (s96("IL"), a("RM", 256, 512, 96))])
-            scan(a("YY", p=96), a("NQ", 256, 512, 96), a("B7", 256, 512, 96), 0.0, ALU.mult, ALU.max)
+            es(a("RM", 0, 256, 96), a("RM", 256, 512, 96), LOW)
+            scan(a("YY", p=96), a("NQ", 256, 512, 96), a("RM", 0, 256, 96), 0.0, ALU.mult, ALU.max)
             count(96, 16, "B7", "B6", CQ)
-        tt(a("LC", 0, 128), ind(a("SM", 0, 8), a("BC", 0, 8)), a("MI"), ALU.mult)
-        mm(a("B1", 0, 6), a("LC", 0, 128, 96), a("G8", 0, 6, 96))
+        for j in range(0, 16, 4):
+            mms([(a("B3", 0, 6), smi(0, i), a("IB", i, 96, 96, 16), i == 0, i == 15) for i in range(j, j + 4)])
         for gg in range(8):
-            ts(a("OH", 128 * gg, 128 * gg + 128, 96), a("CC1", p=96), sm(gg, 1), ALU.is_equal)
+            ts(a("OH", 128 * gg, 128 * gg + 128, 96), a("CC1", p=96), a("SM", 15 + 16 * gg, 16 + 16 * gg, 96), ALU.is_equal)
             more(a("B4", 0, 128), a("WB", 112 - 16 * gg, 240 - 16 * gg, 96), a("OH", 128 * gg, 128 * gg + 128, 96), gg == 7)
-        cp(a("OC", 0, 6), a("B1", 0, 6))
+        cp(a("OC", 0, 6), a("B3", 0, 6))
         ec(a("TBW", 1, 129), a("B4", 0, 128))
         ts(sm(8), offer, MAGIC * 2 ** 15, ALU.add, MAGIC * 2 ** 15, ALU.subtract)
         tt(sm(16), high, sm(8), ALU.subtract)
         mms([(d0(c, c + 8), s96(m), sm(k), False, False) for c, m, k in
              ((48, "IB", 0), (8, "P15", 8), (72, "P15", 8), (64, "N15", 8), (16, "N9", 16), (24, "N9", 16), (32, "N9", 16), (72, "N9", 16))])
         lazy[0] = True
-        cut, at16 = a("B1", 0, 384), a("B4", 0, 16, 96)
-        mms([(cut, row(8, 128), row(18, 384), True, False), (a("B1", 0, 256), row(18, 128), row(7), False, False),
-             (a("B1", 256, 384), row(18, 128), row(7, 128), False, False), (a("B1", 256, 384), row(18, 128), row(5, 128, 128), False, False)])
         mms([(at16, row(7, 192, 0, 2), one(16), True, False), (at16, one(96), row(5, 16, 64), False, False)])
         lazy[0] = False
         ec(a("GT"), ind(a("TBW"), a("OC", 0, 6)))
         more(d0(0, 160), a("GT"), a("SL2"), True)
-        tt(a("LC", 128, 384), ind(a("SM", 0, 32), a("BC", 8, 24)), a("M6", 128, 384), ALU.mult)
-        mms([(a("B2", 0, 12), a("LC", 128, 256, 96), a("R6", 12, 24, 96), False, False),
-             (a("B2", 6, 12), a("LC", 256, 384, 96), a("R6", 24, 30, 96), False, False)])
+        tt(a("LC"), ind(a("SM"), a("BC", 16, 32)), a("MI"), ALU.mult)
+        mms([(a("B2", 0, 12), a("LC", 0, 128, 96), a("E6", 192, 204, 96), False, False),
+             (a("B2", 6, 12), a("LC", 128, 256, 96), a("E6", 204, 210, 96), False, False)])
         ts(a("TK", p=96), d0(80, 160), col(4, 96), ALU.is_lt)
         tt(a("SQ", 0, 80, 96), d0(0, 80), a("TK", p=96), ALU.mult)
-        tt(a("PB"), ind(a("SQ", 0, 24), a("BC", 32, 48)), a("M6", 0, 256), ALU.mult)
+        tt(sm(24), d0(16, 24), a("TK", 16, 24, 96), ALU.mult)
         ec(a("QQ", 0, 128), ind(a("SQ"), a("BC", 48, 56)))
         es(a("QQ", 128, 256), ind(a("SQ"), a("BC", 56, 64)), -1.0)
-        mms([(a("B2", 0, 12), a("PB", 0, 128, 96), a("R6", 32, 44, 96), False, False),
-             (a("B2", 0, 12), a("PB", 128, 256, 96), a("R6", 0, 12, 96), False, True)])
-        mms([(a("B5", 96 * k, 96 * k + 96), a("QQ", 128 * k, 128 * k + 128, 96), a("PM", p=96), True, True) for k in range(2)])
+        mms([(a("B2", 0, 12), smi(24, i), a("E6", 12 * i, 12 * i + 12, 96), False, i == 15) for i in range(16)])
+        mms([(a("B5", 96 * k, 96 * k + 96), a("QQ", 128 * k, 128 * k + 128, 96), i96, True, True) for k in range(2)])
         ts(a("OP", 0, 12), a("B2", 0, 12), MAGIC, ALU.add, MAGIC, ALU.subtract)
         ec(a("QV"), a("B5", 0, 192))
         cp(ind(a("A", AV[v], AV[v] + 576), a("OP", 0, 12)), a("QV"))
@@ -812,8 +943,8 @@ def rank_program(g, core, T, topo):
         ts(a("OS", 0, 24), bank, float(R + 16), ALU.add, float(R + 3088), ALU.min)
         es(a("XM"), cut, -1.0, q="S")
         hf = lambda c: a("HF", c, c + 16, 96)
-        ts(hf(0), at16, 1.0 / 256, ALU.mult, MAGIC, ALU.add)
-        ts(hf(32), hf(0), MAGIC, ALU.subtract, 256.0, ALU.mult)
+        es(hf(0), at16, 1.0 / 256, MAGIC)
+        es(hf(32), hf(0), 256.0, -256 * MAGIC)
         tt(hf(16), at16, hf(32), ALU.subtract)
         tt(a("AD", 512, 768), ind(a("HF", 0, 16), a("BC", 0, 16)), a("CD"), ALU.is_lt)
         tt(a("AD", 0, 256), ind(a("HF", 16, 32), a("BC", 0, 16)), a("CA"), ALU.is_lt)
@@ -832,7 +963,10 @@ def rank_program(g, core, T, topo):
             mms([(a("B3", 128, 256), a("I3"), a("TB"), True, False)] +
                 [(a("B3", 128, 256, 32, p0=32 * (gg // 2)), a("Z3", 48 * (gg // 2) + 16 * (gg % 2), 48 * (gg // 2) + 16 * (gg % 2) + 32, 96),
                   a("OH", 128 * gg, 128 * gg + 128, 96), False, gg % 2 == 1) for gg in range(8)])
-            ec(a("TB"), a("B3", 128, 256))
+            if v < 2:
+                ec(a("TB"), a("B3", 128, 256))
+            for m in range(4 * (v // 2)):
+                ec(a("TB", 32 * m, 32 * m + 32), a("B3", 128 + m, 256, st=4))
 
         table()
         if v < 2:
@@ -840,13 +974,15 @@ def rank_program(g, core, T, topo):
                 es(a("OH2", 128 * gg, 128 * gg + 128, 96), a("OH", 128 * gg, 128 * gg + 128, 96), a("TK", gg, gg + 1, 96), q=OQ)
             acc(a("B7", 0, 256), [(one(128), row(7)), (row(8, 128), one(256))], False)
             mms([(a("B7", h, 256, st=2), a("SQ3", 128 * h, 128 * h + 128), a("TB"), False, False) for h in range(2)])
-            for h in range(2):
-                first = lambda gg: 32 * (8 * h + gg) + 16 * (1 - gg % 2)
-                mms([(a("B7", h, 256, 32, 2, 32 * (gg // 2)), a("P2", first(gg), first(gg) + 32, 96),
-                      a("OH2", 128 * gg, 128 * gg + 128, 96), False, h == 1 and gg % 2 == 1) for gg in range(8)])
-            ts(a("OK2"), a("B7", 0, 256), 32.0, ALU.add, 7199.0, ALU.min)
+            first = lambda h, gg: 32 * (8 * h + gg) + 16 * (1 - gg % 2)
+            w = 128 // QUART
+            for l in range(0, 128, w):
+                mms([(a("B7", 2 * l + h, 2 * l + 2 * w, 32, 2, 32 * (gg // 2)), a("P2", first(h, gg), first(h, gg) + 32, 96),
+                      a("OH2", 128 * gg + l, 128 * gg + l + w, 96), False, h == 1 and gg % 2 == 1) for h in range(2) for gg in range(8)])
+                ts(a("OK2", 2 * l, 2 * l + 2 * w), a("B7", 2 * l, 2 * l + 2 * w), 32.0, ALU.add, 7199.0, ALU.min)
             nx = v + 1
-            cp(a("YI", 0, 192), piece)
+            cp(a("YI", 0, 64), ind(a("SN"), a("OX", 0, 4)))
+            cp(a("YI", 64, 192), ind(a("SN"), a("OX", 4, 12)))
             for c in range(3):
                 x, o = a("YI", 64 * c, 64 * c + 64), 192 + 128 * c
                 ts(a("YI", o, o + 64), x, 4095, ALU.bitwise_and)
@@ -860,28 +996,28 @@ def rank_program(g, core, T, topo):
         else:
             def part(y, n, o, out):
                 ts(a("YI", y + n, y + 2 * n), a("YI", y, y + n), 12, ALU.arith_shift_right)
-                ts(a("YI", y + 2 * n, y + 3 * n), a("YI", y, y + n), 4095, ALU.bitwise_and)
+                relu(a(o, 0, n), a("YI", y + n, y + 2 * n), 4096.0)
                 ec(a(out, 0, n), a("YI", y + n, y + 2 * n))
-                tt(a(out, n, 2 * n), a("YI", y + 2 * n, y + 3 * n), a("YI", y, y + n), ALU.min)
-            mm(a("B6", 0, 8), one(128), nil(8, 1), True, False)
-            mms([(a("B6", k, 8, st=2), a("MB", 15 - i, 143 - i), a("TB", 64 * k + 4 * i, 64 * k + 4 * i + 4), False, k == 1 and i == 15)
-                 for k in range(2) for i in range(16)])
+                tt(a(out, n, 2 * n), a("YI", y, y + n), a(o, 0, n), ALU.subtract)
+            for j in (0, 8):
+                mms([(a("B6", 0, 8), a("MB", 15 - i, 143 - i), a("TB", i, 128, st=16), i == 0, i == 15) for i in range(j, j + 8)])
             for h in range(2):
                 ts(a("OK2", 8 * h, 8 * h + 8), a("B6", 0, 8), 16.0 + 16 * h, ALU.add, float(R + 3088), ALU.min)
             acc(a("B7", 0, 256), [(one(128), row(6)), (row(8, 128), row(9))], False)
-            mms([(a("B7", 128 * h + 32 * m, 128 * h + 32 * m + 32), a("SQ3", 256, 384), a("TB", m, 128, st=4), False, h == 1 and m == 3)
+            mms([(a("B7", 128 * h + 32 * m, 128 * h + 32 * m + 32), a("SQ3", 256, 384), a("TB", 32 * m, 32 * m + 32), False, h == 1 and m == 3)
                  for h in range(2) for m in range(4)])
             relu(a("OK"), a("B7", 0, 256), 2.0 ** 25)
             es(a("OK"), a("OK"), 1.0, -1.0, "S")
             tt(a("UT"), ind(win, a("OK2", 0, 16)), a("OK"), ALU.min)
             issue("V", lambda q: g.vector.transpose(T.MX[:], T.UT[:]), [a("UT")], [a("MX")], CALL + CY * 256)
-            cp(a("YI", 576, 832), ind(a("MX"), a("BC", 96, 112)))
-            part(576, 256, 0, "ZO")
-            dmas([(ext(z[h::2, :]), a("ZO", 256 * k + 128 * h, 256 * k + 128 * h + 128))
-                  for k, z in enumerate((T.zu, T.zt)) for h in range(2)], 1.0)
+            cp(a("YI", 384, 640), ind(a("MX"), a("BC", 96, 112)))
+            part(384, 256, "B2", "ZO")
+            for k, z in enumerate((T.zu, T.zt)):
+                dmas([(ext(z[h::2, :]), a("ZO", 256 * k + 128 * h, 256 * k + 128 * h + 128)) for h in range(2)], 0.5)
             tt(a("YI", 0, 192), piece, a("NV"), ALU.min)
-            part(0, 192, 0, "YO")
-            dmas([(ext(T.yu[:]), a("YO", 0, 192)), (ext(T.yt[:]), a("YO", 192, 384))], 0.7)
+            part(0, 192, "B5", "YO")
+            dmas([(ext(T.yu[:]), a("YO", 0, 192))], 0.35)
+            dmas([(ext(T.yt[:]), a("YO", 192, 384))], 0.35)
 
     if not PLAN:
         PLAN["ops"] = ops

import math
import numpy as np
from concourse.mybir import AluOpType as ALU, AxisListType as AX, ActivationFunctionType as ACT

F, BF, I, U, H = "float32", "bfloat16", "int32", "uint16", "float16"
KA, XA, KB, XB, KEND = 4128, 8256, 11328, 15456, 18528
AV = (768, 384, 0)
GP = 512
PARTS = ((0, 64), (64, 32))
MAGIC = 1.5 * 2 ** 23
CY, PC, GA, SCA, CALL, SAME, HAND, LDMA, RDMA, RCALL = 0.87e-3, 0.44e-3, 1.25e-3, 3.2e-3, 0.05, 0.11, 0.12, 2.0, 2.6, 0.55
PASSES, LEAN, PHAND, FIRST = 8, 0.0, 0.26, 2.0
LOADS = "bt pt t0 t1 bk bl pu l8 bu"
XQ, WQ, OQ, CQ, RQ, GR, GW, LZ, AHEAD = "EEEEEE", "EEEEEE", "E", "E", ("E", "E"), 1024, 512, False, True
WAIT, MOVES = 0, 12000
ROUNDS, ALSO = 1000, ((0.8, ((1.4, 1.0), 1.3, 1.3, 1.0, 1.1, 1.2)), (0.8, ((1.0, 1.4), 1.0, 1.0, 1.5, 1.0, 1.0)),
                      (0.8, ((1.0, 1.0), 1.0, 1.4, 1.3, 0.75, 1.8)), (0.7, ((1.2, 1.2), 1.5, 2.0, 1.0, 1.25, 1.0)))
SB = {
    "TON": ([128, 4096], BF), "BIG": ([128, KEND], BF), "PS": ([128, 6144], BF),
    "T0": ([128, 512], BF), "PN": ([128, 192], F), "PD": ([128, 384], BF), "PK": ([128, 128], BF), "SB2": ([128, 272], BF),
    "W": ([128, 13344], F), "A": ([128, 1344], BF), "SE": ([128, 384], BF), "XM": ([128, 384], BF),
    "G1": ([128, 384], F), "SN": ([128, 384], F), "YI": ([128, 896], I), "HT": ([128, 384], H),
    "LIN": ([128, 192], F), "LIB": ([128, 256], F), "HF": ([128, 48], F), "AD": ([128, 784], BF), "XL": ([128, 128], F),
    "OX": ([128, 16], U), "CD": ([128, 256], F), "CA": ([128, 256], BF), "MY": ([128, 256], BF), "TRI": ([128, 192], BF),
    "IN0": ([128, 392], U), "IN1": ([128, 392], U), "IN2": ([128, 392], U), "SD0": ([128, 392], U), "SD1": ([128, 392], U),
    "NQ": ([128, 512], BF), "NL": ([128, 192], BF), "DF": ([128, 384], BF), "MN": ([128, 576], BF),
    "UT": ([128, 256], F), "ZB": ([128, 528], BF),
    "L2": ([128, 384], I), "L3": ([128, 768], I), "LB": ([128, 8], I), "LBF": ([128, 32], F), "LS": ([128, 136], I), "LSF": ([128, 272], F),
    "ST": ([128, 256], BF),
    "ON": ([128, 256], BF), "ONF": ([128, 256], F),
    "IB": ([128, 128], BF), "NS": ([128, 128], BF), "NB": ([128, 128], BF), "NI": ([128, 128], BF),
    "P32": ([128, 128], BF), "EA": ([128, 128], BF), "EB": ([128, 128], BF), "I3": ([128, 128], BF), "I4K": ([128, 128], BF),
    "E8": ([128, 256], F), "SG": ([128, 256], BF),
    "IS": ([128, 128], BF), "I16": ([128, 128], BF), "CAP": ([128, 256], BF),
    "FY": ([128, 256], BF), "RM": ([128, 512], BF), "YY": ([128, 256], BF),
    "G4": ([128, 160], BF), "G8": ([128, 16], BF), "G8T": ([128, 256], F),
    "G8B": ([128, 16], BF), "ROW": ([128, 5632], BF), "ROF": ([128, 1040], F), "JO": ([128, 384], F),
    "COL": ([128, 16], F), "CI": ([128, 8], I), "BC": ([128, 144], U), "BCF": ([128, 176], F),
    "E6": ([128, 224], BF), "MI": ([128, 256], BF), "LC": ([128, 256], BF), "RR": ([128, 128], F),
    "OH2": ([128, 1024], BF), "PL": ([128, 128], BF), "P5": ([128, 128], BF), "P15": ([128, 128], BF),
    "N63": ([128, 128], BF), "N15": ([128, 128], BF), "N9": ([128, 128], BF), "CC1": ([128, 128], BF),
    "SL2": ([128, 160], BF), "MS": ([128, 144], BF), "MB": ([128, 144], BF),
    "WB": ([128, 240], BF), "SQ3": ([128, 384], BF), "THL": ([128, 96], F), "TMP": ([128, 192], BF),
    "NE": ([128, 272], BF), "N12": ([128, 192], BF), "SH32": ([128, 128], BF),
    "CK": ([128, 256], BF), "KK": ([128, 256], BF), "LN": ([128, 256], BF), "FS": ([128, 256], BF),
    "MX": ([128, 256], F), "OK": ([128, 256], BF), "TT": ([128, 512], BF), "P2": ([128, 528], BF),
    "NB0": ([128, 272], BF),
    "SM": ([128, 576], BF), "SF": ([128, 16], F), "TK": ([128, 80], F), "SQ": ([128, 112], BF),
    "OH": ([128, 1024], BF), "QQ": ([128, 256], BF),
    "Z3": ([128, 192], BF), "TB": ([128, 128], BF), "TBW": ([128, 144], BF), "GT": ([128, 96], BF), "QV": ([128, 192], BF),
    "OC": ([128, 8], U), "OP": ([128, 16], U), "OD": ([128, 192], U), "OS": ([128, 32], U),
    "OK2": ([128, 256], U), "OB": ([128, 256], U), "OE": ([128, 8], U), "EV": ([128, 128], BF),
    "NV": ([128, 192], BF), "YO": ([128, 384], F), "ZO": ([128, 512], F),
}
PACK, SANY, QUART, AGAIN, FILLD = False, True, 1, False, False
SB.update({"TP": ([128, 4096], F), "XF": ([128, 3072], F)} if PACK else {"PT": ([128, 4096], BF), "CW": ([128, 3072], BF)})
LIES = {"PR": ("PS", 0, 3072), "SC": ("PS", 3072, 3072), "TH": ("PS", 0, 4096), "WN": ("BIG", KB + 32, 4096), "RW": ("BIG", KA + 32, 4096)}
ZERO, STEP = 65.0 / 2048, 2.0 ** -20
GDMA, GFIRST = 0.6, 1.5
POOL = {}
for _p, _names in (("CB", "IB NI NS NB P32 EA EB IS I16 PL P5 P15 N15 N9 CAP I3 I4K CC1 E6 SL2 G4 G8 CA MY TRI MS MB WB"),
                   ("CF", "RR E8 G8T THL CD")):
    _o = 0
    for _n in _names.split():
        POOL[_n] = (_p, _o)
        _o += (SB[_n][0][1] + 15) // 16 * 16
    SB[_p] = ([128, _o], SB[_n][1])
SCRATCH = {k: ("sbuf", v[0], v[1]) for k, v in SB.items() if k not in POOL}
SB["DL"] = ([8, 13328], F)
SCRATCH["DL"] = ("dram",) + SB["DL"]
for _b in range(8):
    SCRATCH["B%d" % _b] = ("psum", [128, 512], F)
SEMAPHORES = ["qV", "qS", "qP", "qG", "sent"] + ["d%d" % k for k in range(48)] + ["r%d" % k for k in range(10)]
LOW = 2.0 ** -93
AID = 3 * ({1: "B7", 3: "B6"},)
ALONE = (True, True, True)
PLAN = {}


def settle(ops):
    n = len(ops)
    before = [sorted(o["deps"] | o["behind"]) for o in ops]
    after = [[] for _ in ops]
    for k in range(n):
        for j in before[k]:
            after[j].append(k)
    tail = [o["lat"] + o["move"] for o in ops]
    loose = ([o["behind"] - o["deps"] for o in ops], [set() for _ in ops])
    for k in range(n):
        for j in loose[0][k]:
            loose[1][j].add(k)
    hard = [[[j for j in x[k] if j not in y[k]] for k in range(n)] for x, y in zip((before, after), loose)]
    gap = {p + q: (0.0 if q == "P" else SAME) if p == q else (PHAND if p == "P" else HAND) for p in "VSPGY" for q in "VSPGY"}
    way = ["R" if o["sem"] and o["sem"][0][0] == "r" else "D" for o in ops]

    def sweep(rank, back):
        src, dst = (after, before) if back else (before, after)
        left = [len(x) for x in src]
        ready = [(rank[k], k) for k in range(n) if not left[k]]
        slots = {q: [] for q in "VSPGYDR"}
        t0, t1, on = [0.0] * n, [0.0] * n, [None] * n

        def fit(q, t, d):
            x = slots[q]
            i = len(x)
            while i and x[i - 1][1] > t:
                i -= 1
            while i < len(x) and x[i][0] < t + d:
                t = x[i][1]
                i += 1
            return t, i
        while ready:
            k = min(ready)
            ready.remove(k)
            k = k[1]
            o, best = ops[k], None
            for q in ("VS" if o["q"] == "E" else o["q"]):
                t = 0.0
                for j in hard[back][k]:
                    e = t1[j] + (gap[q + on[j]] if back else gap[on[j] + q])
                    if e > t:
                        t = e
                d = o["cost"][q == "V"]
                if back:
                    if o["move"]:
                        t, i = fit(way[k], t, o["move"])
                        slots[way[k]].insert(i, (t, t + o["move"]))
                    t += tail[k]
                for j in loose[back][k]:
                    t = max(t, t0[j] + 1e-3)
                t, i = fit(q, t, d)
                key = t + d + (lean[0] * d if q == "V" else 0.0)
                if best is None or key < best[0]:
                    best = (key, q, t, d, i)
            _, q, t, d, i = best
            on[k], t0[k], t1[k] = q, t, t + d
            slots[q].insert(i, (t, t + d))
            if not back:
                t1[k] += o["lat"]
                if o["move"]:
                    m, i = fit(way[k], t1[k], o["move"])
                    slots[way[k]].insert(i, (m, m + o["move"]))
                    t1[k] = m + o["move"]
            for j in dst[k]:
                left[j] -= 1
                if not left[j]:
                    ready.append((rank[j], j))
        return t0, t1, on

    rank = [0.0] * n
    for k in range(n - 1, -1, -1):
        rank[k] = min(rank[j] for j in after[k]) - 1e-4 if ops[k]["lazy"] and after[k] else k
    def replay(order, on, slow, pe, hand, far, ga, near):
        end, free = [0.0] * n, {q: 0.0 for q in "VSPGYDR"}
        for k in order:
            o, q = ops[k], on[k]
            t = max([free[q]] + [end[j] + (0.0 if q == on[j] == "P" else hand * (PHAND if on[j] == "P" else HAND)) for j in o["deps"]])
            free[q] = t + o["cost"][q == "V"] * (pe if q == "P" else slow[q == "V"] * (ga if o["ga"] else 1.0))
            end[k] = free[q] + o["lat"] * far
            if o["move"]:
                free[way[k]] = end[k] = max(end[k], free[way[k]]) + o["move"] * (far if way[k] == "R" else near)
        return max(end)

    def mixed(r, m=n + 4):
        x = (np.arange(m, dtype=np.uint64) + np.uint64(r * 7919 * 4096 + 1)) * np.uint64(0x9E3779B97F4A7C15)
        x = (x ^ (x >> np.uint64(31))) * np.uint64(0xBF58476D1CE4E5B9)
        return (x >> np.uint64(40)).astype(float) / 2 ** 24

    kept, lean = None, [LEAN]
    for r in range(PASSES + 2 * ROUNDS):
        if r >= PASSES and (r - PASSES) % 2 == 0:
            t, u = np.array(kept[1]), mixed(r)
            lo = u[n] * kept[3]
            rank = list(t + ((t > lo) & (t < lo + 3 + 12 * u[n + 1])) * (u[:n] - 0.5) * (1.0, 2.8, 5.0)[int(3 * u[n + 2])])
            lean[0] = (0.0, 0.1, 0.3)[int(3 * u[n + 3])]
        rank[:len(LOADS.split())] = range(-len(LOADS.split()) - 999, -999)
        t0, t1, on = sweep(rank, False)
        order = sorted(range(n), key=lambda k: (t0[k], k))
        worth = max(t1) + sum(w * replay(order, on, *x) for w, x in ALSO)
        if kept is None or worth < kept[0]:
            kept = (worth, t0, on, max(t1), order)
        if r < PASSES or (r - PASSES) % 2 == 0:
            rank = [-x for x in sweep([-x for x in t1], True)[1]]
    PLAN["time"], PLAN["worth"] = kept[3], kept[0]
    return polish(ops, kept[4], kept[2], way, mixed)


def polish(ops, order, on, way, mixed):
    n = len(ops)
    deps = [sorted(o["deps"]) for o in ops]
    must = [o["deps"] | o["behind"] for o in ops]
    cases = ((1.0, ((1.0, 1.0),) + 5 * (1.0,)),) + ALSO

    def replay(order, on, slow, pe, hand, far, ga, near, why=None):
        end, free, last = [0.0] * n, dict.fromkeys("VSPGYDR", 0.0), {}
        hp, hh = hand * PHAND, hand * HAND
        for k in order:
            o, q = ops[k], on[k]
            t, w = free[q], -1
            for j in deps[k]:
                e = end[j] + ((0.0 if q == "P" else hp) if on[j] == "P" else hh)
                if e > t:
                    t, w = e, j
            if why:
                why[k], last[q] = (w, False) if w >= 0 else (last.get(q), True), k
            t += o["cost"][q == "V"] * (pe if q == "P" else slow[q == "V"] * (ga if o["ga"] else 1.0))
            free[q] = t
            if o["move"]:
                t, x = t + o["lat"] * far, way[k]
                if free[x] > t:
                    t = free[x]
                    if why:
                        why[k] = (last.get(x), True)
                last[x] = k
                free[x] = t = t + o["move"] * (far if x == "R" else near)
            end[k] = t
        return end

    worth = lambda order, on: sum(w * max(replay(order, on, *x)) for w, x in cases)
    now, links = worth(order, on), None
    kept = (now, order, on)
    for r in range(MOVES):
        u = mixed(10 ** 6 + r, 5)
        if links is None:
            why = [0] * n
            end = replay(order, on, *cases[int(u[4] * len(cases))][1], why)
            k, links, either = end.index(max(end)), [], []
            while k is not None:
                j, queued = why[k]
                either += [k] * (ops[k]["q"] == "E")
                links += [(j, k)] * (queued and j is not None)
                k = j
            place = {k: i for i, k in enumerate(order)}
        order2, on2 = order, on
        if u[0] < 0.3:
            k = either[int(u[1] * len(either))]
            on2 = on[:k] + ["S" if on[k] == "V" else "V"] + on[k + 1:]
        else:
            j, k = links[int(u[1] * len(links))]
            lo, hi, up = place[j], place[k], u[0] < 0.65
            for _ in range(int(u[2] * 3)):
                far = [i for i in (range(lo - 1, -1, -1) if up else range(hi + 1, n)) if on[order[i]] == on[k]][:1]
                lo, hi = (far[0] if far and up else lo), (far[0] if far and not up else hi)
            if up:
                need, moved = set(must[k]), {k}
                for x in order[hi - 1:lo - 1 if lo else None:-1]:
                    if x in need:
                        need |= must[x]
                        moved.add(x)
            else:
                moved = {j}
                for x in order[lo + 1:hi + 1]:
                    if must[x] & moved:
                        moved.add(x)
            if order[lo if up else hi] in moved or lo <= max(place[x] for x in range(len(LOADS.split()))):
                continue
            part = order[lo:hi + 1]
            order2 = order[:lo] + [x for x in part if (x in moved) == up] + [x for x in part if (x in moved) != up] + order[hi + 1:]
        w = worth(order2, on2)
        if w < now or u[3] < math.exp((now - w) / (0.04 * (1 - r / MOVES) + 1e-3)):
            order, on, now, links = order2, on2, w, None
            if w < kept[0]:
                kept = (w, order, on)
    PLAN["time"], PLAN["worth"] = max(replay(kept[1], kept[2], *cases[0][1])), kept[0]
    return kept[1], kept[2]


def rank_program(g, core, T, topo):
    rank = T.rank_of(core)
    if rank is None:
        return
    nxt, prv = T.cores[(rank + 3) % 8], T.cores[(rank - 3) % 8]
    Q = {"V": g.vector, "S": g.scalar, "P": g.tensor, "G": g, "Y": g.sync}
    ops, hist, nd, lazy, cast = [], {}, [0], [False], []

    def a(n, c0=None, c1=None, p=128, st=1, p0=0, ps=1):
        w = SB[n][0][1] if n in SB else (LIES[n][2] if n in LIES else 512)
        c0 = 0 if c0 is None else c0
        c1 = w if c1 is None else c1
        if n in LIES:
            n, c0, c1 = LIES[n][0], c0 + LIES[n][1], c1 + LIES[n][1]
        t, o = (T[POOL[n][0]], POOL[n][1]) if n in POOL else (T[n], 0)
        ap = t[p0:p0 + p, o + c0:o + c1:st] if st > 1 else (t[p0::ps, o + c0:o + c1] if ps > 1 else t[p0:p0 + p, o + c0:o + c1])
        return (ap, [(n, c0, c1, st)], (c1 - c0 + st - 1) // st, False)

    def ind(w, o):
        return (w[0].indirect(o[0]), w[1] + o[1], 16 * o[2], True)

    def ext(ap):
        return (ap, [], 0, False)

    def kind(x):
        n = x[1][0][0]
        return SB[n][1] if n in SB else "psum"

    def issue(q, fn, reads, writes, cost, lat=0.0, move=0.0, sem=None, after=()):
        k, deps = len(ops), set(after)
        rw = [(r, False) for x in reads for r in x[1]] + [(r, True) for x in writes for r in x[1]]
        for (n, c0, c1, st), isw in rw:
            for (h0, h1, hw, j, hs) in hist.get(n, []):
                if n in SB:
                    if h1 <= c0 or c1 <= h0 or not (hw or isw) or (st > 1 and hs == st and (c0 - h0) % st != 0):
                        continue
                    if move and ops[j]["move"] and hw and isw:
                        continue
                deps.add(j)
        for (n, c0, c1, st), isw in rw:
            h = hist.setdefault(n, [])
            if n not in SB:
                h[:] = []
            elif isw and st == 1 and not move:
                h[:] = [e for e in h if not (c0 <= e[0] and e[1] <= c1)]
            h.append((c0, c1, isw, k, st))
        deps.discard(k)
        ops.append({"q": q, "fn": fn, "deps": deps, "cost": cost if isinstance(cost, tuple) else (cost, cost), "lat": lat,
                    "move": move, "sem": sem, "ga": any(x[3] for x in reads + writes), "lazy": lazy[0], "behind": set(), "name": (rw[-1][0][:2], rw[0][0][:2]) if rw else ()})
        return ops[k]

    def price(o, ins, f=1.0):
        if o[3]:
            return CALL + SCA * o[2]
        if ins and ins[0][3]:
            return CALL + GA * o[2]
        if f < 2 and all(kind(x) in (BF, U, H) for x in [o] + ins[:2] if x[2] > 1):
            f = 0.5
        return CALL + CY * max(64, f * o[2])

    def both(o, i):
        return (CALL + (GA * o[2] if i[3] else CY * max(64, o[2])), price(o, [i]))

    def dmas(items, move, after=(), q="Y"):
        sem = "d%d" % nd[0]
        nd[0] += 1

        def fn(q):
            for o, i in items:
                Q[q].dma_start(o[0], i[0]).then_inc(T.sem[sem], 16)
        cost = CALL * len(items)
        if q == "G":
            cost = GDMA * len(items) + (0.0 if cast else GFIRST)
            cast.append(sem)
        issue(q, fn, [i for o, i in items], [o for o, i in items], cost, LDMA, move, (sem, 16 * len(items)), after)
        return len(ops) - 1

    def sc(x):
        return x[0] if isinstance(x, tuple) else x

    def tl(*xs):
        return [x for x in xs if isinstance(x, tuple)]

    def cp(o, i):
        if SANY and not o[3]:
            return ec(o, i)
        issue("V", lambda q: g.vector.tensor_copy(o[0], i[0]), [i], [o], price(o, [i]))

    def shift(o, i, scale, bias):
        es(o, i, scale, bias, "E" if SANY else "V")

    def tt(o, x, y, op):
        issue("V", lambda q: g.vector.tensor_tensor(o[0], x[0], y[0], op), [x, y], [o],
              price(o, [x, y], 1.0 if "psum" in (kind(x), kind(y)) else 2.0))

    def ts(o, x, s1, op0, s2=None, op1=None):
        if op1 is None:
            issue("V", lambda q: g.vector.tensor_scalar(o[0], x[0], sc(s1), None, op0), tl(x, s1), [o], price(o, [x]))
        else:
            issue("V", lambda q: g.vector.tensor_scalar(o[0], x[0], sc(s1), sc(s2), op0, op1), tl(x, s1, s2), [o], price(o, [x]))

    def scan(o, d0, d1, init, op0, op1):
        issue("V", lambda q: g.vector.tensor_tensor_scan(o[0], d0[0], d1[0], sc(init), op0, op1), tl(d0, d1, init), [o],
              price(o, [d0, d1]))

    def ms(o, v):
        issue("V", lambda q: g.vector.memset(o[0], v), [], [o], price(o, []))

    def red(o, i):
        issue("V", lambda q: g.vector.tensor_reduce(o[0], i[0], AX.X, ALU.add), [i], [o], CALL + CY * max(64, i[2]))

    def act(o, i, f, scale=1.0, bias=0.0):
        issue("S", lambda q: g.scalar.activation(o[0], i[0], f, bias=sc(bias), scale=scale), tl(i, bias), [o],
              CALL + CY * max(64, o[2]))

    def relu(o, i, scale, bias=0.0):
        act(o, i, ACT.Relu, scale, bias)

    def ec(o, i, q="E"):
        issue(q, lambda q: g.vector.tensor_copy(o[0], i[0]) if q == "V" else g.scalar.activation(o[0], i[0], ACT.Copy),
              [i], [o], both(o, i))

    def es(o, i, scale, bias=0.0, q="E"):
        issue(q, lambda q: g.vector.tensor_scalar(o[0], i[0], sc(scale), sc(bias), ALU.mult, ALU.add) if q == "V" else
              g.scalar.activation(o[0], i[0], ACT.Identity, bias=sc(bias), scale=sc(scale)), tl(i, scale, bias), [o], both(o, i))

    def fill(o, v):
        z = a("ZB", 0, o[2])
        issue("E", lambda q: g.vector.memset(o[0], v) if q == "V" else g.scalar.activation(o[0], z[0], ACT.Identity, bias=v, scale=1.0),
              [z], [o], both(o, z))

    def gather(out, o0, win, offs, n, q="E", gp=GP):
        for l in range(0, n, gp):
            ec(a(out, o0 + l, o0 + l + gp), ind(win, a(offs, l // 16, (l + gp) // 16)), q[l // gp % len(q)])

    def mms(items):
        def fn(q):
            for o, l, r, s0, s1 in items:
                ins = g.tensor.matmul(o[0], l[0], (r if isinstance(r, tuple) else r(None))[0], s0, s1)
            return ins
        rs = [r if isinstance(r, tuple) else r("V") for o, l, r, s0, s1 in items]
        issue("P", fn, [x[1] for x in items] + rs, [x[0] for x in items],
              sum(PC * max(min(64, x[1][2]), r[2] if isinstance(x[2], tuple) else 4) * (4 if kind(x[1]) == F else 1)
                  for x, r in zip(items, rs)))

    def mm(o, l, r, s0=True, s1=True):
        mms([(o, l, r, s0, s1)])

    def more(o, l, r, last=False):
        mm(o, l, r, False, last)

    def acc(o, prs, close=True):
        mms([(o, l, r, k == 0, close and k == len(prs) - 1) for k, (l, r) in enumerate(prs)])

    def io(o, pat, base=0, cm=0):
        if kind(o) == I:
            issue("G", lambda q: g.iota(o[0], pat, base, cm), [], [o], 0.13 + 2 * CY * o[2])
        else:
            issue("G", lambda q: g.iota(o[0], pat, base, cm, allow_small_or_imprecise_dtypes=True), [], [o], 0.13 + 2 * CY * o[2])

    def sel(o, i, pat, op, base, cm, fill=0.0):
        issue("G", lambda q: g.affine_select(o[0], i[0], pat, op, fill, base, cm), [i], [o], 0.17 + 2 * CY * o[2])

    def put(o, i, pat, base, v):
        sel(o, i, [[-s, n] for s, n in pat], ALU.not_equal, -base, 1, v)

    def band(o, tmp, i, pat, lo, hi):
        sel(tmp, i, [[-s, n] for s, n in pat], ALU.is_ge, -lo, 1)
        sel(o, tmp, pat, ALU.is_ge, hi, -1)

    col = lambda k, p=128: a("COL", k, k + 1, p)
    sm = lambda c: a("SM", 18 * c + 15, 18 * c + 143, 96, 16)
    smi = lambda c, i: a("SM", 18 * c + 15 - i, 18 * c + 143 - i, 96)
    i96 = a("IB", 0, 96, 96)
    s96 = lambda n: a(n, 0, 96, 96)
    one = lambda m: a("ON", 0, m, 1)
    nil = lambda m, p=128: a("ZB", 0, m, p)
    row = lambda k, n=256, o=0, st=1: a("ROW", 256 * k + o, 256 * k + o + n, 1, st)
    bar = lambda n, h: a(n, h, 256, 96, 2)
    lis = lambda n, h, o=0: a(n, o + h, o + 192, 128, 2)

    def count(W, gs, tb, cb, q="E"):
        n, off = 16 * gs, gs - 8
        TH = "TH" if off or PACK else "PT"
        if off:
            mms([(a(tb, W * j, W * j + W), a("YY", 128 * (j % 2), 128 * (j % 2) + 128, W), a("IS" if j // 2 else "IB", 0, W, W), True, True)
                 for j in range(4)])
            ec(a("TT", 0, 4 * W), a(tb, 0, 4 * W))
        else:
            for j in range(2):
                mms([(a(tb, W * j + m, W * j + W, 32, 8, 32 * g4), a("YY", 32 * m, 32 * m + 32),
                      a("IB", 64 * j + 16 * g4, 64 * j + 16 * g4 + 16), True, True) for g4 in range(4) for m in range(8)])
            ec(a("TT", 0, 2 * W), a(tb, 0, 2 * W))
            es(a("TT", 2 * W, 4 * W), a("TT", 0, 2 * W), 64.0 ** -16)
        sums = a(cb, 0, n, W)
        mm(sums, one(W), row(13, n) if off else nil(n, 1), True, False)
        for k in range(8):
            o, x, hi = a(TH, 512 * k, 512 * k + 4 * W), a("TT", 0, 4 * W), LOW * 64.0 ** (2 * k + 1)
            op = issue(q, lambda q, o=o, x=x, hi=hi:
                       g.vector.tensor_scalar(o[0], x[0], hi, hi, ALU.min, ALU.subtract) if q == "V" else
                       g.scalar.activation(o[0], x[0], ACT.Relu, bias=hi, scale=-1.0),
                       [x], [o], (CALL + CY * 4 * W, CALL + CY * 2 * W))
            wt = lambda q, op=op, k=k: a("G4", 0, 64) if q else a("G4", 4 * k + 32 * (op["q"] == "V"), 4 * k + 32 * (op["q"] == "V") + 4)
            mms([(a(cb, off + k + 4 * gs * j, 4 * gs * (j + 1), W, gs), a(TH, 512 * k + W * j, 512 * k + W * j + W), wt,
                  False, k == 7 and j == 3) for j in range(4)])
        es(a("P2", 1, 2 * n, W, 2), sums, 1.0 / 64, 128.25)
        if AGAIN:
            more(sums, a("N63", 0, W, W), a("P2", 1, 2 * n, W, 2), True)
            es(a("P2", 0, 2 * n, W, 2), sums, 1.0, 8192.0)
        else:
            es(a("UT", 0, n, W), a("P2", 1, 2 * n, W, 2), 63.0, -8192.0)
            tt(a("P2", 0, 2 * n, W, 2), sums, a("UT", 0, n, W), ALU.subtract)

    def w2b(bank, wide, c, rhs, close):
        mms([(a(bank, s, 256, 32, 32, 32 * c), a(wide[0], wide[1] + 1024 * c + s, wide[1] + 1024 * c + 1024, st=32), rhs,
              False, close and s == 31) for s in range(32)])

    def rebuild(v):
        K = (KA, KB, KA)[v]
        gather("BIG", K + 32, (a("WN"), a("BIG", KA, KB), a("BIG", KB, KEND))[v], "OK2", 4096, RQ[v > 0], GR)
        ec(a("EV"), ind(a("BIG", K, K + 4128), a("OE")))
        cp(ind(a("BIG", 0, KA), a("OE")), a("EV"))

    def spread(lo, n, move):
        return dmas([(a("W", 16 - r + lo, 16 - r + lo + n, p0=r, ps=16), a("DL", lo, lo + n, 8)) for r in range(16)], move)

    loads = {"bt": ([(a("L3", 256, 512), ext(T.bt[:]))], 0.6), "pt": ([(a("L2", 0, 192), ext(T.pt[:]))], 0.5),
             "bk": ([(a("L3", 512, 768), ext(T.bk[:]))], 0.6), "pu": ([(a("L2", 192, 384), ext(T.pu[:]))], 0.5),
             "t0": ([(a("TON", 0, 2048), ext(T.tones[:, 0:2048]))], 1.8), "t1": ([(a("TON", 2048, 4096), ext(T.tones[:, 2048:4096]))], 1.8),
             "bl": ([(a("LS", 0, 128, 8), ext(T.bl[:])), (a("LS", 128, 129, 8), ext(T.pn[:])), (a("LS", 129, 130, 8), ext(T.th[:]))], 0.1),
             "z": ([(a("T0", 0, 256), ext(T.tones[0::16, :]))], 0.4),
             "l8": ([(a("LB", 0, 8), ext(T.bl[:]))], 0.25), "bu": ([(a("L3", 0, 256), ext(T.bu[:]))], 0.6)}
    for k, n in enumerate(LOADS.split()):
        dmas(*loads[n], q="YS"[k % 2])

    ms(a("ZB"), 0.0)
    ms(a("ON"), 1.0)
    ms(a("ONF"), 1.0)
    if FILLD:
        ms(a("SC", 1024, 1024 + KA // 4), 99.0)
    diag = [[1, 128]]
    put(a("IB"), nil(128), diag, 0, 1.0)
    if PACK:
        ec(a("PK", p=16), nil(128, 16))
        x = a("PK", 0, 128, 16, 16)
        put(x, x, [[1, 8]], 0, 1.0)
        put(x, x, [[1, 8]], 8, STEP)
        ts(a("T0", 0, 256), a("T0", 0, 256), 0.0, ALU.is_equal, ZERO, ALU.mult)
        es(a("T0", 256, 512), a("L3", 512, 768), 1.0, -63.0)
        last = dmas([(a("RW", p=8, p0=8 * k), a("T0", 256 * k, 256 * k + 256)) for k in range(2)], 0.8)
        for j in range(8):
            bank, l = a("B%d" % (0, 1, 2, 4, 5)[j % 5]), 512 * j
            acc(bank, [(a("IB"), a("TON", l, l + 512)), (a("PK", p=16), a("RW", l, l + 512, 16))])
            ec(a("TP", l, l + 512), bank)
    lazy[0] = True
    if PACK:
        ec(a("SB2"), nil(272))
        put(a("SB2", 1, 257, st=2), nil(128), diag, 0, 32 / STEP)
        es(row(21), one(256), 2048.0)
    for n, v in (("NI", -1.0), ("P32", 32768.0), ("EA", float(KA)), ("EB", float(KB)), ("I4K", 4096.0),
                 ("NS", -16384.0), ("NB", -float(2 ** 25)), ("IS", 64.0 ** -16), ("I16", 16.0),
                 ("PL", 2.0 ** 15 + 2 ** 9), ("P5", 2.0 ** -5), ("P15", 2.0 ** -15), ("N15", -2.0 ** -15), ("N9", -2.0 ** -9)):
        es(a(n), a("IB"), v)
    sel(a("I3"), a("IB"), [[0, 8], [-1, 16]], ALU.is_ge, 2, 0)
    sel(a("SG"), a("ON"), [[0, 8], [1, 32]], ALU.is_gt, 0, 0)
    sel(a("CAP"), nil(256), [[0, 8], [1, 32]], ALU.is_equal, 0, 0, float(2 ** 99))
    sel(a("CAP"), a("CAP"), [[0, 8], [1, 32]], ALU.is_gt, 0, 0, LOW)
    put(a("E8", p=8), nil(256, 8), [[1, 8], [0, 32]], 0, -1.0)
    sel(a("G4", 64, 96), a("ON", 0, 32), [[0, 8], [1, 4]], ALU.is_gt, 0, 0, 64.0 ** -2)
    ms(col(11), 64.0 ** 2 / LOW / 2 ** 20)
    scan(a("G4", 96, 128), a("G4", 64, 96), a("ON", 0, 32), col(11), ALU.mult, ALU.mult)
    band(a("G4", 96, 128), a("G4", 128, 160), a("G4", 96, 128), [[0, 8], [32, 4]], 0, 30)
    es(a("G4", 0, 32), a("G4", 96, 128), float(2 ** 20))
    es(a("G4", 32, 64), a("G4", 96, 128), -float(2 ** 20))
    grp = [[16, 8]]
    band(a("G8", 0, 8), a("G8", 8, 16), a("ON", 0, 8), grp, 0, 15)
    sel(a("G8T", 0, 128, 8), a("ONF", 0, 128, 8), [[1, 8], [0, 16]], ALU.is_equal, 0, -1)
    sel(a("G8T", 128, 256, 8), a("ONF", 0, 128, 8), [[1, 128]], ALU.is_equal, -2, -16)
    for lo, hi in ((40, 80), (144, 160)):
        ec(a("SL2", lo, hi), nil(hi - lo))
    for lo, hi, r, s in ((0, 24, 0, 1), (24, 40, 2, 0), (80, 144, 3, 0)):
        put(a("SL2", lo, hi), nil(hi - lo), [[s, (hi - lo) // 8], [16, 8]], r, 1.0)
    io(a("CC1"), [[1, 128]], 1)
    io(a("RR"), [[0, 8], [1, 16]])
    io(row(1), [[0, 256]], -16384)
    io(a("ROW", 256 + 31, 512, 1, 32), [[0, 8]], 32768)
    io(row(2), [[0, 256]], -6 * 1024)
    io(row(13), [[0, 16], [-1984, 2], [0, 8]], 1984)
    es(a("G8B", 0, 8), a("G8", 0, 8), float(2 ** 25))
    io(row(3), [[0, 8], [-1, 32]], 31)
    io(row(4, 96), [[-1, 96]], -129)
    io(row(5, 24), [[256, 24]])
    io(row(5, 24, 32), [[0, 24]], 16)
    io(row(5, 16, 64), [[16, 2], [0, 8]], -111)
    sel(row(5, 16, 80), nil(16, 1), [[1, 2], [0, 8]], ALU.is_gt, 0, 0, 14.5)
    sel(row(5, 16, 80), row(5, 16, 80), [[-1, 2], [0, 8]], ALU.is_ge, 0, 0, 0.5)
    io(row(5, 128, 128), [[0, 128]], 4096)
    io(row(6), [[-16, 2], [0, 128]], 1)
    io(row(7), [[16, 256]])
    io(row(8, 128), [[0, 8], [1, 16]])
    io(row(8, 96, 128), [[0, 96]], 2 ** 15)
    io(row(9), [[0, 256]], -1)
    for v in range(3):
        io(row(10 + v // 2, 96, 128 * (v % 2)), [[-1, 48], [0, 2]], -64 - 48 * v)
    io(row(11, 96, 128), [[0, 48], [-32, 2]], -31)
    for k in range(2):
        sel(row(12, 96, 128 * k), nil(96, 1), [[0, 6], [1 - 2 * k, 2], [0, 8]], ALU.is_equal, k, 0, float(2 ** 99))
    es(row(18, 384), nil(384, 1), 1.0, -2.0 ** 26)
    io(row(20, 128), [[0, 8], [16, 16]])
    io(a("ROF", 0, 256, 1), [[1, 16], [512, 8], [0, 2]])
    io(a("ROF", 256, 268, 1), [[34, 2], [2048, 6]], 79)
    sel(a("ROF", 272, 528, 1), a("ONF", p=1), [[-1, 2], [0, 8], [1, 16]], ALU.is_equal, 0, 0)
    io(a("ROF", 528, 656, 1), [[1, 64], [0, 2]])
    io(a("ROF", 656, 784, 1), [[0, 64], [32, 2]])
    io(a("ROF", 784, 912, 1), [[0, 8], [128, 16]])
    es(a("ROF", 912, 1040, 1), a("ONF", 0, 128, 1), 1.0 / 32)
    sel(a("E6", 0, 192), nil(192), [[-1, 16], [-1, 2], [-16, 6]], ALU.is_ge, 0, 1, 2.0 ** -4)
    for o, v in ((192, -2.0 ** -19), (198, -2.0 ** -19), (204, 2.0 ** -13)):
        es(a("E6", o, o + 6), a("G8", 0, 6), v)
    three = ("MS", "MB", "WB")
    ec((T.CB[:, POOL["MS"][1]:POOL["MS"][1] + 528], [a(n)[1][0] for n in three], 528, False), nil(528))
    for n in ("TBW", "SQ", "HF"):
        ec(a(n), nil(SB[n][0][1]))
    for l in (0, 288):
        ec(a("SM", l, l + 288), nil(288))
    ec(a("AD", 768, 784), nil(16))
    es(a("SQ", 88, 96), a("ON", 0, 8), 1.0)
    es(a("SQ", 96, 104), a("ON", 0, 8), -1.0)
    x = a("MS", 15, 143, st=16)
    for j, (r, v) in enumerate(((0, 64.0), (14, -16.0), (15, 0.0))):
        put(x, x if j else a("G8", 0, 8), grp, r, v)
    x = a("MB", 15, 143, st=16)
    put(x, nil(8), grp, 0, 64.0)
    put(x, x, grp, 1, 1.0)
    rows = [[16, 8], [0, 16]]
    put(a("SQ3", 256, 384), nil(128), rows, 2, 1.0)
    for h in range(2):
        x = a("SQ3", 128 * h, 128 * h + 128)
        io(x, [[0, 8], [1, 16]], 16 * h + 128)
        sel(x, x, [[-16, 8], [0, 16]], ALU.is_equal, -14, 1)
        put(x, x, rows, 15, 32.0)
        put(x, x, [[32, 4], [-16, 2], [0, 16]], 30, 159.0)
    x = a("MY", 0, 128)
    sel(x, nil(128), rows, ALU.is_gt, 2, -1, -2.0 ** 26)
    sel(x, x, rows, ALU.is_ge, 13, -1)
    put(x, x, rows, 14, 2.0 ** 31)
    put(a("MY", 128, 256), nil(128), rows, 15, 2.0 ** 26)
    sel(a("TRI", 0, 96), a("ON", 0, 96), [[1, 96]], ALU.is_gt, 0, -1)
    sel(a("TRI", 96, 192), a("ON", 0, 96), [[1, 96]], ALU.is_ge, 0, -1)
    for h in range(2):
        es(a("CA", 128 * h, 128 * h + 128), a("RR"), 16.0, -112.0)
        es(a("CD", 128 * h, 128 * h + 128), a("RR"), 1.0, MAGIC)
    ms(a("TBW", 0, 1), float(2 ** 98))
    for n in ("NB0", "NE"):
        ec(a(n, 0, 16), nil(16))
    put(a("DF", 128, 256), a("IB"), diag, -1, -1.0)
    ec(a("DF", 128, 256, st=16), a("IB", 0, 128, st=16))
    ec(a("DF", 0, 128), a("DF", 128, 256))
    ec(a("DF", 0, 128, st=16), nil(8))
    ec(a("DF", 256, 384), nil(128))
    put(a("DF", 256, 384, st=16), nil(8), grp, 15, -1.0)
    put(a("MN", 0, 288), nil(288), [[16, 9], [1000, 2], [1, 16]], -1000, 1.0)
    es(a("MN", 288, 576), a("MN", 0, 288), 16384.0)
    io(row(16), [[0, 8], [1, 32]], -159)
    io(row(17), [[0, 8], [1, 32]], 64)
    for o in (KA, KB):
        ec(a("BIG", o, o + 32), nil(32))
    for n in ("SD0", "SD1"):
        ms(a(n, 0, 8), 0)
    ec(a("W", 0, 16), nil(16))
    io(a("CI", 0, 1), [[0, 1]], 0, 1)
    ts(a("CI", 1, 2), a("CI", 0, 1), 15, ALU.bitwise_and)
    cp(col(0), a("CI", 1, 2))
    es(col(1), col(0), 2.0)
    ts(col(2), col(0), 15.0, ALU.is_equal, -16384.0, ALU.mult)
    es(col(10), col(0), 256.0)
    io(a("JO", 0, 192), [[32, 96], [1, 2]], 1)
    io(a("JO", 192, 384), [[16, 192]])
    put(a("SH32"), nil(128), diag, 1, 32768.0)
    es(a("TMP", 0, 96, 1), a("ON", 0, 96, 1), 0.25)
    scan(a("TMP", 96, 192, 1), a("TMP", 0, 96, 1), a("ON", 0, 96, 1), float(2 ** 96), ALU.mult, ALU.mult)
    mm(a("B5", 0, 1, 96), a("TMP", 96, 192, 1), one(1))
    es(col(4, 96), a("B5", 0, 1, 96), 2.0)
    ec(a("WB", 115, 116, 96), a("B5", 0, 1, 96))
    ec(a("MX"), nil(256))
    for o in AV:
        es(a("A", o, o + 384), nil(384), 1.0, col(2))
    io(a("BCF", 0, 16), [[1, 16]])
    io(a("BCF", 16, 32), [[144, 2], [16, 8]], 159)
    for h in range(2):
        ts(a("MI", 128 * h, 128 * h + 128), a("RR"), col(0), ALU.is_equal)
    io(a("BCF", 80, 104), [[0, 24]], 10)
    for o, picks in ((80, ((16, 0, 0), (16, 1, 8), (16, 14, 88), (16, 15, 64))),
                     (88, ((16, 0, 0), (16, 1, 8), (18, 2, 24), (18, 3, 32), (16, 14, 96), (16, 15, 72))),
                     (96, ((16, 0, 0), (16, 1, 8), (16, 2, 16), (16, 14, 40), (16, 15, 48)))):
        for s, r, v in picks:
            put(a("BCF", o, o + 8), a("BCF", o, o + 8), [[s, 8]], r, v - 70.0)
        red(col(5 + (o - 80) // 8), a("BCF", o, o + 8))
    es(a("BCF", 48, 56), a("BCF", 0, 8), 1.0, col(5))
    es(a("BCF", 56, 64), a("BCF", 0, 8), 1.0, col(6))
    io(a("BCF", 64, 76), [[0, 12]], 80)
    for o in range(2):
        es(a("BCF", 64 + 2 * o, 76, st=3), a("BCF", o, 8, st=2), 1.0, col(7))
    io(a("BCF", 112, 128), [[1, 8], [0, 2]])
    io(a("BCF", 128, 144), [[16, 2], [32, 4], [128, 2]])
    es(a("BCF", 128, 144), a("BCF", 128, 144), 1.0, col(0))
    io(a("BCF", 144, 160), [[32, 8], [0, 2]], 31)
    io(a("BCF", 160, 162), [[0, 2]], 0, 1)
    cp(a("BC", 0, 16), a("BCF", 0, 16))
    cp(a("BC", 16, 32), a("BCF", 16, 32))
    cp(a("BC", 48, 76), a("BCF", 48, 76))
    cp(a("BC", 80, 96), a("BCF", 112, 128))
    cp(a("BC", 96, 130), a("BCF", 128, 162))

    lazy[0] = False
    tt(a("NB0", 1, 256), a("L3", 257, 512), a("L3", 256, 511), ALU.not_equal)
    es(a("FY"), a("NB0", 0, 256), 63.0, 1.0)
    scan(a("YY"), a("FY"), a("CAP"), LOW, ALU.mult, ALU.min)
    count(128, 8, "B6", "B3")
    if not PACK:
        es(a("ST"), a("L3", 512, 768), 32.0, 32.0)
        last = dmas([(a("PT", p0=0, ps=16), a("ST"))], 0.4)
    if FILLD:
        dmas([(a("BIG", l, l + KA // 4), a("SC", 1024, 1024 + KA // 4)) for l in range(0, KA, KA // 4)], 4.0)
    lazy[0] = True
    for l in range(0, 0 if FILLD else KA, KA // 8):
        fill(a("BIG", l, l + KA // 8), 99.0)
    lazy[0] = False
    for l in range(2):
        cp(a("IN0", 8 + 192 * l, 200 + 192 * l), a("L2", 192 * l, 192 * l + 192))
    cp(a("OB"), a("L3", 256, 512))
    mm(a("B7", 0, 256), a("ONF", 0, 128, 1), a("ROF", 0, 256, 1), True, False)
    mms([(a("B7", h, 256, st=2), a("P2", 128 * h, 128 * h + 128), a("I16"), False, h == 1) for h in range(2)])
    shift(a("OK2"), a("B7", 0, 256), 1.0, -2048.0)
    ms(a("P2", 512, 528), 159.0)
    lazy[0] = True
    es(a("B5", 0, 256), a("L3", 0, 256), 4096.0)
    tt(a("LIB"), a("L3", 256, 512), a("B5", 0, 256), ALU.add)
    dmas([(a("DL", 0, 4096, 8), a("LIB"))] + [(a("DL", 7168 + 3072 * v, 7184 + 3072 * v, 8), a("ONF", 0, 16, 8)) for v in range(3)], 0.6)
    book = spread(0, 4096, 7.3)
    cp(a("LSF", 0, 130, 8), a("LS", 0, 130, 8))
    mm(a("B0", 300, 301), a("G8T", 0, 128, 8), a("LSF", 128, 129, 8))
    cp(a("IN0", 7, 8), a("B0", 300, 301))
    es(a("THL", p=8), a("ONF", 0, 96, 8), a("LSF", 129, 130, 8), -0.5)
    acc(a("B0", 0, 256), [(one(128), row(17)), (a("NI"), a("FY"))])
    ec(a("OK"), a("B0", 0, 256))
    cp(a("LBF", 0, 8), a("LB"))
    tt(a("FS"), ind(a("LBF", 0, 8), a("BC", 80, 96)), a("OK"), ALU.is_gt)
    scan(a("KK"), a("FS"), a("SG"), 0.0, ALU.add, ALU.mult)
    io(a("LBF", 8, 16), [[32, 8]], 32)
    es(a("LBF", 8, 16), a("LBF", 8, 16), 1.0, col(10))
    tt(a("LBF", 16, 24), a("KK", 31, 256, st=32), a("LBF", 8, 16), ALU.add)
    cp(a("OE"), a("LBF", 16, 24))
    es(a("LSF", 136, 264, 8), a("LSF", 0, 128, 8), 1.0, -1.0)
    acc(a("B7", 0, 128), [(a("G8T", 128, 256, 8), a("LSF", 136, 264, 8)), (a("ROF", 272, 400, 1), a("ROF", 528, 656, 1)),
                          (a("ROF", 400, 528, 1), a("ROF", 656, 784, 1))])
    ec(a("TB"), a("B7", 0, 128))
    lazy[0] = False

    rid, pid, _ = topo.addr(nxt)
    sent, calls = [0], []

    def remote(dst, src, sem, move):
        sent[0] += len(topo.engines(core, nxt))
        issue("G", lambda q: g.remote_dma(dst[0], src[0], T.sem[sem], T.sem["sent"], pid, rid, topo.mask(core, nxt)),
              [src], [dst], RCALL + (0.0 if calls else FIRST), RDMA - RCALL, move, (sem, len(topo.engines(prv, core))))
        ops[-1]["behind"].update(calls[-1:])
        calls.append(len(ops) - 1)

    for v in range(3):
        IN, SD = "IN%d" % v, "SD%d" % v
        R = 4096 + 3072 * v
        K = (KA, KB, KA)[v]
        XC = (XA, XB, XA)[v]
        CW, PR, SC = ("CW", 0), ("PR", 0), ("SC", 0)
        wd = lambda n, lo, hi: a(n[0], n[1] + lo, n[1] + hi)
        XR = ("XF", 0) if PACK else ("BIG", XC)
        nb = col(8)
        base = lambda up, lo: 8 + (64 * (up + lo // 1024) if v else 192 * up)
        names_of = lambda up, lo, hi: a(IN, base(up, lo) + lo // 16, base(up, lo) + hi // 16)
        cont, new = a("NE", 0, 256, 96), a("NQ", 0, 256, 96)
        s0, s1, s3, s5 = [a("B%d" % k, 0, 256, 96) for k in (0, 1, 3, 5)]

        def slots(p0, p):
            at = lambda n, lo, hi, st=1: a(n, lo, hi, p, st, p0)
            eye = lambda n: at(n, p0, p0 + p)
            out = lambda h: a("B4", 2 * p0 + p * h, 2 * p0 + p * h + p)
            mm(a("B4", 2 * p0, 2 * (p0 + p)), a("ON", 0, 128, 1, p0=p0), a("ZB", 0, 2 * p, 1, p0=p0), True, False)
            ts(at("NE", 1, 257), at("B0", 0, 256), 0.0, ALU.is_lt)
            more(at("B1", 0, 256), eye("NS"), at("NE", 0, 256), True)
            mms([(out(h), at("NE", 1 + h, 257, 2), eye("EB" if v == 1 else "EA"), False, False) for h in range(2)])
            scan(at("KK", 0, 256), at("NQ", 0, 256), at("NE", 0, 256), 0.0, ALU.add, ALU.mult)
            mms([(out(h), at("KK", h, 256, 2), eye("IB"), False, False) for h in range(2)])
            scan(at("CK", 0, 256), at("NE", 0, 256), at("B1", 0, 256), 0.0, ALU.mult, ALU.max)
            mms([(out(h), at("CK", h, 256, 2), eye("IB"), False, h == 1) for h in range(2)])
            cp(a("OD", 2 * p0, 2 * (p0 + p)), a("B4", 2 * p0, 2 * (p0 + p)))

        def changes(p0, p):
            lo, hi = 2 * p0, 2 * (p0 + p)
            mms([(a("B3", lo, hi, st=2), a("DF", 0, 128), a("HT", lo, hi, st=2), True, True),
                 (a("B3", lo + 1, hi, st=2), a("DF", 128, 256), a("HT", lo + 1, hi, st=2), True, False),
                 (a("B3", lo + 1, hi, st=2), a("DF", 256, 384), a("HT", lo, hi, st=2), False, True)])
            ts(a("NL", lo, hi), a("B3", lo, hi), 0.0, ALU.not_equal)
            turned = lambda bank, o, k, sh, last: [(a(bank, o, o + 256, p, p0=p0), a("NL", lo + h, hi, st=2),
                                                    a("MN", 288 * k + 16 - 16 * h + sh, 288 * k + 272 - 16 * h + sh), False, last and h == 1)
                                                   for h in range(2)]
            mms(turned("B0", 0, 1, 1, False))
            x, y = turned("B2", 0, 0, 0, True)
            mms([x[:3] + (True, False), y])
            ec(a("NQ", 0, 256, p, p0=p0), a("B2", 0, 256, p, p0=p0))

        def differ(c):
            p0, p = [x for x in PARTS if x[0] <= 32 * c][-1]
            for h in range(2):
                l, o = 1024 * c + 512 * h, p0 + p * h + 32 * c
                key, own = ind(a("BIG", 0, K + 4128), a("OD", o, o + 32)), a("BIG", XC + 1024 * c + h, XC + 1024 * c + 1024, st=2)
                bank = AID[v].get(2 * c + h)
                if bank:
                    ec(wd(SC, l, l + 512), key, "S")
                    mm(a(bank), a("NI"), own, True, False)
                    more(a(bank), a("IB"), wd(SC, l, l + 512), True)
                    if ALONE[v]:
                        act(wd(SC, l, l + 512), a(bank), ACT.Sign)
                        act(wd(PR, l, l + 512), wd(SC, l, l + 512), ACT.Abs)
                    else:
                        ts(wd(PR, l, l + 512), a(bank), 0.0, ALU.not_equal)
                else:
                    tt(wd(PR, l, l + 512), key, own, ALU.not_equal)
                mms([(a("B5", 2 * i + h, 256, 32, 32, 32 * c), a(PR[0], PR[1] + l + i, PR[1] + l + 512, st=16), a("G8B", 0, 8),
                      False, h == 1 and i == 15) for i in range(16)])

        shift(col(13), a(IN, 7, 8), -1.0, col(1))
        relu(a("N12"), a("JO", 0, 192), 1.0, col(13))
        if v == 0:
            lazy[0] = True
            gather("WN", 0, a("TP" if PACK else "TON"), "OB", 4096, RQ[0], GR)
            rebuild(0)
            lazy[0] = False
        mms([(s0, a("THL", p=8), a("E8", p=8), True, False), (s0, one(96), row(1), False, False)])
        mms([(bar("B0", h), lis("N12", 1 - h), a("SH32" if h else "P32"), False, False) for h in range(2)])
        mm(s1, one(96), row(21) if PACK else nil(256, 1), True, False)
        mm(s5, row(8, 96, 128), row(2), True, False)
        for up in range(2):
            for c in range(3):
                shift(a("HT", 192 * up + 64 * c, 192 * up + 64 * c + 64), names_of(up, 1024 * c, 1024 * c + 1024), 1.0, -2048.0)
        lazy[0] = True
        for gg in range(8):
            o = lambda b: a("B6", 96 * (gg % 2) + 16 * b, 96 * (gg % 2) + 16 * b + 16, 32, p0=32 * (gg // 2))
            mms([(o(b), a("HT", 192 * k + b, 192 * k + 192, st=6), a(("IB", "I4K")[k], 16 * gg, 16 * gg + 16), k == 0, k == 1)
                 for b in range(6) for k in range(2)])
        es(a("LIN"), a("B6", 0, 192), 1.0, 2048.0 * 4097)
        laid = dmas([(a("DL", R, R + 3072, p0=h, ps=2), a("LIN", 96 * h, 96 * h + 96)) for h in range(2)], 0.5)
        spread(R, 3088, 5.5)
        lazy[0] = False
        for p0, p in PARTS:
            thirds = range(p0 // 32, (p0 + p) // 32)
            changes(p0, p)
            for c in thirds:
                pieces = range(1024 * c, 1024 * c + 1024, GP)
                for l in pieces:
                    ec(wd(XR, l, l + GP), ind(a("TP" if PACK else "TON"), names_of(0, l, l + GP)), XQ[l // GP])
                if PACK:
                    l = 1024 * c
                    dmas([(a("PN", 64 * c, 64 * c + 64), a("XF", l, l + 1024, p0=0, ps=16))], 0.4)
                    dmas([(a("BIG", XC + l, XC + l + 1024), a("XF", l, l + 1024))], 0.95, q="G")
                for l in pieces:
                    tt(wd(PR, l, l + GP), ind(a("TON"), names_of(1, l, l + GP)), wd(XR, l, l + GP), ALU.mult)
                w2b("B0", PR, c, a("G8", 0, 8), True)
            for c in thirds if PACK else ():
                x, r, d = a("PN", 64 * c, 64 * c + 64), a("PD", 192 + 64 * c, 256 + 64 * c), a("PD", 64 * c, 64 * c + 64)
                ec(r, x)
                tt(d, x, r, ALU.subtract)
                mms([(a("B1", 32 * gg, 32 * gg + 32, 32, p0=32 * c), a("SB2", 1 + 32 * gg - h, 33 + 32 * gg - h),
                      a("PD", 64 * c + 32 * h, 64 * c + 32 * h + 32), False, False) for gg in range(8) for h in range(2)])
            for c in () if PACK else thirds:
                for l in range(1024 * c, 1024 * c + 1024, GW):
                    ec(wd(CW, l, l + GW), ind(a("PT"), names_of(0, l, l + GW)), WQ[l // GW])
                w2b("B1", CW, c, a("SL2", 0, 8), False)
            k = len(ops)
            slots(p0, p)
            if p0 == WAIT:
                ops[k + 1]["behind"].add(laid)
        lazy[0] = True
        if v < 2:
            es(a("NQ", 256, 512, 96), a("NQ", 0, 256, 96), 63.0, 1.0)
            ec(a("NQ", 256, 512, 96, 32), nil(8, 96))
        lazy[0] = False
        differ(0)
        lazy[0] = True
        shift(nb, a(IN, 7, 8), -1.0, col(0) if v == 2 else 0.0)
        scan(a("LN", p=96), a("ON", p=96), cont, 0.0, ALU.add, ALU.mult)
        mms([(s3, row(8, 96, 128), row(3), True, False)] +
            [(bar("B3", h), lis("N12", h), a("NB"), False, False) for h in range(2)])
        more(s3, s96("NB"), a("NE", 1, 257, 96))
        more(s3, s96("P5"), a("CK", p=96))
        more(s3, s96("PL"), a("LN", p=96), True)
        d0 = lambda lo, hi: a("B0", lo, hi, 96)
        cut, at16 = a("B1", 0, 384), a("B4", 0, 16, 96)
        mms([(cut, row(8, 128), row(18, 384), True, False), (a("B1", 0, 256), row(18, 128), row(7), False, False),
             (a("B1", 256, 384), row(18, 128), row(7, 128), False, False), (a("B1", 256, 384), row(18, 128), row(5, 128, 128), False, False)])
        mm(a("B4", 0, 128), a("I3"), a("TB"), True, False)
        mms([(d0(0, 160), one(96), nil(160, 1), True, False), (d0(0, 8), row(10 + v // 2, 96, 128 * (v % 2)), one(8), False, False),
             (d0(8, 16), row(11, 96, 128), one(8), False, False), (d0(104, 112), row(12, 96), one(8), False, False),
             (d0(112, 120), row(12, 96, 128), one(8), False, False), (d0(40, 48), one(96), one(8), False, False),
             (d0(48, 56), row(4, 96), one(8), False, False), (d0(64, 80), one(96), row(5, 16, 80), False, False)])
        acc(a("B2", 0, 12), [(a("ROF", 912, 1040, 1), a("ROF", 256, 268, 1)), (a("ROF", 784, 912, 1), a("ROF", 912, 924, 1))], False)
        lazy[0] = False
        differ(1)
        differ(2)
        scan(a("FS", p=96), cont, s5, 0.0, ALU.mult, ALU.max)
        tt(a("UT", p=96), s3, a("FS", p=96), ALU.subtract)
        scan(a("MX", p=96), a("SG", p=96), a("UT", p=96), 0.0, ALU.mult, ALU.max)
        offer, high = a("MX", 31, 256, 96, 32), a("SF", 0, 8, 96)
        ts(high, offer, MAGIC * 2 ** 9, ALU.add, MAGIC * 2 ** 9, ALU.subtract)
        tt(sm(0), offer, high, ALU.subtract)
        if v < 2:
            es(a("RM", 0, 256), ind(a("MX"), a("BC", 112, 128)), 2.0 ** -15, 128.0, "S")
            mm(a("B7", 0, 256, 96), one(96), row(16), True, False)
            more(a("B7", 0, 256, 96), i96, a("RM", 0, 256, 96), True)
            act(a("RM", 256, 512, 96), a("B7", 0, 256, 96), ACT.Sign, 1.0, 0.5)
            es(a("RM", 0, 256, 96), a("RM", 256, 512, 96), LOW)
            scan(a("YY", p=96), a("NQ", 256, 512, 96), a("RM", 0, 256, 96), 0.0, ALU.mult, ALU.max)
            count(96, 16, "B7", "B6", CQ)
        for j in range(0, 16, 4):
            mms([(a("B3", 0, 6), smi(0, i), a("IB", i, 96, 96, 16), i == 0, i == 15) for i in range(j, j + 4)])
        for gg in range(8):
            ts(a("OH", 128 * gg, 128 * gg + 128, 96), a("CC1", p=96), a("SM", 15 + 16 * gg, 16 + 16 * gg, 96), ALU.is_equal)
            more(a("B4", 0, 128), a("WB", 112 - 16 * gg, 240 - 16 * gg, 96), a("OH", 128 * gg, 128 * gg + 128, 96), gg == 7)
        cp(a("OC", 0, 6), a("B3", 0, 6))
        ec(a("TBW", 1, 129), a("B4", 0, 128))
        ts(sm(8), offer, MAGIC * 2 ** 15, ALU.add, MAGIC * 2 ** 15, ALU.subtract)
        tt(sm(16), high, sm(8), ALU.subtract)
        mms([(d0(c, c + 8), s96(m), sm(k), False, False) for c, m, k in
             ((48, "IB", 0), (8, "P15", 8), (72, "P15", 8), (64, "N15", 8), (16, "N9", 16), (24, "N9", 16), (32, "N9", 16), (72, "N9", 16))])
        lazy[0] = True
        mms([(at16, row(7, 192, 0, 2), one(16), True, False), (at16, one(96), row(5, 16, 64), False, False)])
        lazy[0] = False
        ec(a("GT"), ind(a("TBW"), a("OC", 0, 6)))
        more(d0(0, 160), a("GT"), a("SL2"), True)
        tt(a("LC"), ind(a("SM"), a("BC", 16, 32)), a("MI"), ALU.mult)
        mms([(a("B2", 0, 12), a("LC", 0, 128, 96), a("E6", 192, 204, 96), False, False),
             (a("B2", 6, 12), a("LC", 128, 256, 96), a("E6", 204, 210, 96), False, False)])
        ts(a("TK", p=96), d0(80, 160), col(4, 96), ALU.is_lt)
        tt(a("SQ", 0, 80, 96), d0(0, 80), a("TK", p=96), ALU.mult)
        tt(sm(24), d0(16, 24), a("TK", 16, 24, 96), ALU.mult)
        ec(a("QQ", 0, 128), ind(a("SQ"), a("BC", 48, 56)))
        es(a("QQ", 128, 256), ind(a("SQ"), a("BC", 56, 64)), -1.0)
        mms([(a("B2", 0, 12), smi(24, i), a("E6", 12 * i, 12 * i + 12, 96), False, i == 15) for i in range(16)])
        mms([(a("B5", 96 * k, 96 * k + 96), a("QQ", 128 * k, 128 * k + 128, 96), i96, True, True) for k in range(2)])
        ts(a("OP", 0, 12), a("B2", 0, 12), MAGIC, ALU.add, MAGIC, ALU.subtract)
        ec(a("QV"), a("B5", 0, 192))
        cp(ind(a("A", AV[v], AV[v] + 576), a("OP", 0, 12)), a("QV"))
        sq = lambda c: a("SQ", c, c + 8, 96)
        mms([(a("B4", 0, 8, 96), a("TRI", 0, 96, 96), sq(16), False, False), (a("B4", 0, 8, 96), i96, sq(64), False, False),
             (a("B4", 8, 16, 96), a("TRI", 96, 192, 96), sq(16), False, False), (a("B4", 8, 16, 96), s96("NI"), sq(72), False, True)])
        mm(a("B3", 0, 1, 8), a("SQ", 16, 24, 96), a("ON", 0, 1, 96))
        ec(a("SF", 8, 9, 8), a("B3", 0, 1, 8))
        mm(a("B3", 2, 3), a("G8T", 0, 128, 8), a("SF", 8, 9, 8))
        win = a("W", 0, R + 3089)
        if v == 2:
            ts(col(9), a("B3", 2, 3), nb, ALU.subtract, 2.0 ** 25, ALU.mult)
            relu(a("NV"), a("JO", 192, 384), -2.0 ** 25, col(9))
            es(a("NV"), a("NV"), 1.0, -1.0, "S")
        else:
            ts(a(SD, 7, 8), a("B3", 2, 3), nb, ALU.subtract, 3072.0, ALU.min)
            if AHEAD and v == 0:
                remote(a("IN1", 0, 8), a(SD, 0, 8), "r9", 0.3)

        own = a("A", AV[v], AV[v] + 384)
        scan(a("SE"), own, nil(384), 0.0, ALU.add, ALU.add)
        more(cut, a("MY", 128, 256), own)
        more(cut, a("MY", 0, 128), a("SE"), True)
        bank = a("B0", 0, 24)
        acc(bank, [(one(128), row(5, 24)), (row(8, 128), row(5, 24, 32))], False)
        mms([(bank, a("MS", 15 - i, 143 - i), a("SE", i, 384, st=16), False, i == 15) for i in range(16)])
        ts(a("OS", 0, 24), bank, float(R + 16), ALU.add, float(R + 3088), ALU.min)
        es(a("XM"), cut, -1.0, q="S")
        hf = lambda c: a("HF", c, c + 16, 96)
        es(hf(0), at16, 1.0 / 256, MAGIC)
        es(hf(32), hf(0), 256.0, -256 * MAGIC)
        tt(hf(16), at16, hf(32), ALU.subtract)
        tt(a("AD", 512, 768), ind(a("HF", 0, 16), a("BC", 0, 16)), a("CD"), ALU.is_lt)
        tt(a("AD", 0, 256), ind(a("HF", 16, 32), a("BC", 0, 16)), a("CA"), ALU.is_lt)
        es(a("AD", 256, 512, 96), a("AD", 0, 256, 96), -1.0, 1.0, "S")
        ad = lambda c: a("AD", c, c + 128, 96)
        acc(a("B4", 0, 128), [(one(128), row(20, 128)), (row(8, 128), one(128)), (ad(0), ad(513)), (ad(128), ad(641)),
                              (ad(256), ad(512)), (ad(384), ad(640))])
        ec(a("XL"), a("B4", 0, 128))
        cp(a("OX"), ind(a("XL"), a("BC", 128, 129)))
        tt(a("G1"), ind(win, a("OS", 0, 24)), a("XM"), ALU.min)
        scan(a("SN"), cut, a("G1"), 0.0, ALU.min, ALU.max)
        piece = ind(a("SN"), a("OX", 0, 12))

        def table():
            es(a("Z3"), ind(a("SQ"), a("BC", 64, 76)), -1.0)
            mms([(a("B3", 128, 256), a("I3"), a("TB"), True, False)] +
                [(a("B3", 128, 256, 32, p0=32 * (gg // 2)), a("Z3", 48 * (gg // 2) + 16 * (gg % 2), 48 * (gg // 2) + 16 * (gg % 2) + 32, 96),
                  a("OH", 128 * gg, 128 * gg + 128, 96), False, gg % 2 == 1) for gg in range(8)])
            if v < 2:
                ec(a("TB"), a("B3", 128, 256))
            for m in range(4 * (v // 2)):
                ec(a("TB", 32 * m, 32 * m + 32), a("B3", 128 + m, 256, st=4))

        table()
        if v < 2:
            for gg in range(8):
                es(a("OH2", 128 * gg, 128 * gg + 128, 96), a("OH", 128 * gg, 128 * gg + 128, 96), a("TK", gg, gg + 1, 96), q=OQ)
            acc(a("B7", 0, 256), [(one(128), row(7)), (row(8, 128), one(256))], False)
            mms([(a("B7", h, 256, st=2), a("SQ3", 128 * h, 128 * h + 128), a("TB"), False, False) for h in range(2)])
            first = lambda h, gg: 32 * (8 * h + gg) + 16 * (1 - gg % 2)
            w = 128 // QUART
            for l in range(0, 128, w):
                mms([(a("B7", 2 * l + h, 2 * l + 2 * w, 32, 2, 32 * (gg // 2)), a("P2", first(h, gg), first(h, gg) + 32, 96),
                      a("OH2", 128 * gg + l, 128 * gg + l + w, 96), False, h == 1 and gg % 2 == 1) for h in range(2) for gg in range(8)])
                ts(a("OK2", 2 * l, 2 * l + 2 * w), a("B7", 2 * l, 2 * l + 2 * w), 32.0, ALU.add, 7199.0, ALU.min)
            nx = v + 1
            cp(a("YI", 0, 64), ind(a("SN"), a("OX", 0, 4)))
            cp(a("YI", 64, 192), ind(a("SN"), a("OX", 4, 12)))
            for c in range(3):
                x, o = a("YI", 64 * c, 64 * c + 64), 192 + 128 * c
                ts(a("YI", o, o + 64), x, 4095, ALU.bitwise_and)
                ts(a("YI", o + 64, o + 128), x, 12, ALU.arith_shift_right)
                cp(a(SD, 128 * c + 8, 128 * c + 136), a("YI", o, o + 128))
                lo = 128 * c + 8 if c or (AHEAD and v == 0) else 0
                remote(a("IN%d" % nx, lo, 128 * c + 136), a(SD, lo, 128 * c + 136), "r%d" % (5 * v + c), 1.2)
            lazy[0] = LZ
            rebuild(nx)
            lazy[0] = False
        else:
            def part(y, n, o, out):
                ts(a("YI", y + n, y + 2 * n), a("YI", y, y + n), 12, ALU.arith_shift_right)
                relu(a(o, 0, n), a("YI", y + n, y + 2 * n), 4096.0)
                ec(a(out, 0, n), a("YI", y + n, y + 2 * n))
                tt(a(out, n, 2 * n), a("YI", y, y + n), a(o, 0, n), ALU.subtract)
            for j in (0, 8):
                mms([(a("B6", 0, 8), a("MB", 15 - i, 143 - i), a("TB", i, 128, st=16), i == 0, i == 15) for i in range(j, j + 8)])
            for h in range(2):
                ts(a("OK2", 8 * h, 8 * h + 8), a("B6", 0, 8), 16.0 + 16 * h, ALU.add, float(R + 3088), ALU.min)
            acc(a("B7", 0, 256), [(one(128), row(6)), (row(8, 128), row(9))], False)
            mms([(a("B7", 128 * h + 32 * m, 128 * h + 32 * m + 32), a("SQ3", 256, 384), a("TB", 32 * m, 32 * m + 32), False, h == 1 and m == 3)
                 for h in range(2) for m in range(4)])
            relu(a("OK"), a("B7", 0, 256), 2.0 ** 25)
            es(a("OK"), a("OK"), 1.0, -1.0, "S")
            tt(a("UT"), ind(win, a("OK2", 0, 16)), a("OK"), ALU.min)
            issue("V", lambda q: g.vector.transpose(T.MX[:], T.UT[:]), [a("UT")], [a("MX")], CALL + CY * 256)
            cp(a("YI", 384, 640), ind(a("MX"), a("BC", 96, 112)))
            part(384, 256, "B2", "ZO")
            for k, z in enumerate((T.zu, T.zt)):
                dmas([(ext(z[h::2, :]), a("ZO", 256 * k + 128 * h, 256 * k + 128 * h + 128)) for h in range(2)], 0.5)
            tt(a("YI", 0, 192), piece, a("NV"), ALU.min)
            part(0, 192, "B5", "YO")
            dmas([(ext(T.yu[:]), a("YO", 0, 192))], 0.35)
            dmas([(ext(T.yt[:]), a("YO", 192, 384))], 0.35)

    if not PLAN:
        PLAN["ops"] = ops
        PLAN["order"], PLAN["on"] = settle(ops)
    order = PLAN["order"]
    cnt, fin, seen = {}, {"sent": sent[0]}, {q: {} for q in Q}
    for k in order:
        o = ops[k]
        o["q"], o["own"] = PLAN["on"][k], o["sem"] is None
        if o["own"]:
            cnt[o["q"]] = cnt.get(o["q"], 0) + 1
            o["sem"] = ("q" + o["q"], cnt[o["q"]])
        fin[o["sem"][0]] = o["sem"][1]
    for k in order:
        o = ops[k]
        q, need = o["q"], {}
        for d in o["deps"]:
            if not (q == ops[d]["q"] == "P"):
                sem, val = ops[d]["sem"]
                need[sem] = max(need.get(sem, 0), val)
        for sem, val in need.items():
            if seen[q].get(sem, 0) < val:
                Q[q].wait_ge(T.sem[sem], val)
                seen[q][sem] = val
        ins = o["fn"](q)
        if o["own"]:
            ins.then_inc(T.sem[o["sem"][0]], 1)
    for sem, val in fin.items():
        if seen["G"].get(sem, 0) < val:
            g.wait_ge(T.sem[sem], val)
